import numpy as np, ml_dtypes
CORES = [24,25,26,27,28,29,30,31]
N = 8
BF = ml_dtypes.bfloat16
def gentries(a):
    return np.ascontiguousarray(a.reshape(8, 16, -1).transpose(0, 2, 1)).reshape(8, -1)
def gtable(e):
    e = np.asarray(e); return np.ascontiguousarray(e.reshape(8, -1, 16).transpose(0, 2, 1)).reshape(128, -1).astype(np.int32)
I, L, S, T, H, R = 3328, 256, 2, 5, 11, 2
M = L // S
W = I + R * (L + M)
def pack(F, sel, P):
    return {"front": np.ascontiguousarray(F.reshape(N, 128, I)).astype(np.float32).astype(BF), "sel0": np.ascontiguousarray(sel).astype(np.int32), "par": np.stack([gtable(a.reshape(8, -1)) for a in P])}
def rows8(rng):
    return (np.argsort(rng.random((8, 16)), axis=1) < 8)[None, :, :, None]
def of_class(rng, cl, want, n):
    order = np.argsort(cl + 0.5 * rng.random(cl.shape), axis=-1)
    cnt = np.stack([np.add.reduce((cl == c).astype(np.int64), axis=-1) for c in range(n)], axis=-1)
    first = np.add.accumulate(cnt, axis=-1) - cnt; w = want.reshape(N, 8, -1)
    at = np.take_along_axis(first, w, 2) + (np.take_along_axis(cnt, w, 2) * rng.random(w.shape)).astype(np.int64)
    return np.take_along_axis(order, np.minimum(at, I - 1), 2).reshape(want.shape)
def setup_inputs(rng):
    hi = rows8(rng); share = rng.choice(np.array([0.06, 0.12, 0.2]), (N, 8, 1))
    cl = np.where(rng.random((N, 8, I)) < share, 0, 1 + rng.integers(0, 2, (N, 8, I)))
    u = rng.random((N, 8, 16, I)); c = cl[:, :, None, :]
    F = np.where((c > 0) & ((c == 1) == hi), 128 + 128 * u, np.where(c == 0, 64 * u, 101 * u)).astype(np.int64)
    y = rng.random((N, 8, I)); sel = of_class(rng, cl, np.where((cl == 0) | (y < 0.15), 0, np.where(y < 0.2, 3 - cl, cl)), 3)
    free = rng.permutation(8) < 2; F = np.where(free[None, :, None, None], (256 * u).astype(np.int64), F)
    return pack(F, sel, rng.integers(0, I, (N, 8, L, 16)))
def setup_inputs_spread(rng):
    a = np.exp2(8 * rng.random((N, 8, 16, I))); b = np.exp2(8 * rng.random((N, 8, 1, I))) * rng.random((N, 8, 16, I))
    even = (rng.permutation(8) < 5)[None, :, None, None]
    F = np.minimum(np.where(even, a, b).astype(np.int64), 255) * (rng.random((N, 8, 1, I)) > 0.0625)
    low = (rng.permutation(8) < 4)[None, :, None]
    v = (I * rng.random((N, 8, I)) ** 3).astype(np.int64); sel = np.where(low, v, I - 1 - v)
    w = (I * rng.random((N, 8, L, 16)) ** 2).astype(np.int64); P = np.where(low[..., None], I - 1 - w, w)
    return pack(F, sel, P)
def setup_inputs_ends(rng):
    hi = rows8(rng); up = np.where(hi, np.add.accumulate(hi.astype(np.int64), axis=2), np.add.accumulate((~hi).astype(np.int64), axis=2)) - 1
    cl = rng.choice(np.array([0, 1, 1, 1, 2, 2, 2]), (N, 8, I))
    cl[..., [0, 1]] = 2; cl[..., I - 1] = 1; cl[..., [2, 3, I - 2]] = 3; cl[..., [4, 5, I - 3]] = 0
    off = rng.integers(0, 8, (2, N, 8, 1, I)); off[..., [0, 1, I - 1]] = 8; c = cl[:, :, None, :]
    F = 255 * ((c == 3) | ((c > 0) & ((c == 1) == hi) & (up != off[0]) & (up != off[1]))).astype(np.int64)
    F[..., 1] = np.where((~hi & (up == 7))[..., 0], 254, F[..., 1]); F[:, :, 15, 3] = 254
    for g in range(8): F[:, g, 2 * g + 1, 5] = 1
    sel = np.where(rng.random((N, 8, I)) < 0.75, (I - 1) * rng.integers(0, 2, (N, 8, I)), rng.integers(0, I, (N, 8, I)))
    cross = rng.random((N, 8)) < 0.3; cross[0, 0] = False; cross[N - 1, 7] = False; cross[0, 7] = True
    sel[..., 0] = np.where(cross, I - 1, 0); sel[..., I - 1] = np.where(cross, 0, I - 1); sel[..., 1] = 1
    inner = of_class(rng, cl, rng.choice(np.array([0, 1, 1, 1, 2, 2, 2]), (N, 8, L, 16)), 4)
    P = np.where(rng.random((N, 8, L, 16)) < 0.75, np.where(rng.random((N, 8, L, 16)) < rng.random((N, 8, L, 1)), I - 1, 0), inner)
    P[:, :, L - 1] = 1; P[:, :, L - 1, 15] = I - 1; P[:, :, 0] = 1; P[:, :, 0, 8] = I - 1
    P[:, :, L - 2] = 3; P[:, :, L - 2, 12:14] = 0
    P[:, ::2, L - 2, 5] = 2; P[:, ::2, L - 2, 10] = I - 2; P[:, 1::2, L - 2, 5] = I - 2; P[:, 1::2, L - 2, 10] = 2; P[:, :, L - 2, 15] = I - 2
    P[:, :, L - 3] = 4; P[:, :, L - 3, ::3] = I - 3
    P[:, :, L - 4] = 4; P[:, :, L - 4, 3] = 5; P[:, :, L - 4, 15] = 5
    P[::2, :, S] = 4; P[::2, :, S, ::3] = I - 3
    P[1::2, :, S] = 3; P[1::2, :, S, 9] = 2; P[1::2, :, S, 12] = I - 2
    return pack(F, sel, P)
def setup_inputs_corners(rng):
    n = T + 3; hi = rows8(rng); cl = np.argsort(rng.random((N, 8, I)), axis=-1) % n
    u = rng.random((N, 8, 16, I)); c = cl[:, :, None, :]; tall = c == T + 2
    F = np.where(c == 0, 8 * u, np.where(tall == hi, np.where(tall, 208 + 48 * u, 128 + 32 * u), np.where(tall, 8 + 33 * u, 41 * u))).astype(np.int64)
    own = np.arange(I)[None, None, :]; z = rng.integers(0, 3, (N, 8, I)); step = of_class(rng, cl, np.maximum(np.minimum(cl, T) - 1, 0), n)
    sel = np.where(cl == T + 1, own, np.where((cl == 0) | (cl == T + 2), np.where(z == 0, own, np.where(z == 1, 0, I - 1)), step))
    fm = rng.integers(0, 12, (N, 8, 1)); fm[0, 0] = 2; fm[N - 1, 7] = 1; fm[0, 7] = 6; fm[N - 1, 0] = 2; fm[1, 3] = 4; fm[2, 5] = 7
    md = np.where(fm < 6, fm, rng.integers(0, 6, (N, 8, L)))[..., None]
    one = np.arange(16) == rng.integers(0, 16, (N, 8, L, 1)); dd = rng.integers(0, T + 1, (N, 8, L, 1)); mix = rng.integers(0, n, (N, 8, L, 16))
    want = np.where(md == 0, mix, np.where(md == 1, T + 2, np.where(md == 2, np.where(one, T + 2, T + 1), np.where(md == 3, np.where(one, mix, T + 2), np.where(md == 4, np.where(one, T + 2, dd), T + 1)))))
    P = of_class(rng, cl, want, n); P = np.where(md == 1, P[..., :1], P)
    P[:, ::2, 1] = 0; P[:, 1::2, L - 1] = I - 1
    return pack(F, sel, P)
def setup_inputs_ties(rng):
    kind = rng.choice(np.array([0, 1, 1, 2, 2, 3, 4]), (N, 8, I)); rk = np.argsort(rng.random((N, 8, 16, I), dtype=np.float32), axis=2)
    more = np.array([0, 16 - H, 17 - H, 3, 0])[kind][:, :, None, :]; less = np.array([16, 16 - H, 17 - H, 13, 8])[kind][:, :, None, :]
    F = rng.integers(100, 200, (1, 8, 16, 1)) + (rk < more).astype(np.int64) - (rk >= less).astype(np.int64)
    two = rng.permutation(8)[:2]; x = int(rng.integers(0, N))
    for r in (x, (x - 1) % N):
        F[r, two[0]] += 20; F[r, two[1]] += 20
        v = rng.permutation(I)[:I // 16]; F[r, two[1], rng.integers(0, 16, v.size), v] = 0
    return pack(F, rng.integers(0, I, (N, 8, I)), rng.integers(0, I, (N, 8, L, 16)))
def check_inputs(d):
    bad = []
    for k, hi in (("front", 255), ("sel0", I - 1), ("par", I - 1)):
        x = np.asarray(d[k]).astype(np.float64)
        if not (np.min(x) >= 0 and np.max(x) <= hi): bad.append("range of " + k)
        elif np.any(x != np.floor(x)): bad.append("whole numbers in " + k)
    return bad
def reference(front, sel0, par):
    F = np.zeros((N, 8, 16, W), np.int32); F[..., :I] = front.astype(np.float32).reshape(N, 8, 16, I).astype(np.int32)
    sel = np.zeros((N, 8, W), np.int64); sel[..., :I] = sel0
    P = np.stack([gentries(a) for a in par]).astype(np.int64).reshape(N, 8, L, 16)
    i = np.arange(L); k = np.arange(16)
    def fronts(q):
        return np.take_along_axis(F, q.reshape(N, 8, 1, L * 16), 3).reshape(N, 8, 16, L, 16)
    for t in range(R):
        b = I + t * (L + M)
        f = fronts(P); s = np.argmax(np.add.reduce(f, axis=2), axis=3)
        ps = np.take_along_axis(P, s[..., None], 3)[..., 0]; g = np.take_along_axis(F, ps[:, :, None, :], 3)
        q = P; c = np.zeros(P.shape, np.int64); walk = np.ones(P.shape, bool)
        for test in range(T):
            fq = f if test == 0 else fronts(q)
            walk = walk & (np.add.reduce((fq <= g[..., None]).astype(np.int32), axis=2) < H)
            c = c + walk.astype(np.int64)
            q = np.where(walk, np.take_along_axis(sel, q.reshape(N, 8, L * 16), 2).reshape(q.shape), q)
        red = c == T
        new = np.maximum.reduce(fronts(np.where(red, ps[..., None], q)), axis=4)
        new[:, :, (i + t) & 15, i] = np.minimum(255, new[:, :, (i + t) & 15, i] + 1)
        come = np.roll(new[..., ::S], 1 + t % (N - 1), axis=0)
        best = np.argmax(np.add.reduce((f[:, :, :, ::S] <= come[..., None]).astype(np.int32), axis=2), axis=3)
        F[..., b:b + L] = new; F[..., b + L:b + L + M] = come
        sel[..., b:b + L] = ps; sel[..., b + L:b + L + M] = np.take_along_axis(P[:, :, ::S], best[..., None], 3)[..., 0]
        sc = np.add.reduce(c, axis=3)[..., None]; reds = np.add.reduce(red.astype(np.int64), axis=(1, 3))[:, None, :, None]
        P = np.where(k == s[..., None], b + i[:, None], np.where(red, b + ((5 * i[:, None] + 37 * k + sc + reds) & (L - 1)), np.where(c == 0, b + L + ((i[:, None] + k + reds) & (M - 1)), q)))
    return {"yf": np.ascontiguousarray(F[..., I:]).reshape(N, 128, W - I).astype(np.float32).astype(BF), "ys": np.ascontiguousarray(sel[..., I:]).astype(np.float32),
            "yp": np.ascontiguousarray(P.transpose(0, 1, 3, 2)).reshape(N, 128, L).astype(np.float32)}

@@ -1,0 +1,675 @@
+from concourse.mybir import AluOpType, ActivationFunctionType
+
+I0, L, R = 3328, 256, 2
+NB = L + 128
+FW = 4112
+PW = 4160
+BIG = 65536.0
+PR = 8192
+CYC = 1.0e-3
+GAT = 1.56
+WAKE = 0.08
+ORDER = {}
+SUN = [[(0, 1, 0), (0, 1, 1), (0, 1, 3), (2, 1, 2), (3, 1, 0), (3, 1, 1), (4, 0, 0), (4, 0, 1), (4, 0, 2), (4, 0, 3),
+        (4, 1, 0), (4, 1, 1)],
+       [(0, 0, 0), (0, 0, 1), (2, 1, 2), (3, 1, 2), (3, 1, 3), (4, 0, 0), (4, 0, 1), (4, 0, 2), (4, 0, 3), (4, 1, 2),
+        (4, 1, 3)]]
+FQ = ["SSSS", "SVSS"]
+P1Q = ["SSSS", "SSSS"]
+P2Q = ["SSSS", "SSSS"]
+GQ = ["VV", "VV"]
+CQ = "VS"
+DV = ["VS", "VS"]
+S2Q = "VS"
+
+SCRATCH = {}
+for _n, _w, _d in [
+        ("F", FW, "bfloat16"), ("PT", PW, "bfloat16"), ("f0", 4096, "bfloat16"), ("f1", 4096, "bfloat16"),
+        ("pa0", 4096, "bfloat16"), ("pa1", 4096, "bfloat16"), ("px", 4096, "bfloat16"),
+        ("cv0", 2048, "bfloat16"), ("cv1", 2048, "bfloat16"), ("cv2", 2048, "bfloat16"), ("cv3", 2048, "bfloat16"),
+        ("cv4", 2048, "bfloat16"), ("cvc", 2048, "bfloat16"), ("cv5", 2048, "bfloat16"), ("fq", 4096, "bfloat16"), ("s2", 3328, "bfloat16"),
+        ("LEH", 144, "bfloat16"), ("LEa", 144, "bfloat16"), ("LEb", 144, "bfloat16"), ("LEK", 144, "bfloat16"), ("LEC", 144, "bfloat16"),
+        ("ID", 128, "bfloat16"), ("NID", 128, "bfloat16"), ("SU", 128, "bfloat16"),
+        ("SH", 128, "bfloat16"), ("D01", 128, "bfloat16"), ("YSM", 8, "bfloat16"), ("ONES", 128, "bfloat16"),
+        ("KR", 128, "bfloat16"), ("CV", 64, "bfloat16"), ("CS", 64, "bfloat16"),
+        ("PI", 1, "int32"), ("CI", 144, "int32"), ("CU", 128, "int32"), ("CX", 32, "int32"),
+        ("ti", 8, "int32"),
+        ("MA", 256, "int32"), ("MSK0", 256, "bfloat16"), ("MSK1", 256, "bfloat16"),
+        ("K12", 512, "float32"), ("KS0", 256, "float32"), ("KS1", 256, "float32"),
+        ("IDV", 260, "int32"), ("IDW", 260, "int32"), ("IDH", 260, "int32"), ("HB", 260, "bfloat16"),
+        ("LB", 260, "bfloat16"), ("NL", 16, "uint16"), ("NL2", 8, "uint16"), ("NL3", 8, "uint16"), ("XL", 16, "uint16"),
+        ("SELR", 208, "int32"), ("SELP", 208, "int32"), ("SELH", 208, "int32"), ("SELO", 208, "int32"),
+        ("SELL", 208, "uint16"), ("SHB", 208, "bfloat16"), ("SLB", 208, "bfloat16"),
+        ("SHB2", 208, "bfloat16"), ("SLB2", 208, "bfloat16"),
+        ("raw", 256, "int32"), ("PL", 256, "uint16"), ("QLa0", 256, "uint16"), ("QLa1", 256, "uint16"),
+        ("QLb0", 256, "uint16"), ("QLb1", 256, "uint16"), ("LOL0", 128, "uint16"), ("LOL1", 128, "uint16"),
+        ("OFF0", 8, "uint16"), ("OFF1", 8, "uint16"), ("OFFC", 8, "uint16"),
+        ("CO0", 256, "float32"), ("CO1", 256, "float32"), ("CO2", 256, "float32"), ("CO3", 256, "float32"),
+        ("CO4", 256, "float32"), ("ACC", 256, "float32"),
+        ("KEY", 256, "float32"), ("TR", 256, "float32"), ("KC", 128, "float32"), ("MI", 16, "int32"), ("MC", 8, "int32"),
+        ("MN", 24, "int32"), ("G0", 1024, "bfloat16"), ("G1", 1024, "bfloat16"), ("CR", 128, "bfloat16"),
+        ("VI", 256, "int32"), ("HI", 256, "int32"), ("LO", 256, "int32"), ("HIF", 256, "bfloat16"),
+        ("RED", 256, "bfloat16"), ("XA", 32, "float32"),
+        ("E", 256, "float32"), ("XY", 512, "int32"), ("XZ", 512, "int32"), ("T1", 256, "float32"),
+        ("NI", 256, "int32"), ("NUM", 256, "int32"), ("YPR", 256, "float32"),
+        ("DA", 512, "bfloat16"), ("DB", 512, "bfloat16"), ("DC", 512, "bfloat16"), ("DE", 512, "bfloat16"),
+        ("DS", 4096, "bfloat16"),
+        ("NEWP", 256, "bfloat16"), ("NEWN", 256, "bfloat16"), ("SEND0", 128, "bfloat16"), ("SEND1", 128, "bfloat16"),
+        ("PSP", 256, "bfloat16"), ("PSN", 256, "bfloat16"), ("PCP", 128, "bfloat16"), ("PCN", 128, "bfloat16"),
+        ("YS", 768, "float32"), ("cols", 64, "float32")]:
+    SCRATCH[_n] = ("sbuf", [128, _w], _d)
+PSUMS = ["PG0", "PG1", "PCa", "PCb", "PQ0", "PQ1", "PD0", "PD1"]
+for _n in PSUMS:
+    SCRATCH[_n] = ("psum", [128, 512], "float32")
+
+NDMA = 40
+SEMAPHORES = ["sv", "ss", "st", "sg"] + ["d%d" % j for j in range(NDMA)] + ["ar0", "ar1", "lc0", "lc1"]
+
+
+def rank_program(g, core, T, topo):
+    rank = T.rank_of(core)
+    if rank is None:
+        return
+    A = AluOpType
+    AF = ActivationFunctionType
+    ALL = 0xFFFF
+    ops = []
+
+    def X(name, c0, c1, step=1, p=None, rows=ALL):
+        t = T[name]
+        if p is not None:
+            ap = t[0:p, c0:c1]
+        elif step == 1:
+            ap = t[:, c0:c1]
+        else:
+            ap = t[:, c0:c1:step]
+        return (ap, [(name, c0, c1, rows)])
+
+    def ind(win, off):
+        return (win[0].indirect(off[0]), win[1] + off[1], True)
+
+    def rec(kind, q, outs, ins, fn, cost, lat=0.0, data=None):
+        reads = list(dict.fromkeys(r for x in ins for r in x[1]))
+        writes = list(dict.fromkeys(r for x in outs for r in x[1]))
+        ops.append({"kind": kind, "q": q, "r": reads, "w": writes, "fn": fn, "cost": cost, "lat": lat, "data": data})
+
+    def width(x):
+        n = 1
+        for d in x[0].shape[1:]:
+            n *= d
+        return n
+
+    def emit(q, outs, ins, fn, cyc=1.0, gat=False):
+        n = width(outs[0])
+        rec("c", q, outs, ins, fn, 0.06 + n * GAT * CYC if gat else 0.02 + max(64, cyc * n) * CYC)
+
+    def isg(*xs):
+        return any(len(x) > 2 for x in xs)
+
+    def two(*xs):
+        return all(SCRATCH[x[1][0][0]][2] in ("bfloat16", "uint16") for x in xs)
+
+    def vcopy(o, i):
+        emit("V", [o], [i], lambda e: e.tensor_copy(o[0], i[0]), 0.5 if two(o, i) else 1.0, isg(i))
+
+    def vtt(o, a, b, op):
+        cyc = 1.0 if a[1][0][0] in PSUMS or b[1][0][0] in PSUMS else 2.0
+        emit("V", [o], [a, b], lambda e: e.tensor_tensor(o[0], a[0], b[0], op), cyc, isg(a))
+
+    def vts(o, i, s1, op0, s2=None, op1=None):
+        ins = [i] + [s for s in (s1, s2) if isinstance(s, tuple)]
+        a1 = s1[0] if isinstance(s1, tuple) else s1
+        a2 = s2[0] if isinstance(s2, tuple) else s2
+        cyc = 0.5 if two(o, i) else 1.0
+        if op1 is None:
+            emit("V", [o], ins, lambda e: e.tensor_scalar(o[0], i[0], a1, None, op0), cyc)
+        else:
+            emit("V", [o], ins, lambda e: e.tensor_scalar(o[0], i[0], a1, a2, op0, op1), cyc)
+
+    def vset(o, c):
+        emit("V", [o], [], lambda e: e.memset(o[0], c), 0.5 if two(o) else 1.0)
+
+    def act(o, i, func=AF.Copy, bias=0.0, scale=1.0):
+        ins = [i] + [x for x in (bias, scale) if isinstance(x, tuple)]
+        b = bias[0] if isinstance(bias, tuple) else bias
+        s = scale[0] if isinstance(scale, tuple) else scale
+        emit("S", [o], ins, lambda e: e.activation(o[0], i[0], func, bias=b, scale=s), 1.0, isg(i))
+
+    def gather(q, o, i):
+        if q == "V":
+            vcopy(o, i)
+        else:
+            act(o, i)
+
+    def iota(o, pattern, base, cm, fl=False):
+        if fl:
+            emit("G", [o], [], lambda e: e.iota(o[0], pattern, base, cm, allow_small_or_imprecise_dtypes=True), 2.0)
+        else:
+            emit("G", [o], [], lambda e: e.iota(o[0], pattern, base, cm), 2.0)
+
+    def mms(lst):
+        cost = sum(max(64, width(m[2])) for m in lst) * 0.0005
+        rec("t", "T", [m[0] for m in lst], [x for m in lst for x in (m[1], m[2])], None, cost, 0.0, lst)
+
+    def dma(q, outs, ins, pairs, lat=2.3):
+        rec("d", q, outs, ins, None, 0.06 * len(pairs), lat, pairs)
+
+    dma("Y", [X("SELR", 0, 208)], [], [(T.SELR[:], T.sel0[:])])
+    dma("S", [X("F", 16, 16 + I0)], [], [(T.F[:, 16:16 + I0], T.front[:])], 4.8)
+    dma("Y", [X("raw", 0, 256)], [], [(T.raw[:, 16 * k:16 * k + 16], T.par[k::16, :]) for k in range(16)])
+
+    ncol = [0]
+
+    def col():
+        ncol[0] += 1
+        return X("cols", ncol[0] - 1, ncol[0])
+
+    PI, CI, CU = X("PI", 0, 1), X("CI", 0, 128), X("CU", 0, 128)
+    LE = lambda nm, e: X(nm, 15 - e, 143 - e)
+    ti = [X("ti", j, j + 1) for j in range(8)]
+    iota(PI, [[0, 1]], 0, 1)
+    iota(X("CI", 0, 144), [[1, 144]], 0, 0)
+    iota(X("IDV", 0, 260), [[1, 260]], 0, 0)
+    vset(X("PT", 0, PW // 2), 0.0)
+    act(X("PT", PW // 2, PW), X("PT", 0, PW // 2))
+    vset(X("F", 0, 16), 0.0)
+    pf, uf, gf, zf = col(), col(), col(), col()
+    vcopy(pf, PI)
+    vts(ti[0], PI, 15, A.bitwise_and)
+    vts(ti[1], PI, 4, A.arith_shift_right)
+    vcopy(uf, ti[0])
+    vcopy(gf, ti[1])
+    act(zf, gf, AF.Identity, bias=15.0, scale=16.0)
+
+    def split(src, hb, lb):
+        vts(X("SELH", 0, 208), src, 6, A.arith_shift_right)
+        vts(X("SELO", 0, 208), src, 63, A.bitwise_and)
+        vcopy(X(hb, 0, 208), X("SELH", 0, 208))
+        vcopy(X(lb, 0, 208), X("SELO", 0, 208))
+
+    def prow(r, buf, n, c0):
+        o = T.PT[r::16, c0:c0 + 16 * n]
+        dma("Y", [X("PT", c0, c0 + 16 * n, rows=1 << r)], [X(buf, 0, n)], [(o, T[buf][:, 0:n])])
+
+    def wcol(a):
+        o, t = col(), col()
+        vts(o, uf, float(a), A.is_equal, 64.0, A.mult)
+        vts(t, uf, float(a + 1), A.is_equal)
+        vtt(o, o, t, A.add)
+        return o
+
+    SELP = X("SELP", 0, 208)
+    vts(SELP, X("SELR", 0, 208), 16.0, A.add)
+    split(SELP, "SHB", "SLB")
+    prow(2, "SHB", 208, 16)
+    prow(3, "SLB", 208, 16)
+    vcopy(X("SELL", 0, 208), SELP)
+    for h in (0, 1):
+        vts(X("PL", 128 * h, 128 * h + 128), X("raw", h, 256, 2), 16.0, A.add)
+    u260 = col()
+    act(u260, uf, scale=260.0)
+    vts(X("IDW", 0, 260), X("IDV", 0, 260), u260, A.add)
+    vts(X("IDH", 0, 260), X("IDW", 0, 260), 6, A.arith_shift_right)
+    vcopy(X("HB", 0, 260), X("IDH", 0, 260))
+    vts(X("IDV", 0, 260), X("IDW", 0, 260), 63, A.bitwise_and)
+    vcopy(X("LB", 0, 260), X("IDV", 0, 260))
+    swin = X("PT", 0, 16 + I0)
+    gather(S2Q[0], X("s2", 0, 1664), ind(swin, X("SELL", 0, 104)))
+    gather(S2Q[1], X("s2", 1664, 3328), ind(swin, X("SELL", 104, 208)))
+    wa = wcol(2)
+    vts(X("LEa", 0, 144), X("CI", 0, 144), zf, A.is_equal, wa, A.mult)
+    mms([(X("PQ0", 0, 208), LE("LEa", e), X("s2", e, 3328, 16), e == 0, e == 15) for e in range(16)])
+    vcopy(SELP, X("PQ0", 0, 208))
+    split(SELP, "SHB2", "SLB2")
+    prow(4, "SHB2", 208, 16)
+    prow(5, "SLB2", 208, 16)
+    prow(0, "HB", 260, 0)
+    prow(1, "LB", 260, 0)
+    wb = wcol(4)
+    for nm, wt in (("LEb", wb), ("LEK", 4096.0), ("LEC", BIG), ("LEH", 2048.0)):
+        vts(X(nm, 0, 144), X("CI", 0, 144), zf, A.is_equal, wt, A.mult)
+    vset(X("ONES", 0, 128), 1.0)
+    vts(X("KR", 0, 128), CI, -0.125, A.mult, 15.875, A.add)
+    u2032 = col()
+    act(u2032, uf, AF.Identity, bias=2032.0)
+    ID, NID = X("ID", 0, 128), X("NID", 0, 128)
+    vts(ID, CI, pf, A.is_equal)
+    act(NID, ID, scale=-1.0)
+    vset(X("CV", 0, 64), -10.0 * BIG / 128)
+    vset(X("CS", 0, 64), -4.0 * BIG / 128)
+    for h in (0, 1):
+        vts(X("CO0", 128 * h, 128 * h + 128), X("raw", h, 256, 2), 16.0 + 5 * PR, A.add)
+    vts(CU, CI, 15, A.bitwise_and)
+    vts(X("SU", 0, 128), CU, uf, A.is_equal)
+    l4, p3, l2 = col(), col(), col()
+    vts(l4, uf, 4.0, A.is_lt)
+    vts(p3, pf, 3.0, A.add)
+    vtt(p3, p3, l4, A.mult)
+    vts(p3, p3, -1.0, A.add)
+    vts(X("SH", 0, 128), CI, p3, A.is_equal)
+    vts(l2, uf, 2.0, A.is_lt)
+    act(X("D01", 0, 128), ID, scale=l2)
+    w01 = wcol(0)
+    vts(X("YSM", 0, 8), X("CI", 0, 8), gf, A.is_equal, w01, A.mult)
+    na, nb, nc, c7, b3, u8 = col(), col(), col(), col(), col(), col()
+    vts(ti[2], PI, 1, A.bitwise_and)
+    vts(ti[3], PI, 1, A.arith_shift_right, 7, A.bitwise_and)
+    vts(ti[4], PI, 7, A.bitwise_and)
+    vts(ti[5], PI, 3, A.arith_shift_right, 1, A.bitwise_and)
+    vts(na, ti[2], 128.0, A.mult)
+    vts(nb, ti[3], 16.0, A.mult)
+    vtt(na, na, nb, A.add)
+    vts(X("NL", 0, 16), X("CI", 0, 16), na, A.add)
+    act(u8, uf, scale=8.0)
+    vts(X("NL2", 0, 8), X("CI", 0, 8), u8, A.add)
+    vcopy(c7, ti[4])
+    vts(b3, c7, 16.0, A.mult)
+    vcopy(nc, ti[5])
+    vtt(b3, b3, nc, A.add)
+    vts(X("NL3", 0, 8), X("CI", 0, 8), 2.0, A.mult, b3, A.add)
+    vts(X("CX", 0, 16), X("CI", 0, 16), 3, A.arith_shift_right)
+    vts(X("XL", 0, 16), X("CX", 0, 16), 8.0, A.mult, c7, A.add)
+    iota(X("MA", 0, 256), [[1, 256]], 128, -1)
+    vts(X("MA", 0, 256), X("MA", 0, 256), 15, A.bitwise_and)
+    vts(X("MSK0", 0, 256), X("MA", 0, 256), 0.0, A.is_equal)
+    vts(X("MSK1", 0, 256), X("MA", 0, 256), 15.0, A.is_equal)
+    u80, u16 = col(), col()
+    act(u80, uf, scale=80.0)
+    act(u16, uf, scale=16.0)
+    for h in (0, 1):
+        iota(X("K12", 256 * h, 256 * h + 128), [[37, 16], [10, 8]], 80 + 5 * h, 0, True)
+        iota(X("K12", 256 * h + 128, 256 * h + 256), [[1, 16], [2, 8]], h, 0, True)
+        for j, ub in ((0, u80), (128, u16)):
+            kx = X("K12", 256 * h + j, 256 * h + j + 128)
+            act(kx, kx, AF.Identity, bias=ub)
+    for t in range(R):
+        ks = X("KS%d" % t, 0, 256)
+        iota(ks, [[1, 2], [0, 16], [2, 8]], 8 * PR + I0 + NB * t + 16, 0, True)
+        act(ks, ks, AF.Identity, bias=u16)
+
+    def sumto(bank, o0, n, le, src, s0, const=None):
+        o = X(bank, o0, o0 + n)
+        l = []
+        if const is not None:
+            l.append((o, X("ONES", 0, 128), const, True, False))
+        for e in range(16):
+            l.append((o, LE(le, e), X(src, s0 + e, s0 + 16 * n, 16), e == 0 and const is None, e == 15))
+        mms(l)
+
+    def tree(z, src, s0, out, o0, bank, off):
+        r = 128 * (z & 1)
+        vcopy(X(src, s0, s0 + 128), X(bank, 0, 128))
+        vtt(X("TR", r, r + 64), X(src, s0, s0 + 64), X(src, s0 + 64, s0 + 128), A.max)
+        vtt(X("TR", r + 64, r + 96), X("TR", r, r + 32), X("TR", r + 32, r + 64), A.max)
+        vtt(X("TR", r + 96, r + 112), X("TR", r + 64, r + 80), X("TR", r + 80, r + 96), A.max)
+        vtt(X(out, o0, o0 + 8), X("TR", r + 96, r + 104), X("TR", r + 104, r + 112), A.max)
+        vts(X("MN", 8 * z, 8 * z + 8), X(out, o0, o0 + 8), 4095, A.bitwise_and)
+        vts(X(off, 0, 8), X("MN", 8 * z, 8 * z + 8), -1.0, A.mult, u2032, A.add)
+
+    def grow(src, n, c0, y0, tt, bank):
+        yo = 256 if n == 256 else 384
+        y = X(bank, yo, yo + n, p=8)
+        if tt + 1 < R:
+            mms([(X(bank, 0, n), X("SH", 0, 128), X(src, 0, n), True, False),
+                 (X(bank, 0, n), X("D01", 0, 128), X("PT", c0, c0 + n), False, True)])
+            act(X("PT", c0, c0 + n), X(bank, 0, n))
+        mms([(y, X("YSM", 0, 8), X(src, 0, n), True, True)])
+        act(X("YS", y0, y0 + n, p=8), y, AF.Identity, bias=-16.0)
+        dma("Y", [], [X("YS", y0, y0 + n, p=8)], [(T.ys[:, y0:y0 + n], T.YS[0:8, y0:y0 + n])])
+
+    def come(tt):
+        cc = 16 + I0 + NB * tt + L
+        ft, pt = "f%d" % tt, "pa%d" % tt
+        vcopy(X("CR", 0, 128), ind(X("F", cc, cc + 128), X("NL2", 0, 8)))
+        cr, onS = X("CR", 0, 128), CQ[tt] == "S"
+        kb = "PQ1" if onS else "PD0"
+        if not onS:
+            mms([(X("PQ1", 128 * j, 128 * j + 128), ID, cr, True, True) for j in range(4)])
+        for j in range(4):
+            fj, cj, pd = X(ft, 512 * j, 512 * j + 512), X("cvc", 512 * j, 512 * j + 512), "PD%d" % (j & 1)
+            if onS:
+                l = []
+                for i in range(4):
+                    o = X(pd, 128 * i, 128 * i + 128)
+                    l += [(o, ID, cr, True, False), (o, NID, X(ft, 512 * j + 128 * i, 512 * j + 128 * i + 128), False, True)]
+                mms(l)
+                act(cj, X(pd, 0, 512), AF.Sign, bias=0.5)
+            else:
+                vtt(cj, fj, X("PQ1", 0, 512), A.is_le)
+            if j & 1:
+                sumto(kb, 32 * (j - 1), 64, "LEH" if onS else "LEK", "cvc", 512 * (j - 1),
+                      X("KR", 32 * (j - 1), 32 * (j - 1) + 64))
+        tree(2, "KC", 0, "MC", 0, kb, "OFFC")
+        act(X("PCP", 0, 128), ind(X(pt, 0, 2048), X("OFFC", 0, 8)))
+        act(X("PCN", 0, 128), ind(X("PCP", 0, 128), X("NL3", 0, 8)))
+        grow("PCN", 128, cc, NB * tt + L, tt, "PD1")
+
+    for t in range(R):
+        B = I0 + NB * t
+        cc = 16 + B + L
+        fn, pn = "f%d" % t, "pa%d" % t
+        win = X("F", 0, 16 + B)
+        pwin = X("PT", 0, 16 + B)
+        KB = ("PCa", "PCb")
+        for h in (0, 1):
+            for ch in (0, 1):
+                c0 = 128 * h + 64 * ch
+                gather(FQ[t][2 * h + ch], X(fn, 16 * c0, 16 * c0 + 1024), ind(win, X("PL", c0, c0 + 64)))
+                sumto(KB[h], 64 * ch, 64, "LEK", fn, 16 * c0, X("KR", 64 * ch, 64 * ch + 64))
+        for h in (0, 1):
+            tree(h, "KEY", 128 * h, "MI", 8 * h, KB[h], "OFF%d" % h)
+            vcopy(X("G%d" % h, 0, 128), ind(X(fn, 2048 * h, 2048 * h + 2048), X("OFF%d" % h, 0, 8)))
+            mms([(X("PG%d" % h, 128 * j, 128 * j + 128), ID, X("G%d" % h, 0, 128), True, True) for j in range(4)])
+        for h in (0, 1):
+            for n in (128, 256, 512):
+                gather(GQ[t][h], X("G%d" % h, n, 2 * n), X("G%d" % h, 0, n))
+            for j in range(4):
+                s0 = 2048 * h + 512 * j
+                o = X("cv%d" % h, 512 * j, 512 * j + 512)
+                if (0, h, j) in SUN[t]:
+                    pd = X("PD%d" % (j & 1), 0, 512)
+                    mms([(pd, NID, X(fn, s0, s0 + 512), True, False), (pd, ID, X("G%d" % h, 0, 512), False, True)])
+                    act(o, pd, AF.Sign, bias=0.5)
+                else:
+                    vtt(o, X(fn, s0, s0 + 512), X("PG%d" % h, 0, 512), A.is_le)
+                sg = [(0, h, i) in SUN[t] for i in (j - 1, j)]
+                if j & 1 and sg[0] == sg[1]:
+                    sumto(KB[h], 32 * (j - 1), 64, "LEC", "cv%d" % h, 512 * (j - 1), X("CS" if sg[1] else "CV", 0, 64))
+                elif j & 1:
+                    for i in (0, 1):
+                        sumto(KB[h], 32 * (j - 1 + i), 32, "LEC", "cv%d" % h, 512 * (j - 1 + i),
+                              X("CS" if sg[i] else "CV", 0, 32))
+
+        def comb(d, h, bank):
+            hs = (128 * h, 128 * h + 128)
+            acc = X("ACC", *hs)
+            if d == 0:
+                vtt(acc, X(bank, 0, 128), X("CO0", *hs), A.min)
+                act(acc, acc, AF.Relu)
+            else:
+                vtt(X(bank, 128, 256), X(bank, 0, 128), X("CO%d" % d, *hs), A.min)
+                vtt(X("VI", *hs) if d == 4 else acc, X(bank, 128, 256), acc, A.max)
+
+        comb(0, 0, "PCa")
+        comb(0, 1, "PCb")
+
+        def path(h, dst, lst, nm, d0, qs):
+            for ch in (0, 1):
+                s0 = 2048 * h + 1024 * ch
+                gather(qs[2 * h + ch], X(dst, s0, s0 + 1024), ind(pwin, lst(ch)))
+                for d, le in ((0, "LEa"), (1, "LEb")):
+                    sumto("PQ%d" % h, 128 * d + 64 * ch, 64, le, dst, s0)
+            vcopy(X("%s%d" % (nm, h), 0, 256), X("PQ%d" % h, 0, 256))
+            for j in (0, 1):
+                act(X("CO%d" % (d0 + j), 128 * h, 128 * h + 128), X("PQ%d" % h, 128 * j, 128 * j + 128), AF.Identity,
+                    bias=float(PR * (5 - d0 - j)))
+
+        for h in (0, 1):
+            path(h, pn, lambda ch: X("PL", 128 * h + 64 * ch, 128 * h + 64 * ch + 64), "QLa", 1, P1Q[t])
+        for h in (0, 1):
+            path(h, "px", lambda ch: X("QLa%d" % h, 128 + 64 * ch, 192 + 64 * ch), "QLb", 3, P2Q[t])
+
+        ns = [0]
+
+        def test(d, h):
+            nm, o = ("QLa%d" % h, 128 * (d - 1)) if d < 3 else ("QLb%d" % h, 128 * (d - 3))
+            buf = "cv%d" % ((4 * h + d + 1) % 6)
+            bank = (("PCa", "PCb"), ("PG0", "PG1"))[h][d & 1]
+            for j in (0, 2):
+                two_s = [(d, h, j + i) in SUN[t] for i in (0, 1)]
+                if not any(two_s):
+                    vtt(X(buf, 512 * j, 512 * j + 1024), ind(win, X(nm, o + 32 * j, o + 32 * j + 64)),
+                        X("G%d" % h, 0, 1024), A.is_le)
+                for i in (0, 1):
+                    s0, o1 = 512 * (j + i), o + 32 * (j + i)
+                    if two_s[i]:
+                        q = ns[0] % 8
+                        ns[0] += 1
+                        pd = X("PD%d" % (q & 1), 0, 512)
+                        fq = X("fq", 512 * q, 512 * q + 512)
+                        act(fq, ind(win, X(nm, o1, o1 + 32)))
+                        mms([(pd, NID, fq, True, False), (pd, ID, X("G%d" % h, 0, 512), False, True)])
+                        act(X(buf, s0, s0 + 512), pd, AF.Sign, bias=0.5)
+                    elif any(two_s):
+                        vtt(X(buf, s0, s0 + 512), ind(win, X(nm, o1, o1 + 32)), X("G%d" % h, 0, 512), A.is_le)
+                if two_s[0] == two_s[1]:
+                    sumto(bank, 32 * j, 64, "LEC", buf, 512 * j, X("CS" if two_s[0] else "CV", 0, 64))
+                else:
+                    for i in (0, 1):
+                        sumto(bank, 32 * (j + i), 32, "LEC", buf, 512 * (j + i), X("CS" if two_s[i] else "CV", 0, 32))
+            comb(d, h, bank)
+
+        def largest(h):
+            hs = (128 * h, 128 * h + 128)
+            vts(X("LO", *hs), X("VI", *hs), PR - 1, A.bitwise_and)
+            vcopy(X("LOL%d" % h, 0, 128), X("LO", *hs))
+            ll = "LOL%d" % h
+            db = ("PCa", "PCb")
+            ds = [X("DS", 2048 * h + 512 * j, 2048 * h + 512 * j + 512) for j in range(4)]
+            for j in range(4):
+                if j == 3 and DV[t][h] == "V":
+                    vcopy(ds[3], ind(win, X(ll, 96, 128)))
+                else:
+                    act(ds[j], ind(win, X(ll, 32 * j, 32 * j + 32)))
+            for j in range(3):
+                bank = db[(h + j) % 2]
+                jj = j + (DV[t][h] == "S")
+                mms([(X(bank, 0, 512), ID, ds[jj], True, True)])
+                prev, nx = (ds[3] if DV[t][h] == "V" else ds[0]) if j == 0 else X(("DA", "DB")[j - 1], 0, 512), ("DA", "DB", "DC")[j]
+                if j < 2:
+                    vtt(X(nx, 0, 512), X(bank, 0, 512), prev, A.max)
+            vtt(X("DC", 0, 256), X(bank, 0, 256), X("DB", 0, 256), A.max)
+            vtt(X(bank, 256, 512), X(bank, 256, 512), X("DB", 256, 512), A.max)
+            vtt(X("DE", 0, 128), X(bank, 256, 384), X("DC", 0, 128), A.max)
+            vtt(X(bank, 0, 128), X(bank, 384, 512), X("DC", 128, 256), A.max)
+            vtt(X("NEWP", 128 * h, 128 * h + 128), X(bank, 0, 128), X("DE", 0, 128), A.max)
+            nw = X("NEWN", 128 * h, 128 * h + 128)
+            vtt(nw, ind(X("NEWP", 128 * h, 128 * h + 128), X("NL3", 0, 8)), X("MSK%d" % t, h, 256, 2), A.add)
+            if h == 0:
+                vts(X("SEND%d" % t, 0, 128), nw, 255.0, A.min)
+            vts(X("F", 16 + B + h, 16 + B + L, 2), nw, 255.0, A.min)
+
+        for d in (1, 2, 3, 4):
+            test(d, 0)
+        largest(0)
+        dst = T.cores[(rank + 1 + t % 7) % len(T.cores)]
+        src = T.cores[(rank - 1 - t % 7) % len(T.cores)]
+        es = topo.engines(core, dst)[:8]
+        nsrc = len(topo.engines(src, core)[:8])
+        rid, pid, _se = topo.addr(dst)
+        mk = sum(1 << e for e in es)
+
+        def send(e, t=t, cc=cc, rid=rid, pid=pid, mk=mk):
+            e.remote_dma(out_ap=T.F[:, cc:cc + 128], in_ap=T["SEND%d" % t][:], remote_sem=T.sem["ar%d" % t],
+                         local_sem=T.sem["lc%d" % t], pid=pid, routing_id=rid, dma_engine_mask=mk)
+
+        rec("s", "G", [], [X("SEND%d" % t, 0, 128)], send, 0.3, 2.0, ("lc%d" % t, len(es)))
+        rec("a", "R", [X("F", cc, cc + 128)], [X("SEND%d" % t, 0, 128)], None, 0.3, 2.0, ("ar%d" % t, nsrc))
+        for d in (1, 2, 3, 4):
+            test(d, 1)
+        if t + 1 == R:
+            come(t)
+        largest(1)
+        kr, kc = float(7 * PR + B + 16), float(6 * PR + B + L + 16)
+        for h in (0, 1):
+            hs = (128 * h, 128 * h + 128)
+            hif, red = X("HIF", *hs), X("RED", *hs)
+            pq = ("PQ0", "PG0")[h]
+            vts(X("HI", *hs), X("VI", *hs), 13, A.arith_shift_right)
+            vcopy(hif, X("HI", *hs))
+            act(red, hif, AF.Relu, bias=1.0, scale=-1.0)
+            act(X(pq, 0, 128), hif, AF.Relu, bias=kr, scale=-kr)
+            act(X(pq, 128, 256), hif, AF.Relu, bias=-4.0 * kc, scale=kc)
+            kk = [(128 * h + 8 * k, 128 * h + 8 * k + 8) for k in range(16)]
+            o1, o2 = X(pq, 256, 264), X(pq, 264, 272)
+            mms([(o1, NID, X("HIF", *c), n == 0, False) for n, c in enumerate(kk)]
+                + [(o1, X("SU", 0, 128), X("RED", *c), False, n == 15) for n, c in enumerate(kk)]
+                + [(o2, X("SU", 0, 128), X("RED", *c), n == 0, n == 15) for n, c in enumerate(kk)])
+            e = X("E", *hs)
+            vtt(e, ind(X("MI", 8 * h, 8 * h + 8), X("XL", 0, 8)), X("KEY", *hs), A.is_equal)
+            vtt(X(pq, 384, 512), e, X("KS%d" % t, *hs), A.mult)
+            xa = X("XA", 16 * h, 16 * h + 16)
+            vcopy(xa, X(pq, 256, 272))
+            q0 = 256 * h
+            vtt(X("XY", q0, q0 + 256), ind(xa, X("XL", 0, 16)), X("K12", q0, q0 + 256), A.add)
+            vts(X("XZ", q0, q0 + 128), X("XY", q0, q0 + 128), 255, A.bitwise_and)
+            vts(X("XZ", q0 + 128, q0 + 256), X("XY", q0 + 128, q0 + 256), 127, A.bitwise_and)
+            t1 = X("T1", *hs)
+            vtt(X(pq, 256, 384), X(pq, 0, 128), X("XZ", q0, q0 + 128), A.add)
+            vtt(t1, X(pq, 128, 256), X("XZ", q0 + 128, q0 + 256), A.add)
+            vtt(t1, X(pq, 256, 384), t1, A.max)
+            vtt(X(pq, 384, 512), X(pq, 384, 512), X("VI", *hs), A.max)
+            vtt(X("NI", *hs), X(pq, 384, 512), t1, A.max)
+            vts(X("NUM", *hs), X("NI", *hs), PR - 1, A.bitwise_and)
+            if t + 1 < R:
+                vcopy(X("PL", *hs), X("NUM", *hs))
+                vts(X("CO0", *hs), X("NUM", *hs), float(5 * PR), A.add)
+            else:
+                vts(X("YPR", h, 256, 2), X("NUM", *hs), -16.0, A.add)
+        if t + 1 == R:
+            dma("Y", [], [X("YPR", 0, 256)], [(T.yp[k::16, :], T.YPR[:, 16 * k:16 * k + 16]) for k in range(16)])
+        for h in (0, 1):
+            act(X("PSP", 128 * h, 128 * h + 128), ind(X(pn, 2048 * h, 2048 * h + 2048), X("OFF%d" % h, 0, 8)))
+        act(X("PSN", 0, 256), ind(X("PSP", 0, 256), X("NL", 0, 16)))
+        grow("PSN", 256, 16 + B, NB * t, t, "PG1")
+        y0 = NB * t
+        dma("Y", [], [X("F", 16 + B, 16 + B + L)], [(T.yf[:, y0:y0 + L], T.F[:, 16 + B:16 + B + L])])
+        dma("Y", [], [X("F", cc, cc + 128)], [(T.yf[:, y0 + L:y0 + NB], T.F[:, cc:cc + 128])])
+        if t + 1 < R:
+            come(t)
+
+    def schedule():
+        n = len(ops)
+        pred = [set() for _ in range(n)]
+        last = {}
+        for i, o in enumerate(ops):
+            for w, regs in ((0, o["r"]), (1, o["w"])):
+                for (b, c0, c1, rows) in regs:
+                    l = last.setdefault(b, [])
+                    ps = b in PSUMS
+                    for (j, w2, d0, d1, r2) in l:
+                        if j != i and ((ps and ops[j]["q"] != o["q"]) or ((w or w2) and d0 < c1 and c0 < d1 and (rows & r2))):
+                            pred[i].add(j)
+                    if w and not ps:
+                        l[:] = [x for x in l if not (x[2] >= c0 and x[3] <= c1 and (x[4] & ~rows) == 0)]
+                    l.append((i, w, c0, c1, rows))
+        succ = [[] for _ in range(n)]
+        for i in range(n):
+            for j in pred[i]:
+                succ[j].append(i)
+        prio = [0.0] * n
+        for i in range(n - 1, -1, -1):
+            prio[i] = ops[i]["cost"] + ops[i]["lat"] + max([prio[k] + WAKE for k in succ[i]] or [0.0])
+        left = [len(p) for p in pred]
+        ready = {}
+        fin = [0.0] * n
+        free = {}
+        est = [0.0] * n
+        for i in range(n):
+            if not left[i]:
+                ready.setdefault(ops[i]["q"], []).append(i)
+        order = []
+        while len(order) < n:
+            best = None
+            for q, l in ready.items():
+                if not l:
+                    continue
+                f = free.get(q, 0.0)
+                t0 = min(max(f, est[i]) for i in l)
+                i = max((x for x in l if max(f, est[x]) <= t0 + 0.03), key=lambda x: prio[x])
+                st = max(f, est[i])
+                if best is None or st < best[0]:
+                    best = (st, i, q)
+            st, i, q = best
+            ready[q].remove(i)
+            order.append(i)
+            free[q] = st + ops[i]["cost"]
+            fin[i] = free[q] + ops[i]["lat"]
+            for k in succ[i]:
+                est[k] = max(est[k], fin[i] + WAKE)
+                left[k] -= 1
+                if not left[k]:
+                    ready.setdefault(ops[k]["q"], []).append(k)
+        return order
+
+    eng = {"V": g.vector, "S": g.scalar, "T": g.tensor, "G": g, "Y": g.sync}
+    sname = {"V": "sv", "S": "ss", "T": "st", "G": "sg"}
+    cnt = {"V": 0, "S": 0, "T": 0, "G": 0}
+    clk = {q: {} for q in "VSTGY"}
+    log = {}
+    total = {}
+    ndma = [0]
+
+    def waits(q, reads, writes):
+        need = []
+        for w, regs in ((0, reads), (1, writes)):
+            for (b, c0, c1, rows) in regs:
+                ps = b in PSUMS
+                for e in log.get(b, []):
+                    if ps and e["q"] != q:
+                        need.append(e)
+                        continue
+                    if (ps and q == "T") or not (e["w"] or w) or e["c1"] <= c0 or e["c0"] >= c1 or not (e["rows"] & rows):
+                        continue
+                    if e["q"] == q and w and not e["w"]:
+                        continue
+                    need.append(e)
+        want = {}
+        for e in need:
+            if clk[q].get(e["sem"], 0) < e["val"] and want.get(e["sem"], (0, None))[0] < e["val"]:
+                want[e["sem"]] = (e["val"], e)
+        for s in list(want):
+            v = want[s][0]
+            for s2 in want:
+                if s2 != s and want[s2][1]["clk"].get(s, 0) >= v:
+                    del want[s]
+                    break
+        for s, (v, e) in want.items():
+            eng[q].wait_ge(T.sem[s], v)
+            for a, b in e["clk"].items():
+                clk[q][a] = max(clk[q].get(a, 0), b)
+            clk[q][s] = max(clk[q].get(s, 0), v)
+
+    def note(q, reads, writes, sem, val, c):
+        c = dict(c)
+        c[sem] = max(c.get(sem, 0), val)
+        total[sem] = max(total.get(sem, 0), val)
+        for w, regs in ((0, reads), (1, writes)):
+            for (b, c0, c1, rows) in regs:
+                l = log.setdefault(b, [])
+                if b in PSUMS:
+                    l[:] = [e for e in l if not (e["q"] == q and e["c0"] >= c0 and e["c1"] <= c1 and (w or not e["w"]))]
+                elif w:
+                    l[:] = [e for e in l if not (e["c0"] >= c0 and e["c1"] <= c1 and (e["rows"] & ~rows) == 0)]
+                l.append({"q": q, "w": w, "c0": c0, "c1": c1, "rows": rows, "sem": sem, "val": val, "clk": c})
+
+    if "order" not in ORDER:
+        ORDER["order"] = schedule()
+    for i in ORDER["order"]:
+        o = ops[i]
+        q, r, w = o["q"], o["r"], o["w"]
+        if o["kind"] == "a":
+            note("D", [], w, o["data"][0], o["data"][1], {})
+            continue
+        waits(q, r, w)
+        if o["kind"] == "c":
+            cnt[q] += 1
+            o["fn"](eng[q]).then_inc(T.sem[sname[q]], 1)
+            note(q, r, w, sname[q], cnt[q], clk[q])
+        elif o["kind"] == "t":
+            for (x, lh, rh, a, b) in o["data"]:
+                cnt["T"] += 1
+                g.tensor.matmul(x[0], lh[0], rh[0], a, b).then_inc(T.sem.st, 1)
+            note("T", r, w, "st", cnt["T"], clk["T"])
+        elif o["kind"] == "d":
+            sem = "d%d" % ndma[0]
+            ndma[0] += 1
+            for (x, y) in o["data"]:
+                eng[q].dma_start(x, y).then_inc(T.sem[sem], 16)
+            note("D", r, w, sem, 16 * len(o["data"]), clk[q])
+        else:
+            o["fn"](g)
+            note("D", r, w, o["data"][0], o["data"][1], clk["G"])
+    for s, v in total.items():
+        if clk["Y"].get(s, 0) < v:
+            g.sync.wait_ge(T.sem[s], v)

@@ -1,89 +1,271 @@
 from concourse.mybir import AluOpType, ActivationFunctionType
+import math
+import numpy as np
 
 I0, L, R = 3328, 256, 2
 NB = L + 128
 FW = 4112
-PW = 4160
 BIG = 65536.0
 PR = 8192
-CYC = 1.0e-3
+CYC = 0.83e-3
+PEC = 0.42e-3
 GAT = 1.56
-WAKE = 0.08
-ORDER = {}
-SUN = [[(0, 1, 0), (0, 1, 1), (0, 1, 3), (2, 1, 2), (3, 1, 0), (3, 1, 1), (4, 0, 0), (4, 0, 1), (4, 0, 2), (4, 0, 3),
-        (4, 1, 0), (4, 1, 1)],
-       [(0, 0, 0), (0, 0, 1), (2, 1, 2), (3, 1, 2), (3, 1, 3), (4, 0, 0), (4, 0, 1), (4, 0, 2), (4, 0, 3), (4, 1, 2),
-        (4, 1, 3)]]
-FQ = ["SSSS", "SVSS"]
-P1Q = ["SSSS", "SSSS"]
-P2Q = ["SSSS", "SSSS"]
-GQ = ["VV", "VV"]
-CQ = "VS"
-DV = ["VS", "VS"]
-S2Q = "VS"
+WAKE = 0.2
+LOOK = (0.05, 0.25, 0.5)
+ARR = (6.5, 3.0)
+KINDS = [(1.0, 1.0, 0.2, 0.0), (1.25, 1.1, 0.2, 0.3)]
+MOVES = 20000
+HEAT = 0.004
+REACH = 30
+PLAN = {}
+CUT = 1664
+LAT = (3.2, 4.3, 5.0, 2.6)
+SEQ = {"Y": "sel fr0 row1 row0 row2 row3 par fr1",
+       "V": "a0 f000 b0 x000 p000 p001 q000 q001 r000 p010 p011 q010 q011 r010 r011 e011 e013 "
+            "f100 f111 p100 p101 q100 q101 r100 p110 p111 q110 q111 r110 r111 e111 e113",
+       "S": "a1 f001 b1 f010 f011 x001 s000 s001 r001 x010 x011 e000 e001 e002 e003 s010 s011 e010 e012 "
+            "x100 f101 x101 f110 s100 s101 r101 x110 x111 e100 e101 e102 e103 s110 s111 e110 e112"}
+WHO = {_n: _q for _q, _l in SEQ.items() for _n in _l.split()}
 
 SCRATCH = {}
-for _n, _w, _d in [
-        ("F", FW, "bfloat16"), ("PT", PW, "bfloat16"), ("f0", 4096, "bfloat16"), ("f1", 4096, "bfloat16"),
-        ("pa0", 4096, "bfloat16"), ("pa1", 4096, "bfloat16"), ("px", 4096, "bfloat16"),
-        ("cv0", 2048, "bfloat16"), ("cv1", 2048, "bfloat16"), ("cv2", 2048, "bfloat16"), ("cv3", 2048, "bfloat16"),
-        ("cv4", 2048, "bfloat16"), ("cvc", 2048, "bfloat16"), ("cv5", 2048, "bfloat16"), ("fq", 4096, "bfloat16"), ("s2", 3328, "bfloat16"),
-        ("LEH", 144, "bfloat16"), ("LEa", 144, "bfloat16"), ("LEb", 144, "bfloat16"), ("LEK", 144, "bfloat16"), ("LEC", 144, "bfloat16"),
-        ("ID", 128, "bfloat16"), ("NID", 128, "bfloat16"), ("SU", 128, "bfloat16"),
-        ("SH", 128, "bfloat16"), ("D01", 128, "bfloat16"), ("YSM", 8, "bfloat16"), ("ONES", 128, "bfloat16"),
-        ("KR", 128, "bfloat16"), ("CV", 64, "bfloat16"), ("CS", 64, "bfloat16"),
-        ("PI", 1, "int32"), ("CI", 144, "int32"), ("CU", 128, "int32"), ("CX", 32, "int32"),
-        ("ti", 8, "int32"),
-        ("MA", 256, "int32"), ("MSK0", 256, "bfloat16"), ("MSK1", 256, "bfloat16"),
-        ("K12", 512, "float32"), ("KS0", 256, "float32"), ("KS1", 256, "float32"),
-        ("IDV", 260, "int32"), ("IDW", 260, "int32"), ("IDH", 260, "int32"), ("HB", 260, "bfloat16"),
-        ("LB", 260, "bfloat16"), ("NL", 16, "uint16"), ("NL2", 8, "uint16"), ("NL3", 8, "uint16"), ("XL", 16, "uint16"),
-        ("SELR", 208, "int32"), ("SELP", 208, "int32"), ("SELH", 208, "int32"), ("SELO", 208, "int32"),
-        ("SELL", 208, "uint16"), ("SHB", 208, "bfloat16"), ("SLB", 208, "bfloat16"),
-        ("SHB2", 208, "bfloat16"), ("SLB2", 208, "bfloat16"),
-        ("raw", 256, "int32"), ("PL", 256, "uint16"), ("QLa0", 256, "uint16"), ("QLa1", 256, "uint16"),
-        ("QLb0", 256, "uint16"), ("QLb1", 256, "uint16"), ("LOL0", 128, "uint16"), ("LOL1", 128, "uint16"),
-        ("OFF0", 8, "uint16"), ("OFF1", 8, "uint16"), ("OFFC", 8, "uint16"),
-        ("CO0", 256, "float32"), ("CO1", 256, "float32"), ("CO2", 256, "float32"), ("CO3", 256, "float32"),
-        ("CO4", 256, "float32"), ("ACC", 256, "float32"),
-        ("KEY", 256, "float32"), ("TR", 256, "float32"), ("KC", 128, "float32"), ("MI", 16, "int32"), ("MC", 8, "int32"),
-        ("MN", 24, "int32"), ("G0", 1024, "bfloat16"), ("G1", 1024, "bfloat16"), ("CR", 128, "bfloat16"),
-        ("VI", 256, "int32"), ("HI", 256, "int32"), ("LO", 256, "int32"), ("HIF", 256, "bfloat16"),
-        ("RED", 256, "bfloat16"), ("XA", 32, "float32"),
-        ("E", 256, "float32"), ("XY", 512, "int32"), ("XZ", 512, "int32"), ("T1", 256, "float32"),
-        ("NI", 256, "int32"), ("NUM", 256, "int32"), ("YPR", 256, "float32"),
-        ("DA", 512, "bfloat16"), ("DB", 512, "bfloat16"), ("DC", 512, "bfloat16"), ("DE", 512, "bfloat16"),
-        ("DS", 4096, "bfloat16"),
-        ("NEWP", 256, "bfloat16"), ("NEWN", 256, "bfloat16"), ("SEND0", 128, "bfloat16"), ("SEND1", 128, "bfloat16"),
-        ("PSP", 256, "bfloat16"), ("PSN", 256, "bfloat16"), ("PCP", 128, "bfloat16"), ("PCN", 128, "bfloat16"),
-        ("YS", 768, "float32"), ("cols", 64, "float32")]:
-    SCRATCH[_n] = ("sbuf", [128, _w], _d)
-PSUMS = ["PG0", "PG1", "PCa", "PCb", "PQ0", "PQ1", "PD0", "PD1"]
-for _n in PSUMS:
-    SCRATCH[_n] = ("psum", [128, 512], "float32")
+for _d, _l in [
+        ("bfloat16", [("F", FW), ("PT", FW), ("T2", 16 + I0), ("T3", I0),
+                      ("f00", 2048), ("f01", 2048), ("f10", 2048), ("f11", 2048),
+                      ("px00", 2048), ("px01", 2048), ("px10", 2048), ("px11", 2048),
+                      ("GX0", 2048), ("GX1", 2048), ("G", 256), ("cv", 8 * 2048), ("cz", 3 * 2048),
+                      ("fq", 4096), ("DS", 4096), ("DC", 4096),
+                      ("LEa", 144), ("LEc", 144), ("LEn", 144), ("W1", 8), ("WB", 8), ("WX", 32), ("YSM", 8),
+                      ("ID", 128), ("NID", 128), ("N64", 128), ("ONES", 128), ("OS", 128), ("NBD", 128),
+                      ("DB", 128), ("NDB", 128), ("SH", 128), ("D01", 128), ("QM", 224), ("SIX", 128),
+                      ("RST", 128), ("GM0", 528), ("GM1", 528), ("CVO", 512), ("CVX", 512), ("OFR", 128), ("CC", 8),
+                      ("CZ", 128), ("KK0", 384), ("KK1", 384), ("CB0", 384), ("CB1", 384),
+                      ("HB", 256), ("LB", 256), ("SHB", 208), ("SLB", 208),
+                      ("GE", 384), ("GT", 384), ("HIF", 256), ("RZ", 512),
+                      ("WW", 512), ("SEND0", 128), ("SEND1", 128), ("PS", 256), ("PC", 128)]),
+        ("int32", [("PI", 1), ("CI", 144), ("ti", 8), ("KI", 512), ("KJ", 512), ("SELR", 208), ("SELH", 208), ("SELO", 208),
+                   ("raw", 256), ("VI", 256), ("QN", 256), ("MA", 80)]),
+        ("uint16", [("SL1", 208), ("SL2", 208), ("PL", 256), ("QL", 1024), ("LOL", 256), ("BC", 8), ("OFF", 24)]),
+        ("float32", [("ID32", 128), ("SK", 384), ("MX", 24), ("CO", 1024), ("SC", 1024), ("NUM", 256),
+                     ("T0", 256), ("M1", 256), ("YP", 256), ("YS", 768), ("cols", 64)])]:
+    for _n, _w in _l:
+        SCRATCH[_n] = ("sbuf", [128, _w], _d)
+NBANK = 8
+for _j in range(NBANK):
+    SCRATCH["PB%d" % _j] = ("psum", [128, 512], "float32")
 
 NDMA = 40
 SEMAPHORES = ["sv", "ss", "st", "sg"] + ["d%d" % j for j in range(NDMA)] + ["ar0", "ar1", "lc0", "lc1"]
+ALL = 0xFFFF
+
+
+def meet(a, b):
+    return a[1] < b[2] and b[1] < a[2] and (a[4] & b[4]) != 0 and (a[1] - b[1]) % math.gcd(a[3], b[3]) == 0
+
+
+def cover(a, b):
+    return a[1] <= b[1] and b[2] <= a[2] and (b[4] & ~a[4]) == 0 and b[3] % a[3] == 0 and (b[1] - a[1]) % a[3] == 0
+
+
+def lease(x):
+    return x[0] if isinstance(x[0], int) else None
+
+
+def schedule(ops):
+    n = len(ops)
+    pred = [set() for _ in range(n)]
+    last, gap = {}, {}
+    for i, o in enumerate(ops):
+        for w, regs in ((0, o["r"]), (1, o["w"])):
+            for x in regs:
+                l = last.setdefault(x[0], [])
+                ps = lease(x) is not None
+                for (j, w2, y) in l:
+                    if j != i and ((ps and ops[j]["q"] != o["q"]) or ((w or w2) and meet(x, y))):
+                        pred[i].add(j)
+                        own = ops[j]["q"] == o["q"] and (o["q"] == "T" or not w2) and not ops[j]["lat"]
+                        gap[j, i] = max(gap.get((j, i), 0.0), 0.0 if own else ops[j]["lat"] + WAKE)
+                if w and not ps:
+                    l[:] = [e for e in l if not cover(x, e[2])]
+                l.append((i, w, x))
+    need = [set(p) for p in pred]
+    for q, names in SEQ.items():
+        l = [i for name in names.split() for i, o in enumerate(ops) if o["tag"] == name]
+        for j, i in zip(l, l[1:]):
+            gap.setdefault((j, i), 0.0)
+            pred[i].add(j)
+            if q == "Y":
+                need[i].add(j)
+    succ = [set() for _ in range(n)]
+    for i in range(n):
+        for j in pred[i]:
+            succ[j].add(i)
+    held = [([lease(x) for x in o["r"] + o["w"] if lease(x) is not None] + [None])[0] for o in ops]
+
+    def place(look):
+        left = [len(p) for p in pred]
+        est = [0.0] * n
+        ready, free, todo, bank, ends = {}, {}, {}, {}, {}
+        banks = {k: 0.0 for k in range(NBANK)}
+        for i in range(n):
+            todo[held[i]] = todo.get(held[i], 0) + 1
+            if not left[i]:
+                ready.setdefault(ops[i]["q"], []).append(i)
+        start, fin = [0.0] * n, [0.0] * n
+        for _ in range(n):
+            pick, tb = None, min(banks.values()) if banks else 1e9
+            for q, l in ready.items():
+                if l:
+                    f = free.get(q, 0.0)
+                    ts = [max(f, est[i], tb if held[i] is not None and held[i] not in bank else 0.0) for i in l]
+                    t0 = min(ts) + look
+                    k, t, i = min((-tail[i], t, i) for t, i in zip(ts, l) if t <= t0)
+                    if pick is None or t < pick[0]:
+                        pick = (t, i)
+            t, i = pick
+            if t >= 1e9:
+                return 1e9, start, bank
+            o, z = ops[i], held[i]
+            ready[o["q"]].remove(i)
+            free[o["q"]] = fin[i] = t + o["cost"]
+            start[i] = t
+            if z is not None:
+                if z not in bank:
+                    bank[z] = min(banks, key=lambda k: banks[k])
+                    del banks[bank[z]]
+                ends[z] = max(ends.get(z, 0.0), fin[i] + WAKE)
+                todo[z] -= 1
+                if not todo[z]:
+                    banks[bank[z]] = ends[z]
+            for k in succ[i]:
+                est[k] = max(est[k], fin[i] + gap[i, k])
+                left[k] -= 1
+                if not left[k]:
+                    ready.setdefault(ops[k]["q"], []).append(k)
+        return max(fin[i] + ops[i]["lat"] for i in range(n)), start, bank
+
+    tail, todo = [0.0] * n, [len(s) for s in succ]
+    stack = [i for i in range(n) if not todo[i]]
+    while stack:
+        i = stack.pop()
+        tail[i] = ops[i]["cost"] + max([ops[i]["lat"]] + [tail[k] + gap[i, k] for k in succ[i]])
+        for j in pred[i]:
+            todo[j] -= 1
+            if not todo[j]:
+                stack.append(j)
+    assert not any(todo), "the lists of long calls contradict the data flow"
+    best = min((place(look) for look in LOOK), key=lambda x: x[0])
+    order = sorted(range(n), key=lambda i: (best[1][i], i))
+
+    need = [sorted(need[i]) for i in range(n)]
+    qs, nl = [o["q"] for o in ops], {}
+    for z in held:
+        nl[z] = nl.get(z, 0) + 1
+    kinds = []
+    for f, gf, wk, dl in KINDS:
+        cost = [o["cost"] * (f * gf if o["gat"] else f if o["q"] in "VSTG" else 1.0) for o in ops]
+        lat = [o["lat"] + dl if o["lat"] else 0.0 for o in ops]
+        kinds.append((cost, lat, [[(j, (lat[j] + wk) if gap[j, i] else 0.0) for j in need[i]] for i in range(n)], wk))
+
+    def play(order, kind):
+        cost, lat, pre, wk = kind
+        fin, why, free, prev, bank, todo, ends = [0.0] * n, [None] * n, {}, {}, {}, dict(nl), {}
+        banks, end, at = {k: (0.0, None) for k in range(NBANK)}, 0.0, None
+        for i in order:
+            q = qs[i]
+            t, y = free.get(q, 0.0), prev.get(q)
+            for j, d in pre[i]:
+                if fin[j] + d > t:
+                    t, y = fin[j] + d, j
+            z = held[i]
+            if z is not None:
+                if z not in bank:
+                    if not banks:
+                        return 1e9, None, None, None
+                    k = bank[z] = min(banks, key=banks.get)
+                    b = banks.pop(k)
+                    if b[0] > t:
+                        t, y = b
+                todo[z] -= 1
+            free[q] = fin[i] = t + cost[i]
+            prev[q], why[i] = i, y
+            if z is not None:
+                if fin[i] + wk > ends.get(z, (0.0, None))[0]:
+                    ends[z] = (fin[i] + wk, i)
+                if not todo[z]:
+                    banks[bank[z]] = ends[z]
+            if fin[i] + lat[i] > end:
+                end, at = fin[i] + lat[i], i
+        return end, why, at, bank
+
+    rng = np.random.default_rng(0)
+    res = [play(order, k) for k in kinds]
+    ref = [r[0] for r in res]
+    now = top = float(len(kinds))
+    keep = order
+    for it in range(MOVES):
+        end, why, v, bank = res[int(rng.integers(len(kinds)))]
+        arcs = []
+        while why[v] is not None:
+            if qs[why[v]] == qs[v] and why[v] not in need[v]:
+                arcs.append((why[v], v))
+            v = why[v]
+        if not arcs:
+            break
+        u, v = arcs[int(rng.integers(len(arcs)))]
+        a, b = order.index(u), order.index(v)
+        a = max(0, a - int(rng.integers(REACH)) * int(rng.integers(2)))
+        mid = order[a:b + 1]
+        if rng.integers(2):
+            up = {v}
+            for i in mid[::-1]:
+                if i in up:
+                    up.update(need[i])
+            if u in up:
+                continue
+            mid = [i for i in mid if i in up] + [i for i in mid if i not in up]
+        else:
+            down = {u}
+            for i in mid:
+                if any(j in down for j in need[i]):
+                    down.add(i)
+            if v in down:
+                continue
+            mid = [i for i in mid if i not in down] + [i for i in mid if i in down]
+        cand = order[:a] + mid + order[b + 1:]
+        r2 = [play(cand, k) for k in kinds]
+        val = sum(r[0] / x for r, x in zip(r2, ref))
+        if val < now + HEAT * (1 - it / MOVES) * float(rng.exponential()):
+            order, res, now = cand, r2, val
+            if val < top:
+                top, keep = val, cand
+    end, why, at, bank = play(keep, kinds[0])
+    PLAN["end"], PLAN["bank"], PLAN["order"] = end, bank, keep
 
 
 def rank_program(g, core, T, topo):
     rank = T.rank_of(core)
     if rank is None:
         return
+    if not PLAN:
+        schedule(record(g, core, T, topo, rank, {}))
+    issue(g, T, record(g, core, T, topo, rank, PLAN["bank"]))
+
+
+def record(g, core, T, topo, rank, banks):
     A = AluOpType
     AF = ActivationFunctionType
-    ALL = 0xFFFF
     ops = []
+    nlease = [0]
+
+    def psum():
+        nlease[0] += 1
+        return nlease[0]
 
     def X(name, c0, c1, step=1, p=None, rows=ALL):
-        t = T[name]
-        if p is not None:
-            ap = t[0:p, c0:c1]
-        elif step == 1:
-            ap = t[:, c0:c1]
-        else:
-            ap = t[:, c0:c1:step]
-        return (ap, [(name, c0, c1, rows)])
+        t = T["PB%d" % banks.get(name, 0)] if isinstance(name, int) else T[name]
+        p0, p1 = p if p else (0, 128)
+        ap = t[p0:p1, c0:c1] if step == 1 else t[p0:p1, c0:c1:step]
+        return (ap, [(name, c0, c0 + (c1 - c0 - 1) // step * step + 1, step, rows)])
 
     def ind(win, off):
         return (win[0].indirect(off[0]), win[1] + off[1], True)
@@ -91,7 +273,8 @@ def rank_program(g, core, T, topo):
     def rec(kind, q, outs, ins, fn, cost, lat=0.0, data=None):
         reads = list(dict.fromkeys(r for x in ins for r in x[1]))
         writes = list(dict.fromkeys(r for x in outs for r in x[1]))
-        ops.append({"kind": kind, "q": q, "r": reads, "w": writes, "fn": fn, "cost": cost, "lat": lat, "data": data})
+        ops.append({"kind": kind, "q": q, "r": reads, "w": writes, "fn": fn, "cost": cost, "lat": lat, "data": data,
+                    "tag": None, "gat": any(len(x) > 2 for x in ins)})
 
     def width(x):
         n = 1
@@ -101,19 +284,22 @@ def rank_program(g, core, T, topo):
 
     def emit(q, outs, ins, fn, cyc=1.0, gat=False):
         n = width(outs[0])
-        rec("c", q, outs, ins, fn, 0.06 + n * GAT * CYC if gat else 0.02 + max(64, cyc * n) * CYC)
+        rec("c", q, outs, ins, fn, 0.06 + n * GAT * CYC if gat else 0.01 + max(64, cyc * n) * CYC)
 
     def isg(*xs):
         return any(len(x) > 2 for x in xs)
 
+    def wide(x):
+        return lease(x[1][0]) is not None or SCRATCH[x[1][0][0]][2] not in ("bfloat16", "uint16")
+
     def two(*xs):
-        return all(SCRATCH[x[1][0][0]][2] in ("bfloat16", "uint16") for x in xs)
+        return not any(wide(x) for x in xs)
 
     def vcopy(o, i):
         emit("V", [o], [i], lambda e: e.tensor_copy(o[0], i[0]), 0.5 if two(o, i) else 1.0, isg(i))
 
     def vtt(o, a, b, op):
-        cyc = 1.0 if a[1][0][0] in PSUMS or b[1][0][0] in PSUMS else 2.0
+        cyc = 2.0 if lease(a[1][0]) is None and lease(b[1][0]) is None else 1.0
         emit("V", [o], [a, b], lambda e: e.tensor_tensor(o[0], a[0], b[0], op), cyc, isg(a))
 
     def vts(o, i, s1, op0, s2=None, op1=None):
@@ -126,6 +312,9 @@ def rank_program(g, core, T, topo):
         else:
             emit("V", [o], ins, lambda e: e.tensor_scalar(o[0], i[0], a1, a2, op0, op1), cyc)
 
+    def scan(o, a, b, init, op0, op1):
+        emit("V", [o], [a, b], lambda e: e.tensor_tensor_scan(o[0], a[0], b[0], init, op0, op1), 0.5 if two(o, a, b) else 1.0)
+
     def vset(o, c):
         emit("V", [o], [], lambda e: e.memset(o[0], c), 0.5 if two(o) else 1.0)
 
@@ -135,28 +324,36 @@ def rank_program(g, core, T, topo):
         s = scale[0] if isinstance(scale, tuple) else scale
         emit("S", [o], ins, lambda e: e.activation(o[0], i[0], func, bias=b, scale=s), 1.0, isg(i))
 
-    def gather(q, o, i):
-        if q == "V":
+    def gather(tag, o, i):
+        if WHO[tag] == "V":
             vcopy(o, i)
         else:
             act(o, i)
+        ops[-1]["tag"] = tag
 
     def iota(o, pattern, base, cm, fl=False):
+        c = 0.14 + 2 * width(o) * CYC
         if fl:
-            emit("G", [o], [], lambda e: e.iota(o[0], pattern, base, cm, allow_small_or_imprecise_dtypes=True), 2.0)
+            rec("c", "G", [o], [], lambda e: e.iota(o[0], pattern, base, cm, allow_small_or_imprecise_dtypes=True), c)
         else:
-            emit("G", [o], [], lambda e: e.iota(o[0], pattern, base, cm), 2.0)
+            rec("c", "G", [o], [], lambda e: e.iota(o[0], pattern, base, cm), c)
 
     def mms(lst):
-        cost = sum(max(64, width(m[2])) for m in lst) * 0.0005
+        cost = sum(max(min(64, width(m[1])), width(m[2])) * (4 if wide(m[1]) else 1) for m in lst) * PEC
         rec("t", "T", [m[0] for m in lst], [x for m in lst for x in (m[1], m[2])], None, cost, 0.0, lst)
+
+    def acc(lst, first=True, last=True):
+        mms([m + (first and n == 0, last and n == len(lst) - 1) for n, m in enumerate(lst)])
 
     def dma(q, outs, ins, pairs, lat=2.3):
         rec("d", q, outs, ins, None, 0.06 * len(pairs), lat, pairs)
 
-    dma("Y", [X("SELR", 0, 208)], [], [(T.SELR[:], T.sel0[:])])
-    dma("S", [X("F", 16, 16 + I0)], [], [(T.F[:, 16:16 + I0], T.front[:])], 4.8)
-    dma("Y", [X("raw", 0, 256)], [], [(T.raw[:, 16 * k:16 * k + 16], T.par[k::16, :]) for k in range(16)])
+    dma("Y", [X("SELR", 0, 208)], [], [(T.SELR[:], T.sel0[:])], 2.5)
+    dma("Y", [X("raw", 0, 256)], [], [(T.raw[:], T.par[:])], LAT[0])
+    dma("Y", [X("F", 16, 16 + CUT)], [], [(T.F[:, 16:16 + CUT], T.front[:, 0:CUT])], LAT[1])
+    dma("Y", [X("F", 16 + CUT, 16 + I0)], [], [(T.F[:, 16 + CUT:16 + I0], T.front[:, CUT:I0])], LAT[2])
+    for j, name in enumerate(("sel", "par", "fr0", "fr1")):
+        ops[j]["tag"] = name
 
     ncol = [0]
 
@@ -164,32 +361,28 @@ def rank_program(g, core, T, topo):
         ncol[0] += 1
         return X("cols", ncol[0] - 1, ncol[0])
 
-    PI, CI, CU = X("PI", 0, 1), X("CI", 0, 128), X("CU", 0, 128)
+    PI, CI = X("PI", 0, 1), X("CI", 0, 128)
+    ID, NID, ONES, ID32 = X("ID", 0, 128), X("NID", 0, 128), X("ONES", 0, 128), X("ID32", 0, 128)
     LE = lambda nm, e: X(nm, 15 - e, 143 - e)
     ti = [X("ti", j, j + 1) for j in range(8)]
     iota(PI, [[0, 1]], 0, 1)
     iota(X("CI", 0, 144), [[1, 144]], 0, 0)
-    iota(X("IDV", 0, 260), [[1, 260]], 0, 0)
-    vset(X("PT", 0, PW // 2), 0.0)
-    act(X("PT", PW // 2, PW), X("PT", 0, PW // 2))
-    vset(X("F", 0, 16), 0.0)
-    pf, uf, gf, zf = col(), col(), col(), col()
+    iota(X("LB", 0, 256), [[0, 4], [1, 64]], 16, 0, True)
+    iota(X("HB", 0, 256), [[1, 4], [0, 64]], 0, 0, True)
+    vset(X("PT", 0, FW), 0.0)
+    pf, uf, gf, zf, u4 = col(), col(), col(), col(), col()
     vcopy(pf, PI)
     vts(ti[0], PI, 15, A.bitwise_and)
     vts(ti[1], PI, 4, A.arith_shift_right)
     vcopy(uf, ti[0])
     vcopy(gf, ti[1])
     act(zf, gf, AF.Identity, bias=15.0, scale=16.0)
+    act(u4, uf, scale=4.0)
+    act(X("HB", 0, 256), X("HB", 0, 256), AF.Identity, bias=u4)
 
-    def split(src, hb, lb):
-        vts(X("SELH", 0, 208), src, 6, A.arith_shift_right)
-        vts(X("SELO", 0, 208), src, 63, A.bitwise_and)
-        vcopy(X(hb, 0, 208), X("SELH", 0, 208))
-        vcopy(X(lb, 0, 208), X("SELO", 0, 208))
-
-    def prow(r, buf, n, c0):
-        o = T.PT[r::16, c0:c0 + 16 * n]
-        dma("Y", [X("PT", c0, c0 + 16 * n, rows=1 << r)], [X(buf, 0, n)], [(o, T[buf][:, 0:n])])
+    def prow(r, buf, n, lat):
+        dma("Y", [X("PT", 16, 16 + 16 * n, rows=1 << r)], [X(buf, 0, n)], [(T.PT[r::16, 16:16 + 16 * n], T[buf][:, 0:n])], lat)
+        ops[-1]["tag"] = "row%d" % r
 
     def wcol(a):
         o, t = col(), col()
@@ -198,280 +391,265 @@ def rank_program(g, core, T, topo):
         vtt(o, o, t, A.add)
         return o
 
-    SELP = X("SELP", 0, 208)
-    vts(SELP, X("SELR", 0, 208), 16.0, A.add)
-    split(SELP, "SHB", "SLB")
-    prow(2, "SHB", 208, 16)
-    prow(3, "SLB", 208, 16)
-    vcopy(X("SELL", 0, 208), SELP)
+    vts(X("SELH", 0, 208), X("SELR", 0, 208), 6, A.arith_shift_right)
+    vts(X("SELO", 0, 208), X("SELR", 0, 208), 63, A.bitwise_and)
+    vcopy(X("SHB", 0, 208), X("SELH", 0, 208))
+    vts(X("SLB", 0, 208), X("SELO", 0, 208), 16.0, A.add)
+    prow(2, "SHB", 208, LAT[3])
+    prow(3, "SLB", 208, LAT[3])
+    prow(0, "HB", 256, LAT[3])
+    prow(1, "LB", 256, LAT[3])
+    w = [wcol(2 * d) for d in range(5)]
+    vts(X("LEa", 0, 144), X("CI", 0, 144), zf, A.is_equal, w[1], A.mult)
+    vset(X("T2", 0, 16), 0.0)
+    vset(X("F", 0, 16), 0.0)
+
+    def steps(src, lst, dst, d0, qs, moves):
+        for j in (0, 1):
+            c0, b = 16 + 1664 * j, psum()
+            acc([(X(b, 0, 104), LE("LEa", e), X(src, c0 + e, c0 + 1664, 16)) for e in range(16)])
+            vcopy(X(lst, 104 * j, 104 * j + 104), X(b, 0, 104))
+        for j in (0, 1):
+            c0 = d0 + 1664 * j
+            gather(qs + str(j), X(dst, c0, c0 + 1664), ind(X(src, 0, 16 + I0), X(lst, 104 * j, 104 * j + 104)))
+        for j in (0, 1):
+            c0, c1 = d0 + 1664 * j, 16 + 1664 * j
+            dma("Y", [X("PT", c1, c1 + 1664, rows=sum(1 << b for a, b in moves))], [X(dst, c0, c0 + 1664)],
+                [(T.PT[b::16, c1:c1 + 1664], T[dst][a::16, c0:c0 + 1664]) for a, b in moves])
+
+    steps("PT", "SL1", "T2", 16, "a", [(2, 4), (3, 5)])
+    steps("T2", "SL2", "T3", 0, "b", [(0, 6), (1, 7), (2, 8), (3, 9)])
+
     for h in (0, 1):
         vts(X("PL", 128 * h, 128 * h + 128), X("raw", h, 256, 2), 16.0, A.add)
-    u260 = col()
-    act(u260, uf, scale=260.0)
-    vts(X("IDW", 0, 260), X("IDV", 0, 260), u260, A.add)
-    vts(X("IDH", 0, 260), X("IDW", 0, 260), 6, A.arith_shift_right)
-    vcopy(X("HB", 0, 260), X("IDH", 0, 260))
-    vts(X("IDV", 0, 260), X("IDW", 0, 260), 63, A.bitwise_and)
-    vcopy(X("LB", 0, 260), X("IDV", 0, 260))
-    swin = X("PT", 0, 16 + I0)
-    gather(S2Q[0], X("s2", 0, 1664), ind(swin, X("SELL", 0, 104)))
-    gather(S2Q[1], X("s2", 1664, 3328), ind(swin, X("SELL", 104, 208)))
-    wa = wcol(2)
-    vts(X("LEa", 0, 144), X("CI", 0, 144), zf, A.is_equal, wa, A.mult)
-    mms([(X("PQ0", 0, 208), LE("LEa", e), X("s2", e, 3328, 16), e == 0, e == 15) for e in range(16)])
-    vcopy(SELP, X("PQ0", 0, 208))
-    split(SELP, "SHB2", "SLB2")
-    prow(4, "SHB2", 208, 16)
-    prow(5, "SLB2", 208, 16)
-    prow(0, "HB", 260, 0)
-    prow(1, "LB", 260, 0)
-    wb = wcol(4)
-    for nm, wt in (("LEb", wb), ("LEK", 4096.0), ("LEC", BIG), ("LEH", 2048.0)):
-        vts(X(nm, 0, 144), X("CI", 0, 144), zf, A.is_equal, wt, A.mult)
-    vset(X("ONES", 0, 128), 1.0)
-    vts(X("KR", 0, 128), CI, -0.125, A.mult, 15.875, A.add)
-    u2032 = col()
-    act(u2032, uf, AF.Identity, bias=2032.0)
-    ID, NID = X("ID", 0, 128), X("NID", 0, 128)
+    C8 = X("CI", 0, 8)
+    vts(X("W1", 0, 8), C8, gf, A.is_equal)
+    vset(X("RST", 0, 128), 0.0)
+    vset(X("RST", 0, 128, 16), -BIG)
+    vcopy(X("BC", 0, 8), C8)
     vts(ID, CI, pf, A.is_equal)
     act(NID, ID, scale=-1.0)
-    vset(X("CV", 0, 64), -10.0 * BIG / 128)
-    vset(X("CS", 0, 64), -4.0 * BIG / 128)
+    act(ID32, ID)
+    vset(ONES, 1.0)
+    vts(X("LEn", 0, 144), X("CI", 0, 144), zf, A.is_equal, -1.0, A.mult)
+    act(X("LEc", 0, 144), X("LEn", 0, 144), scale=-BIG)
+    iota(X("CC", 0, 8), [[2, 8]], 0, 0, True)
+    u16 = col()
+    act(u16, uf, AF.Identity, bias=16.0, scale=16.0)
+    act(X("WB", 0, 8), X("W1", 0, 8), scale=BIG)
+    for d in range(1, 5):
+        act(X("WX", 8 * (4 - d), 8 * (5 - d)), X("W1", 0, 8), scale=w[d])
+    act(X("YSM", 0, 8), X("W1", 0, 8), scale=w[0])
+    iota(X("CVX", 0, 512), [[0, 4], [512, 128]], -5120, 0, True)
+    iota(X("CVO", 0, 512), [[512, 128], [0, 4]], -5120, 0, True)
+    iota(X("OFR", 0, 128), [[-512, 128]], 0, 0, True)
+    vset(X("CZ", 0, 128), -(4 * BIG + 5 * PR) / 128)
     for h in (0, 1):
-        vts(X("CO0", 128 * h, 128 * h + 128), X("raw", h, 256, 2), 16.0 + 5 * PR, A.add)
-    vts(CU, CI, 15, A.bitwise_and)
-    vts(X("SU", 0, 128), CU, uf, A.is_equal)
-    l4, p3, l2 = col(), col(), col()
-    vts(l4, uf, 4.0, A.is_lt)
-    vts(p3, pf, 3.0, A.add)
-    vtt(p3, p3, l4, A.mult)
-    vts(p3, p3, -1.0, A.add)
-    vts(X("SH", 0, 128), CI, p3, A.is_equal)
+        vts(X("NUM", 128 * h, 128 * h + 128), X("raw", h, 256, 2), 16.0, A.add)
+    cd = [None]
+    for d in range(1, 5):
+        cd.append(col())
+        act(cd[d], pf, AF.Identity, bias=float(PR * (5 - d)), scale=BIG)
+    vset(X("QM", 0, 192), 0.0)
+    vset(X("QM", 64, 128), 1.0)
+    vset(X("SIX", 0, 128), 6 * BIG / 128)
+    for j in (0, 1):
+        ma = X("MA", 8 + 36 * j, 41 + 36 * j)
+        vset(X("GM%d" % j, 0, 528), 0.0)
+        iota(ma, [[2, 33]], 128 + j, -1)
+        vts(ma, ma, 15, A.bitwise_and)
+        vts(X("GM%d" % j, 15, 528, 16), ma, 0.0, A.is_equal, -256.0, A.add)
+    act(X("N64", 0, 128), ID, scale=-64.0)
+    vset(X("OS", 0, 128), 1.0 / PR)
+    vts(X("QN", 0, 128), CI, 4, A.arith_shift_right)
+    vts(X("NBD", 0, 128), X("QN", 0, 128), gf, A.is_equal, -1.0, A.mult)
+    p1, l15 = col(), col()
+    vts(l15, uf, 15.0, A.is_lt)
+    vts(p1, pf, 2.0, A.add, l15, A.mult)
+    vts(p1, p1, -1.0, A.add)
+    vts(X("DB", 0, 128), CI, p1, A.is_equal)
+    vtt(X("DB", 0, 128), ID, X("DB", 0, 128), A.subtract)
+    act(X("NDB", 0, 128), X("DB", 0, 128), scale=-float(PR))
+    act(X("DB", 0, 128), X("DB", 0, 128), scale=float(PR))
+    u37 = col()
+    act(u37, uf, scale=37.0)
+    iota(X("KI", 0, 256), [[5, 2], [10, 128]], 0, 0)
+    iota(X("KI", 256, 512), [[1, 2], [2, 128]], 0, 0)
+    vts(X("KJ", 0, 256), X("KI", 0, 256), u37, A.add)
+    vts(X("KJ", 256, 512), X("KI", 256, 512), uf, A.add)
+    vts(X("KJ", 0, 256), X("KJ", 0, 256), 255, A.bitwise_and)
+    vts(X("KJ", 256, 512), X("KJ", 256, 512), 127, A.bitwise_and)
+    for h in (0, 1):
+        iota(X("KK%d" % h, 0, 128), [[2, 128]], h, 0, True)
+        vcopy(X("KK%d" % h, 128, 256), X("KJ", 128 * h, 128 * h + 128))
+        vcopy(X("KK%d" % h, 256, 384), X("KJ", 256 + 128 * h, 384 + 128 * h))
+    for t in range(R):
+        B = I0 + NB * t
+        vset(X("CB%d" % t, 0, 384, p=(0, 64), rows=1), -64.0)
+        for j, c in enumerate((B + 16, B + 2016, B + 208)):
+            vset(X("CB%d" % t, 128 * j, 128 * j + 128, p=(64, 128), rows=2), (c - PR + 4096) / 64.0)
+    l8, p2, l2 = col(), col(), col()
+    vts(l8, uf, 8.0, A.is_lt)
+    vts(p2, pf, 3.0, A.add, l8, A.mult)
+    vts(p2, p2, -1.0, A.add)
+    vts(X("SH", 0, 128), CI, p2, A.is_equal)
     vts(l2, uf, 2.0, A.is_lt)
     act(X("D01", 0, 128), ID, scale=l2)
-    w01 = wcol(0)
-    vts(X("YSM", 0, 8), X("CI", 0, 8), gf, A.is_equal, w01, A.mult)
-    na, nb, nc, c7, b3, u8 = col(), col(), col(), col(), col(), col()
-    vts(ti[2], PI, 1, A.bitwise_and)
-    vts(ti[3], PI, 1, A.arith_shift_right, 7, A.bitwise_and)
-    vts(ti[4], PI, 7, A.bitwise_and)
-    vts(ti[5], PI, 3, A.arith_shift_right, 1, A.bitwise_and)
-    vts(na, ti[2], 128.0, A.mult)
-    vts(nb, ti[3], 16.0, A.mult)
-    vtt(na, na, nb, A.add)
-    vts(X("NL", 0, 16), X("CI", 0, 16), na, A.add)
-    act(u8, uf, scale=8.0)
-    vts(X("NL2", 0, 8), X("CI", 0, 8), u8, A.add)
-    vcopy(c7, ti[4])
-    vts(b3, c7, 16.0, A.mult)
-    vcopy(nc, ti[5])
-    vtt(b3, b3, nc, A.add)
-    vts(X("NL3", 0, 8), X("CI", 0, 8), 2.0, A.mult, b3, A.add)
-    vts(X("CX", 0, 16), X("CI", 0, 16), 3, A.arith_shift_right)
-    vts(X("XL", 0, 16), X("CX", 0, 16), 8.0, A.mult, c7, A.add)
-    iota(X("MA", 0, 256), [[1, 256]], 128, -1)
-    vts(X("MA", 0, 256), X("MA", 0, 256), 15, A.bitwise_and)
-    vts(X("MSK0", 0, 256), X("MA", 0, 256), 0.0, A.is_equal)
-    vts(X("MSK1", 0, 256), X("MA", 0, 256), 15.0, A.is_equal)
-    u80, u16 = col(), col()
-    act(u80, uf, scale=80.0)
-    act(u16, uf, scale=16.0)
-    for h in (0, 1):
-        iota(X("K12", 256 * h, 256 * h + 128), [[37, 16], [10, 8]], 80 + 5 * h, 0, True)
-        iota(X("K12", 256 * h + 128, 256 * h + 256), [[1, 16], [2, 8]], h, 0, True)
-        for j, ub in ((0, u80), (128, u16)):
-            kx = X("K12", 256 * h + j, 256 * h + j + 128)
-            act(kx, kx, AF.Identity, bias=ub)
-    for t in range(R):
-        ks = X("KS%d" % t, 0, 256)
-        iota(ks, [[1, 2], [0, 16], [2, 8]], 8 * PR + I0 + NB * t + 16, 0, True)
-        act(ks, ks, AF.Identity, bias=u16)
 
-    def sumto(bank, o0, n, le, src, s0, const=None):
-        o = X(bank, o0, o0 + n)
-        l = []
-        if const is not None:
-            l.append((o, X("ONES", 0, 128), const, True, False))
-        for e in range(16):
-            l.append((o, LE(le, e), X(src, s0 + e, s0 + 16 * n, 16), e == 0 and const is None, e == 15))
-        mms(l)
+    def choose(b, z):
+        zs = (128 * z, 128 * z + 128)
+        sk = X("SK", *zs)
+        scan(sk, X("RST", 0, 128), X(b, 0, 128), 0.0, A.add, A.max)
+        mx = X("MX", 8 * z, 8 * z + 8)
+        vcopy(mx, X("SK", zs[0] + 15, zs[1], 16))
+        vtt(X("GE", *zs), ind(mx, X("BC", 0, 8)), sk, A.is_equal)
+        b = psum()
+        acc([(X(b, 0, 128), X("GE", *zs), ID)])
+        act(X("GT", *zs), X(b, 0, 128))
+        o = X(psum(), 0, 8)
+        acc([(o, ONES, X("CC", 0, 8))] + [(o, LE("LEn", e), X("GT", zs[0] + e, zs[1], 16)) for e in range(16)])
+        vts(X("OFF", 8 * z, 8 * z + 8), o, u16, A.add)
 
-    def tree(z, src, s0, out, o0, bank, off):
-        r = 128 * (z & 1)
-        vcopy(X(src, s0, s0 + 128), X(bank, 0, 128))
-        vtt(X("TR", r, r + 64), X(src, s0, s0 + 64), X(src, s0 + 64, s0 + 128), A.max)
-        vtt(X("TR", r + 64, r + 96), X("TR", r, r + 32), X("TR", r + 32, r + 64), A.max)
-        vtt(X("TR", r + 96, r + 112), X("TR", r + 64, r + 80), X("TR", r + 80, r + 96), A.max)
-        vtt(X(out, o0, o0 + 8), X("TR", r + 96, r + 104), X("TR", r + 104, r + 112), A.max)
-        vts(X("MN", 8 * z, 8 * z + 8), X(out, o0, o0 + 8), 4095, A.bitwise_and)
-        vts(X(off, 0, 8), X("MN", 8 * z, 8 * z + 8), -1.0, A.mult, u2032, A.add)
+    def signs(z, src, gm):
+        for j in range(4):
+            pd, l = psum(), []
+            for i in range(4):
+                o = X(pd, 128 * i, 128 * i + 128)
+                l += [(o, NID, X(src, 4 * j + i, 2048, 16), True, False), (o, ID, gm, False, True)]
+            mms(l)
+            act(X("cz", 2048 * z + 512 * j, 2048 * z + 512 * j + 512), X(pd, 0, 512), AF.Sign, bias=0.5)
 
-    def grow(src, n, c0, y0, tt, bank):
-        yo = 256 if n == 256 else 384
-        y = X(bank, yo, yo + n, p=8)
+    def grow(src, n, c0, y0, tt):
         if tt + 1 < R:
-            mms([(X(bank, 0, n), X("SH", 0, 128), X(src, 0, n), True, False),
-                 (X(bank, 0, n), X("D01", 0, 128), X("PT", c0, c0 + n), False, True)])
-            act(X("PT", c0, c0 + n), X(bank, 0, n))
-        mms([(y, X("YSM", 0, 8), X(src, 0, n), True, True)])
-        act(X("YS", y0, y0 + n, p=8), y, AF.Identity, bias=-16.0)
-        dma("Y", [], [X("YS", y0, y0 + n, p=8)], [(T.ys[:, y0:y0 + n], T.YS[0:8, y0:y0 + n])])
+            o = X(psum(), 0, n)
+            acc([(o, X("SH", 0, 128), X(src, 0, n)), (o, X("D01", 0, 128), X("PT", c0, c0 + n))])
+            act(X("PT", c0, c0 + n), o)
+        y = X(psum(), 0, n, p=(0, 8))
+        acc([(y, X("YSM", 0, 8), X(src, 0, n))])
+        act(X("YS", y0, y0 + n, p=(0, 8)), y, AF.Identity, bias=-16.0)
+        dma("Y", [], [X("YS", y0, y0 + n)], [(T.ys[:, y0:y0 + n], T.YS[0:8, y0:y0 + n])])
 
     def come(tt):
-        cc = 16 + I0 + NB * tt + L
-        ft, pt = "f%d" % tt, "pa%d" % tt
-        vcopy(X("CR", 0, 128), ind(X("F", cc, cc + 128), X("NL2", 0, 8)))
-        cr, onS = X("CR", 0, 128), CQ[tt] == "S"
-        kb = "PQ1" if onS else "PD0"
-        if not onS:
-            mms([(X("PQ1", 128 * j, 128 * j + 128), ID, cr, True, True) for j in range(4)])
-        for j in range(4):
-            fj, cj, pd = X(ft, 512 * j, 512 * j + 512), X("cvc", 512 * j, 512 * j + 512), "PD%d" % (j & 1)
-            if onS:
-                l = []
-                for i in range(4):
-                    o = X(pd, 128 * i, 128 * i + 128)
-                    l += [(o, ID, cr, True, False), (o, NID, X(ft, 512 * j + 128 * i, 512 * j + 128 * i + 128), False, True)]
-                mms(l)
-                act(cj, X(pd, 0, 512), AF.Sign, bias=0.5)
-            else:
-                vtt(cj, fj, X("PQ1", 0, 512), A.is_le)
-            if j & 1:
-                sumto(kb, 32 * (j - 1), 64, "LEH" if onS else "LEK", "cvc", 512 * (j - 1),
-                      X("KR", 32 * (j - 1), 32 * (j - 1) + 64))
-        tree(2, "KC", 0, "MC", 0, kb, "OFFC")
-        act(X("PCP", 0, 128), ind(X(pt, 0, 2048), X("OFFC", 0, 8)))
-        act(X("PCN", 0, 128), ind(X("PCP", 0, 128), X("NL3", 0, 8)))
-        grow("PCN", 128, cc, NB * tt + L, tt, "PD1")
+        cc, b = 16 + I0 + NB * tt + L, psum()
+        signs(2, "f%d0" % tt, X("F", cc, cc + 128))
+        mms([(X(b, k, 128, 16), X("cz", 4096 + 128 * k, 4224 + 128 * k), X("W1", 0, 8), True, True) for k in range(16)])
+        choose(b, 2)
+        act(X("PC", 0, 128), ind(X("px%d0" % tt, 0, 2048), X("OFF", 16, 24)))
+        grow("PC", 128, cc, NB * tt + L, tt)
 
+    nfq = [0]
     for t in range(R):
         B = I0 + NB * t
         cc = 16 + B + L
-        fn, pn = "f%d" % t, "pa%d" % t
         win = X("F", 0, 16 + B)
         pwin = X("PT", 0, 16 + B)
-        KB = ("PCa", "PCb")
+        HS = [(128 * h, 128 * h + 128) for h in (0, 1)]
         for h in (0, 1):
-            for ch in (0, 1):
-                c0 = 128 * h + 64 * ch
-                gather(FQ[t][2 * h + ch], X(fn, 16 * c0, 16 * c0 + 1024), ind(win, X("PL", c0, c0 + 64)))
-                sumto(KB[h], 64 * ch, 64, "LEK", fn, 16 * c0, X("KR", 64 * ch, 64 * ch + 64))
+            fn, b = "f%d%d" % (t, h), psum()
+            for c in (0, 1):
+                gather("f%d%d%d" % (t, h, c), X(fn, 1024 * c, 1024 * c + 1024), ind(win, X("PL", 128 * h + 64 * c, 128 * h + 64 * c + 64)))
+            mms([(X(b, k, 128, 16), X(fn, k, 2048, 16), X("W1", 0, 8), True, True) for k in range(16)])
+            choose(b, h)
+            vcopy(X("G", *HS[h]), ind(X(fn, 0, 2048), X("OFF", 8 * h, 8 * h + 8)))
+            for k in range(16):
+                vcopy(X("GX%d" % h, k, 2048, 16), X("G", *HS[h]))
         for h in (0, 1):
-            tree(h, "KEY", 128 * h, "MI", 8 * h, KB[h], "OFF%d" % h)
-            vcopy(X("G%d" % h, 0, 128), ind(X(fn, 2048 * h, 2048 * h + 2048), X("OFF%d" % h, 0, 8)))
-            mms([(X("PG%d" % h, 128 * j, 128 * j + 128), ID, X("G%d" % h, 0, 128), True, True) for j in range(4)])
+            pn, b, c0 = "px%d%d" % (t, h), psum(), 512 * h
+            for c in (0, 1):
+                gather("x%d%d%d" % (t, h, c), X(pn, 1024 * c, 1024 * c + 1024), ind(pwin, X("PL", 128 * h + 64 * c, 128 * h + 64 * c + 64)))
+            acc([(X(b, 0, 512), ONES, X("CVX", 0, 512))]
+                + [(X(b, k, 512, 16), X(pn, k, 2048, 16), X("WX", 0, 32)) for k in range(16)])
+            for d in range(1, 5):
+                j = 4 - d
+                act(X("CO", c0 + j, c0 + 512, 4), X(b, 128 * j, 128 * j + 128), AF.Identity, bias=10 * BIG + PR * (5 - d))
+            for d in range(1, 5):
+                j, o = 4 - d, X(psum(), 0, 128)
+                acc([(o, X("CO", c0 + j, c0 + 512, 4), ID32)])
+                vts(X("QL", c0 + 128 * j, c0 + 128 * j + 128), o, cd[d], A.subtract)
         for h in (0, 1):
-            for n in (128, 256, 512):
-                gather(GQ[t][h], X("G%d" % h, n, 2 * n), X("G%d" % h, 0, n))
-            for j in range(4):
-                s0 = 2048 * h + 512 * j
-                o = X("cv%d" % h, 512 * j, 512 * j + 512)
-                if (0, h, j) in SUN[t]:
-                    pd = X("PD%d" % (j & 1), 0, 512)
-                    mms([(pd, NID, X(fn, s0, s0 + 512), True, False), (pd, ID, X("G%d" % h, 0, 512), False, True)])
-                    act(o, pd, AF.Sign, bias=0.5)
-                else:
-                    vtt(o, X(fn, s0, s0 + 512), X("PG%d" % h, 0, 512), A.is_le)
-                sg = [(0, h, i) in SUN[t] for i in (j - 1, j)]
-                if j & 1 and sg[0] == sg[1]:
-                    sumto(KB[h], 32 * (j - 1), 64, "LEC", "cv%d" % h, 512 * (j - 1), X("CS" if sg[1] else "CV", 0, 64))
-                elif j & 1:
+            signs(h, "f%d%d" % (t, h), X("G", *HS[h]))
+            o = X(psum(), 0, 128)
+            acc([(o, ONES, X("CZ", 0, 128))]
+                + [(o, LE("LEc", k), X("cz", 2048 * h + 128 * k, 2048 * h + 128 * k + 128)) for k in range(16)])
+            t0 = X("T0", *HS[h])
+            vtt(t0, o, X("NUM", *HS[h]), A.min)
+            act(t0, t0, AF.Relu, bias=5.0 * PR)
+
+        def tests(h):
+            ca, gx, c0 = psum(), "GX%d" % h, 512 * h
+            for d in range(1, 5):
+                j = 4 - d
+                v0, q0 = 2048 * (4 * h + j), c0 + 128 * j
+                l = [(X(ca, 0, 512), ONES, X("CVO", 0, 512))] if d == 1 else []
+                for c in (0, 1):
+                    tag, lst = "%s%d%d%d" % (" pqrs"[d], t, h, c), X("QL", q0 + 64 * c, q0 + 64 * c + 64)
+                    if WHO[tag] == "V":
+                        vtt(X("cv", v0 + 1024 * c, v0 + 1024 * c + 1024), ind(win, lst), X(gx, 1024 * c, 1024 * c + 1024), A.is_le)
+                        ops[-1]["tag"] = tag
+                        continue
+                    f0 = 1024 * (nfq[0] % 4)
+                    nfq[0] += 1
+                    gather(tag, X("fq", f0, f0 + 1024), ind(win, lst))
                     for i in (0, 1):
-                        sumto(KB[h], 32 * (j - 1 + i), 32, "LEC", "cv%d" % h, 512 * (j - 1 + i),
-                              X("CS" if sg[i] else "CV", 0, 32))
+                        pd, s0 = X(psum(), 0, 512), 1024 * c + 512 * i
+                        acc([(pd, NID, X("fq", f0 + 512 * i, f0 + 512 * i + 512)), (pd, ID, X(gx, s0, s0 + 512))])
+                        act(X("cv", v0 + s0, v0 + s0 + 512), pd, AF.Sign, bias=0.5)
+                    l.append((X(ca, j, 512, 4), X("QM", 64 - 64 * c, 192 - 64 * c), X("SIX", 0, 128)))
+                acc(l + [(X(ca, 4 * k + j, 512, 64), X("cv", v0 + k, v0 + 2048, 16), X("WB", 0, 8)) for k in range(16)],
+                    d == 1, False)
+                ops[-1]["fn"] = ca
+            scan(X("SC", c0, c0 + 512), X(ca, 0, 512), X("CO", c0, c0 + 512), -BIG, A.max, A.min)
 
-        def comb(d, h, bank):
-            hs = (128 * h, 128 * h + 128)
-            acc = X("ACC", *hs)
-            if d == 0:
-                vtt(acc, X(bank, 0, 128), X("CO0", *hs), A.min)
-                act(acc, acc, AF.Relu)
-            else:
-                vtt(X(bank, 128, 256), X(bank, 0, 128), X("CO%d" % d, *hs), A.min)
-                vtt(X("VI", *hs) if d == 4 else acc, X(bank, 128, 256), acc, A.max)
-
-        comb(0, 0, "PCa")
-        comb(0, 1, "PCb")
-
-        def path(h, dst, lst, nm, d0, qs):
-            for ch in (0, 1):
-                s0 = 2048 * h + 1024 * ch
-                gather(qs[2 * h + ch], X(dst, s0, s0 + 1024), ind(pwin, lst(ch)))
-                for d, le in ((0, "LEa"), (1, "LEb")):
-                    sumto("PQ%d" % h, 128 * d + 64 * ch, 64, le, dst, s0)
-            vcopy(X("%s%d" % (nm, h), 0, 256), X("PQ%d" % h, 0, 256))
-            for j in (0, 1):
-                act(X("CO%d" % (d0 + j), 128 * h, 128 * h + 128), X("PQ%d" % h, 128 * j, 128 * j + 128), AF.Identity,
-                    bias=float(PR * (5 - d0 - j)))
-
-        for h in (0, 1):
-            path(h, pn, lambda ch: X("PL", 128 * h + 64 * ch, 128 * h + 64 * ch + 64), "QLa", 1, P1Q[t])
-        for h in (0, 1):
-            path(h, "px", lambda ch: X("QLa%d" % h, 128 + 64 * ch, 192 + 64 * ch), "QLb", 3, P2Q[t])
-
-        ns = [0]
-
-        def test(d, h):
-            nm, o = ("QLa%d" % h, 128 * (d - 1)) if d < 3 else ("QLb%d" % h, 128 * (d - 3))
-            buf = "cv%d" % ((4 * h + d + 1) % 6)
-            bank = (("PCa", "PCb"), ("PG0", "PG1"))[h][d & 1]
-            for j in (0, 2):
-                two_s = [(d, h, j + i) in SUN[t] for i in (0, 1)]
-                if not any(two_s):
-                    vtt(X(buf, 512 * j, 512 * j + 1024), ind(win, X(nm, o + 32 * j, o + 32 * j + 64)),
-                        X("G%d" % h, 0, 1024), A.is_le)
-                for i in (0, 1):
-                    s0, o1 = 512 * (j + i), o + 32 * (j + i)
-                    if two_s[i]:
-                        q = ns[0] % 8
-                        ns[0] += 1
-                        pd = X("PD%d" % (q & 1), 0, 512)
-                        fq = X("fq", 512 * q, 512 * q + 512)
-                        act(fq, ind(win, X(nm, o1, o1 + 32)))
-                        mms([(pd, NID, fq, True, False), (pd, ID, X("G%d" % h, 0, 512), False, True)])
-                        act(X(buf, s0, s0 + 512), pd, AF.Sign, bias=0.5)
-                    elif any(two_s):
-                        vtt(X(buf, s0, s0 + 512), ind(win, X(nm, o1, o1 + 32)), X("G%d" % h, 0, 512), A.is_le)
-                if two_s[0] == two_s[1]:
-                    sumto(bank, 32 * j, 64, "LEC", buf, 512 * j, X("CS" if two_s[0] else "CV", 0, 64))
-                else:
-                    for i in (0, 1):
-                        sumto(bank, 32 * (j + i), 32, "LEC", buf, 512 * (j + i), X("CS" if two_s[i] else "CV", 0, 32))
-            comb(d, h, bank)
-
-        def largest(h):
-            hs = (128 * h, 128 * h + 128)
-            vts(X("LO", *hs), X("VI", *hs), PR - 1, A.bitwise_and)
-            vcopy(X("LOL%d" % h, 0, 128), X("LO", *hs))
-            ll = "LOL%d" % h
-            db = ("PCa", "PCb")
-            ds = [X("DS", 2048 * h + 512 * j, 2048 * h + 512 * j + 512) for j in range(4)]
-            for j in range(4):
-                if j == 3 and DV[t][h] == "V":
-                    vcopy(ds[3], ind(win, X(ll, 96, 128)))
-                else:
-                    act(ds[j], ind(win, X(ll, 32 * j, 32 * j + 32)))
-            for j in range(3):
-                bank = db[(h + j) % 2]
-                jj = j + (DV[t][h] == "S")
-                mms([(X(bank, 0, 512), ID, ds[jj], True, True)])
-                prev, nx = (ds[3] if DV[t][h] == "V" else ds[0]) if j == 0 else X(("DA", "DB")[j - 1], 0, 512), ("DA", "DB", "DC")[j]
-                if j < 2:
-                    vtt(X(nx, 0, 512), X(bank, 0, 512), prev, A.max)
-            vtt(X("DC", 0, 256), X(bank, 0, 256), X("DB", 0, 256), A.max)
-            vtt(X(bank, 256, 512), X(bank, 256, 512), X("DB", 256, 512), A.max)
-            vtt(X("DE", 0, 128), X(bank, 256, 384), X("DC", 0, 128), A.max)
-            vtt(X(bank, 0, 128), X(bank, 384, 512), X("DC", 128, 256), A.max)
-            vtt(X("NEWP", 128 * h, 128 * h + 128), X(bank, 0, 128), X("DE", 0, 128), A.max)
-            nw = X("NEWN", 128 * h, 128 * h + 128)
-            vtt(nw, ind(X("NEWP", 128 * h, 128 * h + 128), X("NL3", 0, 8)), X("MSK%d" % t, h, 256, 2), A.add)
+        def entered(h):
+            hs, o = HS[h], X(psum(), 0, 128)
+            acc([(o, X("OFR", 0, 128), ONES), (o, X("SC", 512 * h + 3, 512 * h + 512, 4), ID32)])
+            vtt(X("VI", *hs), o, X("T0", *hs), A.max)
+            vts(X("QN", *hs), X("VI", *hs), PR - 1, A.bitwise_and)
+            vcopy(X("LOL", *hs), X("QN", *hs))
+            gm, g0 = "GM%d" % ((h + t) & 1), 16 * ((h + t) >> 1)
+            for i in range(4):
+                cs = (2048 * h + 512 * i, 2048 * h + 512 * i + 512)
+                gather("e%d%d%d" % (t, h, i), X("DS", *cs), ind(win, X("LOL", hs[0] + 32 * i, hs[0] + 32 * i + 32)))
+                scan(X("DC", *cs), X("DS", *cs), X(gm, g0, g0 + 512), 0.0, A.max, A.add)
+            new = X("DC", 2048 * h + 15, 2048 * h + 2048, 16)
             if h == 0:
-                vts(X("SEND%d" % t, 0, 128), nw, 255.0, A.min)
-            vts(X("F", 16 + B + h, 16 + B + L, 2), nw, 255.0, A.min)
+                vts(X("SEND%d" % t, 0, 128), new, 256.0, A.add, 255.0, A.min)
+            vts(X("F", 16 + B + h, 16 + B + L, 2), new, 256.0, A.add, 255.0, A.min)
 
-        for d in (1, 2, 3, 4):
-            test(d, 0)
-        largest(0)
+        def rename(h):
+            hs, kk, r0 = HS[h], "KK%d" % h, 256 * h
+            hif, red = X("HIF", *hs), X("RZ", r0, r0 + 128)
+            vts(hif, X("VI", *hs), 1.0 / PR, A.mult, 127.875, A.add)
+            vts(red, hif, 128.0, A.is_equal, float(PR), A.mult)
+            vts(X("RZ", r0 + 128, r0 + 256), hif, 133.0, A.is_equal, float(PR), A.mult)
+
+            def sums(b):
+                return [(X(b, 128, 256), X("NBD", 0, 128), hif), (X(b, 128, 256), X("OS", 0, 128), red),
+                        (X(b, 256, 384), X("OS", 0, 128), red)]
+
+            pm, ca, gt = psum(), psum(), X("GT", *hs)
+            acc([(X(pm, 128, 384), ID, X(kk, 128, 384))] + sums(pm))
+            act(X("WW", r0, r0 + 128), X(pm, 128, 256), AF.Sign, bias=2128 - 255.5)
+            act(X("WW", r0 + 128, r0 + 256), X(pm, 256, 384), AF.Sign, bias=-127.5)
+            acc([(X(ca, 0, 384), ID, X(kk, 0, 384)), (X(ca, 0, 384), ONES, X("CB%d" % t, 0, 384)),
+                 (X(ca, 0, 128), X("DB", 0, 128), gt), (X(ca, 256, 384), X("NDB", 0, 128), gt),
+                 (X(ca, 128, 384), ID, X("RZ", r0, r0 + 256))] + sums(ca), True, False)
+            acc([(X(ca, 128, 384), X("N64", 0, 128), X("WW", r0, r0 + 256)),
+                 (X(ca, 128, 256), X("N64", 0, 128), X("WW", r0, r0 + 128))], False, True)
+            m1 = X("M1", *hs)
+            vtt(m1, X(ca, 0, 128), X("QN", *hs), A.max)
+            vtt(m1, X(ca, 128, 256), m1, A.max)
+            vtt(X("NUM", *hs), X(ca, 256, 384), m1, A.max)
+            if t + 1 < R:
+                vcopy(X("PL", *hs), X("NUM", *hs))
+            else:
+                act(X("YP", h, 256, 2), X("NUM", *hs), AF.Identity, bias=-16.0)
+
+        for h in (0, 1):
+            act(X("PS", h, 256, 2), ind(X("px%d%d" % (t, h), 0, 2048), X("OFF", 8 * h, 8 * h + 8)))
+        grow("PS", 256, 16 + B, NB * t, t)
+        tests(0)
+        entered(0)
         dst = T.cores[(rank + 1 + t % 7) % len(T.cores)]
         src = T.cores[(rank - 1 - t % 7) % len(T.cores)]
         es = topo.engines(core, dst)[:8]
@@ -484,132 +662,46 @@ def rank_program(g, core, T, topo):
                          local_sem=T.sem["lc%d" % t], pid=pid, routing_id=rid, dma_engine_mask=mk)
 
         rec("s", "G", [], [X("SEND%d" % t, 0, 128)], send, 0.3, 2.0, ("lc%d" % t, len(es)))
-        rec("a", "R", [X("F", cc, cc + 128)], [X("SEND%d" % t, 0, 128)], None, 0.3, 2.0, ("ar%d" % t, nsrc))
-        for d in (1, 2, 3, 4):
-            test(d, 1)
+        rec("a", "R", [X("F", cc, cc + 128)], [X("SEND%d" % t, 0, 128)], None, 0.3, ARR[t], ("ar%d" % t, nsrc))
+        rename(0)
+        tests(1)
+        come(t)
+        entered(1)
+        rename(1)
         if t + 1 == R:
-            come(t)
-        largest(1)
-        kr, kc = float(7 * PR + B + 16), float(6 * PR + B + L + 16)
-        for h in (0, 1):
-            hs = (128 * h, 128 * h + 128)
-            hif, red = X("HIF", *hs), X("RED", *hs)
-            pq = ("PQ0", "PG0")[h]
-            vts(X("HI", *hs), X("VI", *hs), 13, A.arith_shift_right)
-            vcopy(hif, X("HI", *hs))
-            act(red, hif, AF.Relu, bias=1.0, scale=-1.0)
-            act(X(pq, 0, 128), hif, AF.Relu, bias=kr, scale=-kr)
-            act(X(pq, 128, 256), hif, AF.Relu, bias=-4.0 * kc, scale=kc)
-            kk = [(128 * h + 8 * k, 128 * h + 8 * k + 8) for k in range(16)]
-            o1, o2 = X(pq, 256, 264), X(pq, 264, 272)
-            mms([(o1, NID, X("HIF", *c), n == 0, False) for n, c in enumerate(kk)]
-                + [(o1, X("SU", 0, 128), X("RED", *c), False, n == 15) for n, c in enumerate(kk)]
-                + [(o2, X("SU", 0, 128), X("RED", *c), n == 0, n == 15) for n, c in enumerate(kk)])
-            e = X("E", *hs)
-            vtt(e, ind(X("MI", 8 * h, 8 * h + 8), X("XL", 0, 8)), X("KEY", *hs), A.is_equal)
-            vtt(X(pq, 384, 512), e, X("KS%d" % t, *hs), A.mult)
-            xa = X("XA", 16 * h, 16 * h + 16)
-            vcopy(xa, X(pq, 256, 272))
-            q0 = 256 * h
-            vtt(X("XY", q0, q0 + 256), ind(xa, X("XL", 0, 16)), X("K12", q0, q0 + 256), A.add)
-            vts(X("XZ", q0, q0 + 128), X("XY", q0, q0 + 128), 255, A.bitwise_and)
-            vts(X("XZ", q0 + 128, q0 + 256), X("XY", q0 + 128, q0 + 256), 127, A.bitwise_and)
-            t1 = X("T1", *hs)
-            vtt(X(pq, 256, 384), X(pq, 0, 128), X("XZ", q0, q0 + 128), A.add)
-            vtt(t1, X(pq, 128, 256), X("XZ", q0 + 128, q0 + 256), A.add)
-            vtt(t1, X(pq, 256, 384), t1, A.max)
-            vtt(X(pq, 384, 512), X(pq, 384, 512), X("VI", *hs), A.max)
-            vtt(X("NI", *hs), X(pq, 384, 512), t1, A.max)
-            vts(X("NUM", *hs), X("NI", *hs), PR - 1, A.bitwise_and)
-            if t + 1 < R:
-                vcopy(X("PL", *hs), X("NUM", *hs))
-                vts(X("CO0", *hs), X("NUM", *hs), float(5 * PR), A.add)
-            else:
-                vts(X("YPR", h, 256, 2), X("NUM", *hs), -16.0, A.add)
-        if t + 1 == R:
-            dma("Y", [], [X("YPR", 0, 256)], [(T.yp[k::16, :], T.YPR[:, 16 * k:16 * k + 16]) for k in range(16)])
-        for h in (0, 1):
-            act(X("PSP", 128 * h, 128 * h + 128), ind(X(pn, 2048 * h, 2048 * h + 2048), X("OFF%d" % h, 0, 8)))
-        act(X("PSN", 0, 256), ind(X("PSP", 0, 256), X("NL", 0, 16)))
-        grow("PSN", 256, 16 + B, NB * t, t, "PG1")
+            dma("Y", [], [X("YP", 0, 256)], [(T.yp[:], T.YP[:])], 2.8)
         y0 = NB * t
-        dma("Y", [], [X("F", 16 + B, 16 + B + L)], [(T.yf[:, y0:y0 + L], T.F[:, 16 + B:16 + B + L])])
         dma("Y", [], [X("F", cc, cc + 128)], [(T.yf[:, y0 + L:y0 + NB], T.F[:, cc:cc + 128])])
-        if t + 1 < R:
-            come(t)
+        dma("Y", [], [X("F", 16 + B, 16 + B + L)], [(T.yf[:, y0:y0 + L], T.F[:, 16 + B:16 + B + L])], 2.6)
+    return ops
 
-    def schedule():
-        n = len(ops)
-        pred = [set() for _ in range(n)]
-        last = {}
-        for i, o in enumerate(ops):
-            for w, regs in ((0, o["r"]), (1, o["w"])):
-                for (b, c0, c1, rows) in regs:
-                    l = last.setdefault(b, [])
-                    ps = b in PSUMS
-                    for (j, w2, d0, d1, r2) in l:
-                        if j != i and ((ps and ops[j]["q"] != o["q"]) or ((w or w2) and d0 < c1 and c0 < d1 and (rows & r2))):
-                            pred[i].add(j)
-                    if w and not ps:
-                        l[:] = [x for x in l if not (x[2] >= c0 and x[3] <= c1 and (x[4] & ~rows) == 0)]
-                    l.append((i, w, c0, c1, rows))
-        succ = [[] for _ in range(n)]
-        for i in range(n):
-            for j in pred[i]:
-                succ[j].append(i)
-        prio = [0.0] * n
-        for i in range(n - 1, -1, -1):
-            prio[i] = ops[i]["cost"] + ops[i]["lat"] + max([prio[k] + WAKE for k in succ[i]] or [0.0])
-        left = [len(p) for p in pred]
-        ready = {}
-        fin = [0.0] * n
-        free = {}
-        est = [0.0] * n
-        for i in range(n):
-            if not left[i]:
-                ready.setdefault(ops[i]["q"], []).append(i)
-        order = []
-        while len(order) < n:
-            best = None
-            for q, l in ready.items():
-                if not l:
-                    continue
-                f = free.get(q, 0.0)
-                t0 = min(max(f, est[i]) for i in l)
-                i = max((x for x in l if max(f, est[x]) <= t0 + 0.03), key=lambda x: prio[x])
-                st = max(f, est[i])
-                if best is None or st < best[0]:
-                    best = (st, i, q)
-            st, i, q = best
-            ready[q].remove(i)
-            order.append(i)
-            free[q] = st + ops[i]["cost"]
-            fin[i] = free[q] + ops[i]["lat"]
-            for k in succ[i]:
-                est[k] = max(est[k], fin[i] + WAKE)
-                left[k] -= 1
-                if not left[k]:
-                    ready.setdefault(ops[k]["q"], []).append(k)
-        return order
 
+def issue(g, T, ops):
     eng = {"V": g.vector, "S": g.scalar, "T": g.tensor, "G": g, "Y": g.sync}
     sname = {"V": "sv", "S": "ss", "T": "st", "G": "sg"}
     cnt = {"V": 0, "S": 0, "T": 0, "G": 0}
     clk = {q: {} for q in "VSTGY"}
     log = {}
     total = {}
-    ndma = [0]
+    ndma = 0
+    todo = {}
+    for o in ops:
+        if o["kind"] == "t" and o["fn"]:
+            todo[o["fn"]] = todo.get(o["fn"], 0) + 1
+
+    def where(x):
+        return x[0] if lease(x) is None else PLAN["bank"][x[0]]
 
     def waits(q, reads, writes):
         need = []
         for w, regs in ((0, reads), (1, writes)):
-            for (b, c0, c1, rows) in regs:
-                ps = b in PSUMS
-                for e in log.get(b, []):
+            for x in regs:
+                ps = lease(x) is not None
+                for e in log.get(where(x), []):
                     if ps and e["q"] != q:
                         need.append(e)
                         continue
-                    if (ps and q == "T") or not (e["w"] or w) or e["c1"] <= c0 or e["c0"] >= c1 or not (e["rows"] & rows):
+                    if (ps and q == "T") or not (e["w"] or w) or not meet(x, e["x"]):
                         continue
                     if e["q"] == q and w and not e["w"]:
                         continue
@@ -635,17 +727,15 @@ def rank_program(g, core, T, topo):
         c[sem] = max(c.get(sem, 0), val)
         total[sem] = max(total.get(sem, 0), val)
         for w, regs in ((0, reads), (1, writes)):
-            for (b, c0, c1, rows) in regs:
-                l = log.setdefault(b, [])
-                if b in PSUMS:
-                    l[:] = [e for e in l if not (e["q"] == q and e["c0"] >= c0 and e["c1"] <= c1 and (w or not e["w"]))]
+            for x in regs:
+                l = log.setdefault(where(x), [])
+                if lease(x) is not None:
+                    l[:] = [e for e in l if not (e["q"] == q and cover(x, e["x"]) and (w or not e["w"]))]
                 elif w:
-                    l[:] = [e for e in l if not (e["c0"] >= c0 and e["c1"] <= c1 and (e["rows"] & ~rows) == 0)]
-                l.append({"q": q, "w": w, "c0": c0, "c1": c1, "rows": rows, "sem": sem, "val": val, "clk": c})
+                    l[:] = [e for e in l if not cover(x, e["x"])]
+                l.append({"q": q, "w": w, "x": x, "sem": sem, "val": val, "clk": c})
 
-    if "order" not in ORDER:
-        ORDER["order"] = schedule()
-    for i in ORDER["order"]:
+    for i in PLAN["order"]:
         o = ops[i]
         q, r, w = o["q"], o["r"], o["w"]
         if o["kind"] == "a":
@@ -657,13 +747,16 @@ def rank_program(g, core, T, topo):
             o["fn"](eng[q]).then_inc(T.sem[sname[q]], 1)
             note(q, r, w, sname[q], cnt[q], clk[q])
         elif o["kind"] == "t":
-            for (x, lh, rh, a, b) in o["data"]:
+            if o["fn"]:
+                todo[o["fn"]] -= 1
+            for n, (x, lh, rh, a, b) in enumerate(o["data"]):
                 cnt["T"] += 1
+                b = b or bool(o["fn"] and not todo[o["fn"]] and n + 1 == len(o["data"]))
                 g.tensor.matmul(x[0], lh[0], rh[0], a, b).then_inc(T.sem.st, 1)
             note("T", r, w, "st", cnt["T"], clk["T"])
         elif o["kind"] == "d":
-            sem = "d%d" % ndma[0]
-            ndma[0] += 1
+            sem = "d%d" % ndma
+            ndma += 1
             for (x, y) in o["data"]:
                 eng[q].dma_start(x, y).then_inc(T.sem[sem], 16)
             note("D", r, w, sem, 16 * len(o["data"]), clk[q])

@@ -7,16 +7,26 @@ NB = L + 128
 FW = 4112
 BIG = 65536.0
 PR = 8192
+HIGH = 129.0 * 64
+GQ = ("VGG", "GGG", "VVG", "GGG")
+TRIAL = 30
+SHIFT = 0.15
+SPOTS = 12
+LEAN = 0.0
+SETTLE = 0.8
 CYC = 0.83e-3
 PEC = 0.42e-3
 GAT = 1.56
 WAKE = 0.2
-LOOK = (0.05, 0.25, 0.5)
+LOOK = (0.05, 0.15)
 ARR = (6.5, 3.0)
-KINDS = [(1.0, 1.0, 0.2, 0.0), (1.25, 1.1, 0.2, 0.3)]
-MOVES = 20000
-HEAT = 0.004
+KINDS = [(1.0, 1.0, 0.2, 0.0), (1.3, 1.2, 0.2, 0.0)]
+MOVES = 13000
+HEAT = 0.003
 REACH = 30
+SEED = 0
+PATIENCE = 0.3
+STRIDE = 24
 PLAN = {}
 CUT = 1664
 LAT = (3.2, 4.3, 5.0, 2.6)
@@ -32,21 +42,21 @@ for _d, _l in [
         ("bfloat16", [("F", FW), ("PT", FW), ("T2", 16 + I0), ("T3", I0),
                       ("f00", 2048), ("f01", 2048), ("f10", 2048), ("f11", 2048),
                       ("px00", 2048), ("px01", 2048), ("px10", 2048), ("px11", 2048),
-                      ("GX0", 2048), ("GX1", 2048), ("G", 256), ("cv", 8 * 2048), ("cz", 3 * 2048),
-                      ("fq", 4096), ("DS", 4096), ("DC", 4096),
-                      ("LEa", 144), ("LEc", 144), ("LEn", 144), ("W1", 8), ("WB", 8), ("WX", 32), ("YSM", 8),
+                      ("GX0", 2048), ("GX1", 2048), ("cv", 8 * 2048), ("cz", 3 * 2048),
+                      ("DS", 4096), ("DC", 4096),
+                      ("LEa", 144), ("LEc", 144), ("W1", 8), ("W16", 8), ("WB", 8), ("WX", 32), ("YSM", 8),
                       ("ID", 128), ("NID", 128), ("N64", 128), ("ONES", 128), ("OS", 128), ("NBD", 128),
-                      ("DB", 128), ("NDB", 128), ("SH", 128), ("D01", 128), ("QM", 224), ("SIX", 128),
+                      ("KC", 128), ("KCON", 128), ("MSK", 128), ("EL", 256), ("SH", 128), ("D01", 128), ("QM", 224), ("SIX", 128),
                       ("RST", 128), ("GM0", 528), ("GM1", 528), ("CVO", 512), ("CVX", 512), ("OFR", 128), ("CC", 8),
                       ("CZ", 128), ("KK0", 384), ("KK1", 384), ("CB0", 384), ("CB1", 384),
                       ("HB", 256), ("LB", 256), ("SHB", 208), ("SLB", 208),
                       ("GE", 384), ("GT", 384), ("HIF", 256), ("RZ", 512),
                       ("WW", 512), ("SEND0", 128), ("SEND1", 128), ("PS", 256), ("PC", 128)]),
-        ("int32", [("PI", 1), ("CI", 144), ("ti", 8), ("KI", 512), ("KJ", 512), ("SELR", 208), ("SELH", 208), ("SELO", 208),
+        ("int32", [("PI", 1), ("CI", 144), ("ti", 8), ("KI", 512), ("KJ", 512), ("SELR", 208), ("MX", 24), ("SELO", 208),
                    ("raw", 256), ("VI", 256), ("QN", 256), ("MA", 80)]),
         ("uint16", [("SL1", 208), ("SL2", 208), ("PL", 256), ("QL", 1024), ("LOL", 256), ("BC", 8), ("OFF", 24)]),
-        ("float32", [("ID32", 128), ("SK", 384), ("MX", 24), ("CO", 1024), ("SC", 1024), ("NUM", 256),
-                     ("T0", 256), ("M1", 256), ("YP", 256), ("YS", 768), ("cols", 64)])]:
+        ("float32", [("ID32", 128), ("SK", 384), ("CO", 1024), ("SC", 1024), ("NUM", 256),
+                     ("T0", 256), ("M1", 256), ("YP", 256), ("YS", 768), ("cols", 64), ("WC", 16)])]:
     for _n, _w in _l:
         SCRATCH[_n] = ("sbuf", [128, _w], _d)
 NBANK = 8
@@ -80,23 +90,35 @@ def schedule(ops):
                 l = last.setdefault(x[0], [])
                 ps = lease(x) is not None
                 for (j, w2, y) in l:
-                    if j != i and ((ps and ops[j]["q"] != o["q"]) or ((w or w2) and meet(x, y))):
+                    p = ops[j]
+                    if o["way"] and p["way"] and o["way"][0] == p["way"][0] and o["way"] != p["way"]:
+                        continue
+                    if j != i and ((ps and p["q"] != o["q"]) or ((w or w2) and meet(x, y))):
                         pred[i].add(j)
-                        own = ops[j]["q"] == o["q"] and (o["q"] == "T" or not w2) and not ops[j]["lat"]
-                        gap[j, i] = max(gap.get((j, i), 0.0), 0.0 if own else ops[j]["lat"] + WAKE)
-                if w and not ps:
+                        own = p["q"] == o["q"] and (o["q"] == "T" or not w2) and not p["lat"] and "g" not in p["kind"] + o["kind"]
+                        gap[j, i] = max(gap.get((j, i), 0.0), 0.0 if own else p["lat"] + WAKE)
+                if w and not ps and not o["way"]:
                     l[:] = [e for e in l if not cover(x, e[2])]
                 l.append((i, w, x))
+    who = {o["tag"]: WHO.get(o["tag"], "S") for o in ops if o["kind"] == "g" or o["way"] and o["tag"] == o["way"][0]}
+    ways = {}
+    for i, o in enumerate(ops):
+        if o["kind"] == "g":
+            o["q"] = who[o["tag"]]
+        ways.setdefault(o["way"], []).append(i)
+    on = [i for i, o in enumerate(ops) if not o["way"] or who[o["way"][0]] == o["way"][1]]
+    flow = [sorted(p) for p in pred]
     need = [set(p) for p in pred]
+    pred = [p & set(on) for p in pred]
     for q, names in SEQ.items():
-        l = [i for name in names.split() for i, o in enumerate(ops) if o["tag"] == name]
+        l = [i for name in names.split() for i in on if ops[i]["tag"] == name]
         for j, i in zip(l, l[1:]):
             gap.setdefault((j, i), 0.0)
             pred[i].add(j)
             if q == "Y":
                 need[i].add(j)
     succ = [set() for _ in range(n)]
-    for i in range(n):
+    for i in on:
         for j in pred[i]:
             succ[j].add(i)
     held = [([lease(x) for x in o["r"] + o["w"] if lease(x) is not None] + [None])[0] for o in ops]
@@ -106,12 +128,12 @@ def schedule(ops):
         est = [0.0] * n
         ready, free, todo, bank, ends = {}, {}, {}, {}, {}
         banks = {k: 0.0 for k in range(NBANK)}
-        for i in range(n):
+        for i in on:
             todo[held[i]] = todo.get(held[i], 0) + 1
             if not left[i]:
                 ready.setdefault(ops[i]["q"], []).append(i)
-        start, fin = [0.0] * n, [0.0] * n
-        for _ in range(n):
+        start, fin, done, redo = [0.0] * n, [0.0] * n, [False] * n, [0] * len(on)
+        for _ in redo:
             pick, tb = None, min(banks.values()) if banks else 1e9
             for q, l in ready.items():
                 if l:
@@ -125,6 +147,35 @@ def schedule(ops):
             if t >= 1e9:
                 return 1e9, start, bank
             o, z = ops[i], held[i]
+            while o["cost"] > 0.3:
+                memo = {}
+
+                def soon(j):
+                    if j not in memo:
+                        memo[j] = max([est[j], t, free.get(ops[j]["q"], 0.0)]
+                                      + [1e9 if k == i else soon(k) + ops[k]["cost"] + gap[k, j] for k in pred[j] if not done[k]])
+                    return memo[j]
+
+                front, seen, wait = [j for l in ready.values() for j in l if j != i], set(), None
+                while front:
+                    j = front.pop()
+                    if j in seen or soon(j) >= t + o["cost"]:
+                        continue
+                    seen.add(j)
+                    front += succ[j]
+                    if ops[j]["q"] == o["q"] and soon(j) > t:
+                        first = max(t + o["cost"] + tail[j], t + tail[i])
+                        later = max(soon(j) + tail[j], soon(j) + ops[j]["cost"] + tail[i])
+                        if later < first - PATIENCE and (wait is None or soon(j) < wait):
+                            wait = soon(j)
+                if wait is None:
+                    break
+                est[i], i = wait + 0.01 + look, None
+                break
+            if i is None:
+                redo.append(0)
+                continue
+            done[i] = True
             ready[o["q"]].remove(i)
             free[o["q"]] = fin[i] = t + o["cost"]
             start[i] = t
@@ -141,10 +192,10 @@ def schedule(ops):
                 left[k] -= 1
                 if not left[k]:
                     ready.setdefault(ops[k]["q"], []).append(k)
-        return max(fin[i] + ops[i]["lat"] for i in range(n)), start, bank
+        return max(fin[i] + ops[i]["lat"] for i in on), start, bank
 
     tail, todo = [0.0] * n, [len(s) for s in succ]
-    stack = [i for i in range(n) if not todo[i]]
+    stack = [i for i in on if not todo[i]]
     while stack:
         i = stack.pop()
         tail[i] = ops[i]["cost"] + max([ops[i]["lat"]] + [tail[k] + gap[i, k] for k in succ[i]])
@@ -154,68 +205,139 @@ def schedule(ops):
                 stack.append(j)
     assert not any(todo), "the lists of long calls contradict the data flow"
     best = min((place(look) for look in LOOK), key=lambda x: x[0])
-    order = sorted(range(n), key=lambda i: (best[1][i], i))
+    order = sorted(on, key=lambda i: (best[1][i], i))
 
     need = [sorted(need[i]) for i in range(n)]
     qs, nl = [o["q"] for o in ops], {}
     for z in held:
         nl[z] = nl.get(z, 0) + 1
-    kinds = []
+    kinds, main = [], [i for i, o in enumerate(ops) if o["q"] == "T" and not o["way"]]
     for f, gf, wk, dl in KINDS:
         cost = [o["cost"] * (f * gf if o["gat"] else f if o["q"] in "VSTG" else 1.0) for o in ops]
         lat = [o["lat"] + dl if o["lat"] else 0.0 for o in ops]
-        kinds.append((cost, lat, [[(j, (lat[j] + wk) if gap[j, i] else 0.0) for j in need[i]] for i in range(n)], wk))
+        pre = [[(j, (lat[j] + wk) if gap[j, i] else 0.0) for j in need[i]] for i in range(n)]
+        rest = [cost[i] + lat[i] for i in range(n)]
+        for i in range(n - 1, -1, -1):
+            for j, d in pre[i]:
+                if j in flow[i] and (not ops[i]["way"] or ops[i]["way"][1] == "V" or ops[i]["way"] == ops[j]["way"]):
+                    rest[j] = max(rest[j], cost[j] + d + rest[i])
+        kinds.append((cost, lat, pre, wk, rest))
 
-    def play(order, kind):
-        cost, lat, pre, wk = kind
-        fin, why, free, prev, bank, todo, ends = [0.0] * n, [None] * n, {}, {}, {}, dict(nl), {}
-        banks, end, at = {k: (0.0, None) for k in range(NBANK)}, 0.0, None
-        for i in order:
+    def play(order, kind, a=0, old=None, limit=1e8, off=()):
+        cost, lat, pre, wk, rest = kind
+        if old:
+            a -= a % STRIDE
+            fin, why, marks = old[1][:], old[2][:], old[5][:a // STRIDE]
+            free, prev, bank, todo, ends, banks, end, at = [x.copy() for x in old[5][a // STRIDE]]
+            end, at = end[0], at[0]
+            for i in off:
+                fin[i] = -1e9
+        else:
+            a = 0
+            fin, why, marks, free, prev, bank, todo, ends = [-1e9] * n, [None] * n, [], {q: 0.0 for q in qs}, {q: None for q in qs}, {}, dict(nl), {}
+            banks, end, at = {k: (0.0, -1) for k in range(NBANK)}, 0.0, None
+        for p in range(a, len(order)):
+            if not p % STRIDE:
+                marks.append((free.copy(), prev.copy(), bank.copy(), todo.copy(), ends.copy(), banks.copy(), [end], [at]))
+            i = order[p]
             q = qs[i]
-            t, y = free.get(q, 0.0), prev.get(q)
+            t, y = free[q], prev[q]
             for j, d in pre[i]:
                 if fin[j] + d > t:
                     t, y = fin[j] + d, j
             z = held[i]
-            if z is not None:
-                if z not in bank:
-                    if not banks:
-                        return 1e9, None, None, None
-                    k = bank[z] = min(banks, key=banks.get)
-                    b = banks.pop(k)
-                    if b[0] > t:
-                        t, y = b
-                todo[z] -= 1
-            free[q] = fin[i] = t + cost[i]
+            if z is not None and z not in bank:
+                if not banks:
+                    return None
+                k = bank[z] = min(banks, key=banks.get)
+                b = banks.pop(k)
+                if b[0] > t:
+                    t, y = b
+            if t + rest[i] > limit:
+                return None
+            free[q] = fin[i] = t = t + cost[i]
             prev[q], why[i] = i, y
             if z is not None:
-                if fin[i] + wk > ends.get(z, (0.0, None))[0]:
-                    ends[z] = (fin[i] + wk, i)
+                if z not in ends or t + wk > ends[z][0]:
+                    ends[z] = (t + wk, i)
+                todo[z] -= 1
                 if not todo[z]:
-                    banks[bank[z]] = ends[z]
-            if fin[i] + lat[i] > end:
-                end, at = fin[i] + lat[i], i
-        return end, why, at, bank
+                    banks[bank[z]] = ends.pop(z)
+            if t + lat[i] > end:
+                end, at = t + lat[i], i
+        return end + LEAN * sum(fin[i] for i in main), fin, why, at, bank, marks
 
-    rng = np.random.default_rng(0)
+    rng = np.random.default_rng(SEED)
     res = [play(order, k) for k in kinds]
     ref = [r[0] for r in res]
     now = top = float(len(kinds))
-    keep = order
-    for it in range(MOVES):
-        end, why, v, bank = res[int(rng.integers(len(kinds)))]
-        arcs = []
-        while why[v] is not None:
-            if qs[why[v]] == qs[v] and why[v] not in need[v]:
-                arcs.append((why[v], v))
-            v = why[v]
-        if not arcs:
+    keep, paths, saved = (order, dict(who), qs[:]), {}, None
+    for it, (r0, r1, r2, r3, r4) in enumerate(rng.random((MOVES, 5)).tolist()):
+        c = int(r0 * len(kinds))
+        room = -HEAT * (1 - it / MOVES) * math.log(1 - r4)
+        if saved and not it % TRIAL:
+            if now > saved[2] + room:
+                order, res, now, paths = saved[0], saved[1], saved[2], {}
+                who.update(saved[3])
+                qs[:] = saved[4]
+            saved = None
+        if c not in paths:
+            why, v, paths[c] = res[c][2], res[c][3], []
+            while why[v] is not None:
+                if qs[why[v]] == qs[v] and why[v] not in need[v]:
+                    paths[c].append((why[v], v))
+                v = why[v]
+        if not paths[c]:
             break
-        u, v = arcs[int(rng.integers(len(arcs)))]
+        u, v = paths[c][int(r1 * len(paths[c]))]
+        if not it % TRIAL and it // TRIAL % 2 and it < MOVES * SETTLE:
+            l = [i for x in paths[c] for i in x if ops[i]["tag"] in who]
+            if l:
+                saved = (order, res, now, dict(who), qs[:])
+                pick = [l[int(r1 * len(l))]]
+                near = [i for i in order if ops[i]["tag"] in who and qs[i] != qs[pick[0]] and abs(res[0][1][i] - res[0][1][pick[0]]) < 8]
+                if r2 < 0.5 and near:
+                    pick.append(near[int(r3 * len(near))])
+                for u in pick:
+                    tag = ops[u]["tag"]
+                    old, who[tag] = ways.get((tag, who[tag]), [u]), "VS"[who[tag] == "V"]
+                    new = ways.get((tag, who[tag]), [u])
+                    first = order.index(old[0])
+                    order = [i for i in order if i not in old]
+                    pre = set(j for i in new for j in need[i])
+                    lo = max(p + 1 for p, i in enumerate(order) if i in pre)
+                    hi = min(p for p, i in enumerate(order) if any(j in new for j in need[i]))
+                    tries = [order[:a] + new + order[a:] for a in range(lo, hi + 1, max(1, (hi - lo) // SPOTS))]
+                    if ops[u]["kind"] == "g":
+                        qs[u] = who[tag]
+                    order = min(tries, key=lambda x: (play(x, kinds[0], lo, res[0] if u == pick[0] and lo <= first else None, 1e8, old) or [1e9])[0])
+                got = [play(order, k) for k in kinds]
+                if None in got:
+                    order, now = saved[0], 1e9
+                else:
+                    res, now = got, sum(r[0] / x for r, x in zip(got, ref))
+                paths = {}
+            continue
+        if now >= 1e9:
+            continue
         a, b = order.index(u), order.index(v)
-        a = max(0, a - int(rng.integers(REACH)) * int(rng.integers(2)))
+        a = max(0, a - max(0, int((2 * r2 - 1) * REACH)))
         mid = order[a:b + 1]
-        if rng.integers(2):
+        if r3 < SHIFT:
+            x = u if r2 < 0.5 else v
+            at = order.index(x)
+            rest = order[:at] + order[at + 1:]
+            a = max([p + 1 for p in range(at) if rest[p] in need[x]] + [0])
+            b = min([p for p in range(at, len(rest)) if x in need[rest[p]]] + [len(rest)])
+            spots = [p for p in range(a, b + 1) if p != at and (p == b or qs[rest[p]] == qs[x])]
+            spots = [spots[k] for k in rng.permutation(len(spots))[:SPOTS].tolist()]
+            if not spots:
+                continue
+            got = [(play(rest[:p] + [x] + rest[p:], kinds[c], min(p, at), res[c], res[c][0] + ref[c] * room) or [1e9])[0] for p in spots]
+            p = spots[got.index(min(got))]
+            a, b = min(p, at), max(p, at)
+            mid = (rest[:p] + [x] + rest[p:])[a:b + 1]
+        elif r3 < 0.5 + SHIFT / 2:
             up = {v}
             for i in mid[::-1]:
                 if i in up:
@@ -232,14 +354,21 @@ def schedule(ops):
                 continue
             mid = [i for i in mid if i not in down] + [i for i in mid if i in down]
         cand = order[:a] + mid + order[b + 1:]
-        r2 = [play(cand, k) for k in kinds]
-        val = sum(r[0] / x for r, x in zip(r2, ref))
-        if val < now + HEAT * (1 - it / MOVES) * float(rng.exponential()):
-            order, res, now = cand, r2, val
-            if val < top:
-                top, keep = val, cand
-    end, why, at, bank = play(keep, kinds[0])
-    PLAN["end"], PLAN["bank"], PLAN["order"] = end, bank, keep
+        new = []
+        for k, r, x in zip(kinds, res, ref):
+            new.append(play(cand, k, a, r, r[0] + x * (room + (0.01 if len(kinds) > 1 else 0.0))))
+            if new[-1] is None:
+                break
+        else:
+            val = sum(r[0] / x for r, x in zip(new, ref))
+            if val <= now + room:
+                order, res, now, paths = cand, new, val, {}
+                if val < top:
+                    top, keep = val, (cand, dict(who), qs[:])
+    qs[:] = keep[2]
+    best = play(keep[0], kinds[0])
+    PLAN["end"], PLAN["bank"], PLAN["order"], PLAN["who"] = best[0], best[4], keep[0], keep[1]
+    PLAN["seq"] = {q: " ".join(dict.fromkeys(ops[i]["tag"] for i in keep[0] if qs[i] == q and ops[i]["tag"])) for q in "YVS"}
 
 
 def rank_program(g, core, T, topo):
@@ -256,6 +385,7 @@ def record(g, core, T, topo, rank, banks):
     AF = ActivationFunctionType
     ops = []
     nlease = [0]
+    at = [""]
 
     def psum():
         nlease[0] += 1
@@ -273,8 +403,15 @@ def record(g, core, T, topo, rank, banks):
     def rec(kind, q, outs, ins, fn, cost, lat=0.0, data=None):
         reads = list(dict.fromkeys(r for x in ins for r in x[1]))
         writes = list(dict.fromkeys(r for x in outs for r in x[1]))
-        ops.append({"kind": kind, "q": q, "r": reads, "w": writes, "fn": fn, "cost": cost, "lat": lat, "data": data,
-                    "tag": None, "gat": any(len(x) > 2 for x in ins)})
+        ops.append({"kind": kind, "q": q, "r": reads, "w": writes, "fn": [fn] if kind == "c" else fn, "cost": cost,
+                    "lat": lat, "data": data, "tag": "%s%s" % (writes[0][0], at[0]) if kind == "c" else None, "way": None, "gat": any(len(x) > 2 for x in ins)})
+
+    def join(n0):
+        run = ops[n0:]
+        del ops[n0 + 1:]
+        for key in ("r", "w", "fn"):
+            run[0][key] = list(dict.fromkeys(x for o in run for x in o[key]))
+        run[0]["cost"] = sum(o["cost"] for o in run)
 
     def width(x):
         n = 1
@@ -325,10 +462,8 @@ def record(g, core, T, topo, rank, banks):
         emit("S", [o], ins, lambda e: e.activation(o[0], i[0], func, bias=b, scale=s), 1.0, isg(i))
 
     def gather(tag, o, i):
-        if WHO[tag] == "V":
-            vcopy(o, i)
-        else:
-            act(o, i)
+        fn = {"V": lambda e: e.tensor_copy(o[0], i[0]), "S": lambda e: e.activation(o[0], i[0], AF.Copy, bias=0.0, scale=1.0)}
+        rec("g", "V", [o], [i], fn, 0.06 + width(o) * GAT * CYC)
         ops[-1]["tag"] = tag
 
     def iota(o, pattern, base, cm, fl=False):
@@ -338,12 +473,19 @@ def record(g, core, T, topo, rank, banks):
         else:
             rec("c", "G", [o], [], lambda e: e.iota(o[0], pattern, base, cm), c)
 
+    def gset(o, c):
+        iota(o, [[0, width(o)]], c, 0, True)
+
+    def gcopy(o, i):
+        n = width(o)
+        rec("c", "G", [o], [i], lambda e: e.affine_select(o[0], i[0], [[0, n]], A.is_ge, 0.0, 0, 0), 0.18 + 2 * n * CYC)
+
     def mms(lst):
-        cost = sum(max(min(64, width(m[1])), width(m[2])) * (4 if wide(m[1]) else 1) for m in lst) * PEC
+        cost = sum(max(min(64, width(m[1])), width(m[2])) * (4 if wide(m[1]) else 1) for m in lst if len(m) == 5) * PEC
         rec("t", "T", [m[0] for m in lst], [x for m in lst for x in (m[1], m[2])], None, cost, 0.0, lst)
 
     def acc(lst, first=True, last=True):
-        mms([m + (first and n == 0, last and n == len(lst) - 1) for n, m in enumerate(lst)])
+        mms([m[:3] + (first and n == 0, last and n == len(lst) - 1) + m[3:] for n, m in enumerate(lst)])
 
     def dma(q, outs, ins, pairs, lat=2.3):
         rec("d", q, outs, ins, None, 0.06 * len(pairs), lat, pairs)
@@ -368,7 +510,7 @@ def record(g, core, T, topo, rank, banks):
     iota(PI, [[0, 1]], 0, 1)
     iota(X("CI", 0, 144), [[1, 144]], 0, 0)
     iota(X("LB", 0, 256), [[0, 4], [1, 64]], 16, 0, True)
-    iota(X("HB", 0, 256), [[1, 4], [0, 64]], 0, 0, True)
+    iota(X("HB", 0, 256), [[1, 4], [0, 64]], 129, 0, True)
     vset(X("PT", 0, FW), 0.0)
     pf, uf, gf, zf, u4 = col(), col(), col(), col(), col()
     vcopy(pf, PI)
@@ -384,31 +526,27 @@ def record(g, core, T, topo, rank, banks):
         dma("Y", [X("PT", 16, 16 + 16 * n, rows=1 << r)], [X(buf, 0, n)], [(T.PT[r::16, 16:16 + 16 * n], T[buf][:, 0:n])], lat)
         ops[-1]["tag"] = "row%d" % r
 
-    def wcol(a):
-        o, t = col(), col()
-        vts(o, uf, float(a), A.is_equal, 64.0, A.mult)
-        vts(t, uf, float(a + 1), A.is_equal)
-        vtt(o, o, t, A.add)
-        return o
-
-    vts(X("SELH", 0, 208), X("SELR", 0, 208), 6, A.arith_shift_right)
+    vts(X("SHB", 0, 208), X("SELR", 0, 208), 1.0 / 64, A.mult, 129 - 31.5 / 64, A.add)
     vts(X("SELO", 0, 208), X("SELR", 0, 208), 63, A.bitwise_and)
-    vcopy(X("SHB", 0, 208), X("SELH", 0, 208))
     vts(X("SLB", 0, 208), X("SELO", 0, 208), 16.0, A.add)
     prow(2, "SHB", 208, LAT[3])
     prow(3, "SLB", 208, LAT[3])
     prow(0, "HB", 256, LAT[3])
     prow(1, "LB", 256, LAT[3])
-    w = [wcol(2 * d) for d in range(5)]
+    vts(X("WC", 0, 5), X("CI", 0, 10, 2), uf, A.is_equal, 64.0, A.mult)
+    vts(X("WC", 5, 10), X("CI", 1, 10, 2), uf, A.is_equal)
+    vtt(X("WC", 10, 15), X("WC", 0, 5), X("WC", 5, 10), A.add)
+    w = [X("WC", 10 + d, 11 + d) for d in range(5)]
     vts(X("LEa", 0, 144), X("CI", 0, 144), zf, A.is_equal, w[1], A.mult)
-    vset(X("T2", 0, 16), 0.0)
-    vset(X("F", 0, 16), 0.0)
+    gset(X("T2", 0, 16), 0)
+    gset(X("F", 0, 16), 0)
 
     def steps(src, lst, dst, d0, qs, moves):
         for j in (0, 1):
             c0, b = 16 + 1664 * j, psum()
             acc([(X(b, 0, 104), LE("LEa", e), X(src, c0 + e, c0 + 1664, 16)) for e in range(16)])
-            vcopy(X(lst, 104 * j, 104 * j + 104), X(b, 0, 104))
+            vts(X(lst, 104 * j, 104 * j + 104), X(b, 0, 104), -HIGH, A.add)
+            ops[-1]["tag"] += str(j)
         for j in (0, 1):
             c0 = d0 + 1664 * j
             gather(qs + str(j), X(dst, c0, c0 + 1664), ind(X(src, 0, 16 + I0), X(lst, 104 * j, 104 * j + 104)))
@@ -424,18 +562,23 @@ def record(g, core, T, topo, rank, banks):
         vts(X("PL", 128 * h, 128 * h + 128), X("raw", h, 256, 2), 16.0, A.add)
     C8 = X("CI", 0, 8)
     vts(X("W1", 0, 8), C8, gf, A.is_equal)
-    vset(X("RST", 0, 128), 0.0)
-    vset(X("RST", 0, 128, 16), -BIG)
     vcopy(X("BC", 0, 8), C8)
     vts(ID, CI, pf, A.is_equal)
     act(NID, ID, scale=-1.0)
     act(ID32, ID)
     vset(ONES, 1.0)
-    vts(X("LEn", 0, 144), X("CI", 0, 144), zf, A.is_equal, -1.0, A.mult)
-    act(X("LEc", 0, 144), X("LEn", 0, 144), scale=-BIG)
-    iota(X("CC", 0, 8), [[2, 8]], 0, 0, True)
-    u16 = col()
-    act(u16, uf, AF.Identity, bias=16.0, scale=16.0)
+    act(X("RST", 0, 128), ONES, scale=0.0)
+    act(X("RST", 0, 128, 16), X("ONES", 0, 8), scale=-BIG)
+    vts(X("LEc", 0, 144), X("CI", 0, 144), zf, A.is_equal, BIG, A.mult)
+    iota(X("CC", 0, 8), [[-2, 8]], 0, 0, True)
+    iota(X("KCON", 0, 128), [[0, 8], [-1, 16]], 15, 0, True)
+    act(X("KC", 0, 128, p=(0, 64), rows=1), X("ONES", 0, 128, p=(0, 64)), scale=4.0)
+    act(X("KC", 0, 128, p=(64, 128), rows=2), X("KCON", 0, 128, p=(64, 128)), scale=1.0 / 64)
+    u15, u16 = col(), col()
+    act(u15, uf, AF.Identity, bias=15.0, scale=-1.0)
+    vts(X("MSK", 0, 128), X("KCON", 0, 128), u15, A.is_equal)
+    act(u16, uf, AF.Identity, bias=15.0, scale=16.0)
+    act(X("W16", 0, 8), X("W1", 0, 8), scale=16.0)
     act(X("WB", 0, 8), X("W1", 0, 8), scale=BIG)
     for d in range(1, 5):
         act(X("WX", 8 * (4 - d), 8 * (5 - d)), X("W1", 0, 8), scale=w[d])
@@ -443,35 +586,28 @@ def record(g, core, T, topo, rank, banks):
     iota(X("CVX", 0, 512), [[0, 4], [512, 128]], -5120, 0, True)
     iota(X("CVO", 0, 512), [[512, 128], [0, 4]], -5120, 0, True)
     iota(X("OFR", 0, 128), [[-512, 128]], 0, 0, True)
-    vset(X("CZ", 0, 128), -(4 * BIG + 5 * PR) / 128)
+    act(X("CZ", 0, 128), ONES, scale=-(4 * BIG + 5 * PR) / 128)
     for h in (0, 1):
         vts(X("NUM", 128 * h, 128 * h + 128), X("raw", h, 256, 2), 16.0, A.add)
     cd = [None]
     for d in range(1, 5):
         cd.append(col())
         act(cd[d], pf, AF.Identity, bias=float(PR * (5 - d)), scale=BIG)
-    vset(X("QM", 0, 192), 0.0)
-    vset(X("QM", 64, 128), 1.0)
-    vset(X("SIX", 0, 128), 6 * BIG / 128)
+    for j in range(3):
+        act(X("QM", 64 * j, 64 * j + 64), X("ONES", 0, 64), scale=float(j & 1))
+    act(X("SIX", 0, 128), ONES, scale=6 * BIG / 128)
     for j in (0, 1):
         ma = X("MA", 8 + 36 * j, 41 + 36 * j)
-        vset(X("GM%d" % j, 0, 528), 0.0)
+        gset(X("GM%d" % j, 0, 528), 0)
         iota(ma, [[2, 33]], 128 + j, -1)
         vts(ma, ma, 15, A.bitwise_and)
         vts(X("GM%d" % j, 15, 528, 16), ma, 0.0, A.is_equal, -256.0, A.add)
     act(X("N64", 0, 128), ID, scale=-64.0)
-    vset(X("OS", 0, 128), 1.0 / PR)
+    act(X("OS", 0, 128), ONES, scale=1.0 / PR)
     vts(X("QN", 0, 128), CI, 4, A.arith_shift_right)
     vts(X("NBD", 0, 128), X("QN", 0, 128), gf, A.is_equal, -1.0, A.mult)
-    p1, l15 = col(), col()
-    vts(l15, uf, 15.0, A.is_lt)
-    vts(p1, pf, 2.0, A.add, l15, A.mult)
-    vts(p1, p1, -1.0, A.add)
-    vts(X("DB", 0, 128), CI, p1, A.is_equal)
-    vtt(X("DB", 0, 128), ID, X("DB", 0, 128), A.subtract)
-    act(X("NDB", 0, 128), X("DB", 0, 128), scale=-float(PR))
-    act(X("DB", 0, 128), X("DB", 0, 128), scale=float(PR))
-    u37 = col()
+    u37, up = col(), col()
+    vts(up, gf, 4.0, A.is_ge)
     act(u37, uf, scale=37.0)
     iota(X("KI", 0, 256), [[5, 2], [10, 128]], 0, 0)
     iota(X("KI", 256, 512), [[1, 2], [2, 128]], 0, 0)
@@ -485,30 +621,33 @@ def record(g, core, T, topo, rank, banks):
         vcopy(X("KK%d" % h, 256, 384), X("KJ", 256 + 128 * h, 384 + 128 * h))
     for t in range(R):
         B = I0 + NB * t
-        vset(X("CB%d" % t, 0, 384, p=(0, 64), rows=1), -64.0)
         for j, c in enumerate((B + 16, B + 2016, B + 208)):
-            vset(X("CB%d" % t, 128 * j, 128 * j + 128, p=(64, 128), rows=2), (c - PR + 4096) / 64.0)
-    l8, p2, l2 = col(), col(), col()
+            cb = col()
+            act(cb, up, AF.Identity, bias=-64.0, scale=(c - PR + 4096) / 64.0 + 64.0)
+            act(X("CB%d" % t, 128 * j, 128 * j + 128), ONES, scale=cb)
+    l8, l2 = col(), col()
     vts(l8, uf, 8.0, A.is_lt)
-    vts(p2, pf, 3.0, A.add, l8, A.mult)
-    vts(p2, p2, -1.0, A.add)
-    vts(X("SH", 0, 128), CI, p2, A.is_equal)
+    act(X("SH", 0, 2), X("ID", 0, 2), scale=0.0)
+    act(X("SH", 2, 128), X("ID", 0, 126), scale=l8)
     vts(l2, uf, 2.0, A.is_lt)
     act(X("D01", 0, 128), ID, scale=l2)
 
-    def choose(b, z):
-        zs = (128 * z, 128 * z + 128)
-        sk = X("SK", *zs)
-        scan(sk, X("RST", 0, 128), X(b, 0, 128), 0.0, A.add, A.max)
+    def choose(z, data):
+        zs, b = (128 * z, 128 * z + 128), psum()
+        acc([(X(b, 0, 128), ONES, X("KC", 0, 128))] + [(X(b, k, 128, 16), data(k), X("W16", 0, 8)) for k in range(16)])
+        scan(X("SK", *zs), X("RST", 0, 128), X(b, 0, 128), 0.0, A.add, A.max)
         mx = X("MX", 8 * z, 8 * z + 8)
         vcopy(mx, X("SK", zs[0] + 15, zs[1], 16))
-        vtt(X("GE", *zs), ind(mx, X("BC", 0, 8)), sk, A.is_equal)
-        b = psum()
-        acc([(X(b, 0, 128), X("GE", *zs), ID)])
-        act(X("GT", *zs), X(b, 0, 128))
+        vts(mx, mx, 15, A.bitwise_and)
+        vtt(X("GE", *zs), ind(mx, X("BC", 0, 8)), X("MSK", 0, 128), A.mult)
         o = X(psum(), 0, 8)
-        acc([(o, ONES, X("CC", 0, 8))] + [(o, LE("LEn", e), X("GT", zs[0] + e, zs[1], 16)) for e in range(16)])
-        vts(X("OFF", 8 * z, 8 * z + 8), o, u16, A.add)
+        acc([(o, ONES, X("CC", 0, 8)), (o, X("GE", *zs), X("W1", 0, 8))])
+        vts(X("OFF", 8 * z, 8 * z + 8), o, -1.0, A.mult, u16, A.add)
+        if z < 2:
+            o = X(psum(), 0, 128)
+            vtt(X("EL", *zs), ind(mx, X("BC", 0, 8)), X("KCON", 0, 128), A.is_equal)
+            acc([(o, X("EL", *zs), ID)])
+            act(X("GT", *zs), o, scale=float(PR))
 
     def signs(z, src, gm):
         for j in range(4):
@@ -518,6 +657,7 @@ def record(g, core, T, topo, rank, banks):
                 l += [(o, NID, X(src, 4 * j + i, 2048, 16), True, False), (o, ID, gm, False, True)]
             mms(l)
             act(X("cz", 2048 * z + 512 * j, 2048 * z + 512 * j + 512), X(pd, 0, 512), AF.Sign, bias=0.5)
+            ops[-1]["tag"] = "z%s%d%d" % (src[1], z, j >> 1)
 
     def grow(src, n, c0, y0, tt):
         if tt + 1 < R:
@@ -526,18 +666,18 @@ def record(g, core, T, topo, rank, banks):
             act(X("PT", c0, c0 + n), o)
         y = X(psum(), 0, n, p=(0, 8))
         acc([(y, X("YSM", 0, 8), X(src, 0, n))])
-        act(X("YS", y0, y0 + n, p=(0, 8)), y, AF.Identity, bias=-16.0)
+        act(X("YS", y0, y0 + n, p=(0, 8)), y, AF.Identity, bias=-16.0 - HIGH)
         dma("Y", [], [X("YS", y0, y0 + n)], [(T.ys[:, y0:y0 + n], T.YS[0:8, y0:y0 + n])])
 
     def come(tt):
-        cc, b = 16 + I0 + NB * tt + L, psum()
+        cc = 16 + I0 + NB * tt + L
+        at[0] = "%d2" % tt
         signs(2, "f%d0" % tt, X("F", cc, cc + 128))
-        mms([(X(b, k, 128, 16), X("cz", 4096 + 128 * k, 4224 + 128 * k), X("W1", 0, 8), True, True) for k in range(16)])
-        choose(b, 2)
-        act(X("PC", 0, 128), ind(X("px%d0" % tt, 0, 2048), X("OFF", 16, 24)))
+        choose(2, lambda k: X("cz", 4096 + 128 * k, 4224 + 128 * k))
+        gather("c%d2" % tt, X("PC", 0, 128), ind(X("px%d0" % tt, 0, 2048), X("OFF", 16, 24)))
         grow("PC", 128, cc, NB * tt + L, tt)
 
-    nfq = [0]
+    G = [X("GX%d" % h, 0, 2048, 16) for h in (0, 1)]
     for t in range(R):
         B = I0 + NB * t
         cc = 16 + B + L
@@ -545,63 +685,70 @@ def record(g, core, T, topo, rank, banks):
         pwin = X("PT", 0, 16 + B)
         HS = [(128 * h, 128 * h + 128) for h in (0, 1)]
         for h in (0, 1):
-            fn, b = "f%d%d" % (t, h), psum()
+            fn, at[0] = "f%d%d" % (t, h), "%d%d" % (t, h)
             for c in (0, 1):
                 gather("f%d%d%d" % (t, h, c), X(fn, 1024 * c, 1024 * c + 1024), ind(win, X("PL", 128 * h + 64 * c, 128 * h + 64 * c + 64)))
-            mms([(X(b, k, 128, 16), X(fn, k, 2048, 16), X("W1", 0, 8), True, True) for k in range(16)])
-            choose(b, h)
-            vcopy(X("G", *HS[h]), ind(X(fn, 0, 2048), X("OFF", 8 * h, 8 * h + 8)))
-            for k in range(16):
-                vcopy(X("GX%d" % h, k, 2048, 16), X("G", *HS[h]))
+            choose(h, lambda k: X(fn, k, 2048, 16))
+            gather("g%d%d" % (t, h), G[h], ind(X(fn, 0, 2048), X("OFF", 8 * h, 8 * h + 8)))
+            for k0 in (1, 6, 11):
+                n0 = len(ops)
+                for k in range(k0, k0 + 5):
+                    (gcopy if GQ[2 * t + h][k0 // 5] == "G" else vcopy)(X("GX%d" % h, k, 2048, 16), G[h])
+                join(n0)
+                ops[-1]["tag"] = "GX" + at[0]
         for h in (0, 1):
-            pn, b, c0 = "px%d%d" % (t, h), psum(), 512 * h
+            pn, b, c0, at[0] = "px%d%d" % (t, h), psum(), 512 * h, "%d%d" % (t, h)
             for c in (0, 1):
                 gather("x%d%d%d" % (t, h, c), X(pn, 1024 * c, 1024 * c + 1024), ind(pwin, X("PL", 128 * h + 64 * c, 128 * h + 64 * c + 64)))
             acc([(X(b, 0, 512), ONES, X("CVX", 0, 512))]
                 + [(X(b, k, 512, 16), X(pn, k, 2048, 16), X("WX", 0, 32)) for k in range(16)])
             for d in range(1, 5):
                 j = 4 - d
-                act(X("CO", c0 + j, c0 + 512, 4), X(b, 128 * j, 128 * j + 128), AF.Identity, bias=10 * BIG + PR * (5 - d))
+                act(X("CO", c0 + j, c0 + 512, 4), X(b, 128 * j, 128 * j + 128), AF.Identity, bias=10 * BIG + PR * (5 - d) - HIGH)
             for d in range(1, 5):
                 j, o = 4 - d, X(psum(), 0, 128)
                 acc([(o, X("CO", c0 + j, c0 + 512, 4), ID32)])
                 vts(X("QL", c0 + 128 * j, c0 + 128 * j + 128), o, cd[d], A.subtract)
+                ops[-1]["tag"] += str(d)
         for h in (0, 1):
-            signs(h, "f%d%d" % (t, h), X("G", *HS[h]))
+            at[0] = "%d%d" % (t, h)
+            signs(h, "f%d%d" % (t, h), G[h])
             o = X(psum(), 0, 128)
             acc([(o, ONES, X("CZ", 0, 128))]
                 + [(o, LE("LEc", k), X("cz", 2048 * h + 128 * k, 2048 * h + 128 * k + 128)) for k in range(16)])
             t0 = X("T0", *HS[h])
             vtt(t0, o, X("NUM", *HS[h]), A.min)
             act(t0, t0, AF.Relu, bias=5.0 * PR)
+            ops[-1]["tag"] = "RL" + at[0]
 
         def tests(h):
-            ca, gx, c0 = psum(), "GX%d" % h, 512 * h
+            ca, gx, c0, at[0] = psum(), "GX%d" % h, 512 * h, "%d%d" % (t, h)
             for d in range(1, 5):
                 j = 4 - d
                 v0, q0 = 2048 * (4 * h + j), c0 + 128 * j
-                l = [(X(ca, 0, 512), ONES, X("CVO", 0, 512))] if d == 1 else []
+                l = []
+                if d == 1:
+                    acc([(X(ca, 0, 512), ONES, X("CVO", 0, 512))], True, False)
+                    ops[-1]["r"] += X("QL", q0, q0 + 128)[1]
                 for c in (0, 1):
                     tag, lst = "%s%d%d%d" % (" pqrs"[d], t, h, c), X("QL", q0 + 64 * c, q0 + 64 * c + 64)
-                    if WHO[tag] == "V":
-                        vtt(X("cv", v0 + 1024 * c, v0 + 1024 * c + 1024), ind(win, lst), X(gx, 1024 * c, 1024 * c + 1024), A.is_le)
-                        ops[-1]["tag"] = tag
-                        continue
-                    f0 = 1024 * (nfq[0] % 4)
-                    nfq[0] += 1
-                    gather(tag, X("fq", f0, f0 + 1024), ind(win, lst))
+                    o, n0 = X("cv", v0 + 1024 * c, v0 + 1024 * c + 1024), len(ops)
+                    vtt(o, ind(win, lst), X(gx, 1024 * c, 1024 * c + 1024), A.is_le)
+                    act(o, ind(win, lst))
                     for i in (0, 1):
                         pd, s0 = X(psum(), 0, 512), 1024 * c + 512 * i
-                        acc([(pd, NID, X("fq", f0 + 512 * i, f0 + 512 * i + 512)), (pd, ID, X(gx, s0, s0 + 512))])
+                        acc([(pd, NID, X("cv", v0 + s0, v0 + s0 + 512)), (pd, ID, X(gx, s0, s0 + 512))])
                         act(X("cv", v0 + s0, v0 + s0 + 512), pd, AF.Sign, bias=0.5)
-                    l.append((X(ca, j, 512, 4), X("QM", 64 - 64 * c, 192 - 64 * c), X("SIX", 0, 128)))
+                    for i, x in enumerate(ops[n0:]):
+                        x["tag"], x["way"] = tag if i < 2 else tag.upper() if x["q"] == "S" else None, (tag, "S" if i else "V")
+                    l.append((X(ca, j, 512, 4), X("QM", 64 - 64 * c, 192 - 64 * c), X("SIX", 0, 128), tag))
                 acc(l + [(X(ca, 4 * k + j, 512, 64), X("cv", v0 + k, v0 + 2048, 16), X("WB", 0, 8)) for k in range(16)],
-                    d == 1, False)
+                    False, False)
                 ops[-1]["fn"] = ca
             scan(X("SC", c0, c0 + 512), X(ca, 0, 512), X("CO", c0, c0 + 512), -BIG, A.max, A.min)
 
         def entered(h):
-            hs, o = HS[h], X(psum(), 0, 128)
+            hs, o, at[0] = HS[h], X(psum(), 0, 128), "%d%d" % (t, h)
             acc([(o, X("OFR", 0, 128), ONES), (o, X("SC", 512 * h + 3, 512 * h + 512, 4), ID32)])
             vtt(X("VI", *hs), o, X("T0", *hs), A.max)
             vts(X("QN", *hs), X("VI", *hs), PR - 1, A.bitwise_and)
@@ -611,6 +758,7 @@ def record(g, core, T, topo, rank, banks):
                 cs = (2048 * h + 512 * i, 2048 * h + 512 * i + 512)
                 gather("e%d%d%d" % (t, h, i), X("DS", *cs), ind(win, X("LOL", hs[0] + 32 * i, hs[0] + 32 * i + 32)))
                 scan(X("DC", *cs), X("DS", *cs), X(gm, g0, g0 + 512), 0.0, A.max, A.add)
+                ops[-1]["tag"] += str(i)
             new = X("DC", 2048 * h + 15, 2048 * h + 2048, 16)
             if h == 0:
                 vts(X("SEND%d" % t, 0, 128), new, 256.0, A.add, 255.0, A.min)
@@ -632,7 +780,7 @@ def record(g, core, T, topo, rank, banks):
             act(X("WW", r0, r0 + 128), X(pm, 128, 256), AF.Sign, bias=2128 - 255.5)
             act(X("WW", r0 + 128, r0 + 256), X(pm, 256, 384), AF.Sign, bias=-127.5)
             acc([(X(ca, 0, 384), ID, X(kk, 0, 384)), (X(ca, 0, 384), ONES, X("CB%d" % t, 0, 384)),
-                 (X(ca, 0, 128), X("DB", 0, 128), gt), (X(ca, 256, 384), X("NDB", 0, 128), gt),
+                 (X(ca, 0, 128), ID, gt), (X(ca, 256, 384), NID, gt),
                  (X(ca, 128, 384), ID, X("RZ", r0, r0 + 256))] + sums(ca), True, False)
             acc([(X(ca, 128, 384), X("N64", 0, 128), X("WW", r0, r0 + 256)),
                  (X(ca, 128, 256), X("N64", 0, 128), X("WW", r0, r0 + 128))], False, True)
@@ -646,7 +794,8 @@ def record(g, core, T, topo, rank, banks):
                 act(X("YP", h, 256, 2), X("NUM", *hs), AF.Identity, bias=-16.0)
 
         for h in (0, 1):
-            act(X("PS", h, 256, 2), ind(X("px%d%d" % (t, h), 0, 2048), X("OFF", 8 * h, 8 * h + 8)))
+            gather("c%d%d" % (t, h), X("PS", h, 256, 2), ind(X("px%d%d" % (t, h), 0, 2048), X("OFF", 8 * h, 8 * h + 8)))
+        at[0] = "%d0" % t
         grow("PS", 256, 16 + B, NB * t, t)
         tests(0)
         entered(0)
@@ -684,6 +833,7 @@ def issue(g, T, ops):
     log = {}
     total = {}
     ndma = 0
+    who = PLAN["who"]
     todo = {}
     for o in ops:
         if o["kind"] == "t" and o["fn"]:
@@ -738,18 +888,26 @@ def issue(g, T, ops):
     for i in PLAN["order"]:
         o = ops[i]
         q, r, w = o["q"], o["r"], o["w"]
+        if o["way"] and who[o["way"][0]] != o["way"][1]:
+            continue
         if o["kind"] == "a":
             note("D", [], w, o["data"][0], o["data"][1], {})
             continue
+        if o["kind"] == "g":
+            q = who[o["tag"]]
         waits(q, r, w)
-        if o["kind"] == "c":
-            cnt[q] += 1
-            o["fn"](eng[q]).then_inc(T.sem[sname[q]], 1)
+        if o["kind"] in "cg":
+            for fn in o["fn"] if o["kind"] == "c" else [o["fn"][q]]:
+                cnt[q] += 1
+                fn(eng[q]).then_inc(T.sem[sname[q]], 1)
             note(q, r, w, sname[q], cnt[q], clk[q])
         elif o["kind"] == "t":
             if o["fn"]:
                 todo[o["fn"]] -= 1
-            for n, (x, lh, rh, a, b) in enumerate(o["data"]):
+            for n, m in enumerate(o["data"]):
+                x, lh, rh, a, b = m[:5]
+                if m[5:] and who[m[5]] != "S":
+                    continue
                 cnt["T"] += 1
                 b = b or bool(o["fn"] and not todo[o["fn"]] and n + 1 == len(o["data"]))
                 g.tensor.matmul(x[0], lh[0], rh[0], a, b).then_inc(T.sem.st, 1)

@@ -8,33 +8,41 @@ FW = 4112
 BIG = 65536.0
 PR = 8192
 HIGH = 129.0 * 64
-GQ = ("VGG", "GGG", "VVG", "GGG")
+GQ = ("VGG", "GGG", "VSV", "GGG")
+PARTS = 4
+PIECES = 4
+TP = 2
 TRIAL = 30
+ROUNDS = (0, 3)
+INIT = None
+NEAR = 8.0
 SHIFT = 0.15
 SPOTS = 12
-LEAN = 0.0
-SETTLE = 0.8
+SETTLE = 0.25
 CYC = 0.83e-3
 PEC = 0.42e-3
 GAT = 1.56
 WAKE = 0.2
 LOOK = (0.05, 0.15)
 ARR = (6.5, 3.0)
-KINDS = [(1.0, 1.0, 0.2, 0.0), (1.3, 1.2, 0.2, 0.0)]
-MOVES = 13000
-HEAT = 0.003
+KINDS = [(1.0, 0.95, 0.17, 0.0), (1.3, 1.25, 0.2, 0.0)]
+MOVES = 14000
+HEAT = 0.002
 REACH = 30
-SEED = 0
+SEED = 8
 PATIENCE = 0.3
 STRIDE = 24
 PLAN = {}
 CUT = 1664
 LAT = (3.2, 4.3, 5.0, 2.6)
 SEQ = {"Y": "sel fr0 row1 row0 row2 row3 par fr1",
-       "V": "a0 f000 b0 x000 p000 p001 q000 q001 r000 p010 p011 q010 q011 r010 r011 e011 e013 "
-            "f100 f111 p100 p101 q100 q101 r100 p110 p111 q110 q111 r110 r111 e111 e113",
-       "S": "a1 f001 b1 f010 f011 x001 s000 s001 r001 x010 x011 e000 e001 e002 e003 s010 s011 e010 e012 "
-            "x100 f101 x101 f110 s100 s101 r101 x110 x111 e100 e101 e102 e103 s110 s111 e110 e112"}
+       "V": "a1 a3 f001 b1 b3 f010 f013 x001 x003 z002 z001 s001 p000 p001 q000 r000 x012 c00 c01 e001 e000 "
+            "q011 q010 p010 r011 r010 z022 z023 e013 e011 f100 f101 x103 f110 f113 g10 z101 q100 q101 s101 p101 p100 r100 "
+            "c11 p111 q110 e102 r111 r110 s110 e113",
+       "S": "a2 f002 f003 a0 f000 b2 b0 f012 f011 g00 x000 x002 z003 z000 x011 s000 g01 q001 r001 Q001 S000 R001 "
+            "x013 x010 z012 e002 e003 z011 z013 z010 p011 s011 P011 s010 S011 S010 z020 z021 e012 c02 e010 "
+            "x102 f103 f102 x100 x101 f111 f112 x110 x111 x113 r101 z100 s100 g11 x112 R101 z103 z102 c10 z111 S100 "
+            "z110 z112 q111 p110 Q111 e101 e100 e103 P110 z113 s111 S111 z120 z122 z121 z123 e111 e110 e112 c12"}
 WHO = {_n: _q for _q, _l in SEQ.items() for _n in _l.split()}
 
 SCRATCH = {}
@@ -44,7 +52,7 @@ for _d, _l in [
                       ("px00", 2048), ("px01", 2048), ("px10", 2048), ("px11", 2048),
                       ("GX0", 2048), ("GX1", 2048), ("cv", 8 * 2048), ("cz", 3 * 2048),
                       ("DS", 4096), ("DC", 4096),
-                      ("LEa", 144), ("LEc", 144), ("W1", 8), ("W16", 8), ("WB", 8), ("WX", 32), ("YSM", 8),
+                      ("LEa", 144), ("LEc", 144), ("LEd", 144), ("KQ", 144), ("W1", 8), ("W8", 8), ("W16", 8), ("WB", 8), ("WX", 32), ("YSM", 8),
                       ("ID", 128), ("NID", 128), ("N64", 128), ("ONES", 128), ("OS", 128), ("NBD", 128),
                       ("KC", 128), ("KCON", 128), ("MSK", 128), ("EL", 256), ("SH", 128), ("D01", 128), ("QM", 224), ("SIX", 128),
                       ("RST", 128), ("GM0", 528), ("GM1", 528), ("CVO", 512), ("CVX", 512), ("OFR", 128), ("CC", 8),
@@ -205,25 +213,29 @@ def schedule(ops):
                 stack.append(j)
     assert not any(todo), "the lists of long calls contradict the data flow"
     best = min((place(look) for look in LOOK), key=lambda x: x[0])
-    order = sorted(on, key=lambda i: (best[1][i], i))
+    order = INIT or sorted(on, key=lambda i: (best[1][i], i))
 
     need = [sorted(need[i]) for i in range(n)]
-    qs, nl = [o["q"] for o in ops], {}
+    qs, nl, short = [o["q"] for o in ops], {}, []
     for z in held:
         nl[z] = nl.get(z, 0) + 1
-    kinds, main = [], [i for i, o in enumerate(ops) if o["q"] == "T" and not o["way"]]
+    kinds, mate = [], [o.get("mate", -1) for o in ops]
+    for i in range(n):
+        far = set(j for k in flow[i] if not ops[k]["way"] and gap[k, i] for j in flow[k])
+        flow[i] = [j for j in flow[i] if j not in far]
+        short.append([j for j in need[i] if j not in far])
     for f, gf, wk, dl in KINDS:
         cost = [o["cost"] * (f * gf if o["gat"] else f if o["q"] in "VSTG" else 1.0) for o in ops]
         lat = [o["lat"] + dl if o["lat"] else 0.0 for o in ops]
-        pre = [[(j, (lat[j] + wk) if gap[j, i] else 0.0) for j in need[i]] for i in range(n)]
+        pre = [[(j, (lat[j] + wk) if gap[j, i] else 0.0) for j in short[i]] for i in range(n)]
         rest = [cost[i] + lat[i] for i in range(n)]
         for i in range(n - 1, -1, -1):
             for j, d in pre[i]:
-                if j in flow[i] and (not ops[i]["way"] or ops[i]["way"][1] == "V" or ops[i]["way"] == ops[j]["way"]):
+                if j in flow[i] and (not ops[i]["way"] or ops[i]["way"] == ops[j]["way"]):
                     rest[j] = max(rest[j], cost[j] + d + rest[i])
         kinds.append((cost, lat, pre, wk, rest))
 
-    def play(order, kind, a=0, old=None, limit=1e8, off=()):
+    def play(order, kind, a=0, old=None, limit=1e8, off=(), upto=n):
         cost, lat, pre, wk, rest = kind
         if old:
             a -= a % STRIDE
@@ -253,9 +265,9 @@ def schedule(ops):
                 b = banks.pop(k)
                 if b[0] > t:
                     t, y = b
-            if t + rest[i] > limit:
+            if t + (rest if p <= upto else old[6])[i] > limit:
                 return None
-            free[q] = fin[i] = t = t + cost[i]
+            free[q] = fin[i] = t = t + cost[i] - (0.055 if prev[q] == mate[i] else 0.0)
             prev[q], why[i] = i, y
             if z is not None:
                 if z not in ends or t + wk > ends[z][0]:
@@ -265,14 +277,33 @@ def schedule(ops):
                     banks[bank[z]] = ends.pop(z)
             if t + lat[i] > end:
                 end, at = t + lat[i], i
-        return end + LEAN * sum(fin[i] for i in main), fin, why, at, bank, marks
+        return [end, fin, why, at, bank, marks, None]
 
-    rng = np.random.default_rng(SEED)
-    res = [play(order, k) for k in kinds]
-    ref = [r[0] for r in res]
-    now = top = float(len(kinds))
-    keep, paths, saved = (order, dict(who), qs[:]), {}, None
-    for it, (r0, r1, r2, r3, r4) in enumerate(rng.random((MOVES, 5)).tolist()):
+    def tails(order, kind):
+        cost, lat, pre, wk, rest = kind
+        tl, nxt = lat[:], {q: 0.0 for q in qs}
+        for i in order[::-1]:
+            q = qs[i]
+            x, y = tl[i], nxt[q]
+            x = nxt[q] = tl[i] = cost[i] + (x if x > y else y)
+            for j, d in pre[i]:
+                if x + d > tl[j]:
+                    tl[j] = x + d
+        return tl
+
+    ref = [90.0 * k[0] * k[1] for k in KINDS]
+    keep = (order, dict(who), qs[:])
+    top = sum(play(order, k)[0] / x for k, x in zip(kinds, ref))
+    for it in range(MOVES * ROUNDS[0], MOVES * ROUNDS[1]):
+        if not it % MOVES:
+            rng = np.random.default_rng([SEED, it // MOVES])
+            draws = rng.random((MOVES, 5)).tolist()
+            order, now, paths, saved = keep[0], top, {}, None
+            who.update(keep[1])
+            qs[:] = keep[2]
+            res = [play(order, k) for k in kinds]
+        it %= MOVES
+        r0, r1, r2, r3, r4 = draws[it]
         c = int(r0 * len(kinds))
         room = -HEAT * (1 - it / MOVES) * math.log(1 - r4)
         if saved and not it % TRIAL:
@@ -289,12 +320,18 @@ def schedule(ops):
                 v = why[v]
         if not paths[c]:
             break
-        u, v = paths[c][int(r1 * len(paths[c]))]
+        if now < 1e9 and res[0][6] is None:
+            for k, r in zip(kinds, res):
+                r[6] = tails(order, k)
+        l = paths[c]
+        if saved:
+            l = [x for x in l if -NEAR < res[c][1][x[1]] - saved[5][c] < 1.5 * NEAR] or l
+        u, v = l[int(r1 * len(l))]
         if not it % TRIAL and it // TRIAL % 2 and it < MOVES * SETTLE:
             l = [i for x in paths[c] for i in x if ops[i]["tag"] in who]
             if l:
-                saved = (order, res, now, dict(who), qs[:])
                 pick = [l[int(r1 * len(l))]]
+                saved = (order, res, now, dict(who), qs[:], [r[1][pick[0]] for r in res])
                 near = [i for i in order if ops[i]["tag"] in who and qs[i] != qs[pick[0]] and abs(res[0][1][i] - res[0][1][pick[0]]) < 8]
                 if r2 < 0.5 and near:
                     pick.append(near[int(r3 * len(near))])
@@ -333,7 +370,7 @@ def schedule(ops):
             spots = [spots[k] for k in rng.permutation(len(spots))[:SPOTS].tolist()]
             if not spots:
                 continue
-            got = [(play(rest[:p] + [x] + rest[p:], kinds[c], min(p, at), res[c], res[c][0] + ref[c] * room) or [1e9])[0] for p in spots]
+            got = [(play(rest[:p] + [x] + rest[p:], kinds[c], min(p, at), res[c], res[c][0] + ref[c] * room, (), max(p, at)) or [1e9])[0] for p in spots]
             p = spots[got.index(min(got))]
             a, b = min(p, at), max(p, at)
             mid = (rest[:p] + [x] + rest[p:])[a:b + 1]
@@ -356,7 +393,7 @@ def schedule(ops):
         cand = order[:a] + mid + order[b + 1:]
         new = []
         for k, r, x in zip(kinds, res, ref):
-            new.append(play(cand, k, a, r, r[0] + x * (room + (0.01 if len(kinds) > 1 else 0.0))))
+            new.append(play(cand, k, a, r, r[0] + x * (room + (0.01 if len(kinds) > 1 else 0.0)), (), b))
             if new[-1] is None:
                 break
         else:
@@ -466,6 +503,11 @@ def record(g, core, T, topo, rank, banks):
         rec("g", "V", [o], [i], fn, 0.06 + width(o) * GAT * CYC)
         ops[-1]["tag"] = tag
 
+    def pair(a, b, wide):
+        wide()
+        fn = ops.pop()["fn"]
+        ops[a]["mate"], ops[b]["mate"], ops[a]["both"], ops[b]["both"] = b, a, fn, fn
+
     def iota(o, pattern, base, cm, fl=False):
         c = 0.14 + 2 * width(o) * CYC
         if fl:
@@ -481,7 +523,8 @@ def record(g, core, T, topo, rank, banks):
         rec("c", "G", [o], [i], lambda e: e.affine_select(o[0], i[0], [[0, n]], A.is_ge, 0.0, 0, 0), 0.18 + 2 * n * CYC)
 
     def mms(lst):
-        cost = sum(max(min(64, width(m[1])), width(m[2])) * (4 if wide(m[1]) else 1) for m in lst if len(m) == 5) * PEC
+        cost = sum(max(min(64, width(m[1])), width(m[2])) * (4 if wide(m[1]) else 1) for m in lst
+                   if len(m) == 5 or m[5][1] == "S" and m[5][0][0] == "z") * PEC
         rec("t", "T", [m[0] for m in lst], [x for m in lst for x in (m[1], m[2])], None, cost, 0.0, lst)
 
     def acc(lst, first=True, last=True):
@@ -542,14 +585,14 @@ def record(g, core, T, topo, rank, banks):
     gset(X("F", 0, 16), 0)
 
     def steps(src, lst, dst, d0, qs, moves):
-        for j in (0, 1):
-            c0, b = 16 + 1664 * j, psum()
-            acc([(X(b, 0, 104), LE("LEa", e), X(src, c0 + e, c0 + 1664, 16)) for e in range(16)])
-            vts(X(lst, 104 * j, 104 * j + 104), X(b, 0, 104), -HIGH, A.add)
-            ops[-1]["tag"] += str(j)
-        for j in (0, 1):
-            c0 = d0 + 1664 * j
-            gather(qs + str(j), X(dst, c0, c0 + 1664), ind(X(src, 0, 16 + I0), X(lst, 104 * j, 104 * j + 104)))
+        n = 208 // PARTS
+        for j in range(PARTS):
+            c0, b = 16 + 16 * n * j, psum()
+            acc([(X(b, 0, n), LE("LEa", e), X(src, c0 + e, c0 + 16 * n, 16)) for e in range(16)])
+            vts(X(lst, n * j, n * j + n), X(b, 0, n), -HIGH, A.add)
+        for j in range(PARTS):
+            c0 = d0 + 16 * n * j
+            gather(qs + str(j), X(dst, c0, c0 + 16 * n), ind(X(src, 0, 16 + I0), X(lst, n * j, n * j + n)))
         for j in (0, 1):
             c0, c1 = d0 + 1664 * j, 16 + 1664 * j
             dma("Y", [X("PT", c1, c1 + 1664, rows=sum(1 << b for a, b in moves))], [X(dst, c0, c0 + 1664)],
@@ -579,6 +622,11 @@ def record(g, core, T, topo, rank, banks):
     vts(X("MSK", 0, 128), X("KCON", 0, 128), u15, A.is_equal)
     act(u16, uf, AF.Identity, bias=15.0, scale=16.0)
     act(X("W16", 0, 8), X("W1", 0, 8), scale=16.0)
+    act(X("W8", 0, 8), X("W1", 0, 8), scale=8.0)
+    act(X("LEd", 0, 144), X("LEc", 0, 144), scale=2.0)
+    iota(X("KQ", 0, 144), [[0, 9], [-1, 16]], 15, 0, True)
+    vts(X("KQ", 0, 144), X("KQ", 0, 144), 12.0, A.is_ge, -float(PR), A.mult)
+    KQ = lambda j: X("KQ", (16 - 4 * j) % 16, (16 - 4 * j) % 16 + 128)
     act(X("WB", 0, 8), X("W1", 0, 8), scale=BIG)
     for d in range(1, 5):
         act(X("WX", 8 * (4 - d), 8 * (5 - d)), X("W1", 0, 8), scale=w[d])
@@ -593,12 +641,12 @@ def record(g, core, T, topo, rank, banks):
     for d in range(1, 5):
         cd.append(col())
         act(cd[d], pf, AF.Identity, bias=float(PR * (5 - d)), scale=BIG)
-    for j in range(3):
-        act(X("QM", 64 * j, 64 * j + 64), X("ONES", 0, 64), scale=float(j & 1))
+    for a, b, c in ((0, 128 - 128 // TP, 0.0), (128 - 128 // TP, 128, 1.0), (128, 256 - 128 // TP, 0.0)):
+        act(X("QM", a, b), X("ONES", 0, b - a), scale=c)
     act(X("SIX", 0, 128), ONES, scale=6 * BIG / 128)
     for j in (0, 1):
         ma = X("MA", 8 + 36 * j, 41 + 36 * j)
-        gset(X("GM%d" % j, 0, 528), 0)
+        vset(X("GM%d" % j, 0, 528), 0.0)
         iota(ma, [[2, 33]], 128 + j, -1)
         vts(ma, ma, 15, A.bitwise_and)
         vts(X("GM%d" % j, 15, 528, 16), ma, 0.0, A.is_equal, -256.0, A.add)
@@ -620,7 +668,7 @@ def record(g, core, T, topo, rank, banks):
         vcopy(X("KK%d" % h, 128, 256), X("KJ", 128 * h, 128 * h + 128))
         vcopy(X("KK%d" % h, 256, 384), X("KJ", 256 + 128 * h, 384 + 128 * h))
     for t in range(R):
-        B = I0 + NB * t
+        B = I0 + NB * t - (16 if t + 1 == R else 0)
         for j, c in enumerate((B + 16, B + 2016, B + 208)):
             cb = col()
             act(cb, up, AF.Identity, bias=-64.0, scale=(c - PR + 4096) / 64.0 + 64.0)
@@ -634,7 +682,7 @@ def record(g, core, T, topo, rank, banks):
 
     def choose(z, data):
         zs, b = (128 * z, 128 * z + 128), psum()
-        acc([(X(b, 0, 128), ONES, X("KC", 0, 128))] + [(X(b, k, 128, 16), data(k), X("W16", 0, 8)) for k in range(16)])
+        acc([(X(b, 0, 128), ONES, X("KC", 0, 128))] + data(b))
         scan(X("SK", *zs), X("RST", 0, 128), X(b, 0, 128), 0.0, A.add, A.max)
         mx = X("MX", 8 * z, 8 * z + 8)
         vcopy(mx, X("SK", zs[0] + 15, zs[1], 16))
@@ -645,9 +693,11 @@ def record(g, core, T, topo, rank, banks):
         vts(X("OFF", 8 * z, 8 * z + 8), o, -1.0, A.mult, u16, A.add)
         if z < 2:
             o = X(psum(), 0, 128)
-            vtt(X("EL", *zs), ind(mx, X("BC", 0, 8)), X("KCON", 0, 128), A.is_equal)
-            acc([(o, X("EL", *zs), ID)])
-            act(X("GT", *zs), o, scale=float(PR))
+            acc([(o, X("GE", *zs), ID)])
+            act(X("EL", *zs), o, scale=-1.0)
+            o = X(psum(), 0, 128)
+            acc([(o, X("NBD", 0, 128), X("EL", *zs))])
+            vts(X("GT", *zs), o, u15, A.is_equal, float(PR), A.mult)
 
     def signs(z, src, gm):
         for j in range(4):
@@ -655,9 +705,16 @@ def record(g, core, T, topo, rank, banks):
             for i in range(4):
                 o = X(pd, 128 * i, 128 * i + 128)
                 l += [(o, NID, X(src, 4 * j + i, 2048, 16), True, False), (o, ID, gm, False, True)]
+            tag, c0, n0 = "z%s%d%d" % (src[1], z, j), 2048 * z + 512 * j, len(ops)
             mms(l)
-            act(X("cz", 2048 * z + 512 * j, 2048 * z + 512 * j + 512), X(pd, 0, 512), AF.Sign, bias=0.5)
-            ops[-1]["tag"] = "z%s%d%d" % (src[1], z, j >> 1)
+            act(X("cz", c0, c0 + 512), X(pd, 0, 512), AF.Sign, bias=0.5)
+            o = X(psum(), 0, 128)
+            acc([(o, ID, gm)])
+            for i in range(4):
+                vtt(X("cz", c0 + 128 * i, c0 + 128 * i + 128), X(src, 4 * j + i, 2048, 16), o, A.is_le)
+            join(n0 + 3)
+            for i, x in enumerate(ops[n0:]):
+                x["tag"], x["way"] = tag if i & 1 else None, (tag, "SSVV"[i])
 
     def grow(src, n, c0, y0, tt):
         if tt + 1 < R:
@@ -673,9 +730,20 @@ def record(g, core, T, topo, rank, banks):
         cc = 16 + I0 + NB * tt + L
         at[0] = "%d2" % tt
         signs(2, "f%d0" % tt, X("F", cc, cc + 128))
-        choose(2, lambda k: X("cz", 4096 + 128 * k, 4224 + 128 * k))
+        tg = ["z%d2%d" % (tt, j) for j in range(4)]
+        choose(2, lambda b: [(X(b, 0, 128), X("OS", 0, 128), KQ(j), (tg[j], "V")) for j in range(4)]
+               + [(X(b, k, 128, 16), X("cz", 4096 + 128 * k, 4224 + 128 * k), X(wt, 0, 8), (tg[k >> 2], q))
+                  for k in range(16) for q, wt in (("S", "W8"), ("V", "W16"))])
         gather("c%d2" % tt, X("PC", 0, 128), ind(X("px%d0" % tt, 0, 2048), X("OFF", 16, 24)))
         grow("PC", 128, cc, NB * tt + L, tt)
+
+    def parents(nm, dst, window):
+        n, p0 = 128 // PIECES, 128 * int(at[0][1])
+        piece = lambda tag, a, b: gather(tag, X(dst, 16 * a, 16 * b), ind(window, X("PL", p0 + a, p0 + b)))
+        for c in range(PIECES):
+            piece(nm + at[0] + str(c), n * c, n * c + n)
+            if c & 1:
+                pair(len(ops) - 2, len(ops) - 1, lambda: piece("", n * c - n, n * c + n))
 
     G = [X("GX%d" % h, 0, 2048, 16) for h in (0, 1)]
     for t in range(R):
@@ -686,20 +754,18 @@ def record(g, core, T, topo, rank, banks):
         HS = [(128 * h, 128 * h + 128) for h in (0, 1)]
         for h in (0, 1):
             fn, at[0] = "f%d%d" % (t, h), "%d%d" % (t, h)
-            for c in (0, 1):
-                gather("f%d%d%d" % (t, h, c), X(fn, 1024 * c, 1024 * c + 1024), ind(win, X("PL", 128 * h + 64 * c, 128 * h + 64 * c + 64)))
-            choose(h, lambda k: X(fn, k, 2048, 16))
+            parents("f", fn, win)
+            choose(h, lambda b: [(X(b, k, 128, 16), X(fn, k, 2048, 16), X("W16", 0, 8)) for k in range(16)])
             gather("g%d%d" % (t, h), G[h], ind(X(fn, 0, 2048), X("OFF", 8 * h, 8 * h + 8)))
             for k0 in (1, 6, 11):
                 n0 = len(ops)
                 for k in range(k0, k0 + 5):
-                    (gcopy if GQ[2 * t + h][k0 // 5] == "G" else vcopy)(X("GX%d" % h, k, 2048, 16), G[h])
+                    {"G": gcopy, "V": vcopy, "S": act}[GQ[2 * t + h][k0 // 5]](X("GX%d" % h, k, 2048, 16), G[h])
                 join(n0)
                 ops[-1]["tag"] = "GX" + at[0]
         for h in (0, 1):
             pn, b, c0, at[0] = "px%d%d" % (t, h), psum(), 512 * h, "%d%d" % (t, h)
-            for c in (0, 1):
-                gather("x%d%d%d" % (t, h, c), X(pn, 1024 * c, 1024 * c + 1024), ind(pwin, X("PL", 128 * h + 64 * c, 128 * h + 64 * c + 64)))
+            parents("x", pn, pwin)
             acc([(X(b, 0, 512), ONES, X("CVX", 0, 512))]
                 + [(X(b, k, 512, 16), X(pn, k, 2048, 16), X("WX", 0, 32)) for k in range(16)])
             for d in range(1, 5):
@@ -714,8 +780,10 @@ def record(g, core, T, topo, rank, banks):
             at[0] = "%d%d" % (t, h)
             signs(h, "f%d%d" % (t, h), G[h])
             o = X(psum(), 0, 128)
-            acc([(o, ONES, X("CZ", 0, 128))]
-                + [(o, LE("LEc", k), X("cz", 2048 * h + 128 * k, 2048 * h + 128 * k + 128)) for k in range(16)])
+            tg = ["z%d%d%d" % (t, h, j) for j in range(4)]
+            acc([(o, ONES, X("CZ", 0, 128))] + [(o, KQ(j), ONES, (tg[j], "V")) for j in range(4)]
+                + [(o, LE(le, k), X("cz", 2048 * h + 128 * k, 2048 * h + 128 * k + 128), (tg[k >> 2], q))
+                   for k in range(16) for q, le in (("S", "LEc"), ("V", "LEd"))])
             t0 = X("T0", *HS[h])
             vtt(t0, o, X("NUM", *HS[h]), A.min)
             act(t0, t0, AF.Relu, bias=5.0 * PR)
@@ -730,18 +798,23 @@ def record(g, core, T, topo, rank, banks):
                 if d == 1:
                     acc([(X(ca, 0, 512), ONES, X("CVO", 0, 512))], True, False)
                     ops[-1]["r"] += X("QL", q0, q0 + 128)[1]
-                for c in (0, 1):
-                    tag, lst = "%s%d%d%d" % (" pqrs"[d], t, h, c), X("QL", q0 + 64 * c, q0 + 64 * c + 64)
-                    o, n0 = X("cv", v0 + 1024 * c, v0 + 1024 * c + 1024), len(ops)
-                    vtt(o, ind(win, lst), X(gx, 1024 * c, 1024 * c + 1024), A.is_le)
-                    act(o, ind(win, lst))
-                    for i in (0, 1):
-                        pd, s0 = X(psum(), 0, 512), 1024 * c + 512 * i
-                        acc([(pd, NID, X("cv", v0 + s0, v0 + s0 + 512)), (pd, ID, X(gx, s0, s0 + 512))])
-                        act(X("cv", v0 + s0, v0 + s0 + 512), pd, AF.Sign, bias=0.5)
+                n = 128 // TP
+                cvs = lambda a, b: X("cv", v0 + 16 * a, v0 + 16 * b)
+                lst = lambda a, b: ind(win, X("QL", q0 + a, q0 + b))
+                for c in range(TP):
+                    tag, a, b, n0 = "%s%d%d%d" % (" pqrs"[d], t, h, c), n * c, n * c + n, len(ops)
+                    vtt(cvs(a, b), lst(a, b), X(gx, 16 * a, 16 * b), A.is_le)
+                    act(cvs(a, b), lst(a, b))
+                    for i in range(a, b, 32):
+                        pd = X(psum(), 0, 512)
+                        acc([(pd, NID, cvs(i, i + 32)), (pd, ID, X(gx, 16 * i, 16 * i + 512))])
+                        act(cvs(i, i + 32), pd, AF.Sign, bias=0.5)
                     for i, x in enumerate(ops[n0:]):
                         x["tag"], x["way"] = tag if i < 2 else tag.upper() if x["q"] == "S" else None, (tag, "S" if i else "V")
-                    l.append((X(ca, j, 512, 4), X("QM", 64 - 64 * c, 192 - 64 * c), X("SIX", 0, 128), tag))
+                    l.append((X(ca, j, 512, 4), X("QM", 128 - b, 256 - b), X("SIX", 0, 128), (tag, "S")))
+                    if c & 1:
+                        n1 = 2 * n0 - len(ops)
+                        pair(n1, n0, lambda: vtt(cvs(a - n, b), lst(a - n, b), X(gx, 16 * (a - n), 16 * b), A.is_le))
                 acc(l + [(X(ca, 4 * k + j, 512, 64), X("cv", v0 + k, v0 + 2048, 16), X("WB", 0, 8)) for k in range(16)],
                     False, False)
                 ops[-1]["fn"] = ca
@@ -784,14 +857,15 @@ def record(g, core, T, topo, rank, banks):
                  (X(ca, 128, 384), ID, X("RZ", r0, r0 + 256))] + sums(ca), True, False)
             acc([(X(ca, 128, 384), X("N64", 0, 128), X("WW", r0, r0 + 256)),
                  (X(ca, 128, 256), X("N64", 0, 128), X("WW", r0, r0 + 128))], False, True)
-            m1 = X("M1", *hs)
-            vtt(m1, X(ca, 0, 128), X("QN", *hs), A.max)
+            m1, q = X("M1", *hs), X("QN", *hs)
+            if t + 1 == R:
+                q = X("NUM", *hs)
+                vts(q, X("QN", *hs), -16.0, A.add)
+            vtt(m1, X(ca, 0, 128), q, A.max)
             vtt(m1, X(ca, 128, 256), m1, A.max)
-            vtt(X("NUM", *hs), X(ca, 256, 384), m1, A.max)
+            vtt(X("NUM", *hs) if t + 1 < R else X("YP", h, 256, 2), X(ca, 256, 384), m1, A.max)
             if t + 1 < R:
                 vcopy(X("PL", *hs), X("NUM", *hs))
-            else:
-                act(X("YP", h, 256, 2), X("NUM", *hs), AF.Identity, bias=-16.0)
 
         for h in (0, 1):
             gather("c%d%d" % (t, h), X("PS", h, 256, 2), ind(X("px%d%d" % (t, h), 0, 2048), X("OFF", 8 * h, 8 * h + 8)))
@@ -818,10 +892,12 @@ def record(g, core, T, topo, rank, banks):
         entered(1)
         rename(1)
         if t + 1 == R:
-            dma("Y", [], [X("YP", 0, 256)], [(T.yp[:], T.YP[:])], 2.8)
+            dma("Y", [], [X("YP", 0, 256)], [(T.yp[:], T.YP[:])], 1.9)
+            ops[-1]["cost"] = 0.7
         y0 = NB * t
         dma("Y", [], [X("F", cc, cc + 128)], [(T.yf[:, y0 + L:y0 + NB], T.F[:, cc:cc + 128])])
-        dma("Y", [], [X("F", 16 + B, 16 + B + L)], [(T.yf[:, y0:y0 + L], T.F[:, 16 + B:16 + B + L])], 2.6)
+        dma("Y", [], [X("F", 16 + B, 16 + B + L)], [(T.yf[:, y0:y0 + L], T.F[:, 16 + B:16 + B + L])], 1.9)
+        ops[-1]["cost"] = 0.4
     return ops
 
 
@@ -885,6 +961,10 @@ def issue(g, T, ops):
                     l[:] = [e for e in l if not cover(x, e["x"])]
                 l.append({"q": q, "w": w, "x": x, "sem": sem, "val": val, "clk": c})
 
+    queue = {i: who[ops[i]["tag"]] if ops[i]["kind"] == "g" else ops[i]["q"] for i in PLAN["order"]}
+    after, nxt = {}, {}
+    for i in PLAN["order"][::-1]:
+        after[i], nxt[queue[i]] = nxt.get(queue[i]), i
     for i in PLAN["order"]:
         o = ops[i]
         q, r, w = o["q"], o["r"], o["w"]
@@ -893,23 +973,26 @@ def issue(g, T, ops):
         if o["kind"] == "a":
             note("D", [], w, o["data"][0], o["data"][1], {})
             continue
-        if o["kind"] == "g":
-            q = who[o["tag"]]
+        q, fns = queue[i], o["fn"]
+        if "mate" in o and after[i] == o["mate"]:
+            continue
+        if "mate" in o and after.get(o["mate"]) == i:
+            fns, r, w = o["both"], r + ops[o["mate"]]["r"], w + ops[o["mate"]]["w"]
         waits(q, r, w)
         if o["kind"] in "cg":
-            for fn in o["fn"] if o["kind"] == "c" else [o["fn"][q]]:
+            for fn in fns if o["kind"] == "c" else [fns[q]]:
                 cnt[q] += 1
                 fn(eng[q]).then_inc(T.sem[sname[q]], 1)
             note(q, r, w, sname[q], cnt[q], clk[q])
         elif o["kind"] == "t":
             if o["fn"]:
                 todo[o["fn"]] -= 1
-            for n, m in enumerate(o["data"]):
+            run = [m for m in o["data"] if len(m) == 5 or who[m[5][0]] == m[5][1]]
+            for n, m in enumerate(run):
                 x, lh, rh, a, b = m[:5]
-                if m[5:] and who[m[5]] != "S":
-                    continue
                 cnt["T"] += 1
-                b = b or bool(o["fn"] and not todo[o["fn"]] and n + 1 == len(o["data"]))
+                if n + 1 == len(run):
+                    b = o["data"][-1][4] or bool(o["fn"] and not todo[o["fn"]])
                 g.tensor.matmul(x[0], lh[0], rh[0], a, b).then_inc(T.sem.st, 1)
             note("T", r, w, "st", cnt["T"], clk["T"])
         elif o["kind"] == "d":

@@ -8,63 +8,59 @@ FW = 4112
 BIG = 65536.0
 PR = 8192
 HIGH = 129.0 * 64
-GQ = ("VGG", "GGG", "VSV", "GGG")
+MID = 768.25 - 1.0 / 2048
+HY = ((0, 0),)
+SPLIT = ((0, 0),)
+DIRECT = ((0, 0, 1), (0, 0, 2), (0, 0, 3), (1, 0, 1), (1, 0, 3))
+ADD = 3.0
+TW = 32
 PARTS = 4
 PIECES = 4
-TP = 2
-TRIAL = 30
-ROUNDS = (0, 3)
-INIT = None
-NEAR = 8.0
-SHIFT = 0.15
-SPOTS = 12
-SETTLE = 0.25
+LAYS = 11000
+LHEAT = 0.002
+LEAN = (1.0, 1.0)
+PULL = 0.5
+AIM = {}
+CRIT = 0.7
+BACK = 0.6
+WIDE = 8.0
+AMP = 1.5
+LOOSE = 0.5
+EPS = 0.25
+SEED = 8
 CYC = 0.83e-3
 PEC = 0.42e-3
 GAT = 1.56
 WAKE = 0.2
-LOOK = (0.05, 0.15)
-ARR = (6.5, 3.0)
+ARR = (4.0, 0.5)
 KINDS = [(1.0, 0.95, 0.17, 0.0), (1.3, 1.25, 0.2, 0.0)]
-MOVES = 14000
-HEAT = 0.002
-REACH = 30
-SEED = 8
-PATIENCE = 0.3
-STRIDE = 24
 PLAN = {}
 CUT = 1664
-LAT = (3.2, 4.3, 5.0, 2.6)
-SEQ = {"Y": "sel fr0 row1 row0 row2 row3 par fr1",
-       "V": "a1 a3 f001 b1 b3 f010 f013 x001 x003 z002 z001 s001 p000 p001 q000 r000 x012 c00 c01 e001 e000 "
-            "q011 q010 p010 r011 r010 z022 z023 e013 e011 f100 f101 x103 f110 f113 g10 z101 q100 q101 s101 p101 p100 r100 "
-            "c11 p111 q110 e102 r111 r110 s110 e113",
-       "S": "a2 f002 f003 a0 f000 b2 b0 f012 f011 g00 x000 x002 z003 z000 x011 s000 g01 q001 r001 Q001 S000 R001 "
-            "x013 x010 z012 e002 e003 z011 z013 z010 p011 s011 P011 s010 S011 S010 z020 z021 e012 c02 e010 "
-            "x102 f103 f102 x100 x101 f111 f112 x110 x111 x113 r101 z100 s100 g11 x112 R101 z103 z102 c10 z111 S100 "
-            "z110 z112 q111 p110 Q111 e101 e100 e103 P110 z113 s111 S111 z120 z122 z121 z123 e111 e110 e112 c12"}
-WHO = {_n: _q for _q, _l in SEQ.items() for _n in _l.split()}
+LAT = (3.2, 4.3, 5.0, 2.6, 2.8)
+LOADS = "sel fr0 fr1 par sr0 sr1 row2 row10 row1 row9 row0 row8 row5 row13 row7 row15"
 
 SCRATCH = {}
 for _d, _l in [
-        ("bfloat16", [("F", FW), ("PT", FW), ("T2", 16 + I0), ("T3", I0),
+        ("bfloat16", [("F", FW), ("PT", FW), ("T2", 16 + I0), ("T3", I0), ("FS", 16 + I0), ("SR", 16 + I0),
                       ("f00", 2048), ("f01", 2048), ("f10", 2048), ("f11", 2048),
-                      ("px00", 2048), ("px01", 2048), ("px10", 2048), ("px11", 2048),
-                      ("GX0", 2048), ("GX1", 2048), ("cv", 8 * 2048), ("cz", 3 * 2048),
-                      ("DS", 4096), ("DC", 4096),
-                      ("LEa", 144), ("LEc", 144), ("LEd", 144), ("KQ", 144), ("W1", 8), ("W8", 8), ("W16", 8), ("WB", 8), ("WX", 32), ("YSM", 8),
-                      ("ID", 128), ("NID", 128), ("N64", 128), ("ONES", 128), ("OS", 128), ("NBD", 128),
-                      ("KC", 128), ("KCON", 128), ("MSK", 128), ("EL", 256), ("SH", 128), ("D01", 128), ("QM", 224), ("SIX", 128),
-                      ("RST", 128), ("GM0", 528), ("GM1", 528), ("CVO", 512), ("CVX", 512), ("OFR", 128), ("CC", 8),
+                      ("px00", 2048), ("px01", 2048), ("px10", 2048), ("px11", 2048), ("py0", 2048), ("py1", 2048),
+                      ("GB", 256), ("cv", 4 * 2048), ("cz", 3 * 2048), ("DS", 4096), ("DC", 4096),
+                      ("SCH", 208), ("SCL", 208), ("HB", 256), ("LB", 256), ("SHB", 208), ("SLB", 208),
+                      ("HH", 256), ("FC", 128), ("PS", 256), ("PC", 128), ("PS2", 384),
+                      ("LEs", 144), ("LE", 144), ("LE1", 144), ("LE2", 144), ("LE3", 144), ("LEc", 144), ("LEd", 144),
+                      ("W1", 8), ("W8", 16), ("W16", 16), ("WB", 8), ("WD", 8), ("WS", 16), ("WX", 32), ("YSM", 8), ("WG", 128),
+                      ("ZERO", 144), ("ONES", 128), ("ID", 128), ("NID", 128), ("N64", 128), ("N8", 128), ("IDK", 128),
+                      ("OS", 128), ("NBD", 128), ("SH", 128), ("SH3", 128), ("D01", 128),
+                      ("SH7", 128), ("KC", 256), ("KCON", 128), ("MSK", 128), ("EL", 256), ("QM", 192), ("SIX", 128), ("CK", 128),
+                      ("RST", 256), ("GM0", 528), ("GM1", 528), ("CVX", 128), ("OFR", 128), ("CC", 8),
                       ("CZ", 128), ("KK0", 384), ("KK1", 384), ("CB0", 384), ("CB1", 384),
-                      ("HB", 256), ("LB", 256), ("SHB", 208), ("SLB", 208),
-                      ("GE", 384), ("GT", 384), ("HIF", 256), ("RZ", 512),
-                      ("WW", 512), ("SEND0", 128), ("SEND1", 128), ("PS", 256), ("PC", 128)]),
-        ("int32", [("PI", 1), ("CI", 144), ("ti", 8), ("KI", 512), ("KJ", 512), ("SELR", 208), ("MX", 24), ("SELO", 208),
+                      ("GE", 384), ("GT", 384), ("HIF", 256), ("RZ", 512), ("WW", 512), ("SEND0", 128), ("SEND1", 128)]),
+        ("int32", [("PI", 1), ("CI", 144), ("ti", 8), ("KI", 512), ("SELR", 208), ("SELO", 208),
                    ("raw", 256), ("VI", 256), ("QN", 256), ("MA", 80)]),
         ("uint16", [("SL1", 208), ("SL2", 208), ("PL", 256), ("QL", 1024), ("LOL", 256), ("BC", 8), ("OFF", 24)]),
-        ("float32", [("ID32", 128), ("SK", 384), ("CO", 1024), ("SC", 1024), ("NUM", 256),
-                     ("T0", 256), ("M1", 256), ("YP", 256), ("YS", 768), ("cols", 64), ("WC", 16)])]:
+        ("float16", [("cd", 4 * 2048)]),
+        ("float32", [("TT", FW), ("GX0", 2048), ("GX1", 2048), ("ID32", 128), ("SK", 768), ("MX", 24), ("CO", 1024), ("SC", 1024),
+                     ("NUM", 256), ("T0", 256), ("M1", 256), ("YP", 256), ("YS", 768), ("cols", 16), ("WC", 8)])]:
     for _n, _w in _l:
         SCRATCH[_n] = ("sbuf", [128, _w], _d)
 NBANK = 8
@@ -72,7 +68,8 @@ for _j in range(NBANK):
     SCRATCH["PB%d" % _j] = ("psum", [128, 512], "float32")
 
 NDMA = 40
-SEMAPHORES = ["sv", "ss", "st", "sg"] + ["d%d" % j for j in range(NDMA)] + ["ar0", "ar1", "lc0", "lc1"]
+SEMAPHORES = (["sv", "ss", "st", "sg"] + ["d%d" % j for j in range(NDMA)]
+              + ["%s%d%d" % (a, t, c) for a in ("ar", "lc") for t in range(R) for c in range(2 if (t, 0) in SPLIT else 1)])
 ALL = 0xFFFF
 
 
@@ -90,8 +87,7 @@ def lease(x):
 
 def schedule(ops):
     n = len(ops)
-    pred = [set() for _ in range(n)]
-    last, gap = {}, {}
+    need, last, gap = [set() for _ in range(n)], {}, {}
     for i, o in enumerate(ops):
         for w, regs in ((0, o["r"]), (1, o["w"])):
             for x in regs:
@@ -99,159 +95,41 @@ def schedule(ops):
                 ps = lease(x) is not None
                 for (j, w2, y) in l:
                     p = ops[j]
-                    if o["way"] and p["way"] and o["way"][0] == p["way"][0] and o["way"] != p["way"]:
-                        continue
-                    if j != i and ((ps and p["q"] != o["q"]) or ((w or w2) and meet(x, y))):
-                        pred[i].add(j)
+                    if j != i and ((ps and (p["q"] != o["q"] or "g" in p["kind"] + o["kind"])) or ((w or w2) and meet(x, y))):
+                        need[i].add(j)
                         own = p["q"] == o["q"] and (o["q"] == "T" or not w2) and not p["lat"] and "g" not in p["kind"] + o["kind"]
                         gap[j, i] = max(gap.get((j, i), 0.0), 0.0 if own else p["lat"] + WAKE)
-                if w and not ps and not o["way"]:
+                if w and not ps:
                     l[:] = [e for e in l if not cover(x, e[2])]
                 l.append((i, w, x))
-    who = {o["tag"]: WHO.get(o["tag"], "S") for o in ops if o["kind"] == "g" or o["way"] and o["tag"] == o["way"][0]}
-    ways = {}
-    for i, o in enumerate(ops):
-        if o["kind"] == "g":
-            o["q"] = who[o["tag"]]
-        ways.setdefault(o["way"], []).append(i)
-    on = [i for i, o in enumerate(ops) if not o["way"] or who[o["way"][0]] == o["way"][1]]
-    flow = [sorted(p) for p in pred]
-    need = [set(p) for p in pred]
-    pred = [p & set(on) for p in pred]
-    for q, names in SEQ.items():
-        l = [i for name in names.split() for i in on if ops[i]["tag"] == name]
-        for j, i in zip(l, l[1:]):
-            gap.setdefault((j, i), 0.0)
-            pred[i].add(j)
-            if q == "Y":
-                need[i].add(j)
-    succ = [set() for _ in range(n)]
-    for i in on:
-        for j in pred[i]:
-            succ[j].add(i)
+    l = [i for name in LOADS.split() for i in range(n) if ops[i]["tag"] == name]
+    for j, i in zip(l, l[1:]):
+        gap.setdefault((j, i), 0.0)
+        need[i].add(j)
     held = [([lease(x) for x in o["r"] + o["w"] if lease(x) is not None] + [None])[0] for o in ops]
-
-    def place(look):
-        left = [len(p) for p in pred]
-        est = [0.0] * n
-        ready, free, todo, bank, ends = {}, {}, {}, {}, {}
-        banks = {k: 0.0 for k in range(NBANK)}
-        for i in on:
-            todo[held[i]] = todo.get(held[i], 0) + 1
-            if not left[i]:
-                ready.setdefault(ops[i]["q"], []).append(i)
-        start, fin, done, redo = [0.0] * n, [0.0] * n, [False] * n, [0] * len(on)
-        for _ in redo:
-            pick, tb = None, min(banks.values()) if banks else 1e9
-            for q, l in ready.items():
-                if l:
-                    f = free.get(q, 0.0)
-                    ts = [max(f, est[i], tb if held[i] is not None and held[i] not in bank else 0.0) for i in l]
-                    t0 = min(ts) + look
-                    k, t, i = min((-tail[i], t, i) for t, i in zip(ts, l) if t <= t0)
-                    if pick is None or t < pick[0]:
-                        pick = (t, i)
-            t, i = pick
-            if t >= 1e9:
-                return 1e9, start, bank
-            o, z = ops[i], held[i]
-            while o["cost"] > 0.3:
-                memo = {}
-
-                def soon(j):
-                    if j not in memo:
-                        memo[j] = max([est[j], t, free.get(ops[j]["q"], 0.0)]
-                                      + [1e9 if k == i else soon(k) + ops[k]["cost"] + gap[k, j] for k in pred[j] if not done[k]])
-                    return memo[j]
-
-                front, seen, wait = [j for l in ready.values() for j in l if j != i], set(), None
-                while front:
-                    j = front.pop()
-                    if j in seen or soon(j) >= t + o["cost"]:
-                        continue
-                    seen.add(j)
-                    front += succ[j]
-                    if ops[j]["q"] == o["q"] and soon(j) > t:
-                        first = max(t + o["cost"] + tail[j], t + tail[i])
-                        later = max(soon(j) + tail[j], soon(j) + ops[j]["cost"] + tail[i])
-                        if later < first - PATIENCE and (wait is None or soon(j) < wait):
-                            wait = soon(j)
-                if wait is None:
-                    break
-                est[i], i = wait + 0.01 + look, None
-                break
-            if i is None:
-                redo.append(0)
-                continue
-            done[i] = True
-            ready[o["q"]].remove(i)
-            free[o["q"]] = fin[i] = t + o["cost"]
-            start[i] = t
-            if z is not None:
-                if z not in bank:
-                    bank[z] = min(banks, key=lambda k: banks[k])
-                    del banks[bank[z]]
-                ends[z] = max(ends.get(z, 0.0), fin[i] + WAKE)
-                todo[z] -= 1
-                if not todo[z]:
-                    banks[bank[z]] = ends[z]
-            for k in succ[i]:
-                est[k] = max(est[k], fin[i] + gap[i, k])
-                left[k] -= 1
-                if not left[k]:
-                    ready.setdefault(ops[k]["q"], []).append(k)
-        return max(fin[i] + ops[i]["lat"] for i in on), start, bank
-
-    tail, todo = [0.0] * n, [len(s) for s in succ]
-    stack = [i for i in on if not todo[i]]
-    while stack:
-        i = stack.pop()
-        tail[i] = ops[i]["cost"] + max([ops[i]["lat"]] + [tail[k] + gap[i, k] for k in succ[i]])
-        for j in pred[i]:
-            todo[j] -= 1
-            if not todo[j]:
-                stack.append(j)
-    assert not any(todo), "the lists of long calls contradict the data flow"
-    best = min((place(look) for look in LOOK), key=lambda x: x[0])
-    order = INIT or sorted(on, key=lambda i: (best[1][i], i))
-
-    need = [sorted(need[i]) for i in range(n)]
-    qs, nl, short = [o["q"] for o in ops], {}, []
+    nl = {}
     for z in held:
         nl[z] = nl.get(z, 0) + 1
-    kinds, mate = [], [o.get("mate", -1) for o in ops]
+    qs, mate = [o["q"] for o in ops], [o.get("mate", -1) for o in ops]
+    short = []
     for i in range(n):
-        far = set(j for k in flow[i] if not ops[k]["way"] and gap[k, i] for j in flow[k])
-        flow[i] = [j for j in flow[i] if j not in far]
-        short.append([j for j in need[i] if j not in far])
+        far = set(j for k in need[i] if gap[k, i] for j in need[k] if gap[j, k] >= gap.get((j, i), 0.0))
+        short.append([j for j in sorted(need[i]) if j not in far])
+    kinds = []
     for f, gf, wk, dl in KINDS:
-        cost = [o["cost"] * (f * gf if o["gat"] else f if o["q"] in "VSTG" else 1.0) for o in ops]
+        costs = [{q: c * (f * gf if o["gat"] else f if q in "VSTG" else 1.0) for q, c in o["cost"].items()} for o in ops]
         lat = [o["lat"] + dl if o["lat"] else 0.0 for o in ops]
-        pre = [[(j, (lat[j] + wk) if gap[j, i] else 0.0) for j in short[i]] for i in range(n)]
-        rest = [cost[i] + lat[i] for i in range(n)]
-        for i in range(n - 1, -1, -1):
+        pre, post = [[(j, (lat[j] + wk) if gap[j, i] else 0.0) for j in short[i]] for i in range(n)], [[] for _ in ops]
+        for i in range(n):
             for j, d in pre[i]:
-                if j in flow[i] and (not ops[i]["way"] or ops[i]["way"] == ops[j]["way"]):
-                    rest[j] = max(rest[j], cost[j] + d + rest[i])
-        kinds.append((cost, lat, pre, wk, rest))
+                post[j].append((i, d))
+        kinds.append((costs, lat, pre, post, wk))
 
-    def play(order, kind, a=0, old=None, limit=1e8, off=(), upto=n):
-        cost, lat, pre, wk, rest = kind
-        if old:
-            a -= a % STRIDE
-            fin, why, marks = old[1][:], old[2][:], old[5][:a // STRIDE]
-            free, prev, bank, todo, ends, banks, end, at = [x.copy() for x in old[5][a // STRIDE]]
-            end, at = end[0], at[0]
-            for i in off:
-                fin[i] = -1e9
-        else:
-            a = 0
-            fin, why, marks, free, prev, bank, todo, ends = [-1e9] * n, [None] * n, [], {q: 0.0 for q in qs}, {q: None for q in qs}, {}, dict(nl), {}
-            banks, end, at = {k: (0.0, -1) for k in range(NBANK)}, 0.0, None
-        for p in range(a, len(order)):
-            if not p % STRIDE:
-                marks.append((free.copy(), prev.copy(), bank.copy(), todo.copy(), ends.copy(), banks.copy(), [end], [at]))
-            i = order[p]
+    def play(order, kind):
+        costs, lat, pre, post, wk = kind
+        fin, why, free, prev = [0.0] * n, [None] * n, dict.fromkeys("VSTGYR", 0.0), dict.fromkeys("VSTGYR")
+        bank, todo, ends, banks, end = {}, dict(nl), {}, {k: (0.0, -1) for k in range(NBANK)}, 0.0
+        for i in order:
             q = qs[i]
             t, y = free[q], prev[q]
             for j, d in pre[i]:
@@ -265,9 +143,7 @@ def schedule(ops):
                 b = banks.pop(k)
                 if b[0] > t:
                     t, y = b
-            if t + (rest if p <= upto else old[6])[i] > limit:
-                return None
-            free[q] = fin[i] = t = t + cost[i] - (0.055 if prev[q] == mate[i] else 0.0)
+            free[q] = fin[i] = t = t + costs[i][q] - (0.055 if prev[q] == mate[i] else 0.0)
             prev[q], why[i] = i, y
             if z is not None:
                 if z not in ends or t + wk > ends[z][0]:
@@ -276,136 +152,142 @@ def schedule(ops):
                 if not todo[z]:
                     banks[bank[z]] = ends.pop(z)
             if t + lat[i] > end:
-                end, at = t + lat[i], i
-        return [end, fin, why, at, bank, marks, None]
+                end = t + lat[i]
+        return end, fin, why, bank
 
-    def tails(order, kind):
-        cost, lat, pre, wk, rest = kind
-        tl, nxt = lat[:], {q: 0.0 for q in qs}
-        for i in order[::-1]:
+    def fit(line, t, c):
+        a, b = line
+        lo, hi = 0, len(b)
+        if not hi or b[-1] <= t:
+            return t, hi
+        while lo < hi:
+            mid = (lo + hi) >> 1
+            if b[mid] <= t:
+                lo = mid + 1
+            else:
+                hi = mid
+        hi = len(b)
+        while lo < hi and a[lo] < t + c - 1e-9:
+            t = b[lo]
+            lo += 1
+        return t, lo
+
+    def lay(order, kind, back, loose, lean):
+        costs, lat, links = kind[0], kind[1], kind[3 if back else 2]
+        lines, fin, start = {q: ([], []) for q in "VSTGYR"}, [0.0] * n, [0.0] * n
+        for i in order:
+            t = lat[i] if back else 0.0
+            for j, d in links[i]:
+                if fin[j] + d > t:
+                    t = fin[j] + d
+            if i in loose:
+                qs[i] = min(costs[i], key=lambda q: fit(lines[q], t, costs[i][q])[0] + costs[i][q] * (1 + lean[0])
+                            + lean[1] * "GSV".index(q))
             q = qs[i]
-            x, y = tl[i], nxt[q]
-            x = nxt[q] = tl[i] = cost[i] + (x if x > y else y)
-            for j, d in pre[i]:
-                if x + d > tl[j]:
-                    tl[j] = x + d
-        return tl
+            c = costs[i][q]
+            s, p = fit(lines[q], t, c)
+            lines[q][0].insert(p, s)
+            lines[q][1].insert(p, s + c)
+            start[i], fin[i] = s, s + c
+        return start, fin
 
     ref = [90.0 * k[0] * k[1] for k in KINDS]
-    keep = (order, dict(who), qs[:])
-    top = sum(play(order, k)[0] / x for k, x in zip(kinds, ref))
-    for it in range(MOVES * ROUNDS[0], MOVES * ROUNDS[1]):
-        if not it % MOVES:
-            rng = np.random.default_rng([SEED, it // MOVES])
-            draws = rng.random((MOVES, 5)).tolist()
-            order, now, paths, saved = keep[0], top, {}, None
-            who.update(keep[1])
-            qs[:] = keep[2]
-            res = [play(order, k) for k in kinds]
-        it %= MOVES
-        r0, r1, r2, r3, r4 = draws[it]
-        c = int(r0 * len(kinds))
-        room = -HEAT * (1 - it / MOVES) * math.log(1 - r4)
-        if saved and not it % TRIAL:
-            if now > saved[2] + room:
-                order, res, now, paths = saved[0], saved[1], saved[2], {}
-                who.update(saved[3])
-                qs[:] = saved[4]
-            saved = None
-        if c not in paths:
-            why, v, paths[c] = res[c][2], res[c][3], []
-            while why[v] is not None:
-                if qs[why[v]] == qs[v] and why[v] not in need[v]:
-                    paths[c].append((why[v], v))
-                v = why[v]
-        if not paths[c]:
-            break
-        if now < 1e9 and res[0][6] is None:
-            for k, r in zip(kinds, res):
-                r[6] = tails(order, k)
-        l = paths[c]
-        if saved:
-            l = [x for x in l if -NEAR < res[c][1][x[1]] - saved[5][c] < 1.5 * NEAR] or l
-        u, v = l[int(r1 * len(l))]
-        if not it % TRIAL and it // TRIAL % 2 and it < MOVES * SETTLE:
-            l = [i for x in paths[c] for i in x if ops[i]["tag"] in who]
-            if l:
-                pick = [l[int(r1 * len(l))]]
-                saved = (order, res, now, dict(who), qs[:], [r[1][pick[0]] for r in res])
-                near = [i for i in order if ops[i]["tag"] in who and qs[i] != qs[pick[0]] and abs(res[0][1][i] - res[0][1][pick[0]]) < 8]
-                if r2 < 0.5 and near:
-                    pick.append(near[int(r3 * len(near))])
-                for u in pick:
-                    tag = ops[u]["tag"]
-                    old, who[tag] = ways.get((tag, who[tag]), [u]), "VS"[who[tag] == "V"]
-                    new = ways.get((tag, who[tag]), [u])
-                    first = order.index(old[0])
-                    order = [i for i in order if i not in old]
-                    pre = set(j for i in new for j in need[i])
-                    lo = max(p + 1 for p, i in enumerate(order) if i in pre)
-                    hi = min(p for p, i in enumerate(order) if any(j in new for j in need[i]))
-                    tries = [order[:a] + new + order[a:] for a in range(lo, hi + 1, max(1, (hi - lo) // SPOTS))]
-                    if ops[u]["kind"] == "g":
-                        qs[u] = who[tag]
-                    order = min(tries, key=lambda x: (play(x, kinds[0], lo, res[0] if u == pick[0] and lo <= first else None, 1e8, old) or [1e9])[0])
-                got = [play(order, k) for k in kinds]
-                if None in got:
-                    order, now = saved[0], 1e9
-                else:
-                    res, now = got, sum(r[0] / x for r, x in zip(got, ref))
-                paths = {}
+
+    def value(order):
+        got = seen_plays[:] = [play(order, k) for k in kinds]
+        return 1e9 if None in got else sum((r[0] + EPS * sum(r[1]) / n) / x for r, x in zip(got, ref))
+
+    rng, seen_plays, chain = np.random.default_rng(SEED), [], []
+    free = [i for i in range(n) if len(ops[i]["cost"]) > 1]
+    pe = [i for i in range(n) if qs[i] == "T"]
+    start = [0.0] * n
+    for i in range(n):
+        start[i] = max([0.0] + [start[j] + kinds[0][0][j][qs[j]] + d for j, d in kinds[0][2][i]])
+    order, now, top, best, last = list(range(n)), 1e9, 1e9, None, [1e9]
+    if AIM:
+        start, aim = [99.0] * n, {}
+        for q, names in AIM.items():
+            t = 0.0
+            for name in names.split():
+                if name[0] == "@":
+                    t = float(name[1:])
+                for i in order:
+                    if ops[i]["tag"] == name:
+                        qs[i], aim[i] = q, t
+                        t += kinds[0][0][i][q]
+        for i in order[::-1]:
+            start[i] = min([aim.get(i, 99.0)] + [start[j] - d - kinds[0][0][i][qs[i]] for j, d in kinds[0][3][i]])
+        start = lay(sorted(order, key=lambda i: (start[i], i)), kinds[0], False, set(free) - set(aim), (0.5, 0.0))[0]
+    for it in range(LAYS):
+        c = 0
+        kind, old = kinds[c], qs[:]
+        r = rng.random(8).tolist()
+        t0, wide, amp = r[0] * 80 - 3, 1 + WIDE * r[1], AMP * r[2] ** 2
+        r[3] *= LOOSE
+        noise, pick = rng.standard_normal(n).tolist(), rng.random(n).tolist()
+        key = [s + amp * x if t0 < s < t0 + wide else s for s, x in zip(start, noise)]
+        loose = set(i for i in free if now > 1e8 and not AIM or t0 < start[i] < t0 + wide and pick[i] < r[3])
+        if r[4] < PULL:
+            v, d = int(r[5] * n), (2 * r[6] - 1) * 3
+            if r[4] < PULL * CRIT and chain:
+                u, v = chain[int(r[5] * len(chain))]
+                d = start[u] - start[v] - 2 * r[2] if d < 0 else start[v] - start[u] + 2 * r[2]
+                v = v if d < 0 else u
+                key = start[:]
+                loose = set(i for i in free if abs(start[i] - start[v]) < 3 and pick[i] < r[3])
+            todo, seen = [v], {v}
+            while todo:
+                i = todo.pop()
+                key[i] += d
+                for j, _ in kind[2 if d < 0 else 3][i]:
+                    if j not in seen and abs(start[j] - start[v]) < wide:
+                        seen.add(j)
+                        todo.append(j)
+        for i in range(n):
+            for j, d in kind[2][i]:
+                if key[j] >= key[i]:
+                    key[i] = key[j] + 1e-6
+        lean = (LEAN[0] * r[7], LEAN[1] * r[5])
+        s, fin = lay(sorted(order, key=lambda i: key[i]), kind, False, loose, lean)
+        if pick[0] < BACK:
+            s, fin = lay(sorted(order, key=lambda i: (-fin[i], -i)), kind, True, loose if it & 1 else (), lean)
+            s, fin = lay(sorted(order, key=lambda i: (-fin[i], i)), kind, False, (), lean)
+        room = -LHEAT * (1 - it / LAYS) * math.log(1 - rng.random())
+        if max(x + y for x, y in zip(fin, kind[1])) > last[0] + 0.6 + room * ref[0]:
+            qs[:] = old
             continue
-        if now >= 1e9:
-            continue
-        a, b = order.index(u), order.index(v)
-        a = max(0, a - max(0, int((2 * r2 - 1) * REACH)))
-        mid = order[a:b + 1]
-        if r3 < SHIFT:
-            x = u if r2 < 0.5 else v
-            at = order.index(x)
-            rest = order[:at] + order[at + 1:]
-            a = max([p + 1 for p in range(at) if rest[p] in need[x]] + [0])
-            b = min([p for p in range(at, len(rest)) if x in need[rest[p]]] + [len(rest)])
-            spots = [p for p in range(a, b + 1) if p != at and (p == b or qs[rest[p]] == qs[x])]
-            spots = [spots[k] for k in rng.permutation(len(spots))[:SPOTS].tolist()]
-            if not spots:
-                continue
-            got = [(play(rest[:p] + [x] + rest[p:], kinds[c], min(p, at), res[c], res[c][0] + ref[c] * room, (), max(p, at)) or [1e9])[0] for p in spots]
-            p = spots[got.index(min(got))]
-            a, b = min(p, at), max(p, at)
-            mid = (rest[:p] + [x] + rest[p:])[a:b + 1]
-        elif r3 < 0.5 + SHIFT / 2:
-            up = {v}
-            for i in mid[::-1]:
-                if i in up:
-                    up.update(need[i])
-            if u in up:
-                continue
-            mid = [i for i in mid if i in up] + [i for i in mid if i not in up]
+        late, line, end = s[:], ([], []), max(fin) + 9
+        for i in sorted(pe, key=lambda i: (-s[i], -i)):
+            t = end - min([end] + [late[j] - d for j, d in kind[3][i]])
+            t, p = fit(line, t, kind[0][i]["T"])
+            line[0].insert(p, t)
+            line[1].insert(p, t + kind[0][i]["T"])
+            late[i] = max(s[i], end - t - kind[0][i]["T"])
+        cand = sorted(order, key=lambda i: (late[i], i))
+        val = value(cand)
+        if val <= now + room:
+            now, start, last = val, s, seen_plays[0] or [1e9]
+            chain = []
+            for end, fin, why, bank in seen_plays if val < 1e8 else ():
+                v = max(order, key=lambda i: fin[i] + kind[1][i])
+                while why[v] is not None and why[v] >= 0:
+                    if qs[why[v]] == qs[v] and why[v] not in need[v]:
+                        chain.append((why[v], v))
+                    v = why[v]
+            if val < top:
+                top, best = val, (cand, qs[:])
         else:
-            down = {u}
-            for i in mid:
-                if any(j in down for j in need[i]):
-                    down.add(i)
-            if v in down:
-                continue
-            mid = [i for i in mid if i not in down] + [i for i in mid if i in down]
-        cand = order[:a] + mid + order[b + 1:]
-        new = []
-        for k, r, x in zip(kinds, res, ref):
-            new.append(play(cand, k, a, r, r[0] + x * (room + (0.01 if len(kinds) > 1 else 0.0)), (), b))
-            if new[-1] is None:
-                break
-        else:
-            val = sum(r[0] / x for r, x in zip(new, ref))
-            if val <= now + room:
-                order, res, now, paths = cand, new, val, {}
-                if val < top:
-                    top, keep = val, (cand, dict(who), qs[:])
-    qs[:] = keep[2]
-    best = play(keep[0], kinds[0])
-    PLAN["end"], PLAN["bank"], PLAN["order"], PLAN["who"] = best[0], best[4], keep[0], keep[1]
-    PLAN["seq"] = {q: " ".join(dict.fromkeys(ops[i]["tag"] for i in keep[0] if qs[i] == q and ops[i]["tag"])) for q in "YVS"}
+            qs[:] = old
+    order, qs[:] = best
+    end, fin, why, bank = play(order, kinds[0])
+    cost = [kinds[0][0][i][qs[i]] for i in range(n)]
+    place = {i: p for p, i in enumerate(order)}
+    PLAN["apart"] = set(j for i in order for j in need[i] if mate[j] >= 0 and mate[j] != i and (
+        place[i] < place[mate[j]] or fin[i] - cost[i] < fin[mate[j]]))
+    PLAN["bank"], PLAN["order"], PLAN["qs"] = bank, order, qs
+    PLAN["who"] = {ops[i]["tag"]: qs[i] for i in free}
+    PLAN["fin"], PLAN["why"], PLAN["cost"], PLAN["ends"] = fin, why, cost, [play(order, k)[0] for k in kinds]
+    PLAN["pre"] = kinds[0][2]
 
 
 def rank_program(g, core, T, topo):
@@ -440,41 +322,34 @@ def record(g, core, T, topo, rank, banks):
     def rec(kind, q, outs, ins, fn, cost, lat=0.0, data=None):
         reads = list(dict.fromkeys(r for x in ins for r in x[1]))
         writes = list(dict.fromkeys(r for x in outs for r in x[1]))
-        ops.append({"kind": kind, "q": q, "r": reads, "w": writes, "fn": [fn] if kind == "c" else fn, "cost": cost,
-                    "lat": lat, "data": data, "tag": "%s%s" % (writes[0][0], at[0]) if kind == "c" else None, "way": None, "gat": any(len(x) > 2 for x in ins)})
+        ops.append({"kind": kind, "q": q, "r": reads, "w": writes, "fn": fn, "cost": {q: cost}, "lat": lat, "data": data,
+                    "tag": "%s%s" % (writes[0][0], at[0]) if kind == "c" else None, "gat": any(len(x) > 2 for x in ins)})
 
-    def join(n0):
-        run = ops[n0:]
-        del ops[n0 + 1:]
-        for key in ("r", "w", "fn"):
-            run[0][key] = list(dict.fromkeys(x for o in run for x in o[key]))
-        run[0]["cost"] = sum(o["cost"] for o in run)
+    def either(tag, k):
+        run = ops[-k:]
+        del ops[len(ops) - k + 1:]
+        run[0].update(kind="g", tag=tag or run[0]["tag"], r=list(dict.fromkeys(x for o in run for x in o["r"])), fn={o["q"]: o["fn"] for o in run},
+                      cost={o["q"]: o["cost"][o["q"]] for o in run})
 
     def width(x):
-        n = 1
-        for d in x[0].shape[1:]:
-            n *= d
-        return n
+        return x[0].shape[1]
 
-    def emit(q, outs, ins, fn, cyc=1.0, gat=False):
+    def emit(q, outs, ins, fn, cyc=1.0):
         n = width(outs[0])
-        rec("c", q, outs, ins, fn, 0.06 + n * GAT * CYC if gat else 0.01 + max(64, cyc * n) * CYC)
-
-    def isg(*xs):
-        return any(len(x) > 2 for x in xs)
+        rec("c", q, outs, ins, fn, 0.06 + n * GAT * CYC if len(ins[0] if ins else ()) > 2 else 0.01 + max(64, cyc * n) * CYC)
 
     def wide(x):
-        return lease(x[1][0]) is not None or SCRATCH[x[1][0][0]][2] not in ("bfloat16", "uint16")
+        return lease(x[1][0]) is not None or SCRATCH[x[1][0][0]][2] not in ("bfloat16", "uint16", "float16")
 
     def two(*xs):
         return not any(wide(x) for x in xs)
 
     def vcopy(o, i):
-        emit("V", [o], [i], lambda e: e.tensor_copy(o[0], i[0]), 0.5 if two(o, i) else 1.0, isg(i))
+        emit("V", [o], [i], lambda e: e.tensor_copy(o[0], i[0]), 0.5 if two(o, i) else 1.0)
 
     def vtt(o, a, b, op):
         cyc = 2.0 if lease(a[1][0]) is None and lease(b[1][0]) is None else 1.0
-        emit("V", [o], [a, b], lambda e: e.tensor_tensor(o[0], a[0], b[0], op), cyc, isg(a))
+        emit("V", [o], [a, b], lambda e: e.tensor_tensor(o[0], a[0], b[0], op), cyc)
 
     def vts(o, i, s1, op0, s2=None, op1=None):
         ins = [i] + [s for s in (s1, s2) if isinstance(s, tuple)]
@@ -496,12 +371,18 @@ def record(g, core, T, topo, rank, banks):
         ins = [i] + [x for x in (bias, scale) if isinstance(x, tuple)]
         b = bias[0] if isinstance(bias, tuple) else bias
         s = scale[0] if isinstance(scale, tuple) else scale
-        emit("S", [o], ins, lambda e: e.activation(o[0], i[0], func, bias=b, scale=s), 1.0, isg(i))
+        emit("S", [o], ins, lambda e: e.activation(o[0], i[0], func, bias=b, scale=s))
+
+    def move(o, i, bias=0.0, scale=1.0, tag=None):
+        if bias or scale != 1.0:
+            vts(o, i, scale, A.mult, bias, A.add)
+        else:
+            vcopy(o, i)
+        act(o, i, AF.Identity if bias else AF.Copy, bias, scale)
+        either(tag, 2)
 
     def gather(tag, o, i):
-        fn = {"V": lambda e: e.tensor_copy(o[0], i[0]), "S": lambda e: e.activation(o[0], i[0], AF.Copy, bias=0.0, scale=1.0)}
-        rec("g", "V", [o], [i], fn, 0.06 + width(o) * GAT * CYC)
-        ops[-1]["tag"] = tag
+        move(o, i, tag=tag)
 
     def pair(a, b, wide):
         wide()
@@ -518,27 +399,28 @@ def record(g, core, T, topo, rank, banks):
     def gset(o, c):
         iota(o, [[0, width(o)]], c, 0, True)
 
+    def gsel(o, i, pattern, op, fill, base, cm):
+        rec("c", "G", [o], [i], lambda e: e.affine_select(o[0], i[0], pattern, op, fill, base, cm), 0.18 + 2 * width(o) * CYC)
+
     def gcopy(o, i):
-        n = width(o)
-        rec("c", "G", [o], [i], lambda e: e.affine_select(o[0], i[0], [[0, n]], A.is_ge, 0.0, 0, 0), 0.18 + 2 * n * CYC)
+        gsel(o, i, [[0, width(o)]], A.is_ge, 0.0, 0, 0)
 
     def mms(lst):
         cost = sum(max(min(64, width(m[1])), width(m[2])) * (4 if wide(m[1]) else 1) for m in lst
-                   if len(m) == 5 or m[5][1] == "S" and m[5][0][0] == "z") * PEC
+                   if len(m) == 5 or m[5][1] == "S") * PEC
         rec("t", "T", [m[0] for m in lst], [x for m in lst for x in (m[1], m[2])], None, cost, 0.0, lst)
 
     def acc(lst, first=True, last=True):
         mms([m[:3] + (first and n == 0, last and n == len(lst) - 1) + m[3:] for n, m in enumerate(lst)])
 
-    def dma(q, outs, ins, pairs, lat=2.3):
+    def dma(q, outs, ins, pairs, lat=2.3, tag=None):
         rec("d", q, outs, ins, None, 0.06 * len(pairs), lat, pairs)
+        ops[-1]["tag"] = tag
 
-    dma("Y", [X("SELR", 0, 208)], [], [(T.SELR[:], T.sel0[:])], 2.5)
-    dma("Y", [X("raw", 0, 256)], [], [(T.raw[:], T.par[:])], LAT[0])
-    dma("Y", [X("F", 16, 16 + CUT)], [], [(T.F[:, 16:16 + CUT], T.front[:, 0:CUT])], LAT[1])
-    dma("Y", [X("F", 16 + CUT, 16 + I0)], [], [(T.F[:, 16 + CUT:16 + I0], T.front[:, CUT:I0])], LAT[2])
-    for j, name in enumerate(("sel", "par", "fr0", "fr1")):
-        ops[j]["tag"] = name
+    dma("Y", [X("SELR", 0, 208)], [], [(T.SELR[:], T.sel0[:])], 2.5, "sel")
+    dma("Y", [X("F", 16, 16 + CUT)], [], [(T.F[:, 16:16 + CUT], T.front[:, 0:CUT])], LAT[1], "fr0")
+    dma("Y", [X("F", 16 + CUT, 16 + I0)], [], [(T.F[:, 16 + CUT:16 + I0], T.front[:, CUT:I0])], LAT[2], "fr1")
+    dma("Y", [X("raw", 0, 256)], [], [(T.raw[:], T.par[:])], LAT[0], "par")
 
     ncol = [0]
 
@@ -548,145 +430,189 @@ def record(g, core, T, topo, rank, banks):
 
     PI, CI = X("PI", 0, 1), X("CI", 0, 128)
     ID, NID, ONES, ID32 = X("ID", 0, 128), X("NID", 0, 128), X("ONES", 0, 128), X("ID32", 0, 128)
-    LE = lambda nm, e: X(nm, 15 - e, 143 - e)
+    LE = lambda nm, e, p=None: X(nm, 15 - e, 143 - e, p=p)
     ti = [X("ti", j, j + 1) for j in range(8)]
     iota(PI, [[0, 1]], 0, 1)
     iota(X("CI", 0, 144), [[1, 144]], 0, 0)
     iota(X("LB", 0, 256), [[0, 4], [1, 64]], 16, 0, True)
     iota(X("HB", 0, 256), [[1, 4], [0, 64]], 129, 0, True)
     vset(X("PT", 0, FW), 0.0)
-    pf, uf, gf, zf, u4 = col(), col(), col(), col(), col()
-    vcopy(pf, PI)
+    uf, gf, zf, u4, u3, zs = col(), col(), col(), col(), col(), col()
     vts(ti[0], PI, 15, A.bitwise_and)
     vts(ti[1], PI, 4, A.arith_shift_right)
+    vts(ti[2], PI, 7, A.bitwise_and)
     vcopy(uf, ti[0])
     vcopy(gf, ti[1])
-    act(zf, gf, AF.Identity, bias=15.0, scale=16.0)
-    act(u4, uf, scale=4.0)
-    act(X("HB", 0, 256), X("HB", 0, 256), AF.Identity, bias=u4)
+    vts(zf, ti[1], 16.0, A.mult, 15.0, A.add)
+    vts(zs, ti[2], 16.0, A.mult, 15.0, A.add)
+    act(u4, uf, scale=256.0)
+    act(X("HB", 0, 256), X("HB", 0, 256), AF.Identity, bias=u4, scale=64.0)
+    Z = lambda n: X("ZERO", 0, n)
+    vset(Z(144), 0.0)
 
-    def prow(r, buf, n, lat):
-        dma("Y", [X("PT", 16, 16 + 16 * n, rows=1 << r)], [X(buf, 0, n)], [(T.PT[r::16, 16:16 + 16 * n], T[buf][:, 0:n])], lat)
-        ops[-1]["tag"] = "row%d" % r
+    def line(o, c, pattern, base, i=None):
+        gsel(o, i or Z(width(o)), pattern, A.not_equal, c, base, 1)
 
-    vts(X("SHB", 0, 208), X("SELR", 0, 208), 1.0 / 64, A.mult, 129 - 31.5 / 64, A.add)
+    def block(o, c, pattern):
+        gsel(o, Z(width(o)), [[-a, n] for a, n in pattern], A.is_gt, c, 0, -1)
+        gsel(o, o, [[-a, n] for a, n in pattern], A.is_ge, 0.0, 15, -1)
+
+    def prow(r, buf, n, tab="PT"):
+        dma("Y", [X(tab, 16, 16 + 16 * n, rows=1 << r)], [X(buf, 0, n)], [(T[tab][r::16, 16:16 + 16 * n], T[buf][:, 0:n])],
+            LAT[3], "row%d" % r)
+
+    vts(X("SHB", 0, 208), X("SELR", 0, 208), HIGH - 31.5, A.add)
     vts(X("SELO", 0, 208), X("SELR", 0, 208), 63, A.bitwise_and)
     vts(X("SLB", 0, 208), X("SELO", 0, 208), 16.0, A.add)
-    prow(2, "SHB", 208, LAT[3])
-    prow(3, "SLB", 208, LAT[3])
-    prow(0, "HB", 256, LAT[3])
-    prow(1, "LB", 256, LAT[3])
-    vts(X("WC", 0, 5), X("CI", 0, 10, 2), uf, A.is_equal, 64.0, A.mult)
-    vts(X("WC", 5, 10), X("CI", 1, 10, 2), uf, A.is_equal)
-    vtt(X("WC", 10, 15), X("WC", 0, 5), X("WC", 5, 10), A.add)
-    w = [X("WC", 10 + d, 11 + d) for d in range(5)]
-    vts(X("LEa", 0, 144), X("CI", 0, 144), zf, A.is_equal, w[1], A.mult)
-    gset(X("T2", 0, 16), 0)
-    gset(X("F", 0, 16), 0)
+    for j, buf in enumerate(("SHB", "SLB")):
+        dma("Y", [X("SR", 16, 16 + I0, rows=1 << j)], [X(buf, 0, 208)], [(T.SR[8 * j:8 * j + 8, 16:16 + I0], T[buf][:, 0:208])],
+            LAT[3], "sr%d" % j)
+    vset(X("T2", 0, 16 + I0), 0.0)
+    prow(2, "SHB", 208, "T2")
+    prow(10, "SLB", 208, "T2")
+    prow(1, "SHB", 208)
+    prow(9, "SLB", 208)
+    prow(0, "HB", 256)
+    prow(8, "LB", 256)
+    vts(X("LEs", 0, 144), X("CI", 0, 144), zs, A.is_equal)
+    vts(X("LE", 0, 144), X("CI", 0, 144), zf, A.is_equal)
+    vcopy(u3, ti[2])
+    vts(X("WC", 0, 8), X("CI", 0, 8), u3, A.is_equal)
+    w = [X("WC", d, d + 1) for d in range(8)]
+    for d in (1, 2, 3):
+        act(X("LE%d" % d, 0, 144), X("LE", 0, 144), scale=w[d])
+    for nm in ("F", "TT") if ADD else ("F", "FS", "TT"):
+        act(X(nm, 0, 16), Z(16))
 
-    def steps(src, lst, dst, d0, qs, moves):
-        n = 208 // PARTS
-        for j in range(PARTS):
-            c0, b = 16 + 16 * n * j, psum()
-            acc([(X(b, 0, n), LE("LEa", e), X(src, c0 + e, c0 + 16 * n, 16)) for e in range(16)])
-            vts(X(lst, n * j, n * j + n), X(b, 0, n), -HIGH, A.add)
-        for j in range(PARTS):
-            c0 = d0 + 16 * n * j
-            gather(qs + str(j), X(dst, c0, c0 + 16 * n), ind(X(src, 0, 16 + I0), X(lst, n * j, n * j + n)))
-        for j in (0, 1):
-            c0, c1 = d0 + 1664 * j, 16 + 1664 * j
-            dma("Y", [X("PT", c1, c1 + 1664, rows=sum(1 << b for a, b in moves))], [X(dst, c0, c0 + 1664)],
-                [(T.PT[b::16, c1:c1 + 1664], T[dst][a::16, c0:c0 + 1664]) for a, b in moves])
+    def lists(src, s0, lst, l0, n, le, p=None):
+        b = psum()
+        acc([(X(b, 0, n), LE(le, e, p), X(src, s0 + e, s0 + 16 * n, 16, p=p)) for e in range(16)])
+        vts(X(lst, l0, l0 + n), X(b, 0, n), -HIGH, A.add)
 
-    steps("PT", "SL1", "T2", 16, "a", [(2, 4), (3, 5)])
-    steps("T2", "SL2", "T3", 0, "b", [(0, 6), (1, 7), (2, 8), (3, 9)])
+    for j in (0, 1):
+        lists("SR", 16 + CUT * j, "SL1", 104 * j, 104, "LEs", (0, 16))
+    b = psum()
+    for j in (0, 1):
+        acc([(X(b, 0, 208), LE("LE", e), X("F", 16 + 208 * e, 224 + 208 * e)) for e in range(8 * j, 8 * j + 8)], j == 0, j == 1)
+    vcopy(X("SCH", 0, 208), X(b, 0, 208))
+    vtt(X("SCL", 0, 208), X(b, 0, 208), X("SCH", 0, 208), A.subtract)
+    prow(5, "SCH", 208, "T2")
+    prow(13, "SCL", 208, "T2")
+    prow(7, "SCH", 208)
+    prow(15, "SCL", 208)
+
+    def shift(dst, d0, moves):
+        dma("Y", [X("PT", 16, 16 + I0, rows=sum(257 << b for a, b in moves))], [X(dst, d0, d0 + I0)],
+            [(T.PT[b::8, 16:16 + I0], T[dst][a::8, d0:d0 + I0]) for a, b in moves], LAT[4])
+
+    n = 208 // PARTS
+    for j in range(PARTS):
+        o = X("PT", 16 + 16 * n * j, 16 + 16 * n * j + 16 * n)
+        vtt(o, ind(X("T2", 0, 16 + I0), X("SL1", n * j, n * j + n)), o, A.add)
+        ops[-1]["tag"] = "a%d" % j
+    for j in (0, 1):
+        lists("PT", 16 + CUT * j, "SL2", 104 * j, 104, "LE2")
+    for j in range(PARTS):
+        gather("b%d" % j, X("T3", 16 * n * j, 16 * n * j + 16 * n), ind(X("PT", 0, 16 + I0), X("SL2", n * j, n * j + n)))
+    for j in (0, 1) if not ADD else ():
+        move(X("FS", 16 + CUT * j, 16 + CUT * j + CUT), X("F", 16 + CUT * j, 16 + CUT * j + CUT), scale=1.0 / 1024, tag="u%d" % j)
+    for j in range(PARTS):
+        c0 = 16 + 16 * n * j
+        o = X("TT", c0, c0 + 16 * n)
+        if ADD:
+            move(o, ind(X("F", 0, 16 + I0), X("SL1", n * j, n * j + n)), scale=1.0 / 1024, tag="t%d" % j)
+            dma("G", [o], [o], [(o[0], T.front[:, c0 - 16:c0 - 16 + 16 * n])], ADD + 0.4 * j, "add%d" % j)
+            ops[-1]["cost"]["G"] = 1.0 if j else 2.0
+        else:
+            vtt(o, ind(X("FS", 0, 16 + I0), X("SL1", n * j, n * j + n)), X("F", c0, c0 + 16 * n), A.add)
+            ops[-1]["tag"] = "t%d" % j
 
     for h in (0, 1):
         vts(X("PL", 128 * h, 128 * h + 128), X("raw", h, 256, 2), 16.0, A.add)
+        vts(X("NUM", 128 * h, 128 * h + 128), X("raw", h, 256, 2), 16.0, A.add)
     C8 = X("CI", 0, 8)
     vts(X("W1", 0, 8), C8, gf, A.is_equal)
     vcopy(X("BC", 0, 8), C8)
-    vts(ID, CI, pf, A.is_equal)
-    act(NID, ID, scale=-1.0)
-    act(ID32, ID)
     vset(ONES, 1.0)
-    act(X("RST", 0, 128), ONES, scale=0.0)
-    act(X("RST", 0, 128, 16), X("ONES", 0, 8), scale=-BIG)
-    vts(X("LEc", 0, 144), X("CI", 0, 144), zf, A.is_equal, BIG, A.mult)
     iota(X("CC", 0, 8), [[-2, 8]], 0, 0, True)
     iota(X("KCON", 0, 128), [[0, 8], [-1, 16]], 15, 0, True)
-    act(X("KC", 0, 128, p=(0, 64), rows=1), X("ONES", 0, 128, p=(0, 64)), scale=4.0)
-    act(X("KC", 0, 128, p=(64, 128), rows=2), X("KCON", 0, 128, p=(64, 128)), scale=1.0 / 64)
+    act(X("KC", 0, 128), X("KCON", 0, 128))
+    for j in (0, 1):
+        act(X("RST", 128 * j, 128 * j + 128), ONES, scale=0.0)
+    act(X("KC", 128, 256), ONES, scale=0.0)
+    act(X("RST", 0, 256, 16), X("ONES", 0, 16), scale=-BIG)
     u15, u16 = col(), col()
     act(u15, uf, AF.Identity, bias=15.0, scale=-1.0)
     vts(X("MSK", 0, 128), X("KCON", 0, 128), u15, A.is_equal)
     act(u16, uf, AF.Identity, bias=15.0, scale=16.0)
-    act(X("W16", 0, 8), X("W1", 0, 8), scale=16.0)
-    act(X("W8", 0, 8), X("W1", 0, 8), scale=8.0)
-    act(X("LEd", 0, 144), X("LEc", 0, 144), scale=2.0)
-    iota(X("KQ", 0, 144), [[0, 9], [-1, 16]], 15, 0, True)
-    vts(X("KQ", 0, 144), X("KQ", 0, 144), 12.0, A.is_ge, -float(PR), A.mult)
-    KQ = lambda j: X("KQ", (16 - 4 * j) % 16, (16 - 4 * j) % 16 + 128)
-    act(X("WB", 0, 8), X("W1", 0, 8), scale=BIG)
+    for j in (0, 1):
+        act(X("W16", 8 * j, 8 * j + 8), X("W1", 0, 8), scale=16.0)
+    line(ID, 1.0, [[-1, 128]], 0)
+    for o, c in ((NID, -1.0), (ID32, 1.0), (X("N64", 0, 128), -64.0), (X("IDK", 0, 128), 1.0 / 1024)):
+        line(o, c, [[-1, 128]], 0)
+        act(o, ID, scale=c)
+        either(None, 2)
+    line(X("N8", 0, 128), -1.0, [[-1, 128]], 8)
+    block(X("NBD", 0, 128), -1.0, [[-16, 8], [0, 16]])
+    act(X("WG", 0, 128), X("NBD", 0, 128), scale=2 * BIG)
+    for nm, c in (("LEc", BIG), ("LEd", 2 * BIG)):
+        act(X(nm, 0, 144), X("LE", 0, 144), scale=c)
+    act(X("W8", 0, 16), X("W16", 0, 16), scale=0.5)
+    for nm, c in (("WB", BIG), ("WD", -2 * BIG)):
+        act(X(nm, 0, 8), X("W1", 0, 8), scale=c)
     for d in range(1, 5):
         act(X("WX", 8 * (4 - d), 8 * (5 - d)), X("W1", 0, 8), scale=w[d])
     act(X("YSM", 0, 8), X("W1", 0, 8), scale=w[0])
-    iota(X("CVX", 0, 512), [[0, 4], [512, 128]], -5120, 0, True)
-    iota(X("CVO", 0, 512), [[512, 128], [0, 4]], -5120, 0, True)
+    for j in (0, 1):
+        vts(X("WS", 8 * j, 8 * j + 8), X("W1", 0, 8), w[5 + 2 * j], A.mult, 2 * BIG, A.mult)
+    iota(X("CVX", 0, 128), [[512, 128]], -5120, 0, True)
     iota(X("OFR", 0, 128), [[-512, 128]], 0, 0, True)
-    act(X("CZ", 0, 128), ONES, scale=-(4 * BIG + 5 * PR) / 128)
-    for h in (0, 1):
-        vts(X("NUM", 128 * h, 128 * h + 128), X("raw", h, 256, 2), 16.0, A.add)
-    cd = [None]
-    for d in range(1, 5):
-        cd.append(col())
-        act(cd[d], pf, AF.Identity, bias=float(PR * (5 - d)), scale=BIG)
-    for a, b, c in ((0, 128 - 128 // TP, 0.0), (128 - 128 // TP, 128, 1.0), (128, 256 - 128 // TP, 0.0)):
-        act(X("QM", a, b), X("ONES", 0, b - a), scale=c)
-    act(X("SIX", 0, 128), ONES, scale=6 * BIG / 128)
+    act(X("CK", 0, 128, p=(0, 64), rows=1), X("ONES", 0, 128, p=(0, 64)), scale=24576.0 * 1024)
+    act(X("CK", 0, 128, p=(64, 128), rows=2), X("ONES", 0, 128, p=(64, 128)), scale=16.0 * 1024)
+    for o, c in ((X("CZ", 0, 128), -(4 * BIG + 5 * PR) / 128), (X("SIX", 0, 128), 6 * BIG / 128), (X("OS", 0, 128), 1.0 / PR),
+                 (X("QM", 0, 64), 0.0), (X("QM", 64, 128), 1.0), (X("QM", 128, 192), 0.0)):
+        gsel(o, Z(width(o)), [[0, width(o)]], A.is_gt, c, 0, 0)
+        act(o, X("ONES", 0, width(o)), scale=c)
+        either(None, 2)
+    cd = {d: col() for d in (1, 2, 3)}
+    for d in cd:
+        iota(cd[d], [[0, 1]], PR * (5 - d), int(BIG), True)
     for j in (0, 1):
         ma = X("MA", 8 + 36 * j, 41 + 36 * j)
-        vset(X("GM%d" % j, 0, 528), 0.0)
+        gset(X("GM%d" % j, 0, 528), 0)
         iota(ma, [[2, 33]], 128 + j, -1)
         vts(ma, ma, 15, A.bitwise_and)
         vts(X("GM%d" % j, 15, 528, 16), ma, 0.0, A.is_equal, -256.0, A.add)
-    act(X("N64", 0, 128), ID, scale=-64.0)
-    act(X("OS", 0, 128), ONES, scale=1.0 / PR)
-    vts(X("QN", 0, 128), CI, 4, A.arith_shift_right)
-    vts(X("NBD", 0, 128), X("QN", 0, 128), gf, A.is_equal, -1.0, A.mult)
-    u37, up = col(), col()
-    vts(up, gf, 4.0, A.is_ge)
-    act(u37, uf, scale=37.0)
-    iota(X("KI", 0, 256), [[5, 2], [10, 128]], 0, 0)
-    iota(X("KI", 256, 512), [[1, 2], [2, 128]], 0, 0)
-    vts(X("KJ", 0, 256), X("KI", 0, 256), u37, A.add)
-    vts(X("KJ", 256, 512), X("KI", 256, 512), uf, A.add)
-    vts(X("KJ", 0, 256), X("KJ", 0, 256), 255, A.bitwise_and)
-    vts(X("KJ", 256, 512), X("KJ", 256, 512), 127, A.bitwise_and)
+    iota(X("KI", 0, 256), [[5, 2], [10, 128]], 0, 37)
+    iota(X("KI", 256, 512), [[1, 2], [2, 128]], 0, 1)
+    vts(X("KI", 0, 256), X("KI", 0, 256), 255, A.bitwise_and)
+    vts(X("KI", 256, 512), X("KI", 256, 512), 127, A.bitwise_and)
     for h in (0, 1):
         iota(X("KK%d" % h, 0, 128), [[2, 128]], h, 0, True)
-        vcopy(X("KK%d" % h, 128, 256), X("KJ", 128 * h, 128 * h + 128))
-        vcopy(X("KK%d" % h, 256, 384), X("KJ", 256 + 128 * h, 384 + 128 * h))
+        vcopy(X("KK%d" % h, 128, 256), X("KI", 128 * h, 128 * h + 128))
+        vcopy(X("KK%d" % h, 256, 384), X("KI", 256 + 128 * h, 384 + 128 * h))
     for t in range(R):
         B = I0 + NB * t - (16 if t + 1 == R else 0)
-        for j, c in enumerate((B + 16, B + 2016, B + 208)):
-            cb = col()
-            act(cb, up, AF.Identity, bias=-64.0, scale=(c - PR + 4096) / 64.0 + 64.0)
-            act(X("CB%d" % t, 128 * j, 128 * j + 128), ONES, scale=cb)
-    l8, l2 = col(), col()
-    vts(l8, uf, 8.0, A.is_lt)
-    act(X("SH", 0, 2), X("ID", 0, 2), scale=0.0)
-    act(X("SH", 2, 128), X("ID", 0, 126), scale=l8)
-    vts(l2, uf, 2.0, A.is_lt)
-    act(X("D01", 0, 128), ID, scale=l2)
+        for j, c in enumerate((B + 16 - PR, B + 2016 - PR, B + 208 - PR)):
+            iota(X("CB%d" % t, 128 * j, 128 * j + 128, p=(0, 2)), [[0, 128]], c // 256 * 256, c % 256 - c // 256 * 256, True)
+    line(X("SH", 0, 128), 1.0, [[-1, 128]], 1)
+    for c in (0, 5):
+        gset(X("SH", c, 128, 8), 0)
+    gset(X("D01", 0, 128), 0)
+    line(X("D01", 0, 128, 8), 1.0, [[-8, 16]], 0)
+    if HY:
+        gset(X("SH3", 0, 128), 0)
+        line(X("SH3", 4, 128, 8), 1.0, [[-8, 16]], -1)
+        line(X("SH3", 7, 128, 8), 1.0, [[-8, 16]], -7)
+        gset(X("SH7", 0, 128), 0)
+        line(X("SH7", 5, 128, 8), 1.0, [[-8, 16]], -7)
 
     def choose(z, data):
         zs, b = (128 * z, 128 * z + 128), psum()
-        acc([(X(b, 0, 128), ONES, X("KC", 0, 128))] + data(b))
-        scan(X("SK", *zs), X("RST", 0, 128), X(b, 0, 128), 0.0, A.add, A.max)
+        acc([(X(b, 0, 256), X("ONES", 0, 128, p=(0, 1)), X("KC", 0, 256, p=(0, 1)))] + data(b))
+        scan(X("SK", 256 * z, 256 * z + 256), X("RST", 0, 256), X(b, 0, 256), 0.0, A.add, A.max)
         mx = X("MX", 8 * z, 8 * z + 8)
-        vcopy(mx, X("SK", zs[0] + 15, zs[1], 16))
-        vts(mx, mx, 15, A.bitwise_and)
+        vtt(mx, X("SK", 256 * z + 15, 256 * z + 128, 16), X("SK", 256 * z + 143, 256 * z + 256, 16), A.subtract)
         vtt(X("GE", *zs), ind(mx, X("BC", 0, 8)), X("MSK", 0, 128), A.mult)
         o = X(psum(), 0, 8)
         acc([(o, ONES, X("CC", 0, 8)), (o, X("GE", *zs), X("W1", 0, 8))])
@@ -694,58 +620,72 @@ def record(g, core, T, topo, rank, banks):
         if z < 2:
             o = X(psum(), 0, 128)
             acc([(o, X("GE", *zs), ID)])
-            act(X("EL", *zs), o, scale=-1.0)
+            move(X("EL", *zs), o, scale=-1.0)
             o = X(psum(), 0, 128)
             acc([(o, X("NBD", 0, 128), X("EL", *zs))])
             vts(X("GT", *zs), o, u15, A.is_equal, float(PR), A.mult)
 
     def signs(z, src, gm):
         for j in range(4):
-            pd, l = psum(), []
-            for i in range(4):
-                o = X(pd, 128 * i, 128 * i + 128)
-                l += [(o, NID, X(src, 4 * j + i, 2048, 16), True, False), (o, ID, gm, False, True)]
-            tag, c0, n0 = "z%s%d%d" % (src[1], z, j), 2048 * z + 512 * j, len(ops)
-            mms(l)
-            act(X("cz", c0, c0 + 512), X(pd, 0, 512), AF.Sign, bias=0.5)
-            o = X(psum(), 0, 128)
-            acc([(o, ID, gm)])
-            for i in range(4):
-                vtt(X("cz", c0 + 128 * i, c0 + 128 * i + 128), X(src, 4 * j + i, 2048, 16), o, A.is_le)
-            join(n0 + 3)
-            for i, x in enumerate(ops[n0:]):
-                x["tag"], x["way"] = tag if i & 1 else None, (tag, "SSVV"[i])
+            pd = psum()
+            acc([(X(pd, 128 * i, 128 * i + 128), NID, X(src, 4 * j + i, 2048, 16)) for i in range(4)], True, False)
+            acc([(X(pd, 128 * i, 128 * i + 128), ID, gm) for i in range(4)], False, True)
+            o = X("cz", 2048 * z + 512 * j, 2048 * z + 512 * j + 512)
+            act(o, X(pd, 0, 512), AF.Sign, bias=0.5)
+            vts(o, X(pd, 0, 512), 0.0, A.is_ge, 0.5, A.subtract)
+            either("z%s%d%d" % (src[1], z, j), 2)
 
-    def grow(src, n, c0, y0, tt):
+    def grow(src, n, c0, y0, tt, fronts, more):
         if tt + 1 < R:
-            o = X(psum(), 0, n)
-            acc([(o, X("SH", 0, 128), X(src, 0, n)), (o, X("D01", 0, 128), X("PT", c0, c0 + n))])
-            act(X("PT", c0, c0 + n), o)
+            b, st, l = psum(), n // 128, []
+            for j, x in enumerate(fronts):
+                if j in dict(more):
+                    l += [(X(b, j, n, st), X("SH7", 0, 128), X(src, j, n, st)), (X(b, j, n, st), X("SH3", 0, 128), dict(more)[j])]
+                    continue
+                o, hh = X(psum(), 0, 128), X("HH", 128 * j, 128 * j + 128)
+                acc([(o, LE("LE", 5), x)])
+                move(hh, o)
+                l += [(X(b, j, n, st), ID, hh), (X(b, j, n, st), X("N8", 0, 128), hh), (X(b, j, n, st), LE("LE", 13), x)]
+            o = X(b, 0, n)
+            acc([(o, X("SH", 0, 128), X(src, 0, n)), (o, X("D01", 0, 128), X("PT", c0, c0 + n))] + l)
+            move(X("PT", c0, c0 + n), o)
         y = X(psum(), 0, n, p=(0, 8))
         acc([(y, X("YSM", 0, 8), X(src, 0, n))])
-        act(X("YS", y0, y0 + n, p=(0, 8)), y, AF.Identity, bias=-16.0 - HIGH)
+        move(X("YS", y0, y0 + n, p=(0, 8)), y, bias=-16.0 - HIGH)
         dma("Y", [], [X("YS", y0, y0 + n)], [(T.ys[:, y0:y0 + n], T.YS[0:8, y0:y0 + n])])
+
+    def pairs(out, own, far):
+        o = X(psum(), 0, 128)
+        acc([(o, ID, own), (o, X("IDK", 0, 128), far)])
+        move(out, o)
 
     def come(tt):
         cc = 16 + I0 + NB * tt + L
         at[0] = "%d2" % tt
         signs(2, "f%d0" % tt, X("F", cc, cc + 128))
         tg = ["z%d2%d" % (tt, j) for j in range(4)]
-        choose(2, lambda b: [(X(b, 0, 128), X("OS", 0, 128), KQ(j), (tg[j], "V")) for j in range(4)]
-               + [(X(b, k, 128, 16), X("cz", 4096 + 128 * k, 4224 + 128 * k), X(wt, 0, 8), (tg[k >> 2], q))
-                  for k in range(16) for q, wt in (("S", "W8"), ("V", "W16"))])
+        choose(2, lambda b: [(X(b, k, 256, 16), X("cz", 4096 + 128 * k, 4224 + 128 * k), X(wt, 0, 16), (tg[k >> 2], q))
+                             for k in range(16) for q, wt in (("S", "W8"), ("V", "W16"))])
         gather("c%d2" % tt, X("PC", 0, 128), ind(X("px%d0" % tt, 0, 2048), X("OFF", 16, 24)))
-        grow("PC", 128, cc, NB * tt + L, tt)
+        if tt + 1 < R:
+            gather("h%d2" % tt, X("FC", 0, 128), ind(X("f%d0" % tt, 0, 2048), X("OFF", 16, 24)))
+            pairs(X("TT", cc, cc + 128), X("F", cc, cc + 128), X("FC", 0, 128))
+        more = []
+        if (tt, 0) in HY:
+            more = [(0, X("PS2", 256, 384))]
+            gather("d%d2" % tt, more[0][1], ind(X("py0", 0, 2048), X("OFF", 16, 24)))
+        grow("PC", 128, cc, NB * tt + L, tt, [X("FC", 0, 128)], more)
 
-    def parents(nm, dst, window):
-        n, p0 = 128 // PIECES, 128 * int(at[0][1])
-        piece = lambda tag, a, b: gather(tag, X(dst, 16 * a, 16 * b), ind(window, X("PL", p0 + a, p0 + b)))
+    def parents(nm, dst, window, lst="PL", p0=None):
+        n, p0 = 128 // PIECES, p0 or 128 * int(at[0][1])
+        piece = lambda tag, a, b: gather(tag, X(dst, 16 * a, 16 * b), ind(window, X(lst, p0 + a, p0 + b)))
         for c in range(PIECES):
             piece(nm + at[0] + str(c), n * c, n * c + n)
             if c & 1:
                 pair(len(ops) - 2, len(ops) - 1, lambda: piece("", n * c - n, n * c + n))
 
-    G = [X("GX%d" % h, 0, 2048, 16) for h in (0, 1)]
+    G = [X("GB", 128 * h, 128 * h + 128) for h in (0, 1)]
+    sent = [0]
     for t in range(R):
         B = I0 + NB * t
         cc = 16 + B + L
@@ -753,92 +693,137 @@ def record(g, core, T, topo, rank, banks):
         pwin = X("PT", 0, 16 + B)
         HS = [(128 * h, 128 * h + 128) for h in (0, 1)]
         for h in (0, 1):
-            fn, at[0] = "f%d%d" % (t, h), "%d%d" % (t, h)
+            fn, gx, at[0] = "f%d%d" % (t, h), "GX%d" % h, "%d%d" % (t, h)
             parents("f", fn, win)
-            choose(h, lambda b: [(X(b, k, 128, 16), X(fn, k, 2048, 16), X("W16", 0, 8)) for k in range(16)])
-            gather("g%d%d" % (t, h), G[h], ind(X(fn, 0, 2048), X("OFF", 8 * h, 8 * h + 8)))
-            for k0 in (1, 6, 11):
-                n0 = len(ops)
-                for k in range(k0, k0 + 5):
-                    {"G": gcopy, "V": vcopy, "S": act}[GQ[2 * t + h][k0 // 5]](X("GX%d" % h, k, 2048, 16), G[h])
-                join(n0)
-                ops[-1]["tag"] = "GX" + at[0]
+            choose(h, lambda b: [(X(b, k, 256, 16), X(fn, k, 2048, 16), X("W16", 0, 16)) for k in range(16)])
+            chosen = ind(X(fn, 0, 2048), X("OFF", 8 * h, 8 * h + 8))
+            move(X(gx, 0, 2048, 16), chosen, -MID, 1025.0 / 1024, "G" + at[0])
+            gather("g" + at[0], G[h], chosen)
+            for c in (0, 1):
+                for j, k in enumerate((8, 4, 2, 1)):
+                    for copy in (gcopy, vcopy, act):
+                        copy(X(gx, 1024 * c + k, 1024 * c + 1024, 2 * k), X(gx, 1024 * c, 1024 * c + 1024, 2 * k))
+                    either("r%d%d%d%d" % (t, h, c, j), 3)
         for h in (0, 1):
-            pn, b, c0, at[0] = "px%d%d" % (t, h), psum(), 512 * h, "%d%d" % (t, h)
+            pn, c0, at[0] = "px%d%d" % (t, h), 512 * h, "%d%d" % (t, h)
+
+            def keys(src, ds, ls):
+                for d in ls:
+                    for c in (0, 1) if (t, h, d) in DIRECT else ():
+                        lists(src, 1024 * c, "QL", c0 + 128 * (4 - d) + 64 * c, 64, "LE%d" % (d - ds[0] + 1))
+                        ops[-1]["tag"] += "%d%d" % (d, c)
+                n, b = 128 * len(ds), psum()
+                acc([(X(b, c, c + 128), ONES, X("CVX", 0, 128)) for c in range(0, n, 128)]
+                    + [(X(b, k, n, 16), X(src, k, 2048, 16), X("WX", 32 - n // 16, 32)) for k in range(16)])
+                for d in ds:
+                    j, i = 4 - d, ds[-1] - d
+                    move(X("CO", c0 + j, c0 + 512, 4), X(b, 128 * i, 128 * i + 128), bias=10 * BIG + PR * (5 - d) - HIGH)
+                    ops[-1]["tag"] += str(d)
+                for d in ls:
+                    if (t, h, d) not in DIRECT:
+                        j, o = 4 - d, X(psum(), 0, 128)
+                        acc([(o, X("CO", c0 + j, c0 + 512, 4), ID32)])
+                        vts(X("QL", c0 + 128 * j, c0 + 128 * j + 128), o, cd[d], A.subtract)
+                        ops[-1]["tag"] += str(d)
+
+            if t == 0 and h == len(HY):
+                shift("T3", 0, [(1, 3), (2, 4), (5, 7), (7, 6)])
             parents("x", pn, pwin)
-            acc([(X(b, 0, 512), ONES, X("CVX", 0, 512))]
-                + [(X(b, k, 512, 16), X(pn, k, 2048, 16), X("WX", 0, 32)) for k in range(16)])
-            for d in range(1, 5):
-                j = 4 - d
-                act(X("CO", c0 + j, c0 + 512, 4), X(b, 128 * j, 128 * j + 128), AF.Identity, bias=10 * BIG + PR * (5 - d) - HIGH)
-            for d in range(1, 5):
-                j, o = 4 - d, X(psum(), 0, 128)
-                acc([(o, X("CO", c0 + j, c0 + 512, 4), ID32)])
-                vts(X("QL", c0 + 128 * j, c0 + 128 * j + 128), o, cd[d], A.subtract)
-                ops[-1]["tag"] += str(d)
+            if (t, h) in HY:
+                keys(pn, (1, 2), (1, 2))
+                parents("y", "py%d" % h, pwin, "QL", c0 + 256)
+                keys("py%d" % h, (3, 4), (3,))
+            else:
+                keys(pn, (1, 2, 3, 4), (1, 3))
+        if t == 0 and len(HY) == 2:
+            shift("T3", 0, [(1, 3), (2, 4), (5, 7), (7, 6)])
         for h in (0, 1):
             at[0] = "%d%d" % (t, h)
             signs(h, "f%d%d" % (t, h), G[h])
             o = X(psum(), 0, 128)
             tg = ["z%d%d%d" % (t, h, j) for j in range(4)]
-            acc([(o, ONES, X("CZ", 0, 128))] + [(o, KQ(j), ONES, (tg[j], "V")) for j in range(4)]
+            acc([(o, ONES, X("CZ", 0, 128))]
                 + [(o, LE(le, k), X("cz", 2048 * h + 128 * k, 2048 * h + 128 * k + 128), (tg[k >> 2], q))
                    for k in range(16) for q, le in (("S", "LEc"), ("V", "LEd"))])
             t0 = X("T0", *HS[h])
             vtt(t0, o, X("NUM", *HS[h]), A.min)
+            vts(t0, t0, 5.0 * PR, A.add, 0.0, A.max)
             act(t0, t0, AF.Relu, bias=5.0 * PR)
-            ops[-1]["tag"] = "RL" + at[0]
+            either("RL" + at[0], 2)
 
-        def tests(h):
+        def tests(h, a, b):
             ca, gx, c0, at[0] = psum(), "GX%d" % h, 512 * h, "%d%d" % (t, h)
-            for d in range(1, 5):
+            pn, twin, p = "px%d%d" % (t, h), X("TT", 0, 16 + B), (a, b)
+            rows = ALL if b - a == 128 else 1 << a // 64
+            for d in (1, 3):
                 j = 4 - d
-                v0, q0 = 2048 * (4 * h + j), c0 + 128 * j
-                l = []
+                v0, q0 = 2048 * (2 * h + d // 2), c0 + 128 * j
                 if d == 1:
-                    acc([(X(ca, 0, 512), ONES, X("CVO", 0, 512))], True, False)
-                    ops[-1]["r"] += X("QL", q0, q0 + 128)[1]
-                n = 128 // TP
-                cvs = lambda a, b: X("cv", v0 + 16 * a, v0 + 16 * b)
-                lst = lambda a, b: ind(win, X("QL", q0 + a, q0 + b))
-                for c in range(TP):
-                    tag, a, b, n0 = "%s%d%d%d" % (" pqrs"[d], t, h, c), n * c, n * c + n, len(ops)
-                    vtt(cvs(a, b), lst(a, b), X(gx, 16 * a, 16 * b), A.is_le)
-                    act(cvs(a, b), lst(a, b))
-                    for i in range(a, b, 32):
-                        pd = X(psum(), 0, 512)
-                        acc([(pd, NID, cvs(i, i + 32)), (pd, ID, X(gx, 16 * i, 16 * i + 512))])
-                        act(cvs(i, i + 32), pd, AF.Sign, bias=0.5)
-                    for i, x in enumerate(ops[n0:]):
-                        x["tag"], x["way"] = tag if i < 2 else tag.upper() if x["q"] == "S" else None, (tag, "S" if i else "V")
-                    l.append((X(ca, j, 512, 4), X("QM", 128 - b, 256 - b), X("SIX", 0, 128), (tag, "S")))
-                    if c & 1:
-                        n1 = 2 * n0 - len(ops)
-                        pair(n1, n0, lambda: vtt(cvs(a - n, b), lst(a - n, b), X(gx, 16 * (a - n), 16 * b), A.is_le))
-                acc(l + [(X(ca, 4 * k + j, 512, 64), X("cv", v0 + k, v0 + 2048, 16), X("WB", 0, 8)) for k in range(16)],
+                    acc([(X(ca, c, 512, 4, p=p), X("ONES", a, b), X("CVX", 0, 128)) for c in range(4)], True, False)
+                    ops[-1]["r"] += X("QL", q0 + a, q0 + a + 64)[1]
+                src, ws = ("py%d" % h, 0) if d == 3 and (t, h) in HY else (pn, 4 * d - 4)
+                acc([(X(ca, j - 1, 512, 4, p=p), X("ONES", a, b), X("CK", 0, 128)),
+                     (X(ca, j - 1, 512, 4, p=p), X("GB", 128 * h + a, 128 * h + b), X("WG", 0, 128))]
+                    + [(X(ca, 4 * k + j - 1, 512, 64, p=p), X(src, 16 * a + k, 16 * b, 16), X("WS", ws, ws + 8)) for k in range(16)],
                     False, False)
                 ops[-1]["fn"] = ca
-            scan(X("SC", c0, c0 + 512), X(ca, 0, 512), X("CO", c0, c0 + 512), -BIG, A.max, A.min)
-
-        def entered(h):
-            hs, o, at[0] = HS[h], X(psum(), 0, 128), "%d%d" % (t, h)
-            acc([(o, X("OFR", 0, 128), ONES), (o, X("SC", 512 * h + 3, 512 * h + 512, 4), ID32)])
+                cds = lambda a, b: X("cd", v0 + 16 * a, v0 + 16 * b)
+                cvs = lambda a, b: X("cv", v0 + 16 * a, v0 + 16 * b)
+                test = lambda a, b: vtt(cds(a, b), ind(twin, X("QL", q0 + a, q0 + b)), X(gx, 16 * a, 16 * b), A.subtract)
+                for c in range(a, b, TW):
+                    test(c, c + TW)
+                    ops[-1]["tag"] = "%s%d%d%d" % (" p q"[d], t, h, c // TW)
+                    if (c - a) // TW & 1:
+                        pair(len(ops) - 2, len(ops) - 1, lambda: test(c - TW, c + TW))
+                l = []
+                for c in range(a, b, 64):
+                    tag = "%s%d%d%d" % (" P Q"[d], t, h, c // 64)
+                    vts(cvs(c, c + 64), cds(c, c + 64), 768.75, A.is_le)
+                    act(cvs(c, c + 64), cds(c, c + 64), AF.Sign, bias=768.75, scale=-1.0)
+                    either(tag, 2)
+                    l.append((X(ca, j, 512, 4, p=p), X("QM", 64 - c + a, 64 - c + b), X("SIX", 0, 128), (tag, "S")))
+                for src, col0, wt, l in (("cd", j - 1, "WD", []), ("cv", j, "WB", l)):
+                    acc(l + [(X(ca, 4 * k + col0, 512, 64, p=p), X(src, v0 + 16 * a + k, v0 + 16 * b, 16), X(wt, 0, 8))
+                             for k in range(16)], False, False)
+                    ops[-1]["fn"] = ca
+            scan(X("SC", c0, c0 + 512, p=p, rows=rows), X(ca, 0, 512, p=p), X("CO", c0, c0 + 512, p=p), -BIG, A.max, A.min)
+            hs, o = (128 * h + a, 128 * h + b), X(psum(), 0, b - a)
+            acc([(o, X("OFR", 0, 128), X("ONES", a, b)), (o, X("SC", c0 + 3, c0 + 512, 4, p=p, rows=rows), X("ID32", a, b, p=p))])
             vtt(X("VI", *hs), o, X("T0", *hs), A.max)
             vts(X("QN", *hs), X("VI", *hs), PR - 1, A.bitwise_and)
             vcopy(X("LOL", *hs), X("QN", *hs))
             gm, g0 = "GM%d" % ((h + t) & 1), 16 * ((h + t) >> 1)
-            for i in range(4):
+            for i in range(a // 32, b // 32):
                 cs = (2048 * h + 512 * i, 2048 * h + 512 * i + 512)
-                gather("e%d%d%d" % (t, h, i), X("DS", *cs), ind(win, X("LOL", hs[0] + 32 * i, hs[0] + 32 * i + 32)))
+                gather("e%d%d%d" % (t, h, i), X("DS", *cs), ind(win, X("LOL", 128 * h + 32 * i, 128 * h + 32 * i + 32)))
                 scan(X("DC", *cs), X("DS", *cs), X(gm, g0, g0 + 512), 0.0, A.max, A.add)
                 ops[-1]["tag"] += str(i)
-            new = X("DC", 2048 * h + 15, 2048 * h + 2048, 16)
             if h == 0:
-                vts(X("SEND%d" % t, 0, 128), new, 256.0, A.add, 255.0, A.min)
-            vts(X("F", 16 + B + h, 16 + B + L, 2), new, 256.0, A.add, 255.0, A.min)
+                vts(X("SEND%d" % t, a, b), X("DC", 16 * a + 15, 16 * b, 16), 256.0, A.add, 255.0, A.min)
+                send(a, b)
+            if b == 128:
+                vts(X("F", 16 + B + h, 16 + B + L, 2), X("DC", 2048 * h + 15, 2048 * h + 2048, 16), 256.0, A.add, 255.0, A.min)
+                if t + 1 < R:
+                    pairs(X("TT", 16 + B + h, 16 + B + L, 2), X("F", 16 + B + h, 16 + B + L, 2), G[h])
+
+        def send(a, b):
+            dst = T.cores[(rank + 1 + t % 7) % len(T.cores)]
+            src = T.cores[(rank - 1 - t % 7) % len(T.cores)]
+            es = topo.engines(core, dst)[::2]
+            rid, pid, _se = topo.addr(dst)
+            nm = "%d%d" % (t, a // 64)
+            out, buf = T.F[:, cc + a:cc + b], T["SEND%d" % t][:, a:b]
+            gone = (None, [("gone" + nm, 0, 1, 1, ALL)])
+            rec("s", "G", [gone], [X("SEND%d" % t, a, b)],
+                lambda e: e.remote_dma(out_ap=out, in_ap=buf, remote_sem=T.sem["ar" + nm], local_sem=T.sem["lc" + nm],
+                                       pid=pid, routing_id=rid, dma_engine_mask=sum(1 << x for x in es)),
+                0.3, 2.0, ("lc" + nm, len(es)))
+            rec("a", "R", [X("F", cc + a, cc + b)], [gone], None, 0.3, ARR[min(1, sent[0])],
+                ("ar" + nm, len(topo.engines(src, core)[::2])))
+            sent[0] += 1
 
         def rename(h):
-            hs, kk, r0 = HS[h], "KK%d" % h, 256 * h
+            hs, kk, r0, at[0] = HS[h], "KK%d" % h, 256 * h, "%d%d" % (t, h)
             hif, red = X("HIF", *hs), X("RZ", r0, r0 + 128)
             vts(hif, X("VI", *hs), 1.0 / PR, A.mult, 127.875, A.add)
             vts(red, hif, 128.0, A.is_equal, float(PR), A.mult)
@@ -848,11 +833,12 @@ def record(g, core, T, topo, rank, banks):
                 return [(X(b, 128, 256), X("NBD", 0, 128), hif), (X(b, 128, 256), X("OS", 0, 128), red),
                         (X(b, 256, 384), X("OS", 0, 128), red)]
 
-            pm, ca, gt = psum(), psum(), X("GT", *hs)
-            acc([(X(pm, 128, 384), ID, X(kk, 128, 384))] + sums(pm))
+            pm, ca, gt, rows = psum(), psum(), X("GT", *hs), X("MSK", 0, 128, p=(0, 16))
+            acc([(X(pm, 128, 384), rows, X(kk, 128, 384, p=(0, 16)))] + sums(pm))
             act(X("WW", r0, r0 + 128), X(pm, 128, 256), AF.Sign, bias=2128 - 255.5)
             act(X("WW", r0 + 128, r0 + 256), X(pm, 256, 384), AF.Sign, bias=-127.5)
-            acc([(X(ca, 0, 384), ID, X(kk, 0, 384)), (X(ca, 0, 384), ONES, X("CB%d" % t, 0, 384)),
+            acc([(X(ca, 0, 384), rows, X(kk, 0, 384, p=(0, 16))),
+                 (X(ca, 0, 384), X("ONES", 0, 128, p=(0, 2)), X("CB%d" % t, 0, 384, p=(0, 2))),
                  (X(ca, 0, 128), ID, gt), (X(ca, 256, 384), NID, gt),
                  (X(ca, 128, 384), ID, X("RZ", r0, r0 + 256))] + sums(ca), True, False)
             acc([(X(ca, 128, 384), X("N64", 0, 128), X("WW", r0, r0 + 256)),
@@ -869,35 +855,23 @@ def record(g, core, T, topo, rank, banks):
 
         for h in (0, 1):
             gather("c%d%d" % (t, h), X("PS", h, 256, 2), ind(X("px%d%d" % (t, h), 0, 2048), X("OFF", 8 * h, 8 * h + 8)))
+        more = [(h, X("PS2", 128 * h, 128 * h + 128)) for h in (0, 1) if (t, h) in HY]
+        for h, x in more:
+            gather("d%d%d" % (t, h), x, ind(X("py%d" % h, 0, 2048), X("OFF", 8 * h, 8 * h + 8)))
         at[0] = "%d0" % t
-        grow("PS", 256, 16 + B, NB * t, t)
-        tests(0)
-        entered(0)
-        dst = T.cores[(rank + 1 + t % 7) % len(T.cores)]
-        src = T.cores[(rank - 1 - t % 7) % len(T.cores)]
-        es = topo.engines(core, dst)[:8]
-        nsrc = len(topo.engines(src, core)[:8])
-        rid, pid, _se = topo.addr(dst)
-        mk = sum(1 << e for e in es)
-
-        def send(e, t=t, cc=cc, rid=rid, pid=pid, mk=mk):
-            e.remote_dma(out_ap=T.F[:, cc:cc + 128], in_ap=T["SEND%d" % t][:], remote_sem=T.sem["ar%d" % t],
-                         local_sem=T.sem["lc%d" % t], pid=pid, routing_id=rid, dma_engine_mask=mk)
-
-        rec("s", "G", [], [X("SEND%d" % t, 0, 128)], send, 0.3, 2.0, ("lc%d" % t, len(es)))
-        rec("a", "R", [X("F", cc, cc + 128)], [X("SEND%d" % t, 0, 128)], None, 0.3, ARR[t], ("ar%d" % t, nsrc))
-        rename(0)
-        tests(1)
+        grow("PS", 256, 16 + B, NB * t, t, G, more)
+        for h in (0, 1):
+            for a, b in ((0, 64), (64, 128)) if (t, h) in SPLIT else ((0, 128),):
+                tests(h, a, b)
+            rename(h)
         come(t)
-        entered(1)
-        rename(1)
         if t + 1 == R:
             dma("Y", [], [X("YP", 0, 256)], [(T.yp[:], T.YP[:])], 1.9)
-            ops[-1]["cost"] = 0.7
+            ops[-1]["cost"]["Y"] = 0.7
         y0 = NB * t
         dma("Y", [], [X("F", cc, cc + 128)], [(T.yf[:, y0 + L:y0 + NB], T.F[:, cc:cc + 128])])
         dma("Y", [], [X("F", 16 + B, 16 + B + L)], [(T.yf[:, y0:y0 + L], T.F[:, 16 + B:16 + B + L])], 1.9)
-        ops[-1]["cost"] = 0.4
+        ops[-1]["cost"]["Y"] = 0.4
     return ops
 
 
@@ -961,28 +935,25 @@ def issue(g, T, ops):
                     l[:] = [e for e in l if not cover(x, e["x"])]
                 l.append({"q": q, "w": w, "x": x, "sem": sem, "val": val, "clk": c})
 
-    queue = {i: who[ops[i]["tag"]] if ops[i]["kind"] == "g" else ops[i]["q"] for i in PLAN["order"]}
+    queue = PLAN["qs"]
     after, nxt = {}, {}
     for i in PLAN["order"][::-1]:
         after[i], nxt[queue[i]] = nxt.get(queue[i]), i
     for i in PLAN["order"]:
         o = ops[i]
         q, r, w = o["q"], o["r"], o["w"]
-        if o["way"] and who[o["way"][0]] != o["way"][1]:
-            continue
         if o["kind"] == "a":
             note("D", [], w, o["data"][0], o["data"][1], {})
             continue
         q, fns = queue[i], o["fn"]
-        if "mate" in o and after[i] == o["mate"]:
+        if "mate" in o and after[i] == o["mate"] and i not in PLAN["apart"]:
             continue
-        if "mate" in o and after.get(o["mate"]) == i:
+        if "mate" in o and after.get(o["mate"]) == i and o["mate"] not in PLAN["apart"]:
             fns, r, w = o["both"], r + ops[o["mate"]]["r"], w + ops[o["mate"]]["w"]
         waits(q, r, w)
         if o["kind"] in "cg":
-            for fn in fns if o["kind"] == "c" else [fns[q]]:
-                cnt[q] += 1
-                fn(eng[q]).then_inc(T.sem[sname[q]], 1)
+            cnt[q] += 1
+            (fns if o["kind"] == "c" else fns[q])(eng[q]).then_inc(T.sem[sname[q]], 1)
             note(q, r, w, sname[q], cnt[q], clk[q])
         elif o["kind"] == "t":
             if o["fn"]:
@@ -999,7 +970,10 @@ def issue(g, T, ops):
             sem = "d%d" % ndma
             ndma += 1
             for (x, y) in o["data"]:
-                eng[q].dma_start(x, y).then_inc(T.sem[sem], 16)
+                if q == "G":
+                    g.dma_start(x, y, accum_op=AluOpType.add).then_inc(T.sem[sem], 16)
+                else:
+                    eng[q].dma_start(x, y).then_inc(T.sem[sem], 16)
             note("D", r, w, sem, 16 * len(o["data"]), clk[q])
         else:
             o["fn"](g)

@@ -8,66 +8,93 @@ FW = 4112
 BIG = 65536.0
 PR = 8192
 HIGH = 129.0 * 64
-MID = 768.25 - 1.0 / 2048
+MID = (767.25 - 1.0 / 2048) / 16
+TOP = 32768.0
+BYDMA = ()
+DLAT = 3.6
+SLANES = {}
+CUTS = {(1, 0): (0, 32, 64)}
+EARLY = 64
 HY = ((0, 0),)
 SPLIT = ((0, 0),)
-DIRECT = ((0, 0, 1), (0, 0, 2), (0, 0, 3), (1, 0, 1), (1, 0, 3))
+LAST = (0, 64, 96, 128)
+DIRECT = ((0, 0, 1, 0), (0, 0, 2, 0), (0, 0, 3, 0), (0, 0, 1, 64), (0, 0, 3, 64), (0, 1, 1, 0), (1, 0, 1, 0), (1, 0, 3, 0), (1, 1, 1, 0))
 ADD = 3.0
 TW = 32
 PARTS = 4
 PIECES = 4
-LAYS = 11000
-LHEAT = 0.002
+LAYS = 6000
+LHEAT = 0.0017
 LEAN = (1.0, 1.0)
 PULL = 0.5
-AIM = {}
+AIM = {
+    "V": "@5.2 f002 f003 t1 u0 u1 u2 u3 @9.9 a0 a1 a2 a3 @14.5 x000 b1 y001 y000 @18.9 p000 p001 q000 q001 @22.1 x003 Q000 p003 p002 "
+         "q002 q003 @27.5 p010 p011 @29.5 p013 p012 q010 q011 q012 q013 Q011 @37.5 z020 e012 e010 @42 f101 f111 f110 x100 x103 "
+         "@48 p100 p101 q101 q100 p102 p103 q103 q102 Q100 p113 p112 p111 @57 p110 q110 q111 q113 q112 Q110 @64.3 e110 z122 z121",
+    "S": "@5.2 f012 f013 f000 f001 f011 f010 t0 t2 t3 z001 z000 @14.4 x001 b0 b3 b2 @20 P000 @22.1 x002 x012 x013 x010 x011 P001 Q001 "
+         "e000 e001 z010 z011 P010 e003 e002 P011 Q010 @37.8 z021 z023 z022 e011 e013 @41.8 f100 f102 f103 f112 f113 x101 x102 x110 "
+         "z100 z101 x113 x112 x111 P100 P101 Q101 z111 z110 P111 P110 e103 e102 e100 e101 Q111 @64.6 e112 z120 z123 e111 e113"}
 CRIT = 0.7
 BACK = 0.6
 WIDE = 8.0
 AMP = 1.5
 LOOSE = 0.5
 EPS = 0.25
-SEED = 8
+SEED = 3
+SWEEPS, WIN, STRIDE, EACH = 34, 110, 45, 1200
+HEAT, SOFT = 0.0006, 0.4
 CYC = 0.83e-3
 PEC = 0.42e-3
 GAT = 1.56
 WAKE = 0.2
-ARR = (4.0, 0.5)
-KINDS = [(1.0, 0.95, 0.17, 0.0), (1.3, 1.25, 0.2, 0.0)]
+ARR = (4.8, 0.3)
+KINDS = [(1.0, 0.95, 0.19, 0.1), (1.1, 0.74, 0.19, 0.1), (1.35, 1.27, 0.19, 0.1)]
+SCALES = (70.0, 140.0, 105.0)
+LAYK = (0, 0, 2)
 PLAN = {}
 CUT = 1664
 LAT = (3.2, 4.3, 5.0, 2.6, 2.8)
-LOADS = "sel fr0 fr1 par sr0 sr1 row2 row10 row1 row9 row0 row8 row5 row13 row7 row15"
+FRONT = ((0, 10, 4.5), (10, 16, 5.0))
+LOADS = "sel fr0 fr1 fr2 par sr0 sr1 row2 row10 row1 row9 row0 row8 row5 row7 row13 row15"
 
 SCRATCH = {}
 for _d, _l in [
-        ("bfloat16", [("F", FW), ("PT", FW), ("T2", 16 + I0), ("T3", I0), ("FS", 16 + I0), ("SR", 16 + I0),
+        ("bfloat16", [("F", FW), ("PT", FW), ("FS", 16 + I0),
                       ("f00", 2048), ("f01", 2048), ("f10", 2048), ("f11", 2048),
-                      ("px00", 2048), ("px01", 2048), ("px10", 2048), ("px11", 2048), ("py0", 2048), ("py1", 2048),
-                      ("GB", 256), ("cv", 4 * 2048), ("cz", 3 * 2048), ("DS", 4096), ("DC", 4096),
+                      ("px00", 2048), ("px01", 2048), ("px10", 2048), ("px11", 2048), ("py0", 2048),
+                      ("GB", 256), ("cv", 4 * 2048), ("cz", 2048), ("cw", 2048), ("DS", 4096), ("DC", 4096),
                       ("SCH", 208), ("SCL", 208), ("HB", 256), ("LB", 256), ("SHB", 208), ("SLB", 208),
                       ("HH", 256), ("FC", 128), ("PS", 256), ("PC", 128), ("PS2", 384),
-                      ("LEs", 144), ("LE", 144), ("LE1", 144), ("LE2", 144), ("LE3", 144), ("LEc", 144), ("LEd", 144),
+                      ("LEs", 144), ("LE", 144), ("LE1", 144), ("LE2", 144), ("LE3", 144), ("I5", 128), ("SG", 256), ("WN", 8),
+                      ("I16", 128), ("WO", 64), ("WE", 8), ("W8K", 16), ("W16K", 16), ("KCK", 256), ("RSK", 256), ("CE", 128),
                       ("W1", 8), ("W8", 16), ("W16", 16), ("WB", 8), ("WD", 8), ("WS", 16), ("WX", 32), ("YSM", 8), ("WG", 128),
                       ("ZERO", 144), ("ONES", 128), ("ID", 128), ("NID", 128), ("N64", 128), ("N8", 128), ("IDK", 128),
                       ("OS", 128), ("NBD", 128), ("SH", 128), ("SH3", 128), ("D01", 128),
-                      ("SH7", 128), ("KC", 256), ("KCON", 128), ("MSK", 128), ("EL", 256), ("QM", 192), ("SIX", 128), ("CK", 128),
+                      ("SH7", 128), ("KC", 256), ("KCON", 128), ("MSK", 128), ("EL", 256), ("SIX", 128), ("CK", 128),
                       ("RST", 256), ("GM0", 528), ("GM1", 528), ("CVX", 128), ("OFR", 128), ("CC", 8),
-                      ("CZ", 128), ("KK0", 384), ("KK1", 384), ("CB0", 384), ("CB1", 384),
+                      ("KK0", 384), ("KK1", 384), ("CB0", 384), ("CB1", 384),
                       ("GE", 384), ("GT", 384), ("HIF", 256), ("RZ", 512), ("WW", 512), ("SEND0", 128), ("SEND1", 128)]),
         ("int32", [("PI", 1), ("CI", 144), ("ti", 8), ("KI", 512), ("SELR", 208), ("SELO", 208),
                    ("raw", 256), ("VI", 256), ("QN", 256), ("MA", 80)]),
-        ("uint16", [("SL1", 208), ("SL2", 208), ("PL", 256), ("QL", 1024), ("LOL", 256), ("BC", 8), ("OFF", 24)]),
-        ("float16", [("cd", 4 * 2048)]),
-        ("float32", [("TT", FW), ("GX0", 2048), ("GX1", 2048), ("ID32", 128), ("SK", 768), ("MX", 24), ("CO", 1024), ("SC", 1024),
+        ("uint16", [("SL1", 208), ("SL2", 208), ("PL", 256), ("QL", 1024), ("QS", 256), ("LOL", 256), ("BC", 8), ("OFF", 24)]),
+        ("float16", [("cd", 4 * 2048), ("cy", 2048), ("cs", 2048), ("CF", 1024), ("NG", 128)]),
+        ("float32", [("TT", FW), ("GX0", 2048), ("GX1", 2048), ("ID32", 128), ("NI32", 128), ("SK", 768), ("MX", 24), ("CO", 1024), ("SC", 1024),
                      ("NUM", 256), ("T0", 256), ("M1", 256), ("YP", 256), ("YS", 768), ("cols", 16), ("WC", 8)])]:
     for _n, _w in _l:
         SCRATCH[_n] = ("sbuf", [128, _w], _d)
+PACK = {}
+for _n in ("W1 W8 W16 WB WD WS WX YSM WG ZERO ONES ID NID N64 N8 IDK OS NBD SH SH3 D01 SH7 KC KCON MSK SIX CK RST CVX OFR CC "
+           "LEs LE LE1 LE2 LE3 I5 I16 WO WN WE W8K W16K KCK RSK CE").split():
+    PACK[_n] = ("KB", sum(SCRATCH[_m][1][1] for _m in PACK))
+SCRATCH["KB"] = ("sbuf", [128, sum(SCRATCH[_m][1][1] for _m in PACK)], "bfloat16")
+for _n in PACK:
+    del SCRATCH[_n]
+SAME = {"SR": "DS", "T3": "DC", "T2": "cv"}
 NBANK = 8
 for _j in range(NBANK):
     SCRATCH["PB%d" % _j] = ("psum", [128, 512], "float32")
 
-NDMA = 40
+NDMA = 64
 SEMAPHORES = (["sv", "ss", "st", "sg"] + ["d%d" % j for j in range(NDMA)]
               + ["%s%d%d" % (a, t, c) for a in ("ar", "lc") for t in range(R) for c in range(2 if (t, 0) in SPLIT else 1)])
 ALL = 0xFFFF
@@ -110,7 +137,7 @@ def schedule(ops):
     nl = {}
     for z in held:
         nl[z] = nl.get(z, 0) + 1
-    qs, mate = [o["q"] for o in ops], [o.get("mate", -1) for o in ops]
+    qs, mate = [o["q"] for o in ops], [o.get("mate", ()) for o in ops]
     short = []
     for i in range(n):
         far = set(j for k in need[i] if gap[k, i] for j in need[k] if gap[j, k] >= gap.get((j, i), 0.0))
@@ -143,7 +170,7 @@ def schedule(ops):
                 b = banks.pop(k)
                 if b[0] > t:
                     t, y = b
-            free[q] = fin[i] = t = t + costs[i][q] - (0.055 if prev[q] == mate[i] else 0.0)
+            free[q] = fin[i] = t = t + costs[i][q] - (0.055 if prev[q] in mate[i] and y == prev[q] else 0.0)
             prev[q], why[i] = i, y
             if z is not None:
                 if z not in ends or t + wk > ends[z][0]:
@@ -184,18 +211,27 @@ def schedule(ops):
                 qs[i] = min(costs[i], key=lambda q: fit(lines[q], t, costs[i][q])[0] + costs[i][q] * (1 + lean[0])
                             + lean[1] * "GSV".index(q))
             q = qs[i]
-            c = costs[i][q]
-            s, p = fit(lines[q], t, c)
-            lines[q][0].insert(p, s)
-            lines[q][1].insert(p, s + c)
-            start[i], fin[i] = s, s + c
+            c, (a, b) = costs[i][q], lines[q]
+            if b and b[-1] > t:
+                t, p = fit((a, b), t, c)
+                a.insert(p, t)
+                b.insert(p, t + c)
+            else:
+                a.append(t)
+                b.append(t + c)
+            start[i], fin[i] = t, t + c
         return start, fin
 
-    ref = [90.0 * k[0] * k[1] for k in KINDS]
+    ref = SCALES
 
     def value(order):
         got = seen_plays[:] = [play(order, k) for k in kinds]
-        return 1e9 if None in got else sum((r[0] + EPS * sum(r[1]) / n) / x for r, x in zip(got, ref))
+        return 1e9 if None in got else sum((r[0] + EPS * sum([r[1][i] for i in live]) / len(live)) / x for r, x in zip(got, ref))
+
+    live = set()
+    for i in range(n):
+        if ops[i]["kind"] == "d" and not ops[i]["r"] or need[i] & live:
+            live.add(i)
 
     rng, seen_plays, chain = np.random.default_rng(SEED), [], []
     free = [i for i in range(n) if len(ops[i]["cost"]) > 1]
@@ -203,7 +239,7 @@ def schedule(ops):
     start = [0.0] * n
     for i in range(n):
         start[i] = max([0.0] + [start[j] + kinds[0][0][j][qs[j]] + d for j, d in kinds[0][2][i]])
-    order, now, top, best, last = list(range(n)), 1e9, 1e9, None, [1e9]
+    order, now, top, best, last = list(range(n)), 1e9, 1e9, None, [1e9] * 3
     if AIM:
         start, aim = [99.0] * n, {}
         for q, names in AIM.items():
@@ -212,14 +248,14 @@ def schedule(ops):
                 if name[0] == "@":
                     t = float(name[1:])
                 for i in order:
-                    if ops[i]["tag"] == name:
+                    if ops[i]["tag"] == name and q in ops[i]["cost"]:
                         qs[i], aim[i] = q, t
                         t += kinds[0][0][i][q]
         for i in order[::-1]:
             start[i] = min([aim.get(i, 99.0)] + [start[j] - d - kinds[0][0][i][qs[i]] for j, d in kinds[0][3][i]])
         start = lay(sorted(order, key=lambda i: (start[i], i)), kinds[0], False, set(free) - set(aim), (0.5, 0.0))[0]
     for it in range(LAYS):
-        c = 0
+        c = LAYK[it % len(LAYK)]
         kind, old = kinds[c], qs[:]
         r = rng.random(8).tolist()
         t0, wide, amp = r[0] * 80 - 3, 1 + WIDE * r[1], AMP * r[2] ** 2
@@ -253,7 +289,7 @@ def schedule(ops):
             s, fin = lay(sorted(order, key=lambda i: (-fin[i], -i)), kind, True, loose if it & 1 else (), lean)
             s, fin = lay(sorted(order, key=lambda i: (-fin[i], i)), kind, False, (), lean)
         room = -LHEAT * (1 - it / LAYS) * math.log(1 - rng.random())
-        if max(x + y for x, y in zip(fin, kind[1])) > last[0] + 0.6 + room * ref[0]:
+        if max(x + y for x, y in zip(fin, kind[1])) > last[c] + 0.6 + room * ref[0]:
             qs[:] = old
             continue
         late, line, end = s[:], ([], []), max(fin) + 9
@@ -266,7 +302,7 @@ def schedule(ops):
         cand = sorted(order, key=lambda i: (late[i], i))
         val = value(cand)
         if val <= now + room:
-            now, start, last = val, s, seen_plays[0] or [1e9]
+            now, start, last = val, s, [(x or [1e9])[0] for x in seen_plays]
             chain = []
             for end, fin, why, bank in seen_plays if val < 1e8 else ():
                 v = max(order, key=lambda i: fin[i] + kind[1][i])
@@ -279,15 +315,328 @@ def schedule(ops):
         else:
             qs[:] = old
     order, qs[:] = best
+    order, qs[:], took = refine(order, qs, kinds, held, nl, mate, ref, rng)
     end, fin, why, bank = play(order, kinds[0])
+    bank = {z: x[0] for z, x in took.items()}
     cost = [kinds[0][0][i][qs[i]] for i in range(n)]
-    place = {i: p for p, i in enumerate(order)}
-    PLAN["apart"] = set(j for i in order for j in need[i] if mate[j] >= 0 and mate[j] != i and (
-        place[i] < place[mate[j]] or fin[i] - cost[i] < fin[mate[j]]))
+    place, takers, runs, lastq = {i: p for p, i in enumerate(order)}, [[] for _ in ops], {}, {}
+    for i in order:
+        for j in need[i]:
+            takers[j].append(i)
+    for i in order:
+        v = lastq.get(qs[i])
+        run = runs.get(v, [v])
+        if (v in mate[i] and all(fin[j] + d <= fin[run[0]] - cost[run[0]] + 0.1 for j, d in kinds[0][2][i])
+                and all(place[x] > place[i] and fin[x] - cost[x] >= fin[i] for j in run for x in takers[j])):
+            runs.pop(v, None)
+            runs[i] = run + [i]
+        lastq[qs[i]] = i
+    PLAN["runs"] = runs
     PLAN["bank"], PLAN["order"], PLAN["qs"] = bank, order, qs
     PLAN["who"] = {ops[i]["tag"]: qs[i] for i in free}
     PLAN["fin"], PLAN["why"], PLAN["cost"], PLAN["ends"] = fin, why, cost, [play(order, k)[0] for k in kinds]
     PLAN["pre"] = kinds[0][2]
+
+
+def refine_two(order, qs, kinds, held, nl, mate, ref, rng):
+    (c0, l0, p0, s0, w0), (c1, l1, p1, s1, w1) = kinds
+    n = len(order)
+    pre = [[(j, d, e) for (j, d), (_, e) in zip(a, b)] for a, b in zip(p0, p1)]
+    post = [[(j, d, e) for (j, d), (_, e) in zip(a, b)] for a, b in zip(s0, s1)]
+    up, down = [[j for j, _ in a] for a in p0], [[j for j, _ in a] for a in s0]
+    r0, r1 = 1.0 / ref[0], 1.0 / ref[1]
+    tau0, tau1 = SOFT, SOFT * 1.6
+    exp, log = math.exp, math.log
+
+    def play(calls, state, took):
+        line, banks, opened = dict(state[0]), state[1][:], dict(state[2])
+        for i in calls:
+            q = qs[i]
+            t, u, v = line[q]
+            for j, d, e in pre[i]:
+                if f0[j] + d > t:
+                    t = f0[j] + d
+                if f1[j] + e > u:
+                    u = f1[j] + e
+            z = held[i]
+            if z is not None:
+                o = opened.get(z)
+                if o is None:
+                    if not banks:
+                        return None
+                    x = banks.pop(0)
+                    took[z] = x[2:]
+                    if x[0] > t:
+                        t = x[0]
+                    if x[1] > u:
+                        u = x[1]
+                    o = (0.0, 0.0, x[2], nl[z])
+            if v in mate[i] and t == f0[v]:
+                t -= 0.055
+                u -= 0.055
+            f0[i] = t = t + c0[i][q]
+            f1[i] = u = u + c1[i][q]
+            line[q] = (t, u, i)
+            if z is not None:
+                a, b = max(o[0], t + w0), max(o[1], u + w1)
+                if o[3] == 1:
+                    opened.pop(z, None)
+                    banks.append((a, b, o[2], z))
+                    banks.sort()
+                else:
+                    opened[z] = (a, b, o[2], o[3] - 1)
+        return line, banks, opened
+
+    opener = {}
+    for i in range(n):
+        if held[i] is not None:
+            opener.setdefault(held[i], i)
+    first = ({q: (0.0, 0.0, -1) for q in "VSTGYR"}, [(0.0, 0.0, k, -1) for k in range(NBANK)], {})
+    f0, f1, g0, g1 = ([0.0] * n for _ in range(4))
+
+    def whole(order):
+        took = {}
+        if not play(order, first, took):
+            return 1e9, 0, 0, took
+        e0, e1 = max(map(sum, zip(f0, l0))), max(map(sum, zip(f1, l1)))
+        return e0 * r0 + e1 * r1, e0, e1, took
+
+    now, e0, e1, took = whole(order)
+    best = (now, order, qs[:], took)
+    starts = list(range(0, n - WIN + STRIDE, STRIDE))
+    for sweep in range(SWEEPS):
+        cool, off = HEAT * (1 - sweep / SWEEPS) ** 1.5, int(rng.random() * STRIDE)
+        for lo in starts[::-1] if sweep & 1 else starts:
+            lo = max(0, min(lo - off, n - WIN))
+            hi = lo + WIN
+            after, nxt = {x[1]: opener[z] for z, x in took.items()}, {}
+            for p in range(n - 1, lo - 1, -1):
+                i = order[p]
+                if p == hi - 1:
+                    lines = [(q, g0[j], g1[j]) for q, j in nxt.items()]
+                t, u, q = l0[i], l1[i], qs[i]
+                for j, d, e in post[i] + [(j, d, e) for j, d, e in ((after.get(held[i]), w0, w1), (nxt.get(q), 0, 0)) if j is not None]:
+                    t, u = max(t, d + g0[j]), max(u, e + g1[j])
+                nxt[q] = i
+                g0[i], g1[i] = t + c0[i][q], u + c1[i][q]
+            win, later, edge = order[lo:hi], set(order[hi:]), []
+            state = play(order[:lo], first, {})
+            end = play(win, state, {})
+            for p, i in enumerate(order[:hi]):
+                x = [(d + g0[j], e + g1[j]) for j, d, e in post[i] if j in later] + [(l0[i], l1[i])] * (l0[i] > 0)
+                if x:
+                    x, y = max(a for a, b in x), max(b for a, b in x)
+                    if p >= lo or f0[i] + x > e0 - 8 * tau0 or f1[i] + y > e1 - 8 * tau1:
+                        edge.append((i, x, y))
+            takers = [(g0[j], g1[j]) for j in order[hi:] if held[j] is not None and opener[held[j]] == j and
+                      (took[held[j]][1] < 0 or (took[held[j]][1] not in end[2] and opener[took[held[j]][1]] not in later))]
+            nexts = {z: (g0[after[z]], g1[after[z]]) for z in end[2] if z in after}
+
+            def soft(end):
+                a = b = 1e-30
+                for i, x, y in edge:
+                    a += exp((f0[i] + x - e0) / tau0)
+                    b += exp((f1[i] + y - e1) / tau1)
+                for (t, u), (x, y) in ([(end[0][q][:2], (x, y)) for q, x, y in lines] + [(o[:2], x) for o, x in zip(end[1], takers)]
+                                       + [(o[:2], nexts[z]) for z, o in end[2].items() if z in nexts]):
+                    a += exp((t + x - e0) / tau0)
+                    b += exp((u + y - e1) / tau1)
+                return tau0 * log(a) * r0 + tau1 * log(b) * r1
+
+            def again(calls, p):
+                p >>= 4
+                l = marks[:p + 1]
+                for p in range(16 * p, WIN, 16):
+                    l.append(play(calls[p:p + 16], l[-1], {}))
+                    if not l[-1]:
+                        return None
+                return l
+
+            marks = [state]
+            marks, h0, h1 = again(win, 0), f0[:], f1[:]
+            cur = low = soft(end)
+            old = keep = (win, [qs[i] for i in win])
+            wt = np.array([0.1 + exp(min(0.0, max(f0[i] - c0[i][qs[i]] + g0[i] - e0, (f1[i] - c1[i][qs[i]] + g1[i] - e1) * 0.7)) / 0.7)
+                           for i in win])
+
+
+def refine(order, qs, kinds, held, nl, mate, ref, rng):
+    (c0, lat, pre, post, wk), c1, c2 = kinds[0], kinds[1][0], kinds[2][0]
+    n = len(order)
+    up, down = [[j for j, _ in a] for a in pre], [[j for j, _ in a] for a in post]
+    r0, r1, r2 = (1.0 / x for x in ref)
+    exp, log = math.exp, math.log
+
+    def play(calls, state, took):
+        line, banks, opened = dict(state[0]), state[1][:], dict(state[2])
+        for i in calls:
+            q = qs[i]
+            t, u, s, v = line[q]
+            for j, d in pre[i]:
+                a, b, c = fin[j]
+                if a + d > t:
+                    t = a + d
+                if b + d > u:
+                    u = b + d
+                if c + d > s:
+                    s = c + d
+            z = held[i]
+            if z is not None:
+                o = opened.get(z)
+                if o is None:
+                    if not banks:
+                        return None
+                    x = banks.pop(0)
+                    took[z] = x[3:]
+                    t, u, s = max(t, x[0]), max(u, x[1]), max(s, x[2])
+                    o = (0.0, 0.0, 0.0, x[3], nl[z])
+            if v in mate[i] and t == fin[v][0]:
+                t, u, s = t - 0.055, u - 0.055, s - 0.055
+            t += c0[i][q]
+            u += c1[i][q]
+            s += c2[i][q]
+            fin[i], line[q] = (t, u, s), (t, u, s, i)
+            if z is not None:
+                x = (max(o[0], t + wk), max(o[1], u + wk), max(o[2], s + wk), o[3])
+                if o[4] == 1:
+                    opened.pop(z, None)
+                    banks.append(x + (z,))
+                    banks.sort()
+                else:
+                    opened[z] = x + (o[4] - 1,)
+        return line, banks, opened
+
+    opener = {}
+    for i in range(n):
+        if held[i] is not None:
+            opener.setdefault(held[i], i)
+    first = ({q: (0.0, 0.0, 0.0, -1) for q in "VSTGYR"}, [(0.0, 0.0, 0.0, k, -1) for k in range(NBANK)], {})
+    fin, way = [None] * n, [None] * n
+    plus = lambda d, x: (d + x[0], d + x[1], d + x[2])
+    most = lambda l: tuple(map(max, zip(*l)))
+
+    def whole(order):
+        took = {}
+        if not play(order, first, took):
+            return 1e9, None, took
+        e = most([plus(lat[i], fin[i]) for i in order[-80:]])
+        return e[0] * r0 + e[1] * r1 + e[2] * r2, e, took
+
+    now, ends, took = whole(order)
+    best = (now, order, qs[:], took)
+    starts = list(range(0, n - WIN + STRIDE, STRIDE))
+    for sweep in range(SWEEPS):
+        cool, off = HEAT * (1 - sweep / SWEEPS) ** 1.5, int(rng.random() * STRIDE)
+        for lo in starts[::-1] if sweep & 1 else starts:
+            lo = max(0, min(lo - off, n - WIN))
+            hi = lo + WIN
+            after, nxt = {x[1]: opener[z] for z, x in took.items()}, {}
+            for p in range(n - 1, lo - 1, -1):
+                i = order[p]
+                if p == hi - 1:
+                    lines = [(q, way[j]) for q, j in nxt.items()]
+                q = qs[i]
+                t, u, s = most([(lat[i],) * 3] + [plus(d, way[j]) for j, d in post[i] + [(after.get(held[i]), wk), (nxt.get(q), 0)]
+                                                  if j is not None])
+                nxt[q] = i
+                way[i] = (t + c0[i][q], u + c1[i][q], s + c2[i][q])
+            win, later, edge = order[lo:hi], set(order[hi:]), []
+            state = play(order[:lo], first, {})
+            end = play(win, state, {})
+            e0, e1, e2 = ends
+            k0, k1, k2 = 70.0 / SOFT / e0, 70.0 / SOFT / e1, 70.0 / SOFT / e2
+            for p, i in enumerate(order[:hi]):
+                x = [plus(d, way[j]) for j, d in post[i] if j in later] + [(lat[i],) * 3] * (lat[i] > 0)
+                if x and (p >= lo or max(a + b - c for a, b, c in zip(fin[i], most(x), ends)) > -8 * SOFT):
+                    edge.append((i, most(x)))
+            takers = [way[j] for j in order[hi:] if held[j] is not None and opener[held[j]] == j and
+                      (took[held[j]][1] < 0 or (took[held[j]][1] not in end[2] and opener[took[held[j]][1]] not in later))]
+            nexts = {z: way[after[z]] for z in end[2] if z in after}
+
+            def soft(end):
+                a = b = c = 1e-30
+                for x, y in ([(fin[i], y) for i, y in edge] + [(end[0][q], y) for q, y in lines] + list(zip(end[1], takers))
+                             + [(o, nexts[z]) for z, o in end[2].items() if z in nexts]):
+                    a += exp((x[0] + y[0] - e0) * k0)
+                    b += exp((x[1] + y[1] - e1) * k1)
+                    c += exp((x[2] + y[2] - e2) * k2)
+                return log(a) * r0 / k0 + log(b) * r1 / k1 + log(c) * r2 / k2
+
+            def again(calls, p):
+                p >>= 4
+                l = marks[:p + 1]
+                for p in range(16 * p, WIN, 16):
+                    l.append(play(calls[p:p + 16], l[-1], {}))
+                    if not l[-1]:
+                        return None
+                return l
+
+            marks = [state]
+            marks, kept = again(win, 0), fin[:]
+            cur = low = soft(end)
+            old = keep = (win, [qs[i] for i in win])
+            wt = np.array([0.1 + exp(max(fin[i][k] - c[i][qs[i]] + way[i][k] - ends[k] for k, c in enumerate((c0, c1, c2))) / 0.8)
+                           for i in win])
+            for v, r in zip(rng.choice(win, EACH, p=wt / wt.sum()).tolist(), rng.random((EACH, 7)).tolist()):
+                pv, flips, cand = win.index(v), [], win
+                at = pv
+                if r[1] < 0.3 and len(c0[v]) > 1:
+                    q = [x for x in c0[v] if x != qs[v]]
+                    q = q[int(r[2] * len(q))]
+                    flips.append((v, qs[v]))
+                    near = [i for i in win[max(0, pv - 25):pv + 25] if qs[i] == q and qs[v] in c0[i]] if r[3] < 0.4 else []
+                    if near:
+                        w = near[int(r[4] * len(near))]
+                        flips.append((w, q))
+                        qs[w], at = qs[v], min(at, win.index(w))
+                    qs[v] = q
+                if not flips or r[5] < 0.5:
+                    hops, q, step = 1 + int(5 * r[2] ** 3), qs[v], -1 if r[4] < 0.5 else 1
+                    p = pv + step
+                    while 0 <= p < WIN:
+                        if qs[win[p]] == q:
+                            hops -= 1
+                            if not hops:
+                                break
+                        p += step
+                    p, links = min(max(p, 0), WIN - 1), up if step < 0 else down
+                    seen, a, b = set(links[v]), [v], []
+                    for i in win[p:pv][::-1] if step < 0 else win[pv + 1:p + 1]:
+                        if i in seen:
+                            seen.update(links[i])
+                            a.append(i)
+                        else:
+                            b.append(i)
+                    if b:
+                        cand = win[:p] + a[::-1] + b[::-1] + win[pv + 1:] if step < 0 else win[:pv] + b + a + win[p + 1:]
+                        at = min(at, p)
+                    elif not flips:
+                        continue
+                l = again(cand, at)
+                if l:
+                    x = soft(l[-1])
+                    if x <= cur - cool * log(1 - r[6]):
+                        cur, win, marks, kept = x, cand, l, fin[:]
+                        if x < low:
+                            low, keep = x, (win, [qs[i] for i in win])
+                        continue
+                fin[:] = kept
+                for i, q in flips:
+                    qs[i] = q
+            for i, q in zip(*keep):
+                qs[i] = q
+            cand = order[:lo] + keep[0] + order[hi:]
+            got = whole(cand)
+            if got[0] <= now + 2 * cool + 0.0005:
+                order = cand
+                now, ends, took = got
+                if now < best[0]:
+                    best = (now, order, qs[:], took)
+            else:
+                for i, q in zip(*old):
+                    qs[i] = q
+                whole(order)
+    return best[1:]
 
 
 def rank_program(g, core, T, topo):
@@ -303,6 +652,7 @@ def record(g, core, T, topo, rank, banks):
     A = AluOpType
     AF = ActivationFunctionType
     ops = []
+    sg = 16 if BYDMA else 1
     nlease = [0]
     at = [""]
 
@@ -311,9 +661,11 @@ def record(g, core, T, topo, rank, banks):
         return nlease[0]
 
     def X(name, c0, c1, step=1, p=None, rows=ALL):
-        t = T["PB%d" % banks.get(name, 0)] if isinstance(name, int) else T[name]
+        name = SAME.get(name, name)
+        buf, o = PACK.get(name, (name, 0))
+        t = T["PB%d" % banks.get(name, 0)] if isinstance(name, int) else T[buf]
         p0, p1 = p if p else (0, 128)
-        ap = t[p0:p1, c0:c1] if step == 1 else t[p0:p1, c0:c1:step]
+        ap = t[p0:p1, o + c0:o + c1] if step == 1 else t[p0:p1, o + c0:o + c1:step]
         return (ap, [(name, c0, c0 + (c1 - c0 - 1) // step * step + 1, step, rows)])
 
     def ind(win, off):
@@ -331,6 +683,12 @@ def record(g, core, T, topo, rank, banks):
         run[0].update(kind="g", tag=tag or run[0]["tag"], r=list(dict.fromkeys(x for o in run for x in o["r"])), fn={o["q"]: o["fn"] for o in run},
                       cost={o["q"]: o["cost"][o["q"]] for o in run})
 
+    def run(k, tag):
+        l = ops[-k:]
+        del ops[len(ops) - k + 1:]
+        l[0].update(kind="m", tag=tag, fn=[o["fn"] for o in l], cost={l[0]["q"]: sum(o["cost"][o["q"]] for o in l)},
+                    r=list(dict.fromkeys(x for o in l for x in o["r"])), w=[x for o in l for x in o["w"]])
+
     def width(x):
         return x[0].shape[1]
 
@@ -339,7 +697,7 @@ def record(g, core, T, topo, rank, banks):
         rec("c", q, outs, ins, fn, 0.06 + n * GAT * CYC if len(ins[0] if ins else ()) > 2 else 0.01 + max(64, cyc * n) * CYC)
 
     def wide(x):
-        return lease(x[1][0]) is not None or SCRATCH[x[1][0][0]][2] not in ("bfloat16", "uint16", "float16")
+        return lease(x[1][0]) is not None or x[1][0][0] not in PACK and SCRATCH[x[1][0][0]][2] not in ("bfloat16", "uint16", "float16")
 
     def two(*xs):
         return not any(wide(x) for x in xs)
@@ -384,10 +742,17 @@ def record(g, core, T, topo, rank, banks):
     def gather(tag, o, i):
         move(o, i, tag=tag)
 
-    def pair(a, b, wide):
-        wide()
-        fn = ops.pop()["fn"]
-        ops[a]["mate"], ops[b]["mate"], ops[a]["both"], ops[b]["both"] = b, a, fn, fn
+    def pieces(make, a, b, n, name, behind=None):
+        l = []
+        for c in range(a, b, n):
+            make(c, c + n)
+            l.append(len(ops) - 1)
+            ops[-1].update(tag=name + str(c // n), span=(c, c + n), make=make, mate=())
+            if behind:
+                behind(c, c + n)
+        for i, j in zip(l, l[1:]):
+            ops[i]["mate"] += (j,)
+            ops[j]["mate"] += (i,)
 
     def iota(o, pattern, base, cm, fl=False):
         c = 0.14 + 2 * width(o) * CYC
@@ -413,13 +778,20 @@ def record(g, core, T, topo, rank, banks):
     def acc(lst, first=True, last=True):
         mms([m[:3] + (first and n == 0, last and n == len(lst) - 1) + m[3:] for n, m in enumerate(lst)])
 
+    def group(b, head, rest, n, after):
+        acc(head, True, False)
+        ops[-1]["r"] += after[1]
+        for c in range(0, len(rest), n):
+            acc(rest[c:c + n], False, False)
+            ops[-1]["fn"] = b
+
     def dma(q, outs, ins, pairs, lat=2.3, tag=None):
         rec("d", q, outs, ins, None, 0.06 * len(pairs), lat, pairs)
         ops[-1]["tag"] = tag
 
     dma("Y", [X("SELR", 0, 208)], [], [(T.SELR[:], T.sel0[:])], 2.5, "sel")
-    dma("Y", [X("F", 16, 16 + CUT)], [], [(T.F[:, 16:16 + CUT], T.front[:, 0:CUT])], LAT[1], "fr0")
-    dma("Y", [X("F", 16 + CUT, 16 + I0)], [], [(T.F[:, 16 + CUT:16 + I0], T.front[:, CUT:I0])], LAT[2], "fr1")
+    for j, (a, b, lat) in enumerate(FRONT):
+        dma("Y", [X("F", 16 + 208 * a, 16 + 208 * b)], [], [(T.F[:, 16 + 208 * a:16 + 208 * b], T.front[:, 208 * a:208 * b])], lat, "fr%d" % j)
     dma("Y", [X("raw", 0, 256)], [], [(T.raw[:], T.par[:])], LAT[0], "par")
 
     ncol = [0]
@@ -436,7 +808,18 @@ def record(g, core, T, topo, rank, banks):
     iota(X("CI", 0, 144), [[1, 144]], 0, 0)
     iota(X("LB", 0, 256), [[0, 4], [1, 64]], 16, 0, True)
     iota(X("HB", 0, 256), [[1, 4], [0, 64]], 129, 0, True)
-    vset(X("PT", 0, FW), 0.0)
+    vset(X("T2", 0, 1040), 0.0)
+
+    move(X("CF", 0, 1024), X("T2", 0, 1024), TOP, 0.0, "CF")
+
+    def zero(nm, a, b):
+        vset(X(nm, a, b), 0.0)
+        act(X(nm, a, b), X("T2", 0, b - a))
+        gset(X(nm, a, b), 0)
+        either("0%s%d" % (nm, a // 768), 3)
+
+    for a in range(0, FW, 1040):
+        zero("PT", a, min(FW, a + 1040))
     uf, gf, zf, u4, u3, zs = col(), col(), col(), col(), col(), col()
     vts(ti[0], PI, 15, A.bitwise_and)
     vts(ti[1], PI, 4, A.arith_shift_right)
@@ -457,17 +840,27 @@ def record(g, core, T, topo, rank, banks):
         gsel(o, Z(width(o)), [[-a, n] for a, n in pattern], A.is_gt, c, 0, -1)
         gsel(o, o, [[-a, n] for a, n in pattern], A.is_ge, 0.0, 15, -1)
 
+    def fill(o, c, i):
+        vset(o, float(c))
+        act(o, i, scale=float(c))
+        if c:
+            gsel(o, i, [[0, width(o)]], A.is_gt, float(c), 0, 0)
+        else:
+            gset(o, 0)
+        either(None, 3)
+
     def prow(r, buf, n, tab="PT"):
-        dma("Y", [X(tab, 16, 16 + 16 * n, rows=1 << r)], [X(buf, 0, n)], [(T[tab][r::16, 16:16 + 16 * n], T[buf][:, 0:n])],
+        dma("Y", [X(tab, 16, 16 + 16 * n, rows=1 << r)], [X(buf, 0, n)], [(T[SAME.get(tab, tab)][r::16, 16:16 + 16 * n], T[buf][:, 0:n])],
             LAT[3], "row%d" % r)
 
     vts(X("SHB", 0, 208), X("SELR", 0, 208), HIGH - 31.5, A.add)
     vts(X("SELO", 0, 208), X("SELR", 0, 208), 63, A.bitwise_and)
     vts(X("SLB", 0, 208), X("SELO", 0, 208), 16.0, A.add)
     for j, buf in enumerate(("SHB", "SLB")):
-        dma("Y", [X("SR", 16, 16 + I0, rows=1 << j)], [X(buf, 0, 208)], [(T.SR[8 * j:8 * j + 8, 16:16 + I0], T[buf][:, 0:208])],
+        dma("Y", [X("SR", 16, 16 + I0, rows=1 << j)], [X(buf, 0, 208)], [(T[SAME["SR"]][8 * j:8 * j + 8, 16:16 + I0], T[buf][:, 0:208])],
             LAT[3], "sr%d" % j)
-    vset(X("T2", 0, 16 + I0), 0.0)
+    for a in range(1040, 16 + I0, 768):
+        zero("T2", a, a + 768)
     prow(2, "SHB", 208, "T2")
     prow(10, "SLB", 208, "T2")
     prow(1, "SHB", 208)
@@ -481,66 +874,58 @@ def record(g, core, T, topo, rank, banks):
     w = [X("WC", d, d + 1) for d in range(8)]
     for d in (1, 2, 3):
         act(X("LE%d" % d, 0, 144), X("LE", 0, 144), scale=w[d])
-    for nm in ("F", "TT") if ADD else ("F", "FS", "TT"):
+    for nm in ("F", "TT"):
         act(X(nm, 0, 16), Z(16))
 
-    def lists(src, s0, lst, l0, n, le, p=None):
+    def lists(src, s0, n, le, p=None):
         b = psum()
         acc([(X(b, 0, n), LE(le, e, p), X(src, s0 + e, s0 + 16 * n, 16, p=p)) for e in range(16)])
-        vts(X(lst, l0, l0 + n), X(b, 0, n), -HIGH, A.add)
+        return b
 
     for j in (0, 1):
-        lists("SR", 16 + CUT * j, "SL1", 104 * j, 104, "LEs", (0, 16))
+        vts(X("SL1", 104 * j, 104 * j + 104), X(lists("SR", 16 + CUT * j, 104, "LEs", (0, 16)), 0, 104), -HIGH, A.add)
     b = psum()
-    for j in (0, 1):
-        acc([(X(b, 0, 208), LE("LE", e), X("F", 16 + 208 * e, 224 + 208 * e)) for e in range(8 * j, 8 * j + 8)], j == 0, j == 1)
+    for c, d, _ in FRONT:
+        acc([(X(b, 0, 208), LE("LE", e), X("F", 16 + 208 * e, 224 + 208 * e)) for e in range(c, d)], c == 0, d == 16)
     vcopy(X("SCH", 0, 208), X(b, 0, 208))
     vtt(X("SCL", 0, 208), X(b, 0, 208), X("SCH", 0, 208), A.subtract)
     prow(5, "SCH", 208, "T2")
-    prow(13, "SCL", 208, "T2")
     prow(7, "SCH", 208)
+    prow(13, "SCL", 208, "T2")
     prow(15, "SCL", 208)
 
     def shift(dst, d0, moves):
         dma("Y", [X("PT", 16, 16 + I0, rows=sum(257 << b for a, b in moves))], [X(dst, d0, d0 + I0)],
-            [(T.PT[b::8, 16:16 + I0], T[dst][a::8, d0:d0 + I0]) for a, b in moves], LAT[4])
+            [(T.PT[b::8, 16:16 + I0], T[SAME[dst]][a::8, d0:d0 + I0]) for a, b in moves], LAT[4])
 
     n = 208 // PARTS
-    for j in range(PARTS):
-        o = X("PT", 16 + 16 * n * j, 16 + 16 * n * j + 16 * n)
-        vtt(o, ind(X("T2", 0, 16 + I0), X("SL1", n * j, n * j + n)), o, A.add)
-        ops[-1]["tag"] = "a%d" % j
+    pt = lambda a, b: X("PT", 16 + 16 * a, 16 + 16 * b)
+    pieces(lambda a, b: vtt(pt(a, b), ind(X("T2", 0, 16 + I0), X("SL1", a, b)), pt(a, b), A.add), 0, 208, n, "a")
     for j in (0, 1):
-        lists("PT", 16 + CUT * j, "SL2", 104 * j, 104, "LE2")
-    for j in range(PARTS):
-        gather("b%d" % j, X("T3", 16 * n * j, 16 * n * j + 16 * n), ind(X("PT", 0, 16 + I0), X("SL2", n * j, n * j + n)))
-    for j in (0, 1) if not ADD else ():
-        move(X("FS", 16 + CUT * j, 16 + CUT * j + CUT), X("F", 16 + CUT * j, 16 + CUT * j + CUT), scale=1.0 / 1024, tag="u%d" % j)
-    for j in range(PARTS):
-        c0 = 16 + 16 * n * j
-        o = X("TT", c0, c0 + 16 * n)
-        if ADD:
-            move(o, ind(X("F", 0, 16 + I0), X("SL1", n * j, n * j + n)), scale=1.0 / 1024, tag="t%d" % j)
-            dma("G", [o], [o], [(o[0], T.front[:, c0 - 16:c0 - 16 + 16 * n])], ADD + 0.4 * j, "add%d" % j)
-            ops[-1]["cost"]["G"] = 1.0 if j else 2.0
-        else:
-            vtt(o, ind(X("FS", 0, 16 + I0), X("SL1", n * j, n * j + n)), X("F", c0, c0 + 16 * n), A.add)
-            ops[-1]["tag"] = "t%d" % j
+        vts(X("SL2", 104 * j, 104 * j + 104), X(lists("PT", 16 + CUT * j, 104, "LE2"), 0, 104), -HIGH, A.add)
+    pieces(lambda a, b: move(X("T3", 16 * a, 16 * b), ind(X("PT", 0, 16 + I0), X("SL2", a, b))), 0, 208, n, "b")
+    tt = lambda a, b: X("TT", 16 + 16 * a, 16 + 16 * b)
+
+    def own(a, b):
+        dma("G", [tt(a, b)], [tt(a, b)], [(tt(a, b)[0], T.front[:, 16 * a:16 * b])], ADD + 0.4 * a / n, "add%d" % (a // n))
+        ops[-1]["cost"]["G"] = 1.0 if a else 2.0
+
+    pieces(lambda a, b: move(tt(a, b), ind(X("F", 0, 16 + I0), X("SL1", a, b)), scale=1.0 / 1024), 0, 208, n, "t", own)
 
     for h in (0, 1):
         vts(X("PL", 128 * h, 128 * h + 128), X("raw", h, 256, 2), 16.0, A.add)
-        vts(X("NUM", 128 * h, 128 * h + 128), X("raw", h, 256, 2), 16.0, A.add)
+        move(X("NUM", 128 * h, 128 * h + 128), X("raw", h, 256, 2), 16.0)
     C8 = X("CI", 0, 8)
     vts(X("W1", 0, 8), C8, gf, A.is_equal)
     vcopy(X("BC", 0, 8), C8)
     vset(ONES, 1.0)
     iota(X("CC", 0, 8), [[-2, 8]], 0, 0, True)
     iota(X("KCON", 0, 128), [[0, 8], [-1, 16]], 15, 0, True)
-    act(X("KC", 0, 128), X("KCON", 0, 128))
-    for j in (0, 1):
-        act(X("RST", 128 * j, 128 * j + 128), ONES, scale=0.0)
-    act(X("KC", 128, 256), ONES, scale=0.0)
-    act(X("RST", 0, 256, 16), X("ONES", 0, 16), scale=-BIG)
+    move(X("KC", 0, 128), X("KCON", 0, 128))
+    fill(X("KC", 128, 256), 0.0, ONES)
+    for nm, c in (("RST", -BIG), ("RSK", -128 * BIG)):
+        fill(X(nm, 0, 256), 0.0, X("CF", 0, 256))
+        fill(X(nm, 0, 256, 16), c, X("ONES", 0, 16))
     u15, u16 = col(), col()
     act(u15, uf, AF.Identity, bias=15.0, scale=-1.0)
     vts(X("MSK", 0, 128), X("KCON", 0, 128), u15, A.is_equal)
@@ -548,52 +933,52 @@ def record(g, core, T, topo, rank, banks):
     for j in (0, 1):
         act(X("W16", 8 * j, 8 * j + 8), X("W1", 0, 8), scale=16.0)
     line(ID, 1.0, [[-1, 128]], 0)
-    for o, c in ((NID, -1.0), (ID32, 1.0), (X("N64", 0, 128), -64.0), (X("IDK", 0, 128), 1.0 / 1024)):
+    for o, c in ((NID, -1.0), (ID32, 1.0), (X("N64", 0, 128), -64.0), (X("IDK", 0, 128), 1.0 / 16384),
+                 (X("I16", 0, 128), 1.0 / 16), (X("NI32", 0, 128), -1.0), (X("I5", 0, 128), 5.0 * PR)):
         line(o, c, [[-1, 128]], 0)
         act(o, ID, scale=c)
         either(None, 2)
     line(X("N8", 0, 128), -1.0, [[-1, 128]], 8)
     block(X("NBD", 0, 128), -1.0, [[-16, 8], [0, 16]])
     act(X("WG", 0, 128), X("NBD", 0, 128), scale=2 * BIG)
-    for nm, c in (("LEc", BIG), ("LEd", 2 * BIG)):
-        act(X(nm, 0, 144), X("LE", 0, 144), scale=c)
+    vts(X("NG", 0, 128), ID, -1025.0 / 16384, A.mult)
+    act(X("WO", 0, 64), X("NBD", 1, 128, 2), scale=-1.0 / 16)
     act(X("W8", 0, 16), X("W16", 0, 16), scale=0.5)
-    for nm, c in (("WB", BIG), ("WD", -2 * BIG)):
+    act(X("W8K", 0, 16), X("W16", 0, 16), scale=PR / 2)
+    act(X("W16K", 0, 16), X("W16", 0, 16), scale=float(PR))
+    iota(X("KCK", 0, 256), [[0, 16], [-PR, 16]], 15 * PR, 0, True)
+    for nm, c in (("WB", BIG), ("WD", -2 * sg * BIG), ("WN", -1.0 / 16)):
         act(X(nm, 0, 8), X("W1", 0, 8), scale=c)
     for d in range(1, 5):
         act(X("WX", 8 * (4 - d), 8 * (5 - d)), X("W1", 0, 8), scale=w[d])
     act(X("YSM", 0, 8), X("W1", 0, 8), scale=w[0])
     for j in (0, 1):
         vts(X("WS", 8 * j, 8 * j + 8), X("W1", 0, 8), w[5 + 2 * j], A.mult, 2 * BIG, A.mult)
-    iota(X("CVX", 0, 128), [[512, 128]], -5120, 0, True)
+    iota(X("CVX", 0, 128, p=(0, 64), rows=1), [[1024, 128]], -10240, 0, True)
     iota(X("OFR", 0, 128), [[-512, 128]], 0, 0, True)
-    act(X("CK", 0, 128, p=(0, 64), rows=1), X("ONES", 0, 128, p=(0, 64)), scale=24576.0 * 1024)
-    act(X("CK", 0, 128, p=(64, 128), rows=2), X("ONES", 0, 128, p=(64, 128)), scale=16.0 * 1024)
-    for o, c in ((X("CZ", 0, 128), -(4 * BIG + 5 * PR) / 128), (X("SIX", 0, 128), 6 * BIG / 128), (X("OS", 0, 128), 1.0 / PR),
-                 (X("QM", 0, 64), 0.0), (X("QM", 64, 128), 1.0), (X("QM", 128, 192), 0.0)):
-        gsel(o, Z(width(o)), [[0, width(o)]], A.is_gt, c, 0, 0)
-        act(o, X("ONES", 0, width(o)), scale=c)
-        either(None, 2)
+    for nm, a, b in [("CK", 24576 * 1024, -16 * 1024), ("CVX", 0, -768)] + [("CE", 16384 * 1024, 32 * 1024)] * bool(BYDMA):
+        if a:
+            fill(X(nm, 0, 128, p=(0, 64), rows=1), a, X("ONES", 0, 128, p=(0, 64)))
+        fill(X(nm, 0, 128, p=(64, 128), rows=2), b, X("ONES", 0, 128, p=(64, 128)))
+    fill(X("SIX", 0, 128), 6 * BIG / 128, ONES)
+    fill(X("OS", 0, 128), 1.0 / PR, ONES)
     cd = {d: col() for d in (1, 2, 3)}
     for d in cd:
-        iota(cd[d], [[0, 1]], PR * (5 - d), int(BIG), True)
+        iota(cd[d], [[0, 1]], -PR * d, int(BIG), True)
     for j in (0, 1):
-        ma = X("MA", 8 + 36 * j, 41 + 36 * j)
-        gset(X("GM%d" % j, 0, 528), 0)
-        iota(ma, [[2, 33]], 128 + j, -1)
-        vts(ma, ma, 15, A.bitwise_and)
-        vts(X("GM%d" % j, 15, 528, 16), ma, 0.0, A.is_equal, -256.0, A.add)
+        fill(X("GM%d" % j, 0, 528), 0.0, X("CF", 0, 528))
+        move(X("GM%d" % j, 15, 528, 16), X("MSK", j, j + 66, 2), -256.0)
     iota(X("KI", 0, 256), [[5, 2], [10, 128]], 0, 37)
     iota(X("KI", 256, 512), [[1, 2], [2, 128]], 0, 1)
     vts(X("KI", 0, 256), X("KI", 0, 256), 255, A.bitwise_and)
     vts(X("KI", 256, 512), X("KI", 256, 512), 127, A.bitwise_and)
     for h in (0, 1):
         iota(X("KK%d" % h, 0, 128), [[2, 128]], h, 0, True)
-        vcopy(X("KK%d" % h, 128, 256), X("KI", 128 * h, 128 * h + 128))
-        vcopy(X("KK%d" % h, 256, 384), X("KI", 256 + 128 * h, 384 + 128 * h))
+        move(X("KK%d" % h, 128, 256), X("KI", 128 * h, 128 * h + 128))
+        move(X("KK%d" % h, 256, 384), X("KI", 256 + 128 * h, 384 + 128 * h))
+    starts = lambda t: [I0 + NB * t - (16 if t + 1 == R else 0) + c - PR for c in (16, 2016, 208)]
     for t in range(R):
-        B = I0 + NB * t - (16 if t + 1 == R else 0)
-        for j, c in enumerate((B + 16 - PR, B + 2016 - PR, B + 208 - PR)):
+        for j, c in enumerate(starts(t)):
             iota(X("CB%d" % t, 128 * j, 128 * j + 128, p=(0, 2)), [[0, 128]], c // 256 * 256, c % 256 - c // 256 * 256, True)
     line(X("SH", 0, 128), 1.0, [[-1, 128]], 1)
     for c in (0, 5):
@@ -607,9 +992,9 @@ def record(g, core, T, topo, rank, banks):
         gset(X("SH7", 0, 128), 0)
         line(X("SH7", 5, 128, 8), 1.0, [[-8, 16]], -7)
 
-    def choose(z, data):
+    def choose(z, data, after):
         zs, b = (128 * z, 128 * z + 128), psum()
-        acc([(X(b, 0, 256), X("ONES", 0, 128, p=(0, 1)), X("KC", 0, 256, p=(0, 1)))] + data(b))
+        group(b, [(X(b, 0, 256), X("ONES", 0, 128, p=(0, 1)), X("KC", 0, 256, p=(0, 1)))], data(b), 8 if z == 2 else 16, after)
         scan(X("SK", 256 * z, 256 * z + 256), X("RST", 0, 256), X(b, 0, 256), 0.0, A.add, A.max)
         mx = X("MX", 8 * z, 8 * z + 8)
         vtt(mx, X("SK", 256 * z + 15, 256 * z + 128, 16), X("SK", 256 * z + 143, 256 * z + 256, 16), A.subtract)
@@ -630,24 +1015,27 @@ def record(g, core, T, topo, rank, banks):
             pd = psum()
             acc([(X(pd, 128 * i, 128 * i + 128), NID, X(src, 4 * j + i, 2048, 16)) for i in range(4)], True, False)
             acc([(X(pd, 128 * i, 128 * i + 128), ID, gm) for i in range(4)], False, True)
-            o = X("cz", 2048 * z + 512 * j, 2048 * z + 512 * j + 512)
+            o = X("cz", 512 * j, 512 * j + 512)
             act(o, X(pd, 0, 512), AF.Sign, bias=0.5)
             vts(o, X(pd, 0, 512), 0.0, A.is_ge, 0.5, A.subtract)
             either("z%s%d%d" % (src[1], z, j), 2)
 
     def grow(src, n, c0, y0, tt, fronts, more):
         if tt + 1 < R:
-            b, st, l = psum(), n // 128, []
+            b, st, l, late = psum(), n // 128, [], []
             for j, x in enumerate(fronts):
-                if j in dict(more):
-                    l += [(X(b, j, n, st), X("SH7", 0, 128), X(src, j, n, st)), (X(b, j, n, st), X("SH3", 0, 128), dict(more)[j])]
-                    continue
-                o, hh = X(psum(), 0, 128), X("HH", 128 * j, 128 * j + 128)
-                acc([(o, LE("LE", 5), x)])
-                move(hh, o)
-                l += [(X(b, j, n, st), ID, hh), (X(b, j, n, st), X("N8", 0, 128), hh), (X(b, j, n, st), LE("LE", 13), x)]
+                a = EARLY if j in dict(more) else 0
+                if a:
+                    l += [(X(b, j, st * a, st), X("SH7", 0, 128), X(src, j, st * a, st)), (X(b, j, st * a, st), X("SH3", 0, 128), dict(more)[j])]
+                if a < 128:
+                    x = X(x[0], x[1] + a, x[1] + 128)
+                    o, hh, y = X(psum(), 0, 128 - a), X("HH", 128 * j + a, 128 * j + 128), X(b, j + st * a, n, st)
+                    acc([(o, LE("LE", 5), x)])
+                    move(hh, o)
+                    l.append((y, LE("LE", 13), x))
+                    late += [(y, ID, hh), (y, X("N8", 0, 128), hh)]
             o = X(b, 0, n)
-            acc([(o, X("SH", 0, 128), X(src, 0, n)), (o, X("D01", 0, 128), X("PT", c0, c0 + n))] + l)
+            group(b, [(o, X("D01", 0, 128), X("PT", c0, c0 + n)), (o, X("SH", 0, 128), X(src, 0, n))] + l, late, 9, X(src, 0, n))
             move(X("PT", c0, c0 + n), o)
         y = X(psum(), 0, n, p=(0, 8))
         acc([(y, X("YSM", 0, 8), X(src, 0, n))])
@@ -656,33 +1044,39 @@ def record(g, core, T, topo, rank, banks):
 
     def pairs(out, own, far):
         o = X(psum(), 0, 128)
-        acc([(o, ID, own), (o, X("IDK", 0, 128), far)])
-        move(out, o)
+        acc([(o, X("I16", 0, 128), own), (o, X("IDK", 0, 128), far)])
+        move(out, o, scale=16.0 / sg)
 
     def come(tt):
         cc = 16 + I0 + NB * tt + L
         at[0] = "%d2" % tt
         signs(2, "f%d0" % tt, X("F", cc, cc + 128))
         tg = ["z%d2%d" % (tt, j) for j in range(4)]
-        choose(2, lambda b: [(X(b, k, 256, 16), X("cz", 4096 + 128 * k, 4224 + 128 * k), X(wt, 0, 16), (tg[k >> 2], q))
-                             for k in range(16) for q, wt in (("S", "W8"), ("V", "W16"))])
+        data = lambda b, x: [(X(b, k, 256, 16), X("cz", 128 * k, 128 + 128 * k), X(wt + x, 0, 16), (tg[k >> 2], q))
+                             for k in range(16) for q, wt in (("S", "W8"), ("V", "W16"))]
+        if tt + 1 == R:
+            b, y, y0 = psum(), X(psum(), 0, 128, p=(0, 8)), NB * tt + L
+            group(b, [(X(b, 0, 256), X("ONES", 0, 128, p=(0, 1)), X("KCK", 0, 256, p=(0, 1))), (X(b, 0, 128), X("NUM", 0, 128), ID32)],
+                  data(b, "K"), 8, X("F", cc, cc + 128))
+            scan(X("SK", 512, 768), X("RSK", 0, 256), X(b, 0, 256), 0.0, A.add, A.max)
+            acc([(y, X("SK", 527, 640, 16), ID32), (y, X("SK", 655, 768, 16), X("NI32", 0, 128))])
+            move(X("YS", y0, y0 + 128, p=(0, 8)), y, bias=-16.0)
+            dma("Y", [], [X("YS", y0, y0 + 128)], [(T.ys[:, y0:y0 + 128], T.YS[0:8, y0:y0 + 128])])
+            return
+        choose(2, lambda b: data(b, ""), X("F", cc, cc + 128))
         gather("c%d2" % tt, X("PC", 0, 128), ind(X("px%d0" % tt, 0, 2048), X("OFF", 16, 24)))
         if tt + 1 < R:
             gather("h%d2" % tt, X("FC", 0, 128), ind(X("f%d0" % tt, 0, 2048), X("OFF", 16, 24)))
             pairs(X("TT", cc, cc + 128), X("F", cc, cc + 128), X("FC", 0, 128))
         more = []
         if (tt, 0) in HY:
-            more = [(0, X("PS2", 256, 384))]
-            gather("d%d2" % tt, more[0][1], ind(X("py0", 0, 2048), X("OFF", 16, 24)))
-        grow("PC", 128, cc, NB * tt + L, tt, [X("FC", 0, 128)], more)
+            more = [(0, X("PS2", 256, 256 + EARLY))]
+            gather("d%d2" % tt, more[0][1], ind(X("py0", 0, 16 * EARLY), X("OFF", 16, 16 + EARLY // 16)))
+        grow("PC", 128, cc, NB * tt + L, tt, [("FC", 0)], more)
 
-    def parents(nm, dst, window, lst="PL", p0=None):
+    def parents(nm, dst, window, a=0, b=128, lst="PL", p0=None):
         n, p0 = 128 // PIECES, p0 or 128 * int(at[0][1])
-        piece = lambda tag, a, b: gather(tag, X(dst, 16 * a, 16 * b), ind(window, X(lst, p0 + a, p0 + b)))
-        for c in range(PIECES):
-            piece(nm + at[0] + str(c), n * c, n * c + n)
-            if c & 1:
-                pair(len(ops) - 2, len(ops) - 1, lambda: piece("", n * c - n, n * c + n))
+        pieces(lambda a, b: move(X(dst, 16 * a, 16 * b), ind(window, X(lst, p0 + a, p0 + b))), a, b, n, nm + at[0])
 
     G = [X("GB", 128 * h, 128 * h + 128) for h in (0, 1)]
     sent = [0]
@@ -695,121 +1089,174 @@ def record(g, core, T, topo, rank, banks):
         for h in (0, 1):
             fn, gx, at[0] = "f%d%d" % (t, h), "GX%d" % h, "%d%d" % (t, h)
             parents("f", fn, win)
-            choose(h, lambda b: [(X(b, k, 256, 16), X(fn, k, 2048, 16), X("W16", 0, 16)) for k in range(16)])
+            choose(h, lambda b: [(X(b, k, 256, 16), X(fn, k, 2048, 16), X("W16", 0, 16)) for k in range(16)], X(fn, 0, 512))
             chosen = ind(X(fn, 0, 2048), X("OFF", 8 * h, 8 * h + 8))
-            move(X(gx, 0, 2048, 16), chosen, -MID, 1025.0 / 1024, "G" + at[0])
-            gather("g" + at[0], G[h], chosen)
-            for c in (0, 1):
-                for j, k in enumerate((8, 4, 2, 1)):
+            move(X(gx, 0, 2048, 16), chosen, MID * 16 / sg, -1025.0 / 1024 / sg, "G" + at[0])
+            move(G[h], X(gx, 0, 2048, 16), MID * 16384 / 1025, -1024.0 * sg / 1025, "g" + at[0])
+            cuts = CUTS.get((t, h), (0, 64)) + (128 - SLANES.get((t, h), 0),)
+            for c, (a, b) in enumerate(zip(cuts, cuts[1:])):
+                for j, k in enumerate((8, 4, 2, 1) if a < b else ()):
                     for copy in (gcopy, vcopy, act):
-                        copy(X(gx, 1024 * c + k, 1024 * c + 1024, 2 * k), X(gx, 1024 * c, 1024 * c + 1024, 2 * k))
+                        copy(X(gx, 16 * a + k, 16 * b, 2 * k), X(gx, 16 * a, 16 * b, 2 * k))
                     either("r%d%d%d%d" % (t, h, c, j), 3)
         for h in (0, 1):
             pn, c0, at[0] = "px%d%d" % (t, h), 512 * h, "%d%d" % (t, h)
 
-            def keys(src, ds, ls):
+            def tolist(o, a, b, d, less):
+                m = 128 - SLANES.get((t, h), 0) if d & 1 else 128
+                if a < m:
+                    q0 = c0 + 128 * (4 - d)
+                    vts(X("QL", q0 + a, q0 + min(b, m)), X(o, 0, min(b, m) - a), less, A.subtract)
+                    ops[-1]["tag"] += "%d%d" % (d, a // 64)
+                if b > m:
+                    vts(X("QS", 128 * h + d // 2, 128 * h + 256 - 2 * m, 2), X(o, m - a, b - a), less, A.subtract)
+                    ops[-1]["tag"] += str(d)
+
+            def keys(src, ds, ls, a=0, e=128):
                 for d in ls:
-                    for c in (0, 1) if (t, h, d) in DIRECT else ():
-                        lists(src, 1024 * c, "QL", c0 + 128 * (4 - d) + 64 * c, 64, "LE%d" % (d - ds[0] + 1))
-                        ops[-1]["tag"] += "%d%d" % (d, c)
-                n, b = 128 * len(ds), psum()
-                acc([(X(b, c, c + 128), ONES, X("CVX", 0, 128)) for c in range(0, n, 128)]
-                    + [(X(b, k, n, 16), X(src, k, 2048, 16), X("WX", 32 - n // 16, 32)) for k in range(16)])
+                    for c in range(a, e, 64) if (t, h, d, a) in DIRECT else ():
+                        tolist(lists(src, 16 * c, 64, "LE%d" % (d - ds[0] + 1)), c, c + 64, d, HIGH)
+                n, b, p, rows = 128 * len(ds), psum(), (a, e), ALL if e - a == 128 else 1 << a // 64
+                group(b, [(X(b, c, c + 128, p=p), X("ONES", a, e), X("CVX", 0, 128)) for c in range(0, n, 128)],
+                      [(X(b, k, n, 16, p=p), X(src, 16 * a + k, 16 * e, 16), X("WX", 32 - n // 16, 32)) for k in range(16)],
+                      16, X(src, 16 * a, 16 * a + 512))
                 for d in ds:
                     j, i = 4 - d, ds[-1] - d
-                    move(X("CO", c0 + j, c0 + 512, 4), X(b, 128 * i, 128 * i + 128), bias=10 * BIG + PR * (5 - d) - HIGH)
-                    ops[-1]["tag"] += str(d)
+                    move(X("CO", c0 + j, c0 + 512, 4, p=p, rows=rows), X(b, 128 * i, 128 * i + 128, p=p),
+                         bias=10.75 * BIG - PR * d - HIGH)
+                    ops[-1]["tag"] += "%d%d" % (d, a // 64)
                 for d in ls:
-                    if (t, h, d) not in DIRECT:
-                        j, o = 4 - d, X(psum(), 0, 128)
-                        acc([(o, X("CO", c0 + j, c0 + 512, 4), ID32)])
-                        vts(X("QL", c0 + 128 * j, c0 + 128 * j + 128), o, cd[d], A.subtract)
-                        ops[-1]["tag"] += str(d)
+                    if (t, h, d, a) not in DIRECT:
+                        o = psum()
+                        acc([(X(o, 0, e - a), X("CO", c0 + 4 - d, c0 + 512, 4, p=p, rows=rows), X("ID32", a, e, p=p))])
+                        tolist(o, a, e, d, cd[d])
 
-            if t == 0 and h == len(HY):
+            a = EARLY if (t, h) in HY else 0
+            if a:
+                parents("x", pn, pwin, 0, a)
+                keys(pn, (1, 2), (1, 2), 0, a)
+                parents("y", "py%d" % h, pwin, 0, a, "QL", c0 + 256)
+                keys("py%d" % h, (3, 4), (3,), 0, a)
                 shift("T3", 0, [(1, 3), (2, 4), (5, 7), (7, 6)])
-            parents("x", pn, pwin)
-            if (t, h) in HY:
-                keys(pn, (1, 2), (1, 2))
-                parents("y", "py%d" % h, pwin, "QL", c0 + 256)
-                keys("py%d" % h, (3, 4), (3,))
-            else:
-                keys(pn, (1, 2, 3, 4), (1, 3))
-        if t == 0 and len(HY) == 2:
-            shift("T3", 0, [(1, 3), (2, 4), (5, 7), (7, 6)])
+            if a < 128:
+                parents("x", pn, pwin, a)
+                keys(pn, (1, 2, 3, 4), (1, 3), a)
         for h in (0, 1):
             at[0] = "%d%d" % (t, h)
-            signs(h, "f%d%d" % (t, h), G[h])
+            fn, y0 = "f%d%d" % (t, h), 1024 * h
+            for j in (0, 1):
+                pd = psum()
+                for wt, x in (("I16", 0), ("IDK", 1)):
+                    acc([(X(pd, 128 * i, 128 * i + 128), X(wt, 0, 128), X(fn, 8 * j + 2 * i + x, 2048, 16)) for i in range(4)], not x, False)
+                acc([(X(pd, 128 * i, 128 * i + 128), X("NG", 0, 128), G[h]) for i in range(4)], False, True)
+                move(X("cy", y0 + 512 * j, y0 + 512 * j + 512), X(pd, 0, 512), MID, tag="z%d%d%d" % (t, h, j))
+            for j, c in ((1, 767 + 5.5 / 32), (0, 16 * 32832 - 32 * 10.5)):
+                b = psum()
+                l = [(X(b, 0, 64), G[h], X("WO", 0, 64))] + [(X(b, i, 64, 8), X(fn, 2 * i, 2048, 16), X("WN", 0, 8)) for i in range(8)]
+                acc(l * j + [(X(b, i, 64, 8), X("cy", y0 + 128 * i, y0 + 128 * i + 128), X("W1", 0, 8)) for i in range(8)])
+                act(X("SG", 128 * h + j, 128 * h + 128, 2), X(b, 0, 64), AF.Sign, bias=c, scale=-1.0)
+                if j:
+                    cy = X("cy", y0, y0 + 1024)
+                    dma("G", [cy], [cy, X("CF", 0, 1024)], [(cy[0], T.CF[:])], DLAT, "Z" + at[0])
+                    ops[-1]["cost"]["G"] = 1.0
             o = X(psum(), 0, 128)
-            tg = ["z%d%d%d" % (t, h, j) for j in range(4)]
-            acc([(o, ONES, X("CZ", 0, 128))]
-                + [(o, LE(le, k), X("cz", 2048 * h + 128 * k, 2048 * h + 128 * k + 128), (tg[k >> 2], q))
-                   for k in range(16) for q, le in (("S", "LEc"), ("V", "LEd"))])
-            t0 = X("T0", *HS[h])
-            vtt(t0, o, X("NUM", *HS[h]), A.min)
-            vts(t0, t0, 5.0 * PR, A.add, 0.0, A.max)
-            act(t0, t0, AF.Relu, bias=5.0 * PR)
-            either("RL" + at[0], 2)
+            acc([(o, X("SG", *HS[h]), X("I5", 0, 128))])
+            vtt(X("T0", *HS[h]), o, X("NUM", *HS[h]), A.min)
 
         def tests(h, a, b):
             ca, gx, c0, at[0] = psum(), "GX%d" % h, 512 * h, "%d%d" % (t, h)
             pn, twin, p = "px%d%d" % (t, h), X("TT", 0, 16 + B), (a, b)
             rows = ALL if b - a == 128 else 1 << a // 64
+            m = min(b, 128 - SLANES.get((t, h), 0))
+            thr = 767.75 / sg
+
+            def compare(tag, o, x, outs):
+                vts(o, x, thr, A.is_le)
+                act(o, x, AF.Sign, bias=thr, scale=-1.0)
+                either(tag, 2)
+                return [(y, X("ONES", 0, y[0].shape[0]), X("SIX", 0, 128), (tag, "S")) for y in outs]
+
+            def sums(l, col0, src, x0, step, wt, a, b):
+                acc(l + [(X(ca, 4 * k + col0, 512, 64, p=(a, b)), X(src, x0 + k, x0 + step * (b - a - 1) + 16, step), X(wt, 0, 8))
+                         for k in range(16)] + [(X(ca, col0, 512, 64, p=p), X("ONES", *p), Z(8))] * ((a, b) != p), False, False)
+                ops[-1]["fn"] = ca
+
             for d in (1, 3):
                 j = 4 - d
                 v0, q0 = 2048 * (2 * h + d // 2), c0 + 128 * j
                 if d == 1:
                     acc([(X(ca, c, 512, 4, p=p), X("ONES", a, b), X("CVX", 0, 128)) for c in range(4)], True, False)
-                    ops[-1]["r"] += X("QL", q0 + a, q0 + a + 64)[1]
-                src, ws = ("py%d" % h, 0) if d == 3 and (t, h) in HY else (pn, 4 * d - 4)
+                    ops[-1]["r"] += X("QL", q0 + a, q0 + a + 32)[1]
+                src, ws = ("py%d" % h, 0) if d == 3 and (t, h) in HY and a < EARLY else (pn, 4 * d - 4)
                 acc([(X(ca, j - 1, 512, 4, p=p), X("ONES", a, b), X("CK", 0, 128)),
                      (X(ca, j - 1, 512, 4, p=p), X("GB", 128 * h + a, 128 * h + b), X("WG", 0, 128))]
                     + [(X(ca, 4 * k + j - 1, 512, 64, p=p), X(src, 16 * a + k, 16 * b, 16), X("WS", ws, ws + 8)) for k in range(16)],
                     False, False)
                 ops[-1]["fn"] = ca
-                cds = lambda a, b: X("cd", v0 + 16 * a, v0 + 16 * b)
+                cds = lambda a, b, v0=v0: X("cd", v0 + 16 * a, v0 + 16 * b)
                 cvs = lambda a, b: X("cv", v0 + 16 * a, v0 + 16 * b)
-                test = lambda a, b: vtt(cds(a, b), ind(twin, X("QL", q0 + a, q0 + b)), X(gx, 16 * a, 16 * b), A.subtract)
-                for c in range(a, b, TW):
-                    test(c, c + TW)
-                    ops[-1]["tag"] = "%s%d%d%d" % (" p q"[d], t, h, c // TW)
-                    if (c - a) // TW & 1:
-                        pair(len(ops) - 2, len(ops) - 1, lambda: test(c - TW, c + TW))
-                l = []
-                for c in range(a, b, 64):
-                    tag = "%s%d%d%d" % (" P Q"[d], t, h, c // 64)
-                    vts(cvs(c, c + 64), cds(c, c + 64), 768.75, A.is_le)
-                    act(cvs(c, c + 64), cds(c, c + 64), AF.Sign, bias=768.75, scale=-1.0)
-                    either(tag, 2)
-                    l.append((X(ca, j, 512, 4, p=p), X("QM", 64 - c + a, 64 - c + b), X("SIX", 0, 128), (tag, "S")))
-                for src, col0, wt, l in (("cd", j - 1, "WD", []), ("cv", j, "WB", l)):
-                    acc(l + [(X(ca, 4 * k + col0, 512, 64, p=p), X(src, v0 + 16 * a + k, v0 + 16 * b, 16), X(wt, 0, 8))
-                             for k in range(16)], False, False)
-                    ops[-1]["fn"] = ca
-            scan(X("SC", c0, c0 + 512, p=p, rows=rows), X(ca, 0, 512, p=p), X("CO", c0, c0 + 512, p=p), -BIG, A.max, A.min)
-            hs, o = (128 * h + a, 128 * h + b), X(psum(), 0, b - a)
-            acc([(o, X("OFR", 0, 128), X("ONES", a, b)), (o, X("SC", c0 + 3, c0 + 512, 4, p=p, rows=rows), X("ID32", a, b, p=p))])
+                pieces(lambda a, b, cds=cds, q0=q0: vtt(cds(a, b), ind(twin, X("QL", q0 + a, q0 + b)), X(gx, 16 * a, 16 * b), A.add),
+                       a, m, TW, "%s%d%d" % (" p q"[d], t, h))
+                l, by = [], (t, h, d) in BYDMA
+                sums([], j - 1, "cd", v0 + 16 * a, 16, "WD", a, m)
+                cuts = LAST if h and d == 3 else range(a, b + 1, 64)
+                for c, e in zip(cuts, cuts[1:]):
+                    tag = "%s%d%d%d" % (" P Q"[d], t, h, c // 64 + c // 96)
+                    if by:
+                        cf = X("CF", 0, 16 * (e - c))
+                        dma("G", [cds(c, e)], [cds(c, e), cf], [(cds(c, e)[0], cf[0])], DLAT, tag)
+                        ops[-1]["cost"]["G"] = 1.0
+                    else:
+                        l += compare(tag, cvs(c, e), cds(c, e), [X(ca, j, 512, 4, p=(c, e))])
+                    if e == b or e == 96:
+                        c = 96 if c == 96 else a
+                        sums(l, j, "cv", v0 + 16 * c, 16, "WB", c, e)
+                        l = []
+            for c in range(m, b, 32):
+                x0 = 1024 * h + 32 * (c - m)
+                for i in range(c, c + 32, 8):
+                    for u in range(i, i + 8):
+                        y0, q0 = 1024 * h + 32 * (u - m), 128 * h + 2 * (u - m)
+                        act(X("cs", y0, y0 + 32), ind(twin, X("QS", q0, q0 + 2)), AF.Identity, X(gx, 16 * u, 16 * u + 1))
+                    run(8, "s%d%d%d" % (t, h, i // 8))
+                l = compare("R%d%d%d" % (t, h, c // 32), X("cw", x0, x0 + 1024), X("cs", x0, x0 + 1024),
+                            [X(ca, j, 512, 4, p=(c, c + 32)) for j in (1, 3)])
+                for d in (1, 3):
+                    sums([], 3 - d, "cs", x0 + 8 * (d - 1), 32, "WD", c, c + 32)
+                    sums(l if d == 1 else [], 4 - d, "cw", x0 + 8 * (d - 1), 32, "WB", c, c + 32)
+            scan(X("SC", c0, c0 + 512, p=p, rows=rows), X(ca, 0, 512, p=p), X("CO", c0, c0 + 512, p=p, rows=rows), -BIG, A.max, A.min)
+            hs, x = (128 * h + a, 128 * h + b), psum()
+            o = X(x, 0, b - a)
+            group(x, [(o, X("OFR", 0, 128), X("ONES", a, b))], [(o, X("SC", c0 + 3, c0 + 512, 4, p=p, rows=rows), X("ID32", a, b, p=p))],
+                  1, cds(b - 32, b))
             vtt(X("VI", *hs), o, X("T0", *hs), A.max)
             vts(X("QN", *hs), X("VI", *hs), PR - 1, A.bitwise_and)
             vcopy(X("LOL", *hs), X("QN", *hs))
             gm, g0 = "GM%d" % ((h + t) & 1), 16 * ((h + t) >> 1)
-            for i in range(a // 32, b // 32):
-                cs = (2048 * h + 512 * i, 2048 * h + 512 * i + 512)
-                gather("e%d%d%d" % (t, h, i), X("DS", *cs), ind(win, X("LOL", 128 * h + 32 * i, 128 * h + 32 * i + 32)))
-                scan(X("DC", *cs), X("DS", *cs), X(gm, g0, g0 + 512), 0.0, A.max, A.add)
-                ops[-1]["tag"] += str(i)
+            cs = lambda nm, a, b: X(nm, 2048 * h + 16 * a, 2048 * h + 16 * b)
+
+            def largest(a, b):
+                scan(cs("DC", a, b), cs("DS", a, b), X(gm, g0, g0 + 512), 0.0, A.max, A.add)
+                ops[-1]["tag"] += str(a // 32)
+
+            pieces(lambda a, b, win=win: move(cs("DS", a, b), ind(win, X("LOL", 128 * h + a, 128 * h + b))), a, b, 32, "e%d%d" % (t, h), largest)
             if h == 0:
                 vts(X("SEND%d" % t, a, b), X("DC", 16 * a + 15, 16 * b, 16), 256.0, A.add, 255.0, A.min)
                 send(a, b)
             if b == 128:
-                vts(X("F", 16 + B + h, 16 + B + L, 2), X("DC", 2048 * h + 15, 2048 * h + 2048, 16), 256.0, A.add, 255.0, A.min)
+                if h:
+                    vts(X("F", 17 + B, 16 + B + L, 2), X("DC", 2048 + 15, 4096, 16), 256.0, A.add, 255.0, A.min)
+                else:
+                    for copy in (gcopy, vcopy, act):
+                        copy(X("F", 16 + B, 16 + B + L, 2), X("SEND%d" % t, 0, 128))
+                    either(None, 3)
                 if t + 1 < R:
                     pairs(X("TT", 16 + B + h, 16 + B + L, 2), X("F", 16 + B + h, 16 + B + L, 2), G[h])
 
         def send(a, b):
             dst = T.cores[(rank + 1 + t % 7) % len(T.cores)]
             src = T.cores[(rank - 1 - t % 7) % len(T.cores)]
-            es = topo.engines(core, dst)[::2]
+            es = topo.engines(core, dst)
             rid, pid, _se = topo.addr(dst)
             nm = "%d%d" % (t, a // 64)
             out, buf = T.F[:, cc + a:cc + b], T["SEND%d" % t][:, a:b]
@@ -819,15 +1266,17 @@ def record(g, core, T, topo, rank, banks):
                                        pid=pid, routing_id=rid, dma_engine_mask=sum(1 << x for x in es)),
                 0.3, 2.0, ("lc" + nm, len(es)))
             rec("a", "R", [X("F", cc + a, cc + b)], [gone], None, 0.3, ARR[min(1, sent[0])],
-                ("ar" + nm, len(topo.engines(src, core)[::2])))
+                ("ar" + nm, len(topo.engines(src, core))))
             sent[0] += 1
 
         def rename(h):
             hs, kk, r0, at[0] = HS[h], "KK%d" % h, 256 * h, "%d%d" % (t, h)
             hif, red = X("HIF", *hs), X("RZ", r0, r0 + 128)
-            vts(hif, X("VI", *hs), 1.0 / PR, A.mult, 127.875, A.add)
-            vts(red, hif, 128.0, A.is_equal, float(PR), A.mult)
-            vts(X("RZ", r0 + 128, r0 + 256), hif, 133.0, A.is_equal, float(PR), A.mult)
+            move(hif, X("VI", *hs), 132.875, 1.0 / PR)
+            for x, c, w in ((red, 128.0, -1), (X("RZ", r0 + 128, r0 + 256), 133.0, 1)):
+                vts(x, hif, c, A.is_equal, float(PR), A.mult)
+                act(x, hif, AF.Relu, bias=PR * (1.0 - w * c), scale=float(w * PR))
+                either(None, 2)
 
             def sums(b):
                 return [(X(b, 128, 256), X("NBD", 0, 128), hif), (X(b, 128, 256), X("OS", 0, 128), red),
@@ -845,8 +1294,8 @@ def record(g, core, T, topo, rank, banks):
                  (X(ca, 128, 256), X("N64", 0, 128), X("WW", r0, r0 + 128))], False, True)
             m1, q = X("M1", *hs), X("QN", *hs)
             if t + 1 == R:
-                q = X("NUM", *hs)
-                vts(q, X("QN", *hs), -16.0, A.add)
+                q = X("T0", *hs)
+                move(q, X("QN", *hs), -16.0)
             vtt(m1, X(ca, 0, 128), q, A.max)
             vtt(m1, X(ca, 128, 256), m1, A.max)
             vtt(X("NUM", *hs) if t + 1 < R else X("YP", h, 256, 2), X(ca, 256, 384), m1, A.max)
@@ -855,11 +1304,11 @@ def record(g, core, T, topo, rank, banks):
 
         for h in (0, 1):
             gather("c%d%d" % (t, h), X("PS", h, 256, 2), ind(X("px%d%d" % (t, h), 0, 2048), X("OFF", 8 * h, 8 * h + 8)))
-        more = [(h, X("PS2", 128 * h, 128 * h + 128)) for h in (0, 1) if (t, h) in HY]
+        more = [(h, X("PS2", 128 * h, 128 * h + EARLY)) for h in (0, 1) if (t, h) in HY]
         for h, x in more:
-            gather("d%d%d" % (t, h), x, ind(X("py%d" % h, 0, 2048), X("OFF", 8 * h, 8 * h + 8)))
+            gather("d%d%d" % (t, h), x, ind(X("py%d" % h, 0, 16 * EARLY), X("OFF", 8 * h, 8 * h + EARLY // 16)))
         at[0] = "%d0" % t
-        grow("PS", 256, 16 + B, NB * t, t, G, more)
+        grow("PS", 256, 16 + B, NB * t, t, [("GB", 0), ("GB", 128)], more)
         for h in (0, 1):
             for a, b in ((0, 64), (64, 128)) if (t, h) in SPLIT else ((0, 128),):
                 tests(h, a, b)
@@ -936,9 +1385,7 @@ def issue(g, T, ops):
                 l.append({"q": q, "w": w, "x": x, "sem": sem, "val": val, "clk": c})
 
     queue = PLAN["qs"]
-    after, nxt = {}, {}
-    for i in PLAN["order"][::-1]:
-        after[i], nxt[queue[i]] = nxt.get(queue[i]), i
+    skip = set(j for run in PLAN["runs"].values() for j in run[:-1])
     for i in PLAN["order"]:
         o = ops[i]
         q, r, w = o["q"], o["r"], o["w"]
@@ -946,14 +1393,22 @@ def issue(g, T, ops):
             note("D", [], w, o["data"][0], o["data"][1], {})
             continue
         q, fns = queue[i], o["fn"]
-        if "mate" in o and after[i] == o["mate"] and i not in PLAN["apart"]:
+        if i in skip:
             continue
-        if "mate" in o and after.get(o["mate"]) == i and o["mate"] not in PLAN["apart"]:
-            fns, r, w = o["both"], r + ops[o["mate"]]["r"], w + ops[o["mate"]]["w"]
+        if i in PLAN["runs"]:
+            ends = [x for j in PLAN["runs"][i] for x in ops[j]["span"]]
+            o["make"](min(ends), max(ends))
+            x = ops.pop()
+            fns, r, w = x["fn"], x["r"], x["w"]
         waits(q, r, w)
         if o["kind"] in "cg":
             cnt[q] += 1
             (fns if o["kind"] == "c" else fns[q])(eng[q]).then_inc(T.sem[sname[q]], 1)
+            note(q, r, w, sname[q], cnt[q], clk[q])
+        elif o["kind"] == "m":
+            for fn in fns:
+                cnt[q] += 1
+                fn(eng[q]).then_inc(T.sem[sname[q]], 1)
             note(q, r, w, sname[q], cnt[q], clk[q])
         elif o["kind"] == "t":
             if o["fn"]:

from concourse.mybir import AluOpType, ActivationFunctionType
import math
import numpy as np

I0, L, R = 3328, 256, 2
NB = L + 128
FW = 4112
BIG = 65536.0
PR = 8192
HIGH = 129.0 * 64
MID = (767.25 - 1.0 / 2048) / 16
TOP = 32768.0
BYDMA = ()
DLAT = 3.6
SLANES = {}
CUTS = {(1, 0): (0, 32, 64)}
EARLY = 64
HY = ((0, 0),)
SPLIT = ((0, 0),)
LAST = (0, 64, 96, 128)
DIRECT = ((0, 0, 1, 0), (0, 0, 2, 0), (0, 0, 3, 0), (0, 0, 1, 64), (0, 0, 3, 64), (0, 1, 1, 0), (1, 0, 1, 0), (1, 0, 3, 0), (1, 1, 1, 0))
ADD = 3.0
TW = 32
PARTS = 4
PIECES = 4
LAYS = 6000
LHEAT = 0.0017
LEAN = (1.0, 1.0)
PULL = 0.5
AIM = {
    "V": "@5.2 f002 f003 t1 u0 u1 u2 u3 @9.9 a0 a1 a2 a3 @14.5 x000 b1 y001 y000 @18.9 p000 p001 q000 q001 @22.1 x003 Q000 p003 p002 "
         "q002 q003 @27.5 p010 p011 @29.5 p013 p012 q010 q011 q012 q013 Q011 @37.5 z020 e012 e010 @42 f101 f111 f110 x100 x103 "
         "@48 p100 p101 q101 q100 p102 p103 q103 q102 Q100 p113 p112 p111 @57 p110 q110 q111 q113 q112 Q110 @64.3 e110 z122 z121",
    "S": "@5.2 f012 f013 f000 f001 f011 f010 t0 t2 t3 z001 z000 @14.4 x001 b0 b3 b2 @20 P000 @22.1 x002 x012 x013 x010 x011 P001 Q001 "
         "e000 e001 z010 z011 P010 e003 e002 P011 Q010 @37.8 z021 z023 z022 e011 e013 @41.8 f100 f102 f103 f112 f113 x101 x102 x110 "
         "z100 z101 x113 x112 x111 P100 P101 Q101 z111 z110 P111 P110 e103 e102 e100 e101 Q111 @64.6 e112 z120 z123 e111 e113"}
CRIT = 0.7
BACK = 0.6
WIDE = 8.0
AMP = 1.5
LOOSE = 0.5
EPS = 0.25
SEED = 3
SWEEPS, WIN, STRIDE, EACH = 34, 110, 45, 1200
HEAT, SOFT = 0.0006, 0.4
CYC = 0.83e-3
PEC = 0.42e-3
GAT = 1.56
WAKE = 0.2
ARR = (4.8, 0.3)
KINDS = [(1.0, 0.95, 0.19, 0.1), (1.1, 0.74, 0.19, 0.1), (1.35, 1.27, 0.19, 0.1)]
SCALES = (70.0, 140.0, 105.0)
LAYK = (0, 0, 2)
PLAN = {}
CUT = 1664
LAT = (3.2, 4.3, 5.0, 2.6, 2.8)
FRONT = ((0, 10, 4.5), (10, 16, 5.0))
LOADS = "sel fr0 fr1 fr2 par sr0 sr1 row2 row10 row1 row9 row0 row8 row5 row7 row13 row15"

SCRATCH = {}
for _d, _l in [
        ("bfloat16", [("F", FW), ("PT", FW), ("FS", 16 + I0),
                      ("f00", 2048), ("f01", 2048), ("f10", 2048), ("f11", 2048),
                      ("px00", 2048), ("px01", 2048), ("px10", 2048), ("px11", 2048), ("py0", 2048),
                      ("GB", 256), ("cv", 4 * 2048), ("cz", 2048), ("cw", 2048), ("DS", 4096), ("DC", 4096),
                      ("SCH", 208), ("SCL", 208), ("HB", 256), ("LB", 256), ("SHB", 208), ("SLB", 208),
                      ("HH", 256), ("FC", 128), ("PS", 256), ("PC", 128), ("PS2", 384),
                      ("LEs", 144), ("LE", 144), ("LE1", 144), ("LE2", 144), ("LE3", 144), ("I5", 128), ("SG", 256), ("WN", 8),
                      ("I16", 128), ("WO", 64), ("WE", 8), ("W8K", 16), ("W16K", 16), ("KCK", 256), ("RSK", 256), ("CE", 128),
                      ("W1", 8), ("W8", 16), ("W16", 16), ("WB", 8), ("WD", 8), ("WS", 16), ("WX", 32), ("YSM", 8), ("WG", 128),
                      ("ZERO", 144), ("ONES", 128), ("ID", 128), ("NID", 128), ("N64", 128), ("N8", 128), ("IDK", 128),
                      ("OS", 128), ("NBD", 128), ("SH", 128), ("SH3", 128), ("D01", 128),
                      ("SH7", 128), ("KC", 256), ("KCON", 128), ("MSK", 128), ("EL", 256), ("SIX", 128), ("CK", 128),
                      ("RST", 256), ("GM0", 528), ("GM1", 528), ("CVX", 128), ("OFR", 128), ("CC", 8),
                      ("KK0", 384), ("KK1", 384), ("CB0", 384), ("CB1", 384),
                      ("GE", 384), ("GT", 384), ("HIF", 256), ("RZ", 512), ("WW", 512), ("SEND0", 128), ("SEND1", 128)]),
        ("int32", [("PI", 1), ("CI", 144), ("ti", 8), ("KI", 512), ("SELR", 208), ("SELO", 208),
                   ("raw", 256), ("VI", 256), ("QN", 256), ("MA", 80)]),
        ("uint16", [("SL1", 208), ("SL2", 208), ("PL", 256), ("QL", 1024), ("QS", 256), ("LOL", 256), ("BC", 8), ("OFF", 24)]),
        ("float16", [("cd", 4 * 2048), ("cy", 2048), ("cs", 2048), ("CF", 1024), ("NG", 128)]),
        ("float32", [("TT", FW), ("GX0", 2048), ("GX1", 2048), ("ID32", 128), ("NI32", 128), ("SK", 768), ("MX", 24), ("CO", 1024), ("SC", 1024),
                     ("NUM", 256), ("T0", 256), ("M1", 256), ("YP", 256), ("YS", 768), ("cols", 16), ("WC", 8)])]:
    for _n, _w in _l:
        SCRATCH[_n] = ("sbuf", [128, _w], _d)
PACK = {}
for _n in ("W1 W8 W16 WB WD WS WX YSM WG ZERO ONES ID NID N64 N8 IDK OS NBD SH SH3 D01 SH7 KC KCON MSK SIX CK RST CVX OFR CC "
           "LEs LE LE1 LE2 LE3 I5 I16 WO WN WE W8K W16K KCK RSK CE").split():
    PACK[_n] = ("KB", sum(SCRATCH[_m][1][1] for _m in PACK))
SCRATCH["KB"] = ("sbuf", [128, sum(SCRATCH[_m][1][1] for _m in PACK)], "bfloat16")
for _n in PACK:
    del SCRATCH[_n]
SAME = {"SR": "DS", "T3": "DC", "T2": "cv"}
NBANK = 8
for _j in range(NBANK):
    SCRATCH["PB%d" % _j] = ("psum", [128, 512], "float32")

NDMA = 64
SEMAPHORES = (["sv", "ss", "st", "sg"] + ["d%d" % j for j in range(NDMA)]
              + ["%s%d%d" % (a, t, c) for a in ("ar", "lc") for t in range(R) for c in range(2 if (t, 0) in SPLIT else 1)])
ALL = 0xFFFF


def meet(a, b):
    return a[1] < b[2] and b[1] < a[2] and (a[4] & b[4]) != 0 and (a[1] - b[1]) % math.gcd(a[3], b[3]) == 0


def cover(a, b):
    return a[1] <= b[1] and b[2] <= a[2] and (b[4] & ~a[4]) == 0 and b[3] % a[3] == 0 and (b[1] - a[1]) % a[3] == 0


def lease(x):
    return x[0] if isinstance(x[0], int) else None


def schedule(ops):
    n = len(ops)
    need, last, gap = [set() for _ in range(n)], {}, {}
    for i, o in enumerate(ops):
        for w, regs in ((0, o["r"]), (1, o["w"])):
            for x in regs:
                l = last.setdefault(x[0], [])
                ps = lease(x) is not None
                for (j, w2, y) in l:
                    p = ops[j]
                    if j != i and ((ps and (p["q"] != o["q"] or "g" in p["kind"] + o["kind"])) or ((w or w2) and meet(x, y))):
                        need[i].add(j)
                        own = p["q"] == o["q"] and (o["q"] == "T" or not w2) and not p["lat"] and "g" not in p["kind"] + o["kind"]
                        gap[j, i] = max(gap.get((j, i), 0.0), 0.0 if own else p["lat"] + WAKE)
                if w and not ps:
                    l[:] = [e for e in l if not cover(x, e[2])]
                l.append((i, w, x))
    l = [i for name in LOADS.split() for i in range(n) if ops[i]["tag"] == name]
    for j, i in zip(l, l[1:]):
        gap.setdefault((j, i), 0.0)
        need[i].add(j)
    held = [([lease(x) for x in o["r"] + o["w"] if lease(x) is not None] + [None])[0] for o in ops]
    nl = {}
    for z in held:
        nl[z] = nl.get(z, 0) + 1
    qs, mate = [o["q"] for o in ops], [o.get("mate", ()) for o in ops]
    short = []
    for i in range(n):
        far = set(j for k in need[i] if gap[k, i] for j in need[k] if gap[j, k] >= gap.get((j, i), 0.0))
        short.append([j for j in sorted(need[i]) if j not in far])
    kinds = []
    for f, gf, wk, dl in KINDS:
        costs = [{q: c * (f * gf if o["gat"] else f if q in "VSTG" else 1.0) for q, c in o["cost"].items()} for o in ops]
        lat = [o["lat"] + dl if o["lat"] else 0.0 for o in ops]
        pre, post = [[(j, (lat[j] + wk) if gap[j, i] else 0.0) for j in short[i]] for i in range(n)], [[] for _ in ops]
        for i in range(n):
            for j, d in pre[i]:
                post[j].append((i, d))
        kinds.append((costs, lat, pre, post, wk))

    def play(order, kind):
        costs, lat, pre, post, wk = kind
        fin, why, free, prev = [0.0] * n, [None] * n, dict.fromkeys("VSTGYR", 0.0), dict.fromkeys("VSTGYR")
        bank, todo, ends, banks, end = {}, dict(nl), {}, {k: (0.0, -1) for k in range(NBANK)}, 0.0
        for i in order:
            q = qs[i]
            t, y = free[q], prev[q]
            for j, d in pre[i]:
                if fin[j] + d > t:
                    t, y = fin[j] + d, j
            z = held[i]
            if z is not None and z not in bank:
                if not banks:
                    return None
                k = bank[z] = min(banks, key=banks.get)
                b = banks.pop(k)
                if b[0] > t:
                    t, y = b
            free[q] = fin[i] = t = t + costs[i][q] - (0.055 if prev[q] in mate[i] and y == prev[q] else 0.0)
            prev[q], why[i] = i, y
            if z is not None:
                if z not in ends or t + wk > ends[z][0]:
                    ends[z] = (t + wk, i)
                todo[z] -= 1
                if not todo[z]:
                    banks[bank[z]] = ends.pop(z)
            if t + lat[i] > end:
                end = t + lat[i]
        return end, fin, why, bank

    def fit(line, t, c):
        a, b = line
        lo, hi = 0, len(b)
        if not hi or b[-1] <= t:
            return t, hi
        while lo < hi:
            mid = (lo + hi) >> 1
            if b[mid] <= t:
                lo = mid + 1
            else:
                hi = mid
        hi = len(b)
        while lo < hi and a[lo] < t + c - 1e-9:
            t = b[lo]
            lo += 1
        return t, lo

    def lay(order, kind, back, loose, lean):
        costs, lat, links = kind[0], kind[1], kind[3 if back else 2]
        lines, fin, start = {q: ([], []) for q in "VSTGYR"}, [0.0] * n, [0.0] * n
        for i in order:
            t = lat[i] if back else 0.0
            for j, d in links[i]:
                if fin[j] + d > t:
                    t = fin[j] + d
            if i in loose:
                qs[i] = min(costs[i], key=lambda q: fit(lines[q], t, costs[i][q])[0] + costs[i][q] * (1 + lean[0])
                            + lean[1] * "GSV".index(q))
            q = qs[i]
            c, (a, b) = costs[i][q], lines[q]
            if b and b[-1] > t:
                t, p = fit((a, b), t, c)
                a.insert(p, t)
                b.insert(p, t + c)
            else:
                a.append(t)
                b.append(t + c)
            start[i], fin[i] = t, t + c
        return start, fin

    ref = SCALES

    def value(order):
        got = seen_plays[:] = [play(order, k) for k in kinds]
        return 1e9 if None in got else sum((r[0] + EPS * sum([r[1][i] for i in live]) / len(live)) / x for r, x in zip(got, ref))

    live = set()
    for i in range(n):
        if ops[i]["kind"] == "d" and not ops[i]["r"] or need[i] & live:
            live.add(i)

    rng, seen_plays, chain = np.random.default_rng(SEED), [], []
    free = [i for i in range(n) if len(ops[i]["cost"]) > 1]
    pe = [i for i in range(n) if qs[i] == "T"]
    start = [0.0] * n
    for i in range(n):
        start[i] = max([0.0] + [start[j] + kinds[0][0][j][qs[j]] + d for j, d in kinds[0][2][i]])
    order, now, top, best, last = list(range(n)), 1e9, 1e9, None, [1e9] * 3
    if AIM:
        start, aim = [99.0] * n, {}
        for q, names in AIM.items():
            t = 0.0
            for name in names.split():
                if name[0] == "@":
                    t = float(name[1:])
                for i in order:
                    if ops[i]["tag"] == name and q in ops[i]["cost"]:
                        qs[i], aim[i] = q, t
                        t += kinds[0][0][i][q]
        for i in order[::-1]:
            start[i] = min([aim.get(i, 99.0)] + [start[j] - d - kinds[0][0][i][qs[i]] for j, d in kinds[0][3][i]])
        start = lay(sorted(order, key=lambda i: (start[i], i)), kinds[0], False, set(free) - set(aim), (0.5, 0.0))[0]
    for it in range(LAYS):
        c = LAYK[it % len(LAYK)]
        kind, old = kinds[c], qs[:]
        r = rng.random(8).tolist()
        t0, wide, amp = r[0] * 80 - 3, 1 + WIDE * r[1], AMP * r[2] ** 2
        r[3] *= LOOSE
        noise, pick = rng.standard_normal(n).tolist(), rng.random(n).tolist()
        key = [s + amp * x if t0 < s < t0 + wide else s for s, x in zip(start, noise)]
        loose = set(i for i in free if now > 1e8 and not AIM or t0 < start[i] < t0 + wide and pick[i] < r[3])
        if r[4] < PULL:
            v, d = int(r[5] * n), (2 * r[6] - 1) * 3
            if r[4] < PULL * CRIT and chain:
                u, v = chain[int(r[5] * len(chain))]
                d = start[u] - start[v] - 2 * r[2] if d < 0 else start[v] - start[u] + 2 * r[2]
                v = v if d < 0 else u
                key = start[:]
                loose = set(i for i in free if abs(start[i] - start[v]) < 3 and pick[i] < r[3])
            todo, seen = [v], {v}
            while todo:
                i = todo.pop()
                key[i] += d
                for j, _ in kind[2 if d < 0 else 3][i]:
                    if j not in seen and abs(start[j] - start[v]) < wide:
                        seen.add(j)
                        todo.append(j)
        for i in range(n):
            for j, d in kind[2][i]:
                if key[j] >= key[i]:
                    key[i] = key[j] + 1e-6
        lean = (LEAN[0] * r[7], LEAN[1] * r[5])
        s, fin = lay(sorted(order, key=lambda i: key[i]), kind, False, loose, lean)
        if pick[0] < BACK:
            s, fin = lay(sorted(order, key=lambda i: (-fin[i], -i)), kind, True, loose if it & 1 else (), lean)
            s, fin = lay(sorted(order, key=lambda i: (-fin[i], i)), kind, False, (), lean)
        room = -LHEAT * (1 - it / LAYS) * math.log(1 - rng.random())
        if max(x + y for x, y in zip(fin, kind[1])) > last[c] + 0.6 + room * ref[0]:
            qs[:] = old
            continue
        late, line, end = s[:], ([], []), max(fin) + 9
        for i in sorted(pe, key=lambda i: (-s[i], -i)):
            t = end - min([end] + [late[j] - d for j, d in kind[3][i]])
            t, p = fit(line, t, kind[0][i]["T"])
            line[0].insert(p, t)
            line[1].insert(p, t + kind[0][i]["T"])
            late[i] = max(s[i], end - t - kind[0][i]["T"])
        cand = sorted(order, key=lambda i: (late[i], i))
        val = value(cand)
        if val <= now + room:
            now, start, last = val, s, [(x or [1e9])[0] for x in seen_plays]
            chain = []
            for end, fin, why, bank in seen_plays if val < 1e8 else ():
                v = max(order, key=lambda i: fin[i] + kind[1][i])
                while why[v] is not None and why[v] >= 0:
                    if qs[why[v]] == qs[v] and why[v] not in need[v]:
                        chain.append((why[v], v))
                    v = why[v]
            if val < top:
                top, best = val, (cand, qs[:])
        else:
            qs[:] = old
    order, qs[:] = best
    order, qs[:], took = refine(order, qs, kinds, held, nl, mate, ref, rng)
    end, fin, why, bank = play(order, kinds[0])
    bank = {z: x[0] for z, x in took.items()}
    cost = [kinds[0][0][i][qs[i]] for i in range(n)]
    place, takers, runs, lastq = {i: p for p, i in enumerate(order)}, [[] for _ in ops], {}, {}
    for i in order:
        for j in need[i]:
            takers[j].append(i)
    for i in order:
        v = lastq.get(qs[i])
        run = runs.get(v, [v])
        if (v in mate[i] and all(fin[j] + d <= fin[run[0]] - cost[run[0]] + 0.1 for j, d in kinds[0][2][i])
                and all(place[x] > place[i] and fin[x] - cost[x] >= fin[i] for j in run for x in takers[j])):
            runs.pop(v, None)
            runs[i] = run + [i]
        lastq[qs[i]] = i
    PLAN["runs"] = runs
    PLAN["bank"], PLAN["order"], PLAN["qs"] = bank, order, qs
    PLAN["who"] = {ops[i]["tag"]: qs[i] for i in free}
    PLAN["fin"], PLAN["why"], PLAN["cost"], PLAN["ends"] = fin, why, cost, [play(order, k)[0] for k in kinds]
    PLAN["pre"] = kinds[0][2]


def refine_two(order, qs, kinds, held, nl, mate, ref, rng):
    (c0, l0, p0, s0, w0), (c1, l1, p1, s1, w1) = kinds
    n = len(order)
    pre = [[(j, d, e) for (j, d), (_, e) in zip(a, b)] for a, b in zip(p0, p1)]
    post = [[(j, d, e) for (j, d), (_, e) in zip(a, b)] for a, b in zip(s0, s1)]
    up, down = [[j for j, _ in a] for a in p0], [[j for j, _ in a] for a in s0]
    r0, r1 = 1.0 / ref[0], 1.0 / ref[1]
    tau0, tau1 = SOFT, SOFT * 1.6
    exp, log = math.exp, math.log

    def play(calls, state, took):
        line, banks, opened = dict(state[0]), state[1][:], dict(state[2])
        for i in calls:
            q = qs[i]
            t, u, v = line[q]
            for j, d, e in pre[i]:
                if f0[j] + d > t:
                    t = f0[j] + d
                if f1[j] + e > u:
                    u = f1[j] + e
            z = held[i]
            if z is not None:
                o = opened.get(z)
                if o is None:
                    if not banks:
                        return None
                    x = banks.pop(0)
                    took[z] = x[2:]
                    if x[0] > t:
                        t = x[0]
                    if x[1] > u:
                        u = x[1]
                    o = (0.0, 0.0, x[2], nl[z])
            if v in mate[i] and t == f0[v]:
                t -= 0.055
                u -= 0.055
            f0[i] = t = t + c0[i][q]
            f1[i] = u = u + c1[i][q]
            line[q] = (t, u, i)
            if z is not None:
                a, b = max(o[0], t + w0), max(o[1], u + w1)
                if o[3] == 1:
                    opened.pop(z, None)
                    banks.append((a, b, o[2], z))
                    banks.sort()
                else:
                    opened[z] = (a, b, o[2], o[3] - 1)
        return line, banks, opened

    opener = {}
    for i in range(n):
        if held[i] is not None:
            opener.setdefault(held[i], i)
    first = ({q: (0.0, 0.0, -1) for q in "VSTGYR"}, [(0.0, 0.0, k, -1) for k in range(NBANK)], {})
    f0, f1, g0, g1 = ([0.0] * n for _ in range(4))

    def whole(order):
        took = {}
        if not play(order, first, took):
            return 1e9, 0, 0, took
        e0, e1 = max(map(sum, zip(f0, l0))), max(map(sum, zip(f1, l1)))
        return e0 * r0 + e1 * r1, e0, e1, took

    now, e0, e1, took = whole(order)
    best = (now, order, qs[:], took)
    starts = list(range(0, n - WIN + STRIDE, STRIDE))
    for sweep in range(SWEEPS):
        cool, off = HEAT * (1 - sweep / SWEEPS) ** 1.5, int(rng.random() * STRIDE)
        for lo in starts[::-1] if sweep & 1 else starts:
            lo = max(0, min(lo - off, n - WIN))
            hi = lo + WIN
            after, nxt = {x[1]: opener[z] for z, x in took.items()}, {}
            for p in range(n - 1, lo - 1, -1):
                i = order[p]
                if p == hi - 1:
                    lines = [(q, g0[j], g1[j]) for q, j in nxt.items()]
                t, u, q = l0[i], l1[i], qs[i]
                for j, d, e in post[i] + [(j, d, e) for j, d, e in ((after.get(held[i]), w0, w1), (nxt.get(q), 0, 0)) if j is not None]:
                    t, u = max(t, d + g0[j]), max(u, e + g1[j])
                nxt[q] = i
                g0[i], g1[i] = t + c0[i][q], u + c1[i][q]
            win, later, edge = order[lo:hi], set(order[hi:]), []
            state = play(order[:lo], first, {})
            end = play(win, state, {})
            for p, i in enumerate(order[:hi]):
                x = [(d + g0[j], e + g1[j]) for j, d, e in post[i] if j in later] + [(l0[i], l1[i])] * (l0[i] > 0)
                if x:
                    x, y = max(a for a, b in x), max(b for a, b in x)
                    if p >= lo or f0[i] + x > e0 - 8 * tau0 or f1[i] + y > e1 - 8 * tau1:
                        edge.append((i, x, y))
            takers = [(g0[j], g1[j]) for j in order[hi:] if held[j] is not None and opener[held[j]] == j and
                      (took[held[j]][1] < 0 or (took[held[j]][1] not in end[2] and opener[took[held[j]][1]] not in later))]
            nexts = {z: (g0[after[z]], g1[after[z]]) for z in end[2] if z in after}

            def soft(end):
                a = b = 1e-30
                for i, x, y in edge:
                    a += exp((f0[i] + x - e0) / tau0)
                    b += exp((f1[i] + y - e1) / tau1)
                for (t, u), (x, y) in ([(end[0][q][:2], (x, y)) for q, x, y in lines] + [(o[:2], x) for o, x in zip(end[1], takers)]
                                       + [(o[:2], nexts[z]) for z, o in end[2].items() if z in nexts]):
                    a += exp((t + x - e0) / tau0)
                    b += exp((u + y - e1) / tau1)
                return tau0 * log(a) * r0 + tau1 * log(b) * r1

            def again(calls, p):
                p >>= 4
                l = marks[:p + 1]
                for p in range(16 * p, WIN, 16):
                    l.append(play(calls[p:p + 16], l[-1], {}))
                    if not l[-1]:
                        return None
                return l

            marks = [state]
            marks, h0, h1 = again(win, 0), f0[:], f1[:]
            cur = low = soft(end)
            old = keep = (win, [qs[i] for i in win])
            wt = np.array([0.1 + exp(min(0.0, max(f0[i] - c0[i][qs[i]] + g0[i] - e0, (f1[i] - c1[i][qs[i]] + g1[i] - e1) * 0.7)) / 0.7)
                           for i in win])


def refine(order, qs, kinds, held, nl, mate, ref, rng):
    (c0, lat, pre, post, wk), c1, c2 = kinds[0], kinds[1][0], kinds[2][0]
    n = len(order)
    up, down = [[j for j, _ in a] for a in pre], [[j for j, _ in a] for a in post]
    r0, r1, r2 = (1.0 / x for x in ref)
    exp, log = math.exp, math.log

    def play(calls, state, took):
        line, banks, opened = dict(state[0]), state[1][:], dict(state[2])
        for i in calls:
            q = qs[i]
            t, u, s, v = line[q]
            for j, d in pre[i]:
                a, b, c = fin[j]
                if a + d > t:
                    t = a + d
                if b + d > u:
                    u = b + d
                if c + d > s:
                    s = c + d
            z = held[i]
            if z is not None:
                o = opened.get(z)
                if o is None:
                    if not banks:
                        return None
                    x = banks.pop(0)
                    took[z] = x[3:]
                    t, u, s = max(t, x[0]), max(u, x[1]), max(s, x[2])
                    o = (0.0, 0.0, 0.0, x[3], nl[z])
            if v in mate[i] and t == fin[v][0]:
                t, u, s = t - 0.055, u - 0.055, s - 0.055
            t += c0[i][q]
            u += c1[i][q]
            s += c2[i][q]
            fin[i], line[q] = (t, u, s), (t, u, s, i)
            if z is not None:
                x = (max(o[0], t + wk), max(o[1], u + wk), max(o[2], s + wk), o[3])
                if o[4] == 1:
                    opened.pop(z, None)
                    banks.append(x + (z,))
                    banks.sort()
                else:
                    opened[z] = x + (o[4] - 1,)
        return line, banks, opened

    opener = {}
    for i in range(n):
        if held[i] is not None:
            opener.setdefault(held[i], i)
    first = ({q: (0.0, 0.0, 0.0, -1) for q in "VSTGYR"}, [(0.0, 0.0, 0.0, k, -1) for k in range(NBANK)], {})
    fin, way = [None] * n, [None] * n
    plus = lambda d, x: (d + x[0], d + x[1], d + x[2])
    most = lambda l: tuple(map(max, zip(*l)))

    def whole(order):
        took = {}
        if not play(order, first, took):
            return 1e9, None, took
        e = most([plus(lat[i], fin[i]) for i in order[-80:]])
        return e[0] * r0 + e[1] * r1 + e[2] * r2, e, took

    now, ends, took = whole(order)
    best = (now, order, qs[:], took)
    starts = list(range(0, n - WIN + STRIDE, STRIDE))
    for sweep in range(SWEEPS):
        cool, off = HEAT * (1 - sweep / SWEEPS) ** 1.5, int(rng.random() * STRIDE)
        for lo in starts[::-1] if sweep & 1 else starts:
            lo = max(0, min(lo - off, n - WIN))
            hi = lo + WIN
            after, nxt = {x[1]: opener[z] for z, x in took.items()}, {}
            for p in range(n - 1, lo - 1, -1):
                i = order[p]
                if p == hi - 1:
                    lines = [(q, way[j]) for q, j in nxt.items()]
                q = qs[i]
                t, u, s = most([(lat[i],) * 3] + [plus(d, way[j]) for j, d in post[i] + [(after.get(held[i]), wk), (nxt.get(q), 0)]
                                                  if j is not None])
                nxt[q] = i
                way[i] = (t + c0[i][q], u + c1[i][q], s + c2[i][q])
            win, later, edge = order[lo:hi], set(order[hi:]), []
            state = play(order[:lo], first, {})
            end = play(win, state, {})
            e0, e1, e2 = ends
            k0, k1, k2 = 70.0 / SOFT / e0, 70.0 / SOFT / e1, 70.0 / SOFT / e2
            for p, i in enumerate(order[:hi]):
                x = [plus(d, way[j]) for j, d in post[i] if j in later] + [(lat[i],) * 3] * (lat[i] > 0)
                if x and (p >= lo or max(a + b - c for a, b, c in zip(fin[i], most(x), ends)) > -8 * SOFT):
                    edge.append((i, most(x)))
            takers = [way[j] for j in order[hi:] if held[j] is not None and opener[held[j]] == j and
                      (took[held[j]][1] < 0 or (took[held[j]][1] not in end[2] and opener[took[held[j]][1]] not in later))]
            nexts = {z: way[after[z]] for z in end[2] if z in after}

            def soft(end):
                a = b = c = 1e-30
                for x, y in ([(fin[i], y) for i, y in edge] + [(end[0][q], y) for q, y in lines] + list(zip(end[1], takers))
                             + [(o, nexts[z]) for z, o in end[2].items() if z in nexts]):
                    a += exp((x[0] + y[0] - e0) * k0)
                    b += exp((x[1] + y[1] - e1) * k1)
                    c += exp((x[2] + y[2] - e2) * k2)
                return log(a) * r0 / k0 + log(b) * r1 / k1 + log(c) * r2 / k2

            def again(calls, p):
                p >>= 4
                l = marks[:p + 1]
                for p in range(16 * p, WIN, 16):
                    l.append(play(calls[p:p + 16], l[-1], {}))
                    if not l[-1]:
                        return None
                return l

            marks = [state]
            marks, kept = again(win, 0), fin[:]
            cur = low = soft(end)
            old = keep = (win, [qs[i] for i in win])
            wt = np.array([0.1 + exp(max(fin[i][k] - c[i][qs[i]] + way[i][k] - ends[k] for k, c in enumerate((c0, c1, c2))) / 0.8)
                           for i in win])
            for v, r in zip(rng.choice(win, EACH, p=wt / wt.sum()).tolist(), rng.random((EACH, 7)).tolist()):
                pv, flips, cand = win.index(v), [], win
                at = pv
                if r[1] < 0.3 and len(c0[v]) > 1:
                    q = [x for x in c0[v] if x != qs[v]]
                    q = q[int(r[2] * len(q))]
                    flips.append((v, qs[v]))
                    near = [i for i in win[max(0, pv - 25):pv + 25] if qs[i] == q and qs[v] in c0[i]] if r[3] < 0.4 else []
                    if near:
                        w = near[int(r[4] * len(near))]
                        flips.append((w, q))
                        qs[w], at = qs[v], min(at, win.index(w))
                    qs[v] = q
                if not flips or r[5] < 0.5:
                    hops, q, step = 1 + int(5 * r[2] ** 3), qs[v], -1 if r[4] < 0.5 else 1
                    p = pv + step
                    while 0 <= p < WIN:
                        if qs[win[p]] == q:
                            hops -= 1
                            if not hops:
                                break
                        p += step
                    p, links = min(max(p, 0), WIN - 1), up if step < 0 else down
                    seen, a, b = set(links[v]), [v], []
                    for i in win[p:pv][::-1] if step < 0 else win[pv + 1:p + 1]:
                        if i in seen:
                            seen.update(links[i])
                            a.append(i)
                        else:
                            b.append(i)
                    if b:
                        cand = win[:p] + a[::-1] + b[::-1] + win[pv + 1:] if step < 0 else win[:pv] + b + a + win[p + 1:]
                        at = min(at, p)
                    elif not flips:
                        continue
                l = again(cand, at)
                if l:
                    x = soft(l[-1])
                    if x <= cur - cool * log(1 - r[6]):
                        cur, win, marks, kept = x, cand, l, fin[:]
                        if x < low:
                            low, keep = x, (win, [qs[i] for i in win])
                        continue
                fin[:] = kept
                for i, q in flips:
                    qs[i] = q
            for i, q in zip(*keep):
                qs[i] = q
            cand = order[:lo] + keep[0] + order[hi:]
            got = whole(cand)
            if got[0] <= now + 2 * cool + 0.0005:
                order = cand
                now, ends, took = got
                if now < best[0]:
                    best = (now, order, qs[:], took)
            else:
                for i, q in zip(*old):
                    qs[i] = q
                whole(order)
    return best[1:]


def rank_program(g, core, T, topo):
    rank = T.rank_of(core)
    if rank is None:
        return
    if not PLAN:
        schedule(record(g, core, T, topo, rank, {}))
    issue(g, T, record(g, core, T, topo, rank, PLAN["bank"]))


def record(g, core, T, topo, rank, banks):
    A = AluOpType
    AF = ActivationFunctionType
    ops = []
    sg = 16 if BYDMA else 1
    nlease = [0]
    at = [""]

    def psum():
        nlease[0] += 1
        return nlease[0]

    def X(name, c0, c1, step=1, p=None, rows=ALL):
        name = SAME.get(name, name)
        buf, o = PACK.get(name, (name, 0))
        t = T["PB%d" % banks.get(name, 0)] if isinstance(name, int) else T[buf]
        p0, p1 = p if p else (0, 128)
        ap = t[p0:p1, o + c0:o + c1] if step == 1 else t[p0:p1, o + c0:o + c1:step]
        return (ap, [(name, c0, c0 + (c1 - c0 - 1) // step * step + 1, step, rows)])

    def ind(win, off):
        return (win[0].indirect(off[0]), win[1] + off[1], True)

    def rec(kind, q, outs, ins, fn, cost, lat=0.0, data=None):
        reads = list(dict.fromkeys(r for x in ins for r in x[1]))
        writes = list(dict.fromkeys(r for x in outs for r in x[1]))
        ops.append({"kind": kind, "q": q, "r": reads, "w": writes, "fn": fn, "cost": {q: cost}, "lat": lat, "data": data,
                    "tag": "%s%s" % (writes[0][0], at[0]) if kind == "c" else None, "gat": any(len(x) > 2 for x in ins)})

    def either(tag, k):
        run = ops[-k:]
        del ops[len(ops) - k + 1:]
        run[0].update(kind="g", tag=tag or run[0]["tag"], r=list(dict.fromkeys(x for o in run for x in o["r"])), fn={o["q"]: o["fn"] for o in run},
                      cost={o["q"]: o["cost"][o["q"]] for o in run})

    def run(k, tag):
        l = ops[-k:]
        del ops[len(ops) - k + 1:]
        l[0].update(kind="m", tag=tag, fn=[o["fn"] for o in l], cost={l[0]["q"]: sum(o["cost"][o["q"]] for o in l)},
                    r=list(dict.fromkeys(x for o in l for x in o["r"])), w=[x for o in l for x in o["w"]])

    def width(x):
        return x[0].shape[1]

    def emit(q, outs, ins, fn, cyc=1.0):
        n = width(outs[0])
        rec("c", q, outs, ins, fn, 0.06 + n * GAT * CYC if len(ins[0] if ins else ()) > 2 else 0.01 + max(64, cyc * n) * CYC)

    def wide(x):
        return lease(x[1][0]) is not None or x[1][0][0] not in PACK and SCRATCH[x[1][0][0]][2] not in ("bfloat16", "uint16", "float16")

    def two(*xs):
        return not any(wide(x) for x in xs)

    def vcopy(o, i):
        emit("V", [o], [i], lambda e: e.tensor_copy(o[0], i[0]), 0.5 if two(o, i) else 1.0)

    def vtt(o, a, b, op):
        cyc = 2.0 if lease(a[1][0]) is None and lease(b[1][0]) is None else 1.0
        emit("V", [o], [a, b], lambda e: e.tensor_tensor(o[0], a[0], b[0], op), cyc)

    def vts(o, i, s1, op0, s2=None, op1=None):
        ins = [i] + [s for s in (s1, s2) if isinstance(s, tuple)]
        a1 = s1[0] if isinstance(s1, tuple) else s1
        a2 = s2[0] if isinstance(s2, tuple) else s2
        cyc = 0.5 if two(o, i) else 1.0
        if op1 is None:
            emit("V", [o], ins, lambda e: e.tensor_scalar(o[0], i[0], a1, None, op0), cyc)
        else:
            emit("V", [o], ins, lambda e: e.tensor_scalar(o[0], i[0], a1, a2, op0, op1), cyc)

    def scan(o, a, b, init, op0, op1):
        emit("V", [o], [a, b], lambda e: e.tensor_tensor_scan(o[0], a[0], b[0], init, op0, op1), 0.5 if two(o, a, b) else 1.0)

    def vset(o, c):
        emit("V", [o], [], lambda e: e.memset(o[0], c), 0.5 if two(o) else 1.0)

    def act(o, i, func=AF.Copy, bias=0.0, scale=1.0):
        ins = [i] + [x for x in (bias, scale) if isinstance(x, tuple)]
        b = bias[0] if isinstance(bias, tuple) else bias
        s = scale[0] if isinstance(scale, tuple) else scale
        emit("S", [o], ins, lambda e: e.activation(o[0], i[0], func, bias=b, scale=s))

    def move(o, i, bias=0.0, scale=1.0, tag=None):
        if bias or scale != 1.0:
            vts(o, i, scale, A.mult, bias, A.add)
        else:
            vcopy(o, i)
        act(o, i, AF.Identity if bias else AF.Copy, bias, scale)
        either(tag, 2)

    def gather(tag, o, i):
        move(o, i, tag=tag)

    def pieces(make, a, b, n, name, behind=None):
        l = []
        for c in range(a, b, n):
            make(c, c + n)
            l.append(len(ops) - 1)
            ops[-1].update(tag=name + str(c // n), span=(c, c + n), make=make, mate=())
            if behind:
                behind(c, c + n)
        for i, j in zip(l, l[1:]):
            ops[i]["mate"] += (j,)
            ops[j]["mate"] += (i,)

    def iota(o, pattern, base, cm, fl=False):
        c = 0.14 + 2 * width(o) * CYC
        if fl:
            rec("c", "G", [o], [], lambda e: e.iota(o[0], pattern, base, cm, allow_small_or_imprecise_dtypes=True), c)
        else:
            rec("c", "G", [o], [], lambda e: e.iota(o[0], pattern, base, cm), c)

    def gset(o, c):
        iota(o, [[0, width(o)]], c, 0, True)

    def gsel(o, i, pattern, op, fill, base, cm):
        rec("c", "G", [o], [i], lambda e: e.affine_select(o[0], i[0], pattern, op, fill, base, cm), 0.18 + 2 * width(o) * CYC)

    def gcopy(o, i):
        gsel(o, i, [[0, width(o)]], A.is_ge, 0.0, 0, 0)

    def mms(lst):
        cost = sum(max(min(64, width(m[1])), width(m[2])) * (4 if wide(m[1]) else 1) for m in lst
                   if len(m) == 5 or m[5][1] == "S") * PEC
        rec("t", "T", [m[0] for m in lst], [x for m in lst for x in (m[1], m[2])], None, cost, 0.0, lst)

    def acc(lst, first=True, last=True):
        mms([m[:3] + (first and n == 0, last and n == len(lst) - 1) + m[3:] for n, m in enumerate(lst)])

    def group(b, head, rest, n, after):
        acc(head, True, False)
        ops[-1]["r"] += after[1]
        for c in range(0, len(rest), n):
            acc(rest[c:c + n], False, False)
            ops[-1]["fn"] = b

    def dma(q, outs, ins, pairs, lat=2.3, tag=None):
        rec("d", q, outs, ins, None, 0.06 * len(pairs), lat, pairs)
        ops[-1]["tag"] = tag

    dma("Y", [X("SELR", 0, 208)], [], [(T.SELR[:], T.sel0[:])], 2.5, "sel")
    for j, (a, b, lat) in enumerate(FRONT):
        dma("Y", [X("F", 16 + 208 * a, 16 + 208 * b)], [], [(T.F[:, 16 + 208 * a:16 + 208 * b], T.front[:, 208 * a:208 * b])], lat, "fr%d" % j)
    dma("Y", [X("raw", 0, 256)], [], [(T.raw[:], T.par[:])], LAT[0], "par")

    ncol = [0]

    def col():
        ncol[0] += 1
        return X("cols", ncol[0] - 1, ncol[0])

    PI, CI = X("PI", 0, 1), X("CI", 0, 128)
    ID, NID, ONES, ID32 = X("ID", 0, 128), X("NID", 0, 128), X("ONES", 0, 128), X("ID32", 0, 128)
    LE = lambda nm, e, p=None: X(nm, 15 - e, 143 - e, p=p)
    ti = [X("ti", j, j + 1) for j in range(8)]
    iota(PI, [[0, 1]], 0, 1)
    iota(X("CI", 0, 144), [[1, 144]], 0, 0)
    iota(X("LB", 0, 256), [[0, 4], [1, 64]], 16, 0, True)
    iota(X("HB", 0, 256), [[1, 4], [0, 64]], 129, 0, True)
    vset(X("T2", 0, 1040), 0.0)

    move(X("CF", 0, 1024), X("T2", 0, 1024), TOP, 0.0, "CF")

    def zero(nm, a, b):
        vset(X(nm, a, b), 0.0)
        act(X(nm, a, b), X("T2", 0, b - a))
        gset(X(nm, a, b), 0)
        either("0%s%d" % (nm, a // 768), 3)

    for a in range(0, FW, 1040):
        zero("PT", a, min(FW, a + 1040))
    uf, gf, zf, u4, u3, zs = col(), col(), col(), col(), col(), col()
    vts(ti[0], PI, 15, A.bitwise_and)
    vts(ti[1], PI, 4, A.arith_shift_right)
    vts(ti[2], PI, 7, A.bitwise_and)
    vcopy(uf, ti[0])
    vcopy(gf, ti[1])
    vts(zf, ti[1], 16.0, A.mult, 15.0, A.add)
    vts(zs, ti[2], 16.0, A.mult, 15.0, A.add)
    act(u4, uf, scale=256.0)
    act(X("HB", 0, 256), X("HB", 0, 256), AF.Identity, bias=u4, scale=64.0)
    Z = lambda n: X("ZERO", 0, n)
    vset(Z(144), 0.0)

    def line(o, c, pattern, base, i=None):
        gsel(o, i or Z(width(o)), pattern, A.not_equal, c, base, 1)

    def block(o, c, pattern):
        gsel(o, Z(width(o)), [[-a, n] for a, n in pattern], A.is_gt, c, 0, -1)
        gsel(o, o, [[-a, n] for a, n in pattern], A.is_ge, 0.0, 15, -1)

    def fill(o, c, i):
        vset(o, float(c))
        act(o, i, scale=float(c))
        if c:
            gsel(o, i, [[0, width(o)]], A.is_gt, float(c), 0, 0)
        else:
            gset(o, 0)
        either(None, 3)

    def prow(r, buf, n, tab="PT"):
        dma("Y", [X(tab, 16, 16 + 16 * n, rows=1 << r)], [X(buf, 0, n)], [(T[SAME.get(tab, tab)][r::16, 16:16 + 16 * n], T[buf][:, 0:n])],
            LAT[3], "row%d" % r)

    vts(X("SHB", 0, 208), X("SELR", 0, 208), HIGH - 31.5, A.add)
    vts(X("SELO", 0, 208), X("SELR", 0, 208), 63, A.bitwise_and)
    vts(X("SLB", 0, 208), X("SELO", 0, 208), 16.0, A.add)
    for j, buf in enumerate(("SHB", "SLB")):
        dma("Y", [X("SR", 16, 16 + I0, rows=1 << j)], [X(buf, 0, 208)], [(T[SAME["SR"]][8 * j:8 * j + 8, 16:16 + I0], T[buf][:, 0:208])],
            LAT[3], "sr%d" % j)
    for a in range(1040, 16 + I0, 768):
        zero("T2", a, a + 768)
    prow(2, "SHB", 208, "T2")
    prow(10, "SLB", 208, "T2")
    prow(1, "SHB", 208)
    prow(9, "SLB", 208)
    prow(0, "HB", 256)
    prow(8, "LB", 256)
    vts(X("LEs", 0, 144), X("CI", 0, 144), zs, A.is_equal)
    vts(X("LE", 0, 144), X("CI", 0, 144), zf, A.is_equal)
    vcopy(u3, ti[2])
    vts(X("WC", 0, 8), X("CI", 0, 8), u3, A.is_equal)
    w = [X("WC", d, d + 1) for d in range(8)]
    for d in (1, 2, 3):
        act(X("LE%d" % d, 0, 144), X("LE", 0, 144), scale=w[d])
    for nm in ("F", "TT"):
        act(X(nm, 0, 16), Z(16))

    def lists(src, s0, n, le, p=None):
        b = psum()
        acc([(X(b, 0, n), LE(le, e, p), X(src, s0 + e, s0 + 16 * n, 16, p=p)) for e in range(16)])
        return b

    for j in (0, 1):
        vts(X("SL1", 104 * j, 104 * j + 104), X(lists("SR", 16 + CUT * j, 104, "LEs", (0, 16)), 0, 104), -HIGH, A.add)
    b = psum()
    for c, d, _ in FRONT:
        acc([(X(b, 0, 208), LE("LE", e), X("F", 16 + 208 * e, 224 + 208 * e)) for e in range(c, d)], c == 0, d == 16)
    vcopy(X("SCH", 0, 208), X(b, 0, 208))
    vtt(X("SCL", 0, 208), X(b, 0, 208), X("SCH", 0, 208), A.subtract)
    prow(5, "SCH", 208, "T2")
    prow(7, "SCH", 208)
    prow(13, "SCL", 208, "T2")
    prow(15, "SCL", 208)

    def shift(dst, d0, moves):
        dma("Y", [X("PT", 16, 16 + I0, rows=sum(257 << b for a, b in moves))], [X(dst, d0, d0 + I0)],
            [(T.PT[b::8, 16:16 + I0], T[SAME[dst]][a::8, d0:d0 + I0]) for a, b in moves], LAT[4])

    n = 208 // PARTS
    pt = lambda a, b: X("PT", 16 + 16 * a, 16 + 16 * b)
    pieces(lambda a, b: vtt(pt(a, b), ind(X("T2", 0, 16 + I0), X("SL1", a, b)), pt(a, b), A.add), 0, 208, n, "a")
    for j in (0, 1):
        vts(X("SL2", 104 * j, 104 * j + 104), X(lists("PT", 16 + CUT * j, 104, "LE2"), 0, 104), -HIGH, A.add)
    pieces(lambda a, b: move(X("T3", 16 * a, 16 * b), ind(X("PT", 0, 16 + I0), X("SL2", a, b))), 0, 208, n, "b")
    tt = lambda a, b: X("TT", 16 + 16 * a, 16 + 16 * b)

    def own(a, b):
        dma("G", [tt(a, b)], [tt(a, b)], [(tt(a, b)[0], T.front[:, 16 * a:16 * b])], ADD + 0.4 * a / n, "add%d" % (a // n))
        ops[-1]["cost"]["G"] = 1.0 if a else 2.0

    pieces(lambda a, b: move(tt(a, b), ind(X("F", 0, 16 + I0), X("SL1", a, b)), scale=1.0 / 1024), 0, 208, n, "t", own)

    for h in (0, 1):
        vts(X("PL", 128 * h, 128 * h + 128), X("raw", h, 256, 2), 16.0, A.add)
        move(X("NUM", 128 * h, 128 * h + 128), X("raw", h, 256, 2), 16.0)
    C8 = X("CI", 0, 8)
    vts(X("W1", 0, 8), C8, gf, A.is_equal)
    vcopy(X("BC", 0, 8), C8)
    vset(ONES, 1.0)
    iota(X("CC", 0, 8), [[-2, 8]], 0, 0, True)
    iota(X("KCON", 0, 128), [[0, 8], [-1, 16]], 15, 0, True)
    move(X("KC", 0, 128), X("KCON", 0, 128))
    fill(X("KC", 128, 256), 0.0, ONES)
    for nm, c in (("RST", -BIG), ("RSK", -128 * BIG)):
        fill(X(nm, 0, 256), 0.0, X("CF", 0, 256))
        fill(X(nm, 0, 256, 16), c, X("ONES", 0, 16))
    u15, u16 = col(), col()
    act(u15, uf, AF.Identity, bias=15.0, scale=-1.0)
    vts(X("MSK", 0, 128), X("KCON", 0, 128), u15, A.is_equal)
    act(u16, uf, AF.Identity, bias=15.0, scale=16.0)
    for j in (0, 1):
        act(X("W16", 8 * j, 8 * j + 8), X("W1", 0, 8), scale=16.0)
    line(ID, 1.0, [[-1, 128]], 0)
    for o, c in ((NID, -1.0), (ID32, 1.0), (X("N64", 0, 128), -64.0), (X("IDK", 0, 128), 1.0 / 16384),
                 (X("I16", 0, 128), 1.0 / 16), (X("NI32", 0, 128), -1.0), (X("I5", 0, 128), 5.0 * PR)):
        line(o, c, [[-1, 128]], 0)
        act(o, ID, scale=c)
        either(None, 2)
    line(X("N8", 0, 128), -1.0, [[-1, 128]], 8)
    block(X("NBD", 0, 128), -1.0, [[-16, 8], [0, 16]])
    act(X("WG", 0, 128), X("NBD", 0, 128), scale=2 * BIG)
    vts(X("NG", 0, 128), ID, -1025.0 / 16384, A.mult)
    act(X("WO", 0, 64), X("NBD", 1, 128, 2), scale=-1.0 / 16)
    act(X("W8", 0, 16), X("W16", 0, 16), scale=0.5)
    act(X("W8K", 0, 16), X("W16", 0, 16), scale=PR / 2)
    act(X("W16K", 0, 16), X("W16", 0, 16), scale=float(PR))
    iota(X("KCK", 0, 256), [[0, 16], [-PR, 16]], 15 * PR, 0, True)
    for nm, c in (("WB", BIG), ("WD", -2 * sg * BIG), ("WN", -1.0 / 16)):
        act(X(nm, 0, 8), X("W1", 0, 8), scale=c)
    for d in range(1, 5):
        act(X("WX", 8 * (4 - d), 8 * (5 - d)), X("W1", 0, 8), scale=w[d])
    act(X("YSM", 0, 8), X("W1", 0, 8), scale=w[0])
    for j in (0, 1):
        vts(X("WS", 8 * j, 8 * j + 8), X("W1", 0, 8), w[5 + 2 * j], A.mult, 2 * BIG, A.mult)
    iota(X("CVX", 0, 128, p=(0, 64), rows=1), [[1024, 128]], -10240, 0, True)
    iota(X("OFR", 0, 128), [[-512, 128]], 0, 0, True)
    for nm, a, b in [("CK", 24576 * 1024, -16 * 1024), ("CVX", 0, -768)] + [("CE", 16384 * 1024, 32 * 1024)] * bool(BYDMA):
        if a:
            fill(X(nm, 0, 128, p=(0, 64), rows=1), a, X("ONES", 0, 128, p=(0, 64)))
        fill(X(nm, 0, 128, p=(64, 128), rows=2), b, X("ONES", 0, 128, p=(64, 128)))
    fill(X("SIX", 0, 128), 6 * BIG / 128, ONES)
    fill(X("OS", 0, 128), 1.0 / PR, ONES)
    cd = {d: col() for d in (1, 2, 3)}
    for d in cd:
        iota(cd[d], [[0, 1]], -PR * d, int(BIG), True)
    for j in (0, 1):
        fill(X("GM%d" % j, 0, 528), 0.0, X("CF", 0, 528))
        move(X("GM%d" % j, 15, 528, 16), X("MSK", j, j + 66, 2), -256.0)
    iota(X("KI", 0, 256), [[5, 2], [10, 128]], 0, 37)
    iota(X("KI", 256, 512), [[1, 2], [2, 128]], 0, 1)
    vts(X("KI", 0, 256), X("KI", 0, 256), 255, A.bitwise_and)
    vts(X("KI", 256, 512), X("KI", 256, 512), 127, A.bitwise_and)
    for h in (0, 1):
        iota(X("KK%d" % h, 0, 128), [[2, 128]], h, 0, True)
        move(X("KK%d" % h, 128, 256), X("KI", 128 * h, 128 * h + 128))
        move(X("KK%d" % h, 256, 384), X("KI", 256 + 128 * h, 384 + 128 * h))
    starts = lambda t: [I0 + NB * t - (16 if t + 1 == R else 0) + c - PR for c in (16, 2016, 208)]
    for t in range(R):
        for j, c in enumerate(starts(t)):
            iota(X("CB%d" % t, 128 * j, 128 * j + 128, p=(0, 2)), [[0, 128]], c // 256 * 256, c % 256 - c // 256 * 256, True)
    line(X("SH", 0, 128), 1.0, [[-1, 128]], 1)
    for c in (0, 5):
        gset(X("SH", c, 128, 8), 0)
    gset(X("D01", 0, 128), 0)
    line(X("D01", 0, 128, 8), 1.0, [[-8, 16]], 0)
    if HY:
        gset(X("SH3", 0, 128), 0)
        line(X("SH3", 4, 128, 8), 1.0, [[-8, 16]], -1)
        line(X("SH3", 7, 128, 8), 1.0, [[-8, 16]], -7)
        gset(X("SH7", 0, 128), 0)
        line(X("SH7", 5, 128, 8), 1.0, [[-8, 16]], -7)

    def choose(z, data, after):
        zs, b = (128 * z, 128 * z + 128), psum()
        group(b, [(X(b, 0, 256), X("ONES", 0, 128, p=(0, 1)), X("KC", 0, 256, p=(0, 1)))], data(b), 8 if z == 2 else 16, after)
        scan(X("SK", 256 * z, 256 * z + 256), X("RST", 0, 256), X(b, 0, 256), 0.0, A.add, A.max)
        mx = X("MX", 8 * z, 8 * z + 8)
        vtt(mx, X("SK", 256 * z + 15, 256 * z + 128, 16), X("SK", 256 * z + 143, 256 * z + 256, 16), A.subtract)
        vtt(X("GE", *zs), ind(mx, X("BC", 0, 8)), X("MSK", 0, 128), A.mult)
        o = X(psum(), 0, 8)
        acc([(o, ONES, X("CC", 0, 8)), (o, X("GE", *zs), X("W1", 0, 8))])
        vts(X("OFF", 8 * z, 8 * z + 8), o, -1.0, A.mult, u16, A.add)
        if z < 2:
            o = X(psum(), 0, 128)
            acc([(o, X("GE", *zs), ID)])
            move(X("EL", *zs), o, scale=-1.0)
            o = X(psum(), 0, 128)
            acc([(o, X("NBD", 0, 128), X("EL", *zs))])
            vts(X("GT", *zs), o, u15, A.is_equal, float(PR), A.mult)

    def signs(z, src, gm):
        for j in range(4):
            pd = psum()
            acc([(X(pd, 128 * i, 128 * i + 128), NID, X(src, 4 * j + i, 2048, 16)) for i in range(4)], True, False)
            acc([(X(pd, 128 * i, 128 * i + 128), ID, gm) for i in range(4)], False, True)
            o = X("cz", 512 * j, 512 * j + 512)
            act(o, X(pd, 0, 512), AF.Sign, bias=0.5)
            vts(o, X(pd, 0, 512), 0.0, A.is_ge, 0.5, A.subtract)
            either("z%s%d%d" % (src[1], z, j), 2)

    def grow(src, n, c0, y0, tt, fronts, more):
        if tt + 1 < R:
            b, st, l, late = psum(), n // 128, [], []
            for j, x in enumerate(fronts):
                a = EARLY if j in dict(more) else 0
                if a:
                    l += [(X(b, j, st * a, st), X("SH7", 0, 128), X(src, j, st * a, st)), (X(b, j, st * a, st), X("SH3", 0, 128), dict(more)[j])]
                if a < 128:
                    x = X(x[0], x[1] + a, x[1] + 128)
                    o, hh, y = X(psum(), 0, 128 - a), X("HH", 128 * j + a, 128 * j + 128), X(b, j + st * a, n, st)
                    acc([(o, LE("LE", 5), x)])
                    move(hh, o)
                    l.append((y, LE("LE", 13), x))
                    late += [(y, ID, hh), (y, X("N8", 0, 128), hh)]
            o = X(b, 0, n)
            group(b, [(o, X("D01", 0, 128), X("PT", c0, c0 + n)), (o, X("SH", 0, 128), X(src, 0, n))] + l, late, 9, X(src, 0, n))
            move(X("PT", c0, c0 + n), o)
        y = X(psum(), 0, n, p=(0, 8))
        acc([(y, X("YSM", 0, 8), X(src, 0, n))])
        move(X("YS", y0, y0 + n, p=(0, 8)), y, bias=-16.0 - HIGH)
        dma("Y", [], [X("YS", y0, y0 + n)], [(T.ys[:, y0:y0 + n], T.YS[0:8, y0:y0 + n])])

    def pairs(out, own, far):
        o = X(psum(), 0, 128)
        acc([(o, X("I16", 0, 128), own), (o, X("IDK", 0, 128), far)])
        move(out, o, scale=16.0 / sg)

    def come(tt):
        cc = 16 + I0 + NB * tt + L
        at[0] = "%d2" % tt
        signs(2, "f%d0" % tt, X("F", cc, cc + 128))
        tg = ["z%d2%d" % (tt, j) for j in range(4)]
        data = lambda b, x: [(X(b, k, 256, 16), X("cz", 128 * k, 128 + 128 * k), X(wt + x, 0, 16), (tg[k >> 2], q))
                             for k in range(16) for q, wt in (("S", "W8"), ("V", "W16"))]
        if tt + 1 == R:
            b, y, y0 = psum(), X(psum(), 0, 128, p=(0, 8)), NB * tt + L
            group(b, [(X(b, 0, 256), X("ONES", 0, 128, p=(0, 1)), X("KCK", 0, 256, p=(0, 1))), (X(b, 0, 128), X("NUM", 0, 128), ID32)],
                  data(b, "K"), 8, X("F", cc, cc + 128))
            scan(X("SK", 512, 768), X("RSK", 0, 256), X(b, 0, 256), 0.0, A.add, A.max)
            acc([(y, X("SK", 527, 640, 16), ID32), (y, X("SK", 655, 768, 16), X("NI32", 0, 128))])
            move(X("YS", y0, y0 + 128, p=(0, 8)), y, bias=-16.0)
            dma("Y", [], [X("YS", y0, y0 + 128)], [(T.ys[:, y0:y0 + 128], T.YS[0:8, y0:y0 + 128])])
            return
        choose(2, lambda b: data(b, ""), X("F", cc, cc + 128))
        gather("c%d2" % tt, X("PC", 0, 128), ind(X("px%d0" % tt, 0, 2048), X("OFF", 16, 24)))
        if tt + 1 < R:
            gather("h%d2" % tt, X("FC", 0, 128), ind(X("f%d0" % tt, 0, 2048), X("OFF", 16, 24)))
            pairs(X("TT", cc, cc + 128), X("F", cc, cc + 128), X("FC", 0, 128))
        more = []
        if (tt, 0) in HY:
            more = [(0, X("PS2", 256, 256 + EARLY))]
            gather("d%d2" % tt, more[0][1], ind(X("py0", 0, 16 * EARLY), X("OFF", 16, 16 + EARLY // 16)))
        grow("PC", 128, cc, NB * tt + L, tt, [("FC", 0)], more)

    def parents(nm, dst, window, a=0, b=128, lst="PL", p0=None):
        n, p0 = 128 // PIECES, p0 or 128 * int(at[0][1])
        pieces(lambda a, b: move(X(dst, 16 * a, 16 * b), ind(window, X(lst, p0 + a, p0 + b))), a, b, n, nm + at[0])

    G = [X("GB", 128 * h, 128 * h + 128) for h in (0, 1)]
    sent = [0]
    for t in range(R):
        B = I0 + NB * t
        cc = 16 + B + L
        win = X("F", 0, 16 + B)
        pwin = X("PT", 0, 16 + B)
        HS = [(128 * h, 128 * h + 128) for h in (0, 1)]
        for h in (0, 1):
            fn, gx, at[0] = "f%d%d" % (t, h), "GX%d" % h, "%d%d" % (t, h)
            parents("f", fn, win)
            choose(h, lambda b: [(X(b, k, 256, 16), X(fn, k, 2048, 16), X("W16", 0, 16)) for k in range(16)], X(fn, 0, 512))
            chosen = ind(X(fn, 0, 2048), X("OFF", 8 * h, 8 * h + 8))
            move(X(gx, 0, 2048, 16), chosen, MID * 16 / sg, -1025.0 / 1024 / sg, "G" + at[0])
            move(G[h], X(gx, 0, 2048, 16), MID * 16384 / 1025, -1024.0 * sg / 1025, "g" + at[0])
            cuts = CUTS.get((t, h), (0, 64)) + (128 - SLANES.get((t, h), 0),)
            for c, (a, b) in enumerate(zip(cuts, cuts[1:])):
                for j, k in enumerate((8, 4, 2, 1) if a < b else ()):
                    for copy in (gcopy, vcopy, act):
                        copy(X(gx, 16 * a + k, 16 * b, 2 * k), X(gx, 16 * a, 16 * b, 2 * k))
                    either("r%d%d%d%d" % (t, h, c, j), 3)
        for h in (0, 1):
            pn, c0, at[0] = "px%d%d" % (t, h), 512 * h, "%d%d" % (t, h)

            def tolist(o, a, b, d, less):
                m = 128 - SLANES.get((t, h), 0) if d & 1 else 128
                if a < m:
                    q0 = c0 + 128 * (4 - d)
                    vts(X("QL", q0 + a, q0 + min(b, m)), X(o, 0, min(b, m) - a), less, A.subtract)
                    ops[-1]["tag"] += "%d%d" % (d, a // 64)
                if b > m:
                    vts(X("QS", 128 * h + d // 2, 128 * h + 256 - 2 * m, 2), X(o, m - a, b - a), less, A.subtract)
                    ops[-1]["tag"] += str(d)

            def keys(src, ds, ls, a=0, e=128):
                for d in ls:
                    for c in range(a, e, 64) if (t, h, d, a) in DIRECT else ():
                        tolist(lists(src, 16 * c, 64, "LE%d" % (d - ds[0] + 1)), c, c + 64, d, HIGH)
                n, b, p, rows = 128 * len(ds), psum(), (a, e), ALL if e - a == 128 else 1 << a // 64
                group(b, [(X(b, c, c + 128, p=p), X("ONES", a, e), X("CVX", 0, 128)) for c in range(0, n, 128)],
                      [(X(b, k, n, 16, p=p), X(src, 16 * a + k, 16 * e, 16), X("WX", 32 - n // 16, 32)) for k in range(16)],
                      16, X(src, 16 * a, 16 * a + 512))
                for d in ds:
                    j, i = 4 - d, ds[-1] - d
                    move(X("CO", c0 + j, c0 + 512, 4, p=p, rows=rows), X(b, 128 * i, 128 * i + 128, p=p),
                         bias=10.75 * BIG - PR * d - HIGH)
                    ops[-1]["tag"] += "%d%d" % (d, a // 64)
                for d in ls:
                    if (t, h, d, a) not in DIRECT:
                        o = psum()
                        acc([(X(o, 0, e - a), X("CO", c0 + 4 - d, c0 + 512, 4, p=p, rows=rows), X("ID32", a, e, p=p))])
                        tolist(o, a, e, d, cd[d])

            a = EARLY if (t, h) in HY else 0
            if a:
                parents("x", pn, pwin, 0, a)
                keys(pn, (1, 2), (1, 2), 0, a)
                parents("y", "py%d" % h, pwin, 0, a, "QL", c0 + 256)
                keys("py%d" % h, (3, 4), (3,), 0, a)
                shift("T3", 0, [(1, 3), (2, 4), (5, 7), (7, 6)])
            if a < 128:
                parents("x", pn, pwin, a)
                keys(pn, (1, 2, 3, 4), (1, 3), a)
        for h in (0, 1):
            at[0] = "%d%d" % (t, h)
            fn, y0 = "f%d%d" % (t, h), 1024 * h
            for j in (0, 1):
                pd = psum()
                for wt, x in (("I16", 0), ("IDK", 1)):
                    acc([(X(pd, 128 * i, 128 * i + 128), X(wt, 0, 128), X(fn, 8 * j + 2 * i + x, 2048, 16)) for i in range(4)], not x, False)
                acc([(X(pd, 128 * i, 128 * i + 128), X("NG", 0, 128), G[h]) for i in range(4)], False, True)
                move(X("cy", y0 + 512 * j, y0 + 512 * j + 512), X(pd, 0, 512), MID, tag="z%d%d%d" % (t, h, j))
            for j, c in ((1, 767 + 5.5 / 32), (0, 16 * 32832 - 32 * 10.5)):
                b = psum()
                l = [(X(b, 0, 64), G[h], X("WO", 0, 64))] + [(X(b, i, 64, 8), X(fn, 2 * i, 2048, 16), X("WN", 0, 8)) for i in range(8)]
                acc(l * j + [(X(b, i, 64, 8), X("cy", y0 + 128 * i, y0 + 128 * i + 128), X("W1", 0, 8)) for i in range(8)])
                act(X("SG", 128 * h + j, 128 * h + 128, 2), X(b, 0, 64), AF.Sign, bias=c, scale=-1.0)
                if j:
                    cy = X("cy", y0, y0 + 1024)
                    dma("G", [cy], [cy, X("CF", 0, 1024)], [(cy[0], T.CF[:])], DLAT, "Z" + at[0])
                    ops[-1]["cost"]["G"] = 1.0
            o = X(psum(), 0, 128)
            acc([(o, X("SG", *HS[h]), X("I5", 0, 128))])
            vtt(X("T0", *HS[h]), o, X("NUM", *HS[h]), A.min)

        def tests(h, a, b):
            ca, gx, c0, at[0] = psum(), "GX%d" % h, 512 * h, "%d%d" % (t, h)
            pn, twin, p = "px%d%d" % (t, h), X("TT", 0, 16 + B), (a, b)
            rows = ALL if b - a == 128 else 1 << a // 64
            m = min(b, 128 - SLANES.get((t, h), 0))
            thr = 767.75 / sg

            def compare(tag, o, x, outs):
                vts(o, x, thr, A.is_le)
                act(o, x, AF.Sign, bias=thr, scale=-1.0)
                either(tag, 2)
                return [(y, X("ONES", 0, y[0].shape[0]), X("SIX", 0, 128), (tag, "S")) for y in outs]

            def sums(l, col0, src, x0, step, wt, a, b):
                acc(l + [(X(ca, 4 * k + col0, 512, 64, p=(a, b)), X(src, x0 + k, x0 + step * (b - a - 1) + 16, step), X(wt, 0, 8))
                         for k in range(16)] + [(X(ca, col0, 512, 64, p=p), X("ONES", *p), Z(8))] * ((a, b) != p), False, False)
                ops[-1]["fn"] = ca

            for d in (1, 3):
                j = 4 - d
                v0, q0 = 2048 * (2 * h + d // 2), c0 + 128 * j
                if d == 1:
                    acc([(X(ca, c, 512, 4, p=p), X("ONES", a, b), X("CVX", 0, 128)) for c in range(4)], True, False)
                    ops[-1]["r"] += X("QL", q0 + a, q0 + a + 32)[1]
                src, ws = ("py%d" % h, 0) if d == 3 and (t, h) in HY and a < EARLY else (pn, 4 * d - 4)
                acc([(X(ca, j - 1, 512, 4, p=p), X("ONES", a, b), X("CK", 0, 128)),
                     (X(ca, j - 1, 512, 4, p=p), X("GB", 128 * h + a, 128 * h + b), X("WG", 0, 128))]
                    + [(X(ca, 4 * k + j - 1, 512, 64, p=p), X(src, 16 * a + k, 16 * b, 16), X("WS", ws, ws + 8)) for k in range(16)],
                    False, False)
                ops[-1]["fn"] = ca
                cds = lambda a, b, v0=v0: X("cd", v0 + 16 * a, v0 + 16 * b)
                cvs = lambda a, b: X("cv", v0 + 16 * a, v0 + 16 * b)
                pieces(lambda a, b, cds=cds, q0=q0: vtt(cds(a, b), ind(twin, X("QL", q0 + a, q0 + b)), X(gx, 16 * a, 16 * b), A.add),
                       a, m, TW, "%s%d%d" % (" p q"[d], t, h))
                l, by = [], (t, h, d) in BYDMA
                sums([], j - 1, "cd", v0 + 16 * a, 16, "WD", a, m)
                cuts = LAST if h and d == 3 else range(a, b + 1, 64)
                for c, e in zip(cuts, cuts[1:]):
                    tag = "%s%d%d%d" % (" P Q"[d], t, h, c // 64 + c // 96)
                    if by:
                        cf = X("CF", 0, 16 * (e - c))
                        dma("G", [cds(c, e)], [cds(c, e), cf], [(cds(c, e)[0], cf[0])], DLAT, tag)
                        ops[-1]["cost"]["G"] = 1.0
                    else:
                        l += compare(tag, cvs(c, e), cds(c, e), [X(ca, j, 512, 4, p=(c, e))])
                    if e == b or e == 96:
                        c = 96 if c == 96 else a
                        sums(l, j, "cv", v0 + 16 * c, 16, "WB", c, e)
                        l = []
            for c in range(m, b, 32):
                x0 = 1024 * h + 32 * (c - m)
                for i in range(c, c + 32, 8):
                    for u in range(i, i + 8):
                        y0, q0 = 1024 * h + 32 * (u - m), 128 * h + 2 * (u - m)
                        act(X("cs", y0, y0 + 32), ind(twin, X("QS", q0, q0 + 2)), AF.Identity, X(gx, 16 * u, 16 * u + 1))
                    run(8, "s%d%d%d" % (t, h, i // 8))
                l = compare("R%d%d%d" % (t, h, c // 32), X("cw", x0, x0 + 1024), X("cs", x0, x0 + 1024),
                            [X(ca, j, 512, 4, p=(c, c + 32)) for j in (1, 3)])
                for d in (1, 3):
                    sums([], 3 - d, "cs", x0 + 8 * (d - 1), 32, "WD", c, c + 32)
                    sums(l if d == 1 else [], 4 - d, "cw", x0 + 8 * (d - 1), 32, "WB", c, c + 32)
            scan(X("SC", c0, c0 + 512, p=p, rows=rows), X(ca, 0, 512, p=p), X("CO", c0, c0 + 512, p=p, rows=rows), -BIG, A.max, A.min)
            hs, x = (128 * h + a, 128 * h + b), psum()
            o = X(x, 0, b - a)
            group(x, [(o, X("OFR", 0, 128), X("ONES", a, b))], [(o, X("SC", c0 + 3, c0 + 512, 4, p=p, rows=rows), X("ID32", a, b, p=p))],
                  1, cds(b - 32, b))
            vtt(X("VI", *hs), o, X("T0", *hs), A.max)
            vts(X("QN", *hs), X("VI", *hs), PR - 1, A.bitwise_and)
            vcopy(X("LOL", *hs), X("QN", *hs))
            gm, g0 = "GM%d" % ((h + t) & 1), 16 * ((h + t) >> 1)
            cs = lambda nm, a, b: X(nm, 2048 * h + 16 * a, 2048 * h + 16 * b)

            def largest(a, b):
                scan(cs("DC", a, b), cs("DS", a, b), X(gm, g0, g0 + 512), 0.0, A.max, A.add)
                ops[-1]["tag"] += str(a // 32)

            pieces(lambda a, b, win=win: move(cs("DS", a, b), ind(win, X("LOL", 128 * h + a, 128 * h + b))), a, b, 32, "e%d%d" % (t, h), largest)
            if h == 0:
                vts(X("SEND%d" % t, a, b), X("DC", 16 * a + 15, 16 * b, 16), 256.0, A.add, 255.0, A.min)
                send(a, b)
            if b == 128:
                if h:
                    vts(X("F", 17 + B, 16 + B + L, 2), X("DC", 2048 + 15, 4096, 16), 256.0, A.add, 255.0, A.min)
                else:
                    for copy in (gcopy, vcopy, act):
                        copy(X("F", 16 + B, 16 + B + L, 2), X("SEND%d" % t, 0, 128))
                    either(None, 3)
                if t + 1 < R:
                    pairs(X("TT", 16 + B + h, 16 + B + L, 2), X("F", 16 + B + h, 16 + B + L, 2), G[h])

        def send(a, b):
            dst = T.cores[(rank + 1 + t % 7) % len(T.cores)]
            src = T.cores[(rank - 1 - t % 7) % len(T.cores)]
            es = topo.engines(core, dst)
            rid, pid, _se = topo.addr(dst)
            nm = "%d%d" % (t, a // 64)
            out, buf = T.F[:, cc + a:cc + b], T["SEND%d" % t][:, a:b]
            gone = (None, [("gone" + nm, 0, 1, 1, ALL)])
            rec("s", "G", [gone], [X("SEND%d" % t, a, b)],
                lambda e: e.remote_dma(out_ap=out, in_ap=buf, remote_sem=T.sem["ar" + nm], local_sem=T.sem["lc" + nm],
                                       pid=pid, routing_id=rid, dma_engine_mask=sum(1 << x for x in es)),
                0.3, 2.0, ("lc" + nm, len(es)))
            rec("a", "R", [X("F", cc + a, cc + b)], [gone], None, 0.3, ARR[min(1, sent[0])],
                ("ar" + nm, len(topo.engines(src, core))))
            sent[0] += 1

        def rename(h):
            hs, kk, r0, at[0] = HS[h], "KK%d" % h, 256 * h, "%d%d" % (t, h)
            hif, red = X("HIF", *hs), X("RZ", r0, r0 + 128)
            move(hif, X("VI", *hs), 132.875, 1.0 / PR)
            for x, c, w in ((red, 128.0, -1), (X("RZ", r0 + 128, r0 + 256), 133.0, 1)):
                vts(x, hif, c, A.is_equal, float(PR), A.mult)
                act(x, hif, AF.Relu, bias=PR * (1.0 - w * c), scale=float(w * PR))
                either(None, 2)

            def sums(b):
                return [(X(b, 128, 256), X("NBD", 0, 128), hif), (X(b, 128, 256), X("OS", 0, 128), red),
                        (X(b, 256, 384), X("OS", 0, 128), red)]

            pm, ca, gt, rows = psum(), psum(), X("GT", *hs), X("MSK", 0, 128, p=(0, 16))
            acc([(X(pm, 128, 384), rows, X(kk, 128, 384, p=(0, 16)))] + sums(pm))
            act(X("WW", r0, r0 + 128), X(pm, 128, 256), AF.Sign, bias=2128 - 255.5)
            act(X("WW", r0 + 128, r0 + 256), X(pm, 256, 384), AF.Sign, bias=-127.5)
            acc([(X(ca, 0, 384), rows, X(kk, 0, 384, p=(0, 16))),
                 (X(ca, 0, 384), X("ONES", 0, 128, p=(0, 2)), X("CB%d" % t, 0, 384, p=(0, 2))),
                 (X(ca, 0, 128), ID, gt), (X(ca, 256, 384), NID, gt),
                 (X(ca, 128, 384), ID, X("RZ", r0, r0 + 256))] + sums(ca), True, False)
            acc([(X(ca, 128, 384), X("N64", 0, 128), X("WW", r0, r0 + 256)),
                 (X(ca, 128, 256), X("N64", 0, 128), X("WW", r0, r0 + 128))], False, True)
            m1, q = X("M1", *hs), X("QN", *hs)
            if t + 1 == R:
                q = X("T0", *hs)
                move(q, X("QN", *hs), -16.0)
            vtt(m1, X(ca, 0, 128), q, A.max)
            vtt(m1, X(ca, 128, 256), m1, A.max)
            vtt(X("NUM", *hs) if t + 1 < R else X("YP", h, 256, 2), X(ca, 256, 384), m1, A.max)
            if t + 1 < R:
                vcopy(X("PL", *hs), X("NUM", *hs))

        for h in (0, 1):
            gather("c%d%d" % (t, h), X("PS", h, 256, 2), ind(X("px%d%d" % (t, h), 0, 2048), X("OFF", 8 * h, 8 * h + 8)))
        more = [(h, X("PS2", 128 * h, 128 * h + EARLY)) for h in (0, 1) if (t, h) in HY]
        for h, x in more:
            gather("d%d%d" % (t, h), x, ind(X("py%d" % h, 0, 16 * EARLY), X("OFF", 8 * h, 8 * h + EARLY // 16)))
        at[0] = "%d0" % t
        grow("PS", 256, 16 + B, NB * t, t, [("GB", 0), ("GB", 128)], more)
        for h in (0, 1):
            for a, b in ((0, 64), (64, 128)) if (t, h) in SPLIT else ((0, 128),):
                tests(h, a, b)
            rename(h)
        come(t)
        if t + 1 == R:
            dma("Y", [], [X("YP", 0, 256)], [(T.yp[:], T.YP[:])], 1.9)
            ops[-1]["cost"]["Y"] = 0.7
        y0 = NB * t
        dma("Y", [], [X("F", cc, cc + 128)], [(T.yf[:, y0 + L:y0 + NB], T.F[:, cc:cc + 128])])
        dma("Y", [], [X("F", 16 + B, 16 + B + L)], [(T.yf[:, y0:y0 + L], T.F[:, 16 + B:16 + B + L])], 1.9)
        ops[-1]["cost"]["Y"] = 0.4
    return ops


def issue(g, T, ops):
    eng = {"V": g.vector, "S": g.scalar, "T": g.tensor, "G": g, "Y": g.sync}
    sname = {"V": "sv", "S": "ss", "T": "st", "G": "sg"}
    cnt = {"V": 0, "S": 0, "T": 0, "G": 0}
    clk = {q: {} for q in "VSTGY"}
    log = {}
    total = {}
    ndma = 0
    who = PLAN["who"]
    todo = {}
    for o in ops:
        if o["kind"] == "t" and o["fn"]:
            todo[o["fn"]] = todo.get(o["fn"], 0) + 1

    def where(x):
        return x[0] if lease(x) is None else PLAN["bank"][x[0]]

    def waits(q, reads, writes):
        need = []
        for w, regs in ((0, reads), (1, writes)):
            for x in regs:
                ps = lease(x) is not None
                for e in log.get(where(x), []):
                    if ps and e["q"] != q:
                        need.append(e)
                        continue
                    if (ps and q == "T") or not (e["w"] or w) or not meet(x, e["x"]):
                        continue
                    if e["q"] == q and w and not e["w"]:
                        continue
                    need.append(e)
        want = {}
        for e in need:
            if clk[q].get(e["sem"], 0) < e["val"] and want.get(e["sem"], (0, None))[0] < e["val"]:
                want[e["sem"]] = (e["val"], e)
        for s in list(want):
            v = want[s][0]
            for s2 in want:
                if s2 != s and want[s2][1]["clk"].get(s, 0) >= v:
                    del want[s]
                    break
        for s, (v, e) in want.items():
            eng[q].wait_ge(T.sem[s], v)
            for a, b in e["clk"].items():
                clk[q][a] = max(clk[q].get(a, 0), b)
            clk[q][s] = max(clk[q].get(s, 0), v)

    def note(q, reads, writes, sem, val, c):
        c = dict(c)
        c[sem] = max(c.get(sem, 0), val)
        total[sem] = max(total.get(sem, 0), val)
        for w, regs in ((0, reads), (1, writes)):
            for x in regs:
                l = log.setdefault(where(x), [])
                if lease(x) is not None:
                    l[:] = [e for e in l if not (e["q"] == q and cover(x, e["x"]) and (w or not e["w"]))]
                elif w:
                    l[:] = [e for e in l if not cover(x, e["x"])]
                l.append({"q": q, "w": w, "x": x, "sem": sem, "val": val, "clk": c})

    queue = PLAN["qs"]
    skip = set(j for run in PLAN["runs"].values() for j in run[:-1])
    for i in PLAN["order"]:
        o = ops[i]
        q, r, w = o["q"], o["r"], o["w"]
        if o["kind"] == "a":
            note("D", [], w, o["data"][0], o["data"][1], {})
            continue
        q, fns = queue[i], o["fn"]
        if i in skip:
            continue
        if i in PLAN["runs"]:
            ends = [x for j in PLAN["runs"][i] for x in ops[j]["span"]]
            o["make"](min(ends), max(ends))
            x = ops.pop()
            fns, r, w = x["fn"], x["r"], x["w"]
        waits(q, r, w)
        if o["kind"] in "cg":
            cnt[q] += 1
            (fns if o["kind"] == "c" else fns[q])(eng[q]).then_inc(T.sem[sname[q]], 1)
            note(q, r, w, sname[q], cnt[q], clk[q])
        elif o["kind"] == "m":
            for fn in fns:
                cnt[q] += 1
                fn(eng[q]).then_inc(T.sem[sname[q]], 1)
            note(q, r, w, sname[q], cnt[q], clk[q])
        elif o["kind"] == "t":
            if o["fn"]:
                todo[o["fn"]] -= 1
            run = [m for m in o["data"] if len(m) == 5 or who[m[5][0]] == m[5][1]]
            for n, m in enumerate(run):
                x, lh, rh, a, b = m[:5]
                cnt["T"] += 1
                if n + 1 == len(run):
                    b = o["data"][-1][4] or bool(o["fn"] and not todo[o["fn"]])
                g.tensor.matmul(x[0], lh[0], rh[0], a, b).then_inc(T.sem.st, 1)
            note("T", r, w, "st", cnt["T"], clk["T"])
        elif o["kind"] == "d":
            sem = "d%d" % ndma
            ndma += 1
            for (x, y) in o["data"]:
                if q == "G":
                    g.dma_start(x, y, accum_op=AluOpType.add).then_inc(T.sem[sem], 16)
                else:
                    eng[q].dma_start(x, y).then_inc(T.sem[sem], 16)
            note("D", r, w, sem, 16 * len(o["data"]), clk[q])
        else:
            o["fn"](g)
            note("D", r, w, o["data"][0], o["data"][1], clk["G"])
    for s, v in total.items():
        if clk["Y"].get(s, 0) < v:
            g.sync.wait_ge(T.sem[s], v)
